import numpy as np, ml_dtypes
CORES = [9,25,41,57]
N = 4
BF = ml_dtypes.bfloat16
W, L, CAP, EQ, CNT, RO = 4096, 256, 64, 13, 9, 5
TAU = [96, 700, 24, 2496, 300]
WA = np.array([7, 113, 51, 229, 87, 19, 161, 203, 35, 149, 71, 247, 93, 181, 125, 11])
WB = np.array([1, 3, 2, 7, 5, 1, 6, 3, 7, 2, 5, 4, 1, 6, 3, 5])
KP = np.array([3, 18, 45, 71, 102, 125, 150, 187, 208, 233, 260, 291, 318, 345, 382, 407])
KZ = np.array([0, 0, 0, 0, 0, 0, 25, 0, 0, 0, 1, 0, 0, 0, 0, 0])
TOP = 130560
def home(k):
    return (k @ WB) & (N - 1)
def look(k, n):
    u = (k @ WA) & (W - 1)
    return ((u * (2 * n + 1) >> 5)[..., None] + KP * u[..., None]) & (W - 1)
def whole8(x):
    return np.minimum(np.rint(np.asarray(x, np.float32)), TOP).astype(BF).astype(np.float32)
def pool(rng, keys):
    keys = keys[np.any(keys > 0, axis=1)]; z = home(keys); out = []
    for r in range(N):
        a = np.nonzero(z == r)[0]
        if len(a) == 0: a = np.arange(len(keys))
        out.append(keys[np.resize(rng.permutation(a), 4)])
    return np.stack(out)
def bend(rng, k, c, flip):
    n = len(k); i = (np.arange(16) * (2 * rng.integers(0, 8, (n, 1)) + 1) + rng.integers(0, 16, (n, 1))) & 15
    new = 255 - k if flip else (k + rng.integers(1, 256, k.shape)) & 255
    return np.where(i < np.asarray(c)[:, None], new, k)
def cut(rng, a, ln):
    col = np.arange(16)[None, :]; ln = np.asarray(ln)[:, None]
    a = np.where(col == ln, 0, a)
    return np.where((col > ln) & (rng.random((len(a), 1)) < 0.6), 0, a)
def thin(rng, k):
    i = np.where(rng.random(k) < 0.5, 15, rng.integers(0, 16, k))
    x = np.where(rng.random(k) < 0.5, rng.choice(np.array([1, 255]), k), rng.integers(1, 256, k))
    return np.where(np.arange(16)[None, :] == i[:, None], x[:, None], 0)
def nought(cand):
    at = np.nonzero((((cand @ WA) & (W - 1)) == 0) & ((home(cand) & 1) == 1))[0]
    return cand[at[0]] if len(at) else KZ
def keys_plain(rng):
    return rng.integers(0, 256, (512, 16))
def name_plain(rng, shape):
    return rng.integers(1, 256, shape)
def vt_plain(rng, k):
    x = np.exp2(8 + 9 * rng.random((k, 1))) * (0.25 + 0.75 * rng.random((k, 16)))
    x = np.where(rng.random((k, 16)) < 0.15, np.exp2(8 * rng.random((k, 16))) - 1, x)
    return whole8(np.where(rng.random((k, 1)) < 0.25, TOP, x))
def vl_plain(rng, k):
    x = np.exp2(11 + 6 * rng.random((k, 1))) * (0.25 + 0.75 * rng.random((k, 16)))
    return whole8(np.where(rng.random((k, 16)) < 0.1, np.exp2(8 * rng.random((k, 16))) - 1, x))
def make(rng, keys, flip, vt, vl, name, fill, lens):
    P = np.stack([pool(rng, keys(rng)) for g in range(8)]); few = [name(rng, 24) for g in range(8)]
    F = np.zeros((N, 8, W, 16), np.int64); G = np.zeros((N, 8, W, 16), np.int64); V = np.zeros((N, 8, W, 16), np.float32)
    f = np.zeros((N, 8, L, 16), np.int64); v = np.zeros((N, 8, L, 16), np.float32); nm = np.zeros((N, 8, L, 16), np.int64)
    for r in range(N):
        for g in range(8):
            Q = P[g].reshape(-1, 16)
            F[r, g] = bend(rng, P[g, r][rng.integers(0, 4, W)], rng.integers(0, 18 - EQ, W), flip) * (rng.random((W, 1)) < fill[g])
            G[r, g] = bend(rng, Q[rng.integers(0, len(Q), W)], rng.integers(0, 3, W) * (rng.random(W) < 0.2), flip)
            G[r, g] *= (rng.random((W, 1)) >= 0.04)
            V[r, g] = vt(rng, W)
            k = np.where(rng.random((L, 1)) < 0.7, P[g, r][rng.integers(0, 4, L)], Q[rng.integers(0, len(Q), L)])
            f[r, g] = bend(rng, k, rng.integers(0, 3, L) * (rng.random(L) < 0.2), flip) * (rng.random((L, 1)) >= 0.05)
            v[r, g] = vl(rng, L)
            a = np.where(rng.random((L, 16)) < 0.5, few[g][rng.integers(0, 24, (L, 16))], name(rng, (L, 16)))
            nm[r, g] = cut(rng, a, rng.choice(np.array(lens), L))
    return P, F, G, V, f, v, nm
def pack(F, G, V, f, v, nm):
    on = np.any(F > 0, axis=3, keepdims=True); d = {}
    for k, a in (("rf", F), ("rg", np.where(on, G, 0)), ("rv", np.where(on, V, 0)), ("wf", f), ("wv", v), ("nm", nm)):
        a = np.ascontiguousarray(np.swapaxes(a, 2, 3).reshape(N, 128, -1))
        d[k] = a.astype(np.int32) if k == "nm" else a.astype(np.float32).astype(BF)
    return d
def setup_inputs(rng):
    m = make(rng, keys_plain, False, vt_plain, vl_plain, name_plain, rng.uniform(0.4, 0.6, 8), [0, 1, 1, 2, 2, 3, 4, 6, 9, 16])
    return pack(*m[1:])
def setup_inputs_spread(rng):
    def keys(rng): return np.exp2(8 * rng.random((512, 16))).astype(np.int64) - 1
    def vt(rng, k): return whole8(np.exp2(17 * rng.random((k, 1))) * np.exp2(-3 * rng.random((k, 16))) * (rng.random((k, 16)) > 0.0625))
    def vl(rng, k): return whole8(np.exp2(9 + 8 * rng.random((k, 1))) * np.exp2(-3 * rng.random((k, 16))))
    def name(rng, shape): return np.exp2(8 * rng.random(shape)).astype(np.int64)
    m = make(rng, keys, False, vt, vl, name, rng.permutation(np.linspace(0.1, 0.95, 8)), [0, 1, 2, 3, 5, 8, 12, 15, 16])
    return pack(*m[1:])
def setup_inputs_near(rng):
    def keys(rng):
        b = np.repeat(rng.integers(0, 256, (1, 16)), 512, axis=0); return bend(rng, b, rng.integers(0, 19 - EQ, 512), False)
    def vt(rng, k):
        o = np.argsort(rng.random((k, 16)), axis=1); c = CNT - rng.integers(0, 2, (k, 1)); tau = np.array(TAU)[rng.integers(0, RO, (k, 1))]
        low = np.where((o == c) | (rng.random((k, 16)) < 0.5), tau, 0)
        a = whole8(np.where(o < c, TOP * (0.5 + 0.5 * rng.random((k, 16))), low))
        return np.where(rng.random((k, 1)) < 0.3, a, vt_plain(rng, k))
    def vl(rng, k):
        a = whole8(TOP * (0.5 + 0.5 * rng.random((k, 16))))
        return np.where(rng.random((k, 1)) < 0.6, a, vl_plain(rng, k))
    m = make(rng, keys, False, vt, vl, name_plain, rng.uniform(0.3, 0.7, 8), [0, 1, 2, 3, 4, 5, 7, 16])
    return pack(*m[1:])
def setup_inputs_ends(rng):
    def keys(rng): return 255 * rng.integers(0, 2, (512, 16))
    def vt(rng, k):
        a = np.where(rng.random((k, 16)) < 0.75, TOP, 0); z = rng.random((k, 1)); one = np.arange(16)[None, :] == rng.integers(0, 16, (k, 1))
        a = np.where((z >= 0.6) & (z < 0.75) & (a == 0) & (rng.random((k, 16)) < 0.5), 1, a)
        a = np.where(z < 0.6, TOP, a); a = np.where((z >= 0.4) & (z < 0.6) & one, 130048, a)
        return np.where(z > 0.95, 0, a).astype(np.float32)
    def vl(rng, k):
        a = np.where(rng.random((k, 16)) < 0.8, TOP, 0); z = rng.random((k, 1))
        a = np.where((z >= 0.8) & (z < 0.95) & (a == 0), 1, a); a = np.where(z < 0.5, TOP, a)
        return np.where(z > 0.95, 0, a).astype(np.float32)
    def name(rng, shape): return rng.choice(np.array([255] * 8 + [254, 1]), shape)
    P, F, G, V, f, v, nm = make(rng, keys, True, vt, vl, name, rng.uniform(0.4, 0.6, 8), [0, 1, 1, 2, 3, 15, 16, 16])
    col = np.arange(16)
    for g in range(8):
        Q = P[g].reshape(-1, 16); H = look(Q[:, None, :], np.arange(1, 256)[None, :]); at = np.argwhere(H == W - 1)
        odd = np.nonzero(((Q @ WA) & 1) == 1)[0]
        for r in range(N):
            away = odd[(odd >> 2) != r]
            if len(away):
                for lane, ln in ((L - 2, 16), (L // 2, 2), (1, 1)):
                    x = Q[away[rng.integers(0, len(away))]]; n = int(rng.choice(np.array([1, 255]))); h = look(x[None, :], np.array([n]))[0]
                    j = int(rng.integers(0, 16)); a = np.full((16, 16), TOP); a[:, j] = 0; a[15, j] = 1; a[1:15, (j + 1) & 15] = 0
                    F[r, g, h] = x; G[r, g, h] = Q[rng.permutation(len(Q))[:16]]; V[r, g, h] = a
                    f[r, g, lane] = x; v[r, g, lane] = TOP; nm[r, g, lane] = np.where(col == 0, n, np.where(col < ln, 255, 0))
            if len(at) == 0: continue
            i, n, m = at[rng.integers(0, len(at))]; h = H[i, n]
            F[r, g, h] = Q[i]; G[r, g, h] = Q[rng.integers(0, len(Q), 16)]
            a = np.full((16, 16), TOP); a[:m, rng.integers(0, 16)] = 130048; V[r, g, h] = a
            for lane, ln in ((0, 2), (L // 2 + 1, 16), (L - 1, 16)):
                f[r, g, lane] = Q[i]; v[r, g, lane] = TOP; nm[r, g, lane] = np.where(col == 0, n + 1, np.where(col < ln, 255, 0))
    return pack(F, G, V, f, v, nm)
def setup_inputs_corners(rng):
    fill = np.array([1.0, 0.0, 0.0, 0.0, 0.5, 0.5, 0.5, 0.5])
    P, F, G, V, f, v, nm = make(rng, keys_plain, False, vt_plain, vl_plain, name_plain, fill, [0, 1, 1, 2, 3, 15, 16])
    F[:, 0, :, 0] = np.maximum(F[:, 0, :, 0], 1)
    cand = rng.integers(0, 256, (131072, 16)); cand[:, 0] = np.maximum(cand[:, 0], 1)
    kz = nought(cand)
    H = look(cand, np.zeros(len(cand), np.int64)); at = np.argwhere(H == W - 1)
    for r in range(N):
        v[r, 0, ::2] = np.where(rng.random((L // 2, 1)) < 0.5, 0, TOP)
        for g in (1, 2, 3): nm[r, g] = cut(rng, rng.integers(1, 256, (L, 16)), rng.choice(np.array([1, 16]), L))
        f[r, 2] = P[2, (r + 1) % N][rng.integers(0, 4, L)]
        to = np.concatenate([np.full(CAP, (r + 1) % N), np.full(CAP + 1, (r + 2) % N), np.full(CAP - 1, (r + 3) % N), (r + np.arange(4, N)) % N]).astype(np.int64)
        f[r, 3] = 0; f[r, 3, rng.permutation(L)[:len(to)]] = P[3][to, rng.integers(0, 4, len(to))]
        f[r, 4] = 0
        if r % 2:
            for lane in (0, L // 2, L - 1): f[r, 4, lane] = P[4, r, lane % 4]
        f[r, 5] = P[5, r, 0]; nm[r, 5] = 0
        if r == N - 1: f[r, 5, 1::2] = P[5, r, 1]
        f[r, 6, 1::2] = kz; nm[r, 6] = cut(rng, rng.integers(1, 256, (L, 16)), np.where(np.arange(L) % 4 == 3, 16, rng.choice(np.array([1, 2, 16]), L)))
        F[r, 6, 0] = 0 if r % 2 else kz; G[r, 6, 0] = kz; V[r, 6, 0] = TOP; v[r, 6, 3::4] = TOP
        if len(at):
            i = at[rng.integers(0, len(at)), 0]; h = H[i]
            F[r, 7, h] = P[7, r][rng.integers(0, 4, 16)]; F[r, 7, h, 0] = np.maximum(F[r, 7, h, 0], 1); F[r, 7, W - 1] = 0
            for lane in ((L - 1,) if r % 2 else (5, L - 1)): f[r, 7, lane] = cand[i]; nm[r, 7, lane] = 0
    return pack(F, G, V, f, v, nm)
def setup_inputs_thin(rng):
    P, F, G, V, f, v, nm = make(rng, keys_plain, False, vt_plain, vl_plain, name_plain, rng.uniform(0.4, 0.6, 8), [0, 1, 1, 2, 2, 3, 4, 6, 9, 16])
    cand = rng.integers(0, 256, (131072, 16)); cand[:, 0] = np.maximum(cand[:, 0], 1)
    kz = nought(cand); z = int(home(kz))
    for r in range(N):
        f[r, 0] = rng.integers(0, 256, (L, 16)); nm[r, 0, :, 0] *= (rng.random(L) < 0.25 * (r & 1))
        F[r, 1] = thin(rng, W) * (rng.random((W, 1)) < 0.5); G[r, 1] = np.where(rng.random((W, 1)) < 0.5, thin(rng, W), G[r, 1])
        f[r, 1] = thin(rng, L); nm[r, 1, ::2, 0] = 0
        for g in (2, 3):
            G[r, g] *= (rng.random((W, 1)) >= 0.5); V[r, g] = np.where(rng.random((W, 1)) < 0.5, TOP, V[r, g])
            v[r, g] = np.where(rng.random((L, 1)) < 0.5, TOP, v[r, g])
            nm[r, g] = cut(rng, rng.integers(1, 256, (L, 16)), rng.choice(np.array([2, 3, 4, 16]), L))
        keep = rng.permutation(L)[:CAP // 2]; m = np.zeros((L, 1), np.int64); m[keep] = 1
        f[r, 6] *= m; nm[r, 6, :, 0] = np.maximum(nm[r, 6, :, 0], 1)
        F[r, 6, 0] = 0 if r == z else kz; G[r, 6, 0] = P[6, (r + 1) % N, 0]; V[r, 6, 0] = TOP
        if r == 0: f[r, 6] = 0
        elif r != z:
            f[r, 6, keep[:3]] = kz; v[r, 6, keep[:3]] = TOP; nm[r, 6, keep[:3]] = cut(rng, rng.integers(1, 256, (3, 16)), np.ones(3, np.int64))
    F[0, 2, 0] = np.where(rng.permutation(16) < 16 - EQ, rng.integers(1, 256, 16), 0); F[0, 3, 0] = thin(rng, 1)[0]
    for g in (2, 3): G[0, g, 0] = P[g, N - 1, 0]; V[0, g, 0] = TOP
    return pack(F, G, V, f, v, nm)
def check_inputs(d):
    bad = []
    for k, hi in (("rf", 255), ("rg", 255), ("rv", TOP), ("wf", 255), ("wv", TOP), ("nm", 255)):
        a = np.asarray(d[k]).astype(np.float64)
        if not np.all((a >= 0) & (a <= hi) & (a == np.floor(a))): bad.append("range of " + k)
    on = np.any(np.asarray(d["rf"]).astype(np.float32).reshape(N, 8, 16, W) != 0, axis=2, keepdims=True)
    for k in ("rg", "rv"):
        if np.any((np.asarray(d[k]).astype(np.float32).reshape(N, 8, 16, W) != 0) & ~on): bad.append("empty places of " + k)
    return bad
def reference(rf, rg, rv, wf, wv, nm):
    F, G, V = [a.astype(np.float32).astype(np.int32).reshape(N, 8, 16, W) for a in (rf, rg, rv)]
    f, v = [a.astype(np.float32).astype(np.int64).reshape(N, 8, 16, L) for a in (wf, wv)]
    na = nm.astype(np.int64).reshape(N, 8, 16, L); f0 = f.copy(); n0 = na[:, :, 0].copy()
    for t in range(RO):
        there = np.any(f0 != 0, axis=2)
        done = there & (na[:, :, 0] == 0); wait = there & (na[:, :, 0] != 0)
        q = np.where(done[:, :, None], f0, f); n = np.where(done, n0, na[:, :, 0])
        u = np.sum(WA[:, None] * q, axis=2) & (W - 1)
        h = ((u * (2 * n + 1) >> 5)[:, :, None] + KP[:, None] * u[:, :, None]) & (W - 1)
        ix = h.reshape(N, 8, 1, 16 * L)
        Fh = np.take_along_axis(F, ix, 3).reshape(N, 8, 16, 16, L)
        lo = np.minimum(np.take_along_axis(V, ix, 3).reshape(N, 8, 16, 16, L), v[:, :, :, None, :].astype(np.int32))
        same = np.sum(Fh == f[:, :, :, None, :].astype(np.int32), axis=2); over = np.sum(lo > TAU[t], axis=2)
        ok = (same >= EQ) & (over >= CNT) & wait[:, :, None]
        best = np.argmax(np.where(ok, np.sum(lo, axis=2), -1), axis=2)
        hit = np.any(ok, axis=2)[:, :, None]; bh = np.take_along_axis(h, best[:, :, None], 2)
        Gb = np.take_along_axis(G, bh, 3); Vb = np.take_along_axis(V, bh, 3)
        free = np.all(Fh == 0, axis=2); can = np.any(free, axis=2) & done
        place = np.take_along_axis(h, np.argmax(free, axis=2)[:, :, None], 2)[:, :, 0]
        for r in range(N):
            for g in range(8):
                lanes = np.nonzero(can[r, g])[0]; pl, first = np.unique(place[r, g, lanes], return_index=True); w = lanes[first]
                F[r, g][:, pl] = f0[r, g][:, w]; G[r, g][:, pl] = f[r, g][:, w]; V[r, g][:, pl] = v[r, g][:, w]
        f = np.where(hit, Gb, f); v = np.where(hit, np.minimum(v, Vb), v)
        na = np.where(hit, np.concatenate([na[:, :, 1:], np.zeros((N, 8, 1, L), np.int64)], axis=2), na)
        if t < RO - 1:
            goal = np.sum(WB[:, None] * np.where(na[:, :, :1] == 0, f0, f), axis=2) & (N - 1)
            S = np.concatenate([f0, f, v, na, n0[:, :, None]], axis=2); S2 = np.zeros_like(S)
            for q in range(N):
                for d in range(N):
                    go = (wait[q] & (goal[q] == d)).astype(np.int64); before = np.add.accumulate(go, axis=1) - go
                    gi, li = np.nonzero((go == 1) & (before < CAP))
                    S2[d, gi, :, q * CAP + before[gi, li]] = S[q, gi, :, li]
            f0, f, v, na, n0 = S2[:, :, :16], S2[:, :, 16:32], S2[:, :, 32:48], S2[:, :, 48:64], S2[:, :, 64]
    yf = np.where(wait[:, :, None], f, 0); yv = np.where(wait[:, :, None], v, 0)
    z = [np.sum(a.reshape(N, 128, 32, W // 32), axis=2).astype(np.float32) for a in (F, G, V)]
    return {"zf": z[0], "zg": z[1], "zv": z[2], "yf": yf.reshape(N, 128, L).astype(np.float32).astype(BF), "yv": yv.reshape(N, 128, L).astype(np.float32).astype(BF)}

@@ -1,0 +1,647 @@
+from concourse.mybir import AluOpType, AxisListType, ActivationFunctionType
+
+W, L, RO = 4096, 256, 5
+TAU = [96, 700, 24, 2496, 300]
+WA = [7, 113, 51, 229, 87, 19, 161, 203, 35, 149, 71, 247, 93, 181, 125, 11]
+WB = [1, 3, 2, 7, 5, 1, 6, 3, 7, 2, 5, 4, 1, 6, 3, 5]
+KP = [3, 18, 45, 71, 102, 125, 150, 187, 208, 233, 260, 291, 318, 345, 382, 407]
+LC, NS, ZG, WGN = 4352, 5376, 5888, 5904
+LV, ZV, LON = 4096, 5120, 5136
+B16, F16, F32, I32, U16 = "bfloat16", "float16", "float32", "int32", "uint16"
+
+_SB = {
+    "tF": (4352, B16), "tV": (4352, B16), "tG": (WGN, B16), "lo": (LON, B16),
+    "vg": (W, B16), "eqf": (W, B16), "sg": (W, B16), "eqd": (W, B16),
+    "lnd0": (1024, B16), "lnd1": (1024, B16), "lnd2": (1024, B16), "lnd3": (1024, B16), "lnd4": (1024, B16),
+    "snd0": (768, B16), "snd1": (768, B16), "snd2": (768, B16), "snd3": (768, B16),
+    "pre": (1040, B16), "idt": (1280, B16), "yfb": (L, B16), "yvb": (L, B16), "zb": (384, F32),
+    "wfs": (L, B16), "wvs": (L, B16), "nms": (L, I32), "nmb": (L, B16), "thf": (L, B16),
+    "pcol": (8, I32), "col": (32, F32), "jf": (L, F32), "jr": (L, F32), "jq": (L, F32), "j4": (144, F32), "lo16": (16, F32),
+    "jb": (L, B16), "ab": (16, F32), "ab2": (16, F32), "ib": (128, B16), "ih": (128, F16), "i3": (128, B16), "i117": (128, B16),
+    "ineg": (128, B16), "ones": (128, B16), "onesh": (128, F16), "uge": (128, B16), "uget": (128, B16), "wn": (128, B16), "shf": (128, B16),
+    "zA": (144, B16), "zB": (144, B16), "z0": (144, B16), "z15": (144, B16), "zt": (144, B16), "zn": (144, B16),
+    "z65": (144, B16), "z16": (144, B16), "z4": (144, B16), "dk": (2048, F16), "dm": (L, B16), "hc": (L, B16),
+    "c13": (L, B16), "c1": (128, B16), "c2": (L, B16), "crm": (L, F32), "msk": (64, B16), "cst": (64, F16), "dmp": (16, F16),
+    "cd": (16, F32), "c0": (96, F32), "cp": (96, F32), "cq": (96, F32), "rep": (16, U16), "exo": (16, U16),
+    "patf": (8, U16), "patv": (8, U16), "patt": (16, F32), "z1": (144, B16), "zw": (144, B16), "z21": (144, B16),
+    "ui": (16, I32), "u": (16, I32), "zf_": (16, B16), "prod": (16, I32),
+    "cc": (16, I32), "uh": (16, F16), "ch": (16, F16), "hi": (L, I32), "h16": (L, U16), "cmp": (2 * L, B16),
+    "fl": (80, F32), "ta": (16, F32), "tb": (16, F32), "nw": (16, F32), "p6": (96, F32), "q6": (96, F32),
+    "pen": (512, B16), "ka": (128, F32), "k1": (128, F32), "k2": (64, F32), "k3": (32, F32), "best": (16, F32),
+    "ki": (16, I32), "vld": (16, F32), "val": (32, I32), "oh": (L, F16), "vq": (96, F32), "vp": (96, F32), "vp2": (96, F32),
+    "ha": (16, F32), "hb": (16, I32), "t6": (96, F32), "s6": (96, F32), "s16": (64, U16),
+    "gi": (16, I32), "g3": (16, I32), "go4": (64, B16), "inc": (64, B16), "tt4": (64, F16), "pos": (16, U16), "src": (64, U16),
+    "ex": (L, F16), "plr": (L, F16), "dmk": (L, B16), "win": (16, F32), "wt": (16, F32), "ot": (16, F32), "o16": (16, U16),
+}
+_PS = ["pV", "pE0", "pE1", "pK0", "pK1", "pA", "pB", "pC"]
+SCRATCH = {}
+_AT = {}
+for _k in _SB:
+    if _SB[_k][0] <= 96:
+        _a = "small_" + _SB[_k][1]
+        _n = SCRATCH[_a][1][1] if _a in SCRATCH else 0
+        _AT[_k] = (_a, _n)
+        SCRATCH[_a] = ("sbuf", [128, _n + (_SB[_k][0] + 15) // 16 * 16], _SB[_k][1])
+    else:
+        SCRATCH[_k] = ("sbuf", [128, _SB[_k][0]], _SB[_k][1])
+for _k in _PS:
+    SCRATCH[_k] = ("psum", [128, 512], F32)
+NDMA = 24
+SEMAPHORES = ["cv", "ca", "cp_", "cg"] + ["d%d" % i for i in range(NDMA)] + ["arr%d" % i for i in range(4)] + \
+             ["out%d" % i for i in range(12)]
+
+
+def S(name, lo, hi, step=1):
+    if name in _AT:
+        return ("ap", _AT[name][0], _AT[name][1] + lo, _AT[name][1] + hi, step)
+    return ("ap", name, lo, hi, step)
+
+
+def IND(win, off):
+    return ("ind", win, off)
+
+
+def _mask(a):
+    if a[1] in _PS:
+        return 1
+    m = 0
+    if a[4] == 1:
+        return ((1 << (a[3] - a[2])) - 1) << a[2]
+    for i in range(a[2], a[3], a[4]):
+        m |= 1 << i
+    return m
+
+
+def emit(g, T, ops):
+    Q = {"v": g.vector, "a": g.scalar, "p": g.tensor, "s": g.sync, "g": g}
+    CS = {"v": "cv", "a": "ca", "p": "cp_", "g": "cg"}
+    cnt = {"v": 0, "a": 0, "p": 0, "g": 0}
+    known = {q: {} for q in Q}
+    acc = {}
+    total = {}
+    tok = []
+    for i, o in enumerate(ops):
+        q = o["q"]
+        need = {}
+        touch = [(a, False) for a in o["r"]] + [(a, True) for a in o["w"]]
+        for a, wr in touch:
+            m = _mask(a)
+            ps = a[1] in _PS
+            for j, mj, wj in acc.get(a[1], []):
+                if not (m & mj):
+                    continue
+                qj = ops[j]["q"]
+                if ps:
+                    if qj == q:
+                        continue
+                elif not (wr or wj):
+                    continue
+                s, n, k = tok[j]
+                if known[q].get(s, 0) < n and need.get(s, (0, None))[0] < n:
+                    need[s] = (n, k)
+        if o["kind"] != "land":
+            order = sorted(need.items(), key=lambda e: -len(e[1][1]))
+            for s, (n, k) in order:
+                if known[q].get(s, 0) >= n:
+                    continue
+                Q[q].wait_ge(T.sem[s], n)
+                known[q][s] = n
+                for s2 in k:
+                    if known[q].get(s2, 0) < k[s2]:
+                        known[q][s2] = k[s2]
+        if o["kind"] == "c":
+            cnt[q] += 1
+            o["f"]().then_inc(T.sem[CS[q]], 1)
+            tok.append((CS[q], cnt[q], dict(known[q])))
+            total[CS[q]] = cnt[q]
+        elif o["kind"] == "dma":
+            o["f"]().then_inc(T.sem[o["sem"]], 16)
+            tok.append((o["sem"], 16, dict(known[q])))
+            total[o["sem"]] = 16
+        elif o["kind"] == "rem":
+            o["f"]()
+            tok.append((o["sem"], o["n"], dict(known[q])))
+            total[o["sem"]] = o["n"]
+        else:
+            tok.append((o["sem"], o["n"], {}))
+            total[o["sem"]] = o["n"]
+        for a, wr in touch:
+            m = _mask(a)
+            lst = acc.setdefault(a[1], [])
+            if wr and a[1] not in _PS:
+                lst[:] = [e for e in lst if e[1] & ~m]
+            if a[1] in _PS:
+                lst[:] = [e for e in lst if ops[e[0]]["q"] != q]
+            lst.append((i, m, wr))
+    for s in total:
+        if known["g"].get(s, 0) < total[s]:
+            g.wait_ge(T.sem[s], total[s])
+
+
+def rank_program(g, core, T, topo):
+    rank = T.rank_of(core)
+    if rank is None:
+        return
+    N = len(T.cores)
+    A = AluOpType
+    F = ActivationFunctionType
+    ops = []
+    nd = [0]
+
+    def ap(a):
+        if a[0] == "ind":
+            return ap(a[1]).indirect(ap(a[2]))
+        if a[4] == 1:
+            return T[a[1]][:, a[2]:a[3]]
+        return T[a[1]][:, a[2]:a[3]:a[4]]
+
+    def parts(a):
+        return [a[1], a[2]] if a[0] == "ind" else [a]
+
+    def rec(q, f, outs, ins, kind="c", **kw):
+        r, w = [], []
+        for a in ins:
+            if isinstance(a, tuple):
+                r += parts(a)
+        for a in outs:
+            if a[0] == "ind":
+                w.append(a[1])
+                r.append(a[2])
+            else:
+                w.append(a)
+        d = {"q": q, "f": f, "r": r, "w": w, "kind": kind}
+        d.update(kw)
+        ops.append(d)
+
+    def sc(x):
+        return ap(x) if isinstance(x, tuple) else x
+
+    def tt(o, a, b, op):
+        rec("v", lambda: g.vector.tensor_tensor(ap(o), ap(a), ap(b), op), [o], [a, b])
+
+    def ts(o, a, s1, op0, s2=None, op1=None):
+        if op1 is None:
+            rec("v", lambda: g.vector.tensor_scalar(ap(o), ap(a), sc(s1), None, op0), [o], [a, s1])
+        else:
+            rec("v", lambda: g.vector.tensor_scalar(ap(o), ap(a), sc(s1), sc(s2), op0, op1), [o], [a, s1, s2])
+
+    def cp(o, a):
+        rec("v", lambda: g.vector.tensor_copy(ap(o), ap(a)), [o], [a])
+
+    def ms(o, c):
+        rec("v", lambda: g.vector.memset(ap(o), c), [o], [])
+
+    def act(o, a, func=None, bias=None, scale=None):
+        fn = F.Identity if func is None else func
+        kw = {}
+        if bias is not None:
+            kw["bias"] = sc(bias)
+        if scale is not None:
+            kw["scale"] = sc(scale)
+        rec("a", lambda: g.scalar.activation(ap(o), ap(a), fn, **kw), [o], [a, bias, scale])
+
+    def fill(name, lo, hi, c):
+        for b in range(lo, hi, L):
+            e = min(hi, b + L)
+            act(S(name, b, e), S("jf", 0, e - b), None, c, 0.0)
+
+    def mm(o, wt, mv, start, stop):
+        rec("p", lambda: g.tensor.matmul(ap(o), ap(wt), ap(mv), start, stop), [o], [wt, mv])
+
+    def iota(o, pat, base, cm, isint=False):
+        if isint:
+            rec("g", lambda: g.iota(ap(o), pat, base, cm), [o], [])
+        else:
+            rec("g", lambda: g.iota(ap(o), pat, base, cm, allow_small_or_imprecise_dtypes=True), [o], [])
+
+    def dma(q, o, a):
+        s = "d%d" % nd[0]
+        nd[0] += 1
+        e = g.sync if q == "s" else g.scalar
+        oo = ap(o) if isinstance(o, tuple) else o
+        aa = ap(a) if isinstance(a, tuple) else a
+        rec(q, lambda: e.dma_start(oo, aa), [o] if isinstance(o, tuple) else [], [a], kind="dma", sem=s)
+
+    def conv(o, z, buf, base, n, stride, first=True, last=True):
+        for r in range(16):
+            mm(o, S(z, 15 - r, 143 - r), S(buf, base + stride * r, base + stride * (r + 16 * n - 16) + 1, stride * 16),
+               first and r == 0, last and r == 15)
+
+    def C(i):
+        return S("col", i, i + 1)
+
+    def whole(name):
+        return S(name, 0, _SB[name][0])
+
+    dma("s", whole("wfs"), T.wf[:])
+    dma("s", whole("nms"), T.nm[:])
+    dma("s", whole("wvs"), T.wv[:])
+    dma("s", S("tV", 0, W), T.rv[:])
+    dma("s", S("tF", 0, W), T.rf[:])
+    dma("s", S("tG", 0, W), T.rg[:])
+
+    iota(S("pcol", 0, 1), [[0, 1]], 0, 1, True)
+    iota(whole("jf"), [[1, L]], 0, 0)
+    iota(whole("jr"), [[0, 16], [1, 16]], 0, 0)
+    iota(whole("jq"), [[1, 16], [0, 16]], 0, 0)
+    iota(whole("lo16"), [[16, 16]], 0, 1)
+    iota(whole("j4"), [[1, 36], [0, 4]], 0, 0)
+    for i in range(16):
+        ms(S("ab", i, i + 1), float(WA[i] + 256 * WB[i]))
+    (cP, cR, cG, cJ, cA, cB, c20, cE15, cT, c256, cSH, cKEEP, cFLAG, c4G, c40, cZ, cX, cY, cG16, cW, c21, cU, cAB) = range(23)
+    ts(S("pcol", 1, 2), S("pcol", 0, 1), 15, A.bitwise_and)
+    ts(S("pcol", 2, 3), S("pcol", 0, 1), 4, A.arith_shift_right)
+    ts(S("pcol", 3, 4), S("pcol", 0, 1), 3, A.bitwise_and)
+    ms(whole("hc"), 0.0)
+    cp(S("col", 0, 4), S("pcol", 0, 4))
+    for m in range(16):
+        if KP[m] % 2 == 0:
+            ms(S("hc", 16 * m, 16 * m + 16), 2048.0)
+    ts(C(cZ), C(cG), 16.0, A.mult, 15.0, A.add)
+    ts(whole("ib"), S("jf", 0, 128), C(cP), A.is_equal)
+    ts(C(c20), C(cR), 0.0, A.is_equal, 2.0, A.mult)
+    ts(whole("z1"), S("jf", 0, 144), C(cZ), A.is_equal)
+    ts(C(cKEEP), C(cR), 12.0, A.is_le)
+    ts(C(cFLAG), C(cR), 13.0, A.is_equal)
+    ts(whole("dm"), whole("jr"), C(cR), A.is_equal)
+    ts(whole("ones"), S("jq", 0, 128), C(cG), A.is_equal)
+    ts(whole("nmb"), whole("nms"), C(cKEEP), A.mult, C(cFLAG), A.add)
+    tt(whole("ab2"), whole("ab"), S("dm", 0, 16), A.mult)
+    ts(C(cU), C(cR), 14.0, A.is_equal)
+    ts(C(c256), C(cR), 0.0, A.is_equal, 256.0, A.mult)
+    rec("v", lambda: g.vector.tensor_reduce(ap(C(cAB)), ap(whole("ab2")), AxisListType.X, A.add), [C(cAB)], [whole("ab2")])
+    tt(C(cW), C(cU), C(cFLAG), A.add)
+    act(whole("z0"), whole("z1"), scale=C(c20))
+    act(S("lnd0", 0, 1024, 4), whole("wfs"))
+    mm(S("pB", 0, L), whole("ones"), whole("wfs"), True, True)
+    mm(S("pC", 0, L), whole("ib"), whole("nmb"), True, False)
+    mm(S("pC", 0, L), S("z0", 0, 128), whole("nmb"), False, False)
+    mm(S("pC", 0, L), S("z0", 1, 129), whole("nmb"), False, True)
+    cp(S("pcol", 4, 5), C(cAB))
+    ts(whole("thf"), S("pB", 0, L), 0.0, A.is_gt)
+    ts(S("pcol", 5, 6), S("pcol", 4, 5), 255, A.bitwise_and)
+    ts(S("pcol", 6, 7), S("pcol", 4, 5), 8, A.arith_shift_right)
+    tt(S("lnd0", 3, 1024, 4), S("pC", 0, L), whole("thf"), A.mult)
+    cp(S("col", cA, cA + 2), S("pcol", 5, 7))
+    ts(C(cX), C(cR), 13.0, A.is_equal, 256.0, A.mult)
+    ts(C(cY), C(cR), 1.0, A.is_equal)
+    cp(whole("ih"), whole("ib"))
+    tt(C(cT), C(cX), C(cY), A.add)
+    act(whole("zw"), whole("z1"), scale=C(cW))
+    act(whole("zA"), whole("z1"), scale=C(cA))
+    act(whole("wn"), whole("ones"), scale=C(c256))
+    act(S("lnd0", 2, 1024, 4), whole("wvs"))
+    act(whole("zt"), whole("z1"), scale=C(cT))
+    act(S("lnd0", 1, 1024, 4), whole("wfs"))
+    fill("c13", 0, L, 13.0)
+    act(whole("i3"), whole("ib"), scale=3.0)
+    act(whole("i117"), whole("ib"), scale=-117.0)
+    fill("c1", 0, 128, -16777216.0)
+    act(whole("c2"), whole("jq"), None, 15.0, -1.0)
+    act(whole("zn"), whole("z1"), scale=-1.0)
+    act(whole("z16"), whole("z1"), scale=16.0)
+    act(whole("z65"), whole("z1"), scale=-6.5)
+    act(whole("ineg"), whole("ib"), scale=-67108864.0)
+
+    def consts_hash():
+        for m in range(16):
+            ts(S("dk", 128 * m, 128 * m + 128), whole("ib"), float(KP[m]), A.mult)
+
+    def consts_main():
+        ts(C(cE15), C(cR), 15.0, A.is_equal)
+        ts(C(c21), C(cY), 2.0, A.mult)
+        ts(C(cX), C(cU), 256.0, A.mult, C(c256), A.add)
+        tt(C(cAB), C(cP), C(cKEEP), A.subtract)
+        ts(C(cG16), C(cG), 16.0, A.mult)
+        ts(C(c4G), C(cG), 4.0, A.mult, 3.0, A.add)
+        ts(C(c40), C(c20), 2.0, A.mult)
+        tt(C(cSH), C(cAB), C(cX), A.subtract)
+        ts(whole("lo16"), whole("lo16"), C(cG16), A.subtract)
+        ts(whole("z15"), whole("z1"), C(cE15), A.mult)
+        ts(whole("z21"), whole("z1"), C(c21), A.mult)
+        ts(whole("shf"), S("jf", 0, 128), C(cSH), A.is_equal)
+
+    def consts_late():
+        l16 = whole("lo16")
+        ts(whole("rep"), S("jf", 0, 16), 0.0, A.mult, C(cR), A.add)
+        for i, x in enumerate((0, 48, 16, 48, 64, 64)):
+            ms(S("patt", i, i + 1), float(x))
+        ms(S("patt", 8, 14), 0.0)
+        ts(S("c0", 0, 16), l16, 4.0, A.mult, float(LC), A.add)
+        ts(S("c0", 16, 32), l16, 4.0, A.mult, float(LC + 3), A.add)
+        ms(S("patt", 11, 12), 16.0)
+        ts(S("c0", 32, 48), l16, 4.0, A.mult, float(LC + 1), A.add)
+        ts(S("c0", 48, 64), l16, 4.0, A.mult, float(LV + 2), A.add)
+        ms(S("c0", 64, 80), 4096.0)
+        ms(S("c0", 80, 96), 0.0)
+        ts(S("cp", 0, 16), l16, -4.0, A.mult, float(-LC), A.add)
+        ts(S("cp", 16, 32), l16, -3.0, A.mult, float(NS - LC - 3), A.add)
+        ts(S("cp", 32, 48), l16, -4.0, A.mult, float(-LC - 1), A.add)
+        ts(S("cp", 48, 64), l16, -3.0, A.mult, float(3840 - LV - 2), A.add)
+        ms(S("cp", 64, 80), -6144.0)
+        ts(S("cp", 80, 96), l16, -1.0, A.mult, -4096.0, A.add)
+        ms(S("cq", 0, 16), 1.0)
+        ms(S("cq", 16, 32), 0.0)
+        ms(S("cq", 32, 48), 1.0)
+        ms(S("cq", 48, 64), -256.0)
+        ms(S("cq", 64, 96), 1.0)
+        ts(S("patf", 0, 6), S("patt", 0, 6), C(cR), A.add)
+        ts(S("patv", 0, 6), S("patt", 8, 14), C(cR), A.add)
+
+    def consts_tail():
+        ts(whole("z4"), whole("j4"), C(c4G), A.is_equal, C(c40), A.mult)
+        ts(whole("uget"), S("jr", 0, 128), C(cR), A.is_le, -1.0, A.mult)
+        cp(whole("onesh"), whole("ones"))
+        ts(whole("msk"), S("jr", 0, 64), 0.0, A.is_gt)
+        tt(whole("uge"), whole("uget"), whole("ones"), A.mult)
+        for d in range(4):
+            ts(S("cst", 16 * d, 16 * d + 16), whole("lo16"), -1.0, A.mult, float(256 * d - 1024), A.add)
+        ts(whole("dmp"), whole("lo16"), 1024.0, A.add)
+        ts(whole("cd"), whole("lo16"), 4096.0, A.add)
+        cp(whole("exo"), S("jf", 0, 16))
+
+    def consts_scalar():
+        act(whole("crm"), whole("jq"), None, 15.0, -1.0)
+        act(whole("zB"), whole("z1"), scale=C(cB))
+        act(whole("jb"), whole("jf"))
+        fill("tG", W, LC, 0.0)
+        fill("tG", ZG, WGN, 0.0)
+        fill("lo", ZV, LON, 0.0)
+        fill("pre", 1024, 1040, 0.0)
+        fill("tF", W, LC, 0.0)
+        fill("tV", W, LC, 0.0)
+        fill("idt", 0, 1280, 256.0)
+
+    def scatter(tab, lnd, j):
+        cp(IND(S(tab, 0, LC), whole("o16")), S(lnd, j, 1024, 4))
+
+    for t in range(RO):
+        lnd = "lnd%d" % t
+        last = t == RO - 1
+        conv(S("pA", 0, 16), "zA", lnd, 0, 16, 4)
+        conv(S("pB", 0, 16), "zw", lnd, 3, 16, 4)
+        mm(S("pK0", 0, L), whole("wn"), S(lnd, 3, 1024, 4), True, True)
+        conv(S("pC", 0, 16), "z0", lnd, 3, 16, 4)
+        dma("s", S("tG", LC, NS), whole(lnd))
+        dma("s", S("lo", LV, ZV), whole(lnd))
+        if t == 0:
+            consts_hash()
+        cp(whole("ui"), S("pA", 0, 16))
+        ts(whole("u"), whole("ui"), 4095, A.bitwise_and)
+        ts(whole("uh"), whole("u"), -2048.0, A.add)
+        tt(whole("prod"), S("pB", 0, 16), whole("u"), A.mult)
+        ts(whole("cc"), whole("prod"), 5, A.arith_shift_right, 4095, A.bitwise_and)
+        ts(whole("ch"), whole("cc"), -2048.0, A.add)
+        for bank, m0, m1 in (("pE0", 0, 4), ("pE1", 4, 16)):
+            mm(S(bank, 0, 16 * (m1 - m0)), whole("ib"), S("hc", 16 * m0, 16 * m1), True, False)
+            for m in range(m0, m1):
+                mm(S(bank, 16 * (m - m0), 16 * (m - m0) + 16), S("dk", 128 * m, 128 * m + 128), whole("uh"), False, False)
+            for m in range(m0, m1):
+                mm(S(bank, 16 * (m - m0), 16 * (m - m0) + 16), whole("ih"), whole("ch"), False, m == m1 - 1)
+        mm(S("pV", 0, L), whole("ib"), S(lnd, 2, 1024, 4), True, True)
+        mm(S("pV", L, 2 * L), whole("ib"), S(lnd, 2, 1024, 4), True, True)
+        conv(S("pA", 0, 16), "zt", lnd, 3, 16, 4)
+        tt(S("cmp", 0, L), S(lnd, 0, 1024, 4), S("pK0", 0, L), A.min)
+        act(S("cmp", L, 2 * L), S("cmp", 0, L))
+        cp(S("hi", 0, 64), S("pE0", 0, 64))
+        ts(whole("zf_"), S("pC", 0, 16), 0.0, A.is_equal)
+        ts(S("hi", 0, 64), S("hi", 0, 64), 4095, A.bitwise_and)
+        ts(S("fl", 48, 64), S("pC", 0, 16), 0.0, A.is_gt)
+        cp(S("h16", 0, 64), S("hi", 0, 64))
+        ts(whole("nw"), S("pC", 0, 16), 0.0, A.is_equal, 1048576.0, A.mult)
+
+        def gf1(m):
+            tt(S("eqf", L * m, L * m + L), IND(S("tF", 0, W), S("h16", 16 * m, 16 * m + 16)), S("cmp", 0, L), A.is_equal)
+
+        def gf2(m):
+            tt(S("eqf", L * m, L * m + 2 * L), IND(S("tF", 0, W), S("h16", 16 * m, 16 * m + 32)), whole("cmp"), A.is_equal)
+
+        if t > 0:
+            gf1(0)
+        cp(S("hi", 64, L), S("pE1", 0, 192))
+        if t > 0:
+            gf1(1)
+        else:
+            consts_main()
+        ts(S("hi", 64, L), S("hi", 64, L), 4095, A.bitwise_and)
+        if t > 0:
+            gf1(2)
+        cp(S("h16", 64, L), S("hi", 64, L))
+        if t == 0:
+            consts_late()
+            consts_tail()
+            consts_scalar()
+
+        def gv(c):
+            act(S("vg", 1024 * c, 1024 * c + 1024), IND(S("tV", 0, W), S("h16", 64 * c, 64 * c + 64)))
+
+        def sgn(c):
+            act(S("sg", 1024 * c, 1024 * c + 1024), S("lo", 1024 * c, 1024 * c + 1024), F.Sign, -(TAU[t] + 0.5))
+
+        def gf(c):
+            if c == 0 and t > 0:
+                gf1(3)
+            else:
+                gf2(4 * c)
+                gf2(4 * c + 2)
+
+        def mn(c):
+            for h in range(2):
+                b = 1024 * c + 512 * h
+                tt(S("lo", b, b + 512), S("vg", b, b + 512), S("pV", 0, 512), A.min)
+
+        def pe(c, kind, stop=False):
+            h, o = c // 2, 64 * (c % 2)
+            if kind == "E":
+                conv(S("pE%d" % h, o, o + 64), "zn", "eqf", 1024 * c, 64, 1, False, stop)
+            elif kind == "S":
+                conv(S("pE%d" % h, 128 + o, 128 + o + 64), "z65", "sg", 1024 * c, 64, 1, False, stop)
+            else:
+                conv(S("pK%d" % h, o, o + 64), "z16", "lo", 1024 * c, 64, 1, False, False)
+
+        def init(h):
+            e, k = "pE%d" % h, "pK%d" % h
+            mm(S(e, 0, L), whole("ib"), whole("c13"), True, False)
+            for m in range(8):
+                mm(S(e, 16 * m, 16 * m + 16), whole("i3"), whole("zf_"), False, False)
+            for m in range(8):
+                mm(S(e, 128 + 16 * m, 128 + 16 * m + 16), whole("i117"), whole("zf_"), False, False)
+            mm(S(k, 0, 128), whole("ib"), whole("c1"), True, False)
+            mm(S(k, 0, 128), whole("ib"), S("c2", 128 * h, 128 * h + 128), False, False)
+
+        def relu(h):
+            act(S("pen", L * h, L * h + L), S("pE%d" % h, 0, L), F.Relu)
+
+        def pen(h):
+            mm(S("pK%d" % h, 0, 128), whole("ineg"), S("pen", L * h, L * h + 128), False, False)
+            mm(S("pK%d" % h, 0, 128), whole("ineg"), S("pen", L * h + 128, L * h + L), False, True)
+
+        gv(0)
+        init(0)
+        init(1)
+        if not last:
+            for b, z in ((0, "z21"), (L, "z15")):
+                mm(S("pC", b, b + L), whole("shf"), S(lnd, 3, 1024, 4), True, False)
+                mm(S("pC", b, b + L), S(z, 1, 129), S(lnd, 3, 1024, 4), False, True)
+        gf(0); pe(0, "E")
+        gv(1)
+        mn(0); pe(0, "K")
+        sgn(0); pe(0, "S")
+        gf(1); pe(1, "E")
+        gv(2)
+        mn(1); pe(1, "K")
+        sgn(1); pe(1, "S", True)
+        gf(2); pe(2, "E")
+        gv(3)
+        mn(2); pe(2, "K")
+        relu(0); pen(0)
+        sgn(2); pe(2, "S")
+        mn(3); pe(3, "K")
+        sgn(3); pe(3, "S")
+        act(whole("ka"), S("pK0", 0, 128))
+        gf(3); pe(3, "E", True)
+        relu(1); pen(1)
+        ts(whole("tb"), S("pA", 0, 16), 256.0 if not last else -1.0, A.is_equal)
+        ts(whole("ta"), S("pA", 0, 16), 256.0, A.is_ge)
+        tt(S("fl", 16, 32), whole("tb"), S("fl", 48, 64), A.mult)
+        tt(S("fl", 64, 80), whole("ta"), whole("zf_"), A.mult)
+        tt(S("fl", 0, 16), S("fl", 48, 64), S("fl", 16, 32), A.subtract)
+        ts(S("fl", 32, 48), S("fl", 16, 32), 256.0, A.mult)
+        if t > 0:
+            scatter("tG", "lnd%d" % (t - 1), 1)
+        if not last:
+            act(S("tG", NS, ZG), S("pC", 0, 2 * L))
+        tt(whole("p6"), IND(whole("fl"), S("patf", 0, 6)), whole("cp"), A.mult)
+        tt(whole("q6"), IND(whole("fl"), S("patf", 0, 6)), whole("cq"), A.mult)
+        tt(S("p6", 0, 32), S("p6", 0, 32), S("fl", 16, 48), A.add)
+
+        tt(whole("k1"), S("pK1", 0, 128), whole("ka"), A.max)
+        tt(whole("k2"), S("k1", 0, 64), S("k1", 64, 128), A.max)
+        tt(whole("k3"), S("k2", 0, 32), S("k2", 32, 64), A.max)
+        tt(whole("best"), S("k3", 0, 16), S("k3", 16, 32), A.max)
+        ts(whole("ki"), whole("best"), -16777232.0, A.max)
+        ts(whole("vld"), whole("best"), -33554432.0, A.is_gt)
+        ts(S("val", 16, 32), whole("ki"), 15, A.bitwise_and)
+        tt(whole("oh"), IND(S("val", 16, 32), whole("rep")), whole("crm"), A.is_equal)
+        for m in range(16):
+            mm(S("pA", 0, 16), S("dk", 128 * m, 128 * m + 128), S("oh", 16 * m, 16 * m + 16), m == 0, m == 15)
+        tt(whole("vp2"), IND(whole("vld"), S("rep", 0, 6)), whole("p6"), A.mult)
+        tt(whole("vq"), IND(whole("vld"), S("rep", 0, 6)), whole("q6"), A.mult)
+        if last:
+            for b, z in ((0, ZG), (48, ZV)):
+                ts(S("c0", b, b + 16), S("c0", b, b + 16), float(-z), A.add)
+            for b, z in ((0, ZG), (48, ZV)):
+                tt(S("c0", b, b + 16), S("c0", b, b + 16), S("fl", 48, 64), A.mult)
+            for b, z in ((0, ZG), (48, ZV)):
+                ts(S("c0", b, b + 16), S("c0", b, b + 16), float(z), A.add)
+        tt(whole("vp"), whole("vp2"), whole("c0"), A.add)
+        tt(whole("ha"), S("pA", 0, 16), whole("u"), A.mult)
+        tt(whole("hb"), whole("ha"), whole("cc"), A.add)
+        ts(S("val", 0, 16), whole("hb"), 4095, A.bitwise_and)
+        tt(whole("t6"), IND(whole("val"), S("patv", 0, 6)), whole("vq"), A.mult)
+        tt(whole("s6"), whole("t6"), whole("vp"), A.add)
+
+        def claims_a():
+            tt(whole("ex"), IND(S("s6", 64, 80), whole("exo")), whole("dm"), A.mult)
+            mm(S("pE0", 0, L), whole("onesh"), whole("ex"), True, True)
+
+        def claims_b():
+            cp(whole("plr"), S("pE0", 0, L))
+
+        def claims_c(c0, c1):
+            for c in range(c0, c1):
+                ts(S("eqd", L * c + 16 * c, L * c + L), S("plr", 16 * c, L), S("s6", 64 + c, 65 + c), A.is_equal)
+                mm(S("pE1", 16 * c, L), whole("ones"), S("eqd", L * c + 16 * c, L * c + L), c == 0, False)
+                mm(S("pE1", 16 * c, 16 * c + 16), whole("uge"), S("eqd", L * c + 16 * c, L * c + 16 * c + 16), False, c == 15)
+
+        def claims_d():
+            tt(whole("dmk"), S("pE1", 0, L), whole("dm"), A.mult)
+            conv(S("pC", 0, 16), "zn", "dmk", 0, 16, 1)
+
+        def claims_e():
+            ts(whole("win"), S("pC", 0, 16), 0.0, A.is_equal)
+            tt(whole("wt"), whole("win"), S("s6", 80, 96), A.mult)
+            tt(whole("ot"), whole("wt"), whole("cd"), A.add)
+            cp(whole("o16"), whole("ot"))
+
+        if not last:
+            cp(whole("s16"), S("s6", 0, 64))
+            act(S("pre", 0, 1024, 4), IND(whole("tG"), S("s16", 0, 16)))
+            claims_a()
+            conv(S("pB", 0, 16), "zB", "pre", 0, 16, 4)
+            act(S("pre", 1, 1024, 4), IND(whole("tG"), S("s16", 32, 48)))
+            act(S("pre", 2, 1024, 4), IND(whole("lo"), S("s16", 48, 64)))
+            act(S("pre", 3, 1024, 4), IND(whole("tG"), S("s16", 16, 32)))
+            claims_b()
+            claims_c(0, 1)
+            tt(whole("gi"), S("pB", 0, 16), whole("nw"), A.add)
+            ts(whole("g3"), whole("gi"), 1048576 + 3, A.bitwise_and)
+            tt(whole("go4"), IND(whole("g3"), S("rep", 0, 4)), S("jq", 0, 64), A.is_equal)
+            rec("v", lambda: g.vector.tensor_tensor_scan(ap(whole("inc")), ap(whole("msk")), ap(whole("go4")), 0.0, A.mult, A.add),
+                [whole("inc")], [whole("msk"), whole("go4")])
+            mm(S("pC", 0, 64), whole("ih"), whole("cst"), True, False)
+            mm(S("pC", 0, 64), whole("uge"), whole("go4"), False, False)
+            mm(S("pC", 0, 64), whole("ones"), whole("inc"), False, True)
+            claims_c(1, 2)
+            tt(whole("tt4"), S("pC", 0, 64), whole("go4"), A.mult)
+            mm(S("pA", 0, 16), whole("ih"), whole("dmp"), True, False)
+            for d in range(4):
+                mm(S("pA", 0, 16), whole("ih"), S("tt4", 16 * d, 16 * d + 16), False, d == 3)
+            claims_c(2, 4)
+            cp(whole("pos"), S("pA", 0, 16))
+            cp(IND(whole("idt"), whole("pos")), whole("jb"))
+            for k in range(1, N + 1):
+                d = (rank + k) % N
+                for e in range(4):
+                    mm(S("pB" if k == 1 else "pK0", 16 * (k - 1), 16 * k), S("z4", 12 - 4 * e, 140 - 4 * e),
+                       S("idt", L * d + e, L * d + 64, 4), e == 0, e == 3)
+            claims_c(4, 6)
+            ts(S("src", 0, 16), S("pB", 0, 16), C(cJ), A.add)
+            claims_c(6, 9)
+            ts(S("src", 16, 64), S("pK0", 16, 64), C(cJ), A.add)
+            nxt, snd = "lnd%d" % (t + 1), "snd%d" % t
+            for k in range(1, N + 1):
+                d = (rank + k) % N
+                o = S(nxt, L * rank, L * rank + L) if k == N else S(snd, L * (k - 1), L * k)
+                act(o, IND(whole("pre"), S("src", 16 * (k - 1), 16 * k)))
+                if k < N:
+                    dst = T.cores[d]
+                    rid, pid = topo.addr(dst)[0], topo.addr(dst)[1]
+                    msk, ne = topo.mask(core, dst), len(topo.engines(core, dst))
+                    sem = "out%d" % (3 * t + k - 1)
+                    rec("g", lambda o=o, nxt=nxt, sem=sem, t=t, pid=pid, rid=rid, msk=msk: g.remote_dma(
+                        ap(S(nxt, L * rank, L * rank + L)), ap(o), T.sem["arr%d" % t], T.sem[sem], pid, rid, msk),
+                        [], [o], kind="rem", sem=sem, n=ne)
+            n_in = sum(len(topo.engines(T.cores[q], core)) for q in range(N) if q != rank)
+            rec("g", None, [S(nxt, L * q, L * q + L) for q in range(N) if q != rank], [], kind="land", sem="arr%d" % t, n=n_in)
+            claims_c(9, 16)
+            claims_d()
+            if t < RO - 2:
+                for d in range(4):
+                    fill("idt", L * d, L * d + 64, 256.0)
+            claims_e()
+            scatter("tV", lnd, 2)
+            scatter("tF", lnd, 0)
+        else:
+            cp(whole("s16"), S("s6", 0, 64))
+            claims_a()
+            act(whole("yfb"), IND(whole("tG"), S("s16", 0, 16)))
+            act(whole("yvb"), IND(whole("lo"), S("s16", 48, 64)))
+            dma("s", T.yf[:], whole("yfb"))
+            dma("s", T.yv[:], whole("yvb"))
+            claims_b()
+            claims_c(0, 16)
+            claims_d()
+            claims_e()
+            for i, (tab, j, bank, out) in enumerate((("tV", 2, "pE0", T.zv), ("tF", 0, "pE1", T.zf), ("tG", 1, "pK0", T.zg))):
+                scatter(tab, lnd, j)
+                if i < 2:
+                    for k in range(32):
+                        mm(S(bank, 0, 128), whole("ib"), S(tab, 128 * k, 128 * k + 128), k == 0, k == 31)
+                else:
+                    tt(whole("dk"), S(tab, 0, W // 2), S(tab, W // 2, W), A.add)
+                    for k in range(16):
+                        mm(S(bank, 0, 128), whole("ih"), S("dk", 128 * k, 128 * k + 128), k == 0, k == 15)
+                act(S("zb", 128 * i, 128 * i + 128), S(bank, 0, 128))
+                dma("s" if i < 2 else "a", out[:], S("zb", 128 * i, 128 * i + 128))
+    emit(g, T, ops)

@@ -22,14 +22,15 @@ _SB = {
     "zA": (144, B16), "zB": (144, B16), "z0": (144, B16), "z15": (144, B16), "zt": (144, B16), "zn": (144, B16),
     "z65": (144, B16), "z16": (144, B16), "z4": (144, B16), "dk": (2048, F16), "dm": (L, B16), "hc": (L, B16),
     "c13": (L, B16), "c1": (128, B16), "c2": (L, B16), "crm": (L, F32), "msk": (64, B16), "cst": (64, F16), "dmp": (16, F16),
-    "cd": (16, F32), "c0": (96, F32), "cp": (96, F32), "cq": (96, F32), "rep": (16, U16), "exo": (16, U16),
+    "cd": (16, F32), "c0": (80, F32), "cp": (80, F32), "cq": (80, F32), "rep": (16, U16), "x16": (16, U16),
+    "jw": (6160, F32), "plh": (16, F16),
     "patf": (8, U16), "patv": (8, U16), "patt": (16, F32), "z1": (144, B16), "zw": (144, B16), "z21": (144, B16),
     "ui": (16, I32), "u": (16, I32), "zf_": (16, B16), "prod": (16, I32),
     "cc": (16, I32), "uh": (16, F16), "ch": (16, F16), "hi": (L, I32), "h16": (L, U16), "cmp": (2 * L, B16),
-    "fl": (80, F32), "ta": (16, F32), "tb": (16, F32), "nw": (16, F32), "p6": (96, F32), "q6": (96, F32),
+    "fl": (80, F32), "ta": (16, F32), "tb": (16, F32), "nw": (16, F32), "p6": (80, F32), "q6": (80, F32),
     "pen": (512, B16), "ka": (128, F32), "k1": (128, F32), "k2": (64, F32), "k3": (32, F32), "best": (16, F32),
-    "ki": (16, I32), "vld": (16, F32), "val": (32, I32), "oh": (L, F16), "vq": (96, F32), "vp": (96, F32), "vp2": (96, F32),
-    "ha": (16, F32), "hb": (16, I32), "t6": (96, F32), "s6": (96, F32), "s16": (64, U16),
+    "ki": (16, I32), "vld": (16, F32), "val": (32, I32), "oh": (L, F16), "vq": (80, F32), "vp": (80, F32), "vp2": (80, F32),
+    "ha": (16, F32), "hb": (16, I32), "t6": (80, F32), "s6": (80, F32), "s16": (80, U16),
     "gi": (16, I32), "g3": (16, I32), "go4": (64, B16), "inc": (64, B16), "tt4": (64, F16), "pos": (16, U16), "src": (64, U16),
     "ex": (L, F16), "plr": (L, F16), "dmk": (L, B16), "win": (16, F32), "wt": (16, F32), "ot": (16, F32), "o16": (16, U16),
 }
@@ -246,6 +247,7 @@ def rank_program(g, core, T, topo):
     iota(whole("jq"), [[1, 16], [0, 16]], 0, 0)
     iota(whole("lo16"), [[16, 16]], 0, 1)
     iota(whole("j4"), [[1, 36], [0, 4]], 0, 0)
+    iota(whole("jw"), [[1, 6160]], -2048, 0)
     for i in range(16):
         ms(S("ab", i, i + 1), float(WA[i] + 256 * WB[i]))
     (cP, cR, cG, cJ, cA, cB, c20, cE15, cT, c256, cSH, cKEEP, cFLAG, c4G, c40, cZ, cX, cY, cG16, cW, c21, cU, cAB) = range(23)
@@ -293,18 +295,18 @@ def rank_program(g, core, T, topo):
     act(S("lnd0", 2, 1024, 4), whole("wvs"))
     act(whole("zt"), whole("z1"), scale=C(cT))
     act(S("lnd0", 1, 1024, 4), whole("wfs"))
-    fill("c13", 0, L, 13.0)
+    fill("c13", 0, 128, 13.0)
+    fill("c13", 128, L, 2.0)
     act(whole("i3"), whole("ib"), scale=3.0)
-    act(whole("i117"), whole("ib"), scale=-117.0)
+    act(whole("i117"), whole("ib"), scale=-18.0)
     fill("c1", 0, 128, -16777216.0)
     act(whole("c2"), whole("jq"), None, 15.0, -1.0)
     act(whole("zn"), whole("z1"), scale=-1.0)
     act(whole("z16"), whole("z1"), scale=16.0)
-    act(whole("z65"), whole("z1"), scale=-6.5)
-    act(whole("ineg"), whole("ib"), scale=-67108864.0)
+    act(whole("ineg"), whole("ib"), scale=-33554432.0)
 
-    def consts_hash():
-        for m in range(16):
+    def consts_hash(m0, m1):
+        for m in range(m0, m1):
             ts(S("dk", 128 * m, 128 * m + 128), whole("ib"), float(KP[m]), A.mult)
 
     def consts_main():
@@ -323,54 +325,49 @@ def rank_program(g, core, T, topo):
 
     def consts_late():
         l16 = whole("lo16")
+        rows = ((4, LC, -4, -LC, 1), (4, LC + 3, -3, NS - LC - 3, 0), (4, LC + 1, -4, -LC - 1, 1),
+                (4, LV + 2, -3, 3840 - LV - 2, -256), (0, 6144, 0, -6144, 1))
+        for b, (s0, b0, s1, b1, q) in enumerate(rows):
+            act(S("c0", 16 * b, 16 * b + 16), l16, None, float(b0), float(s0))
+            act(S("cp", 16 * b, 16 * b + 16), l16, None, float(b1), float(s1))
+            act(S("cq", 16 * b, 16 * b + 16), l16, None, float(q), 0.0)
+
+    def consts_lists():
         ts(whole("rep"), S("jf", 0, 16), 0.0, A.mult, C(cR), A.add)
         for i, x in enumerate((0, 48, 16, 48, 64, 64)):
             ms(S("patt", i, i + 1), float(x))
-        ms(S("patt", 8, 14), 0.0)
-        ts(S("c0", 0, 16), l16, 4.0, A.mult, float(LC), A.add)
-        ts(S("c0", 16, 32), l16, 4.0, A.mult, float(LC + 3), A.add)
+        ms(S("patt", 8, 11), 0.0)
         ms(S("patt", 11, 12), 16.0)
-        ts(S("c0", 32, 48), l16, 4.0, A.mult, float(LC + 1), A.add)
-        ts(S("c0", 48, 64), l16, 4.0, A.mult, float(LV + 2), A.add)
-        ms(S("c0", 64, 80), 4096.0)
-        ms(S("c0", 80, 96), 0.0)
-        ts(S("cp", 0, 16), l16, -4.0, A.mult, float(-LC), A.add)
-        ts(S("cp", 16, 32), l16, -3.0, A.mult, float(NS - LC - 3), A.add)
-        ts(S("cp", 32, 48), l16, -4.0, A.mult, float(-LC - 1), A.add)
-        ts(S("cp", 48, 64), l16, -3.0, A.mult, float(3840 - LV - 2), A.add)
-        ms(S("cp", 64, 80), -6144.0)
-        ts(S("cp", 80, 96), l16, -1.0, A.mult, -4096.0, A.add)
-        ms(S("cq", 0, 16), 1.0)
-        ms(S("cq", 16, 32), 0.0)
-        ms(S("cq", 32, 48), 1.0)
-        ms(S("cq", 48, 64), -256.0)
-        ms(S("cq", 64, 96), 1.0)
+        ms(S("patt", 12, 14), 0.0)
         ts(S("patf", 0, 6), S("patt", 0, 6), C(cR), A.add)
         ts(S("patv", 0, 6), S("patt", 8, 14), C(cR), A.add)
 
     def consts_tail():
         ts(whole("z4"), whole("j4"), C(c4G), A.is_equal, C(c40), A.mult)
         ts(whole("uget"), S("jr", 0, 128), C(cR), A.is_le, -1.0, A.mult)
-        cp(whole("onesh"), whole("ones"))
         ts(whole("msk"), S("jr", 0, 64), 0.0, A.is_gt)
         tt(whole("uge"), whole("uget"), whole("ones"), A.mult)
         for d in range(4):
             ts(S("cst", 16 * d, 16 * d + 16), whole("lo16"), -1.0, A.mult, float(256 * d - 1024), A.add)
         ts(whole("dmp"), whole("lo16"), 1024.0, A.add)
-        ts(whole("cd"), whole("lo16"), 4096.0, A.add)
-        cp(whole("exo"), S("jf", 0, 16))
+        ts(whole("cd"), whole("lo16"), 2048.0, A.add)
 
     def consts_scalar():
         act(whole("crm"), whole("jq"), None, 15.0, -1.0)
         act(whole("zB"), whole("z1"), scale=C(cB))
-        act(whole("jb"), whole("jf"))
         fill("tG", W, LC, 0.0)
         fill("tG", ZG, WGN, 0.0)
         fill("lo", ZV, LON, 0.0)
         fill("pre", 1024, 1040, 0.0)
+
+    def consts_scalar2():
+        act(whole("jb"), whole("jf"))
+        fill("idt", 0, 1280, 256.0)
+
+    def consts_scalar3():
+        act(whole("z65"), whole("z1"), scale=8192.0)
         fill("tF", W, LC, 0.0)
         fill("tV", W, LC, 0.0)
-        fill("idt", 0, 1280, 256.0)
 
     def scatter(tab, lnd, j):
         cp(IND(S(tab, 0, LC), whole("o16")), S(lnd, j, 1024, 4))
@@ -385,13 +382,17 @@ def rank_program(g, core, T, topo):
         dma("s", S("tG", LC, NS), whole(lnd))
         dma("s", S("lo", LV, ZV), whole(lnd))
         if t == 0:
-            consts_hash()
-        cp(whole("ui"), S("pA", 0, 16))
-        ts(whole("u"), whole("ui"), 4095, A.bitwise_and)
-        ts(whole("uh"), whole("u"), -2048.0, A.add)
-        tt(whole("prod"), S("pB", 0, 16), whole("u"), A.mult)
-        ts(whole("cc"), whole("prod"), 5, A.arith_shift_right, 4095, A.bitwise_and)
-        ts(whole("ch"), whole("cc"), -2048.0, A.add)
+            consts_hash(0, 6)
+        for i, step in enumerate((
+                lambda: cp(whole("ui"), S("pA", 0, 16)),
+                lambda: ts(whole("u"), whole("ui"), 4095, A.bitwise_and),
+                lambda: ts(whole("uh"), whole("u"), -2048.0, A.add),
+                lambda: tt(whole("prod"), S("pB", 0, 16), whole("u"), A.mult),
+                lambda: ts(whole("cc"), whole("prod"), 5, A.arith_shift_right, 4095, A.bitwise_and),
+                lambda: ts(whole("ch"), whole("cc"), -2048.0, A.add))):
+            step()
+            if t == 0 and i < 5:
+                consts_hash(6 + 2 * i, 8 + 2 * i)
         for bank, m0, m1 in (("pE0", 0, 4), ("pE1", 4, 16)):
             mm(S(bank, 0, 16 * (m1 - m0)), whole("ib"), S("hc", 16 * m0, 16 * m1), True, False)
             for m in range(m0, m1):
@@ -419,18 +420,12 @@ def rank_program(g, core, T, topo):
         if t > 0:
             gf1(0)
         cp(S("hi", 64, L), S("pE1", 0, 192))
-        if t > 0:
-            gf1(1)
-        else:
-            consts_main()
         ts(S("hi", 64, L), S("hi", 64, L), 4095, A.bitwise_and)
         if t > 0:
-            gf1(2)
+            gf1(1)
         cp(S("h16", 64, L), S("hi", 64, L))
         if t == 0:
-            consts_late()
-            consts_tail()
-            consts_scalar()
+            consts_main()
 
         def gv(c):
             act(S("vg", 1024 * c, 1024 * c + 1024), IND(S("tV", 0, W), S("h16", 64 * c, 64 * c + 64)))
@@ -440,7 +435,7 @@ def rank_program(g, core, T, topo):
 
         def gf(c):
             if c == 0 and t > 0:
-                gf1(3)
+                gf2(2)
             else:
                 gf2(4 * c)
                 gf2(4 * c + 2)
@@ -455,7 +450,7 @@ def rank_program(g, core, T, topo):
             if kind == "E":
                 conv(S("pE%d" % h, o, o + 64), "zn", "eqf", 1024 * c, 64, 1, False, stop)
             elif kind == "S":
-                conv(S("pE%d" % h, 128 + o, 128 + o + 64), "z65", "sg", 1024 * c, 64, 1, False, stop)
+                conv(S("pE%d" % h, 128 + o, 128 + o + 64), "zn", "sg", 1024 * c, 64, 1, False, stop)
             else:
                 conv(S("pK%d" % h, o, o + 64), "z16", "lo", 1024 * c, 64, 1, False, False)
 
@@ -483,14 +478,26 @@ def rank_program(g, core, T, topo):
             for b, z in ((0, "z21"), (L, "z15")):
                 mm(S("pC", b, b + L), whole("shf"), S(lnd, 3, 1024, 4), True, False)
                 mm(S("pC", b, b + L), S(z, 1, 129), S(lnd, 3, 1024, 4), False, True)
-        gf(0); pe(0, "E")
-        gv(1)
-        mn(0); pe(0, "K")
-        sgn(0); pe(0, "S")
-        gf(1); pe(1, "E")
-        gv(2)
-        mn(1); pe(1, "K")
-        sgn(1); pe(1, "S", True)
+        if t > 0:
+            gf(0); pe(0, "E")
+            gv(1)
+            mn(0); pe(0, "K")
+            sgn(0); pe(0, "S")
+            gf(1); pe(1, "E")
+            gv(2)
+            mn(1); pe(1, "K")
+            sgn(1); pe(1, "S", True)
+        else:
+            gv(1)
+            mn(0); pe(0, "K")
+            sgn(0); pe(0, "S")
+            consts_tail()
+            gv(2)
+            mn(1); pe(1, "K")
+            sgn(1); pe(1, "S")
+            consts_late()
+            gf(0); pe(0, "E")
+            gf(1); pe(1, "E", True)
         gf(2); pe(2, "E")
         gv(3)
         mn(2); pe(2, "K")
@@ -508,25 +515,29 @@ def rank_program(g, core, T, topo):
         tt(S("fl", 0, 16), S("fl", 48, 64), S("fl", 16, 32), A.subtract)
         ts(S("fl", 32, 48), S("fl", 16, 32), 256.0, A.mult)
         if t > 0:
-            scatter("tG", "lnd%d" % (t - 1), 1)
+            cp(IND(S("tG", 0, LC), S("o16", 8, 16)), S("lnd%d" % (t - 1), 513, 1024, 4))
+        else:
+            consts_lists()
+            consts_scalar()
         if not last:
             act(S("tG", NS, ZG), S("pC", 0, 2 * L))
-        tt(whole("p6"), IND(whole("fl"), S("patf", 0, 6)), whole("cp"), A.mult)
-        tt(whole("q6"), IND(whole("fl"), S("patf", 0, 6)), whole("cq"), A.mult)
+        if t == 0:
+            consts_scalar2()
+        tt(whole("p6"), IND(whole("fl"), S("patf", 0, 5)), whole("cp"), A.mult)
+        tt(whole("q6"), IND(whole("fl"), S("patf", 0, 5)), whole("cq"), A.mult)
         tt(S("p6", 0, 32), S("p6", 0, 32), S("fl", 16, 48), A.add)
 
         tt(whole("k1"), S("pK1", 0, 128), whole("ka"), A.max)
         tt(whole("k2"), S("k1", 0, 64), S("k1", 64, 128), A.max)
         tt(whole("k3"), S("k2", 0, 32), S("k2", 32, 64), A.max)
-        tt(whole("best"), S("k3", 0, 16), S("k3", 16, 32), A.max)
-        ts(whole("ki"), whole("best"), -16777232.0, A.max)
-        ts(whole("vld"), whole("best"), -33554432.0, A.is_gt)
+        tt(whole("ki"), S("k3", 0, 16), S("k3", 16, 32), A.max)
         ts(S("val", 16, 32), whole("ki"), 15, A.bitwise_and)
+        ts(whole("vld"), whole("ki"), -16777216.0, A.is_ge)
         tt(whole("oh"), IND(S("val", 16, 32), whole("rep")), whole("crm"), A.is_equal)
         for m in range(16):
             mm(S("pA", 0, 16), S("dk", 128 * m, 128 * m + 128), S("oh", 16 * m, 16 * m + 16), m == 0, m == 15)
-        tt(whole("vp2"), IND(whole("vld"), S("rep", 0, 6)), whole("p6"), A.mult)
-        tt(whole("vq"), IND(whole("vld"), S("rep", 0, 6)), whole("q6"), A.mult)
+        tt(whole("vp2"), IND(whole("vld"), S("rep", 0, 5)), whole("p6"), A.mult)
+        tt(whole("vq"), IND(whole("vld"), S("rep", 0, 5)), whole("q6"), A.mult)
         if last:
             for b, z in ((0, ZG), (48, ZV)):
                 ts(S("c0", b, b + 16), S("c0", b, b + 16), float(-z), A.add)
@@ -538,57 +549,78 @@ def rank_program(g, core, T, topo):
         tt(whole("ha"), S("pA", 0, 16), whole("u"), A.mult)
         tt(whole("hb"), whole("ha"), whole("cc"), A.add)
         ts(S("val", 0, 16), whole("hb"), 4095, A.bitwise_and)
-        tt(whole("t6"), IND(whole("val"), S("patv", 0, 6)), whole("vq"), A.mult)
+        if not last:
+            tt(whole("ta"), S("val", 0, 16), S("vq", 0, 16), A.mult)
+            tt(whole("tb"), whole("ta"), S("vp", 0, 16), A.add)
+            cp(whole("x16"), whole("tb"))
+            act(S("pre", 0, 1024, 4), IND(whole("tG"), whole("x16")))
+            conv(S("pB", 0, 16), "zB", "pre", 0, 16, 4)
+        tt(whole("t6"), IND(whole("val"), S("patv", 0, 5)), whole("vq"), A.mult)
         tt(whole("s6"), whole("t6"), whole("vp"), A.add)
 
         def claims_a():
-            tt(whole("ex"), IND(S("s6", 64, 80), whole("exo")), whole("dm"), A.mult)
-            mm(S("pE0", 0, L), whole("onesh"), whole("ex"), True, True)
+            cp(whole("plr"), IND(whole("jw"), S("s16", 64, 80)))
 
         def claims_b():
-            cp(whole("plr"), S("pE0", 0, L))
+            ts(whole("plh"), S("s6", 64, 80), -2048.0, A.add)
+
+        summed = []
+
+        def eq(*cs):
+            for c in cs:
+                ts(S("eqd", L * c + 16 * c, L * c + L), S("plr", 16 * c, L), 2048.0, A.add, S("s6", 64 + c, 65 + c), A.is_equal)
+
+        def eqm(*cs):
+            for c in cs:
+                summed.append(c)
+                mm(S("pE1", 16 * c, L), whole("ones"), S("eqd", L * c + 16 * c, L * c + L), c == 0, False)
+                mm(S("pE1", 16 * c, 16 * c + 16), whole("uge"), S("eqd", L * c + 16 * c, L * c + 16 * c + 16), False,
+                   len(summed) == 16)
 
         def claims_c(c0, c1):
             for c in range(c0, c1):
-                ts(S("eqd", L * c + 16 * c, L * c + L), S("plr", 16 * c, L), S("s6", 64 + c, 65 + c), A.is_equal)
-                mm(S("pE1", 16 * c, L), whole("ones"), S("eqd", L * c + 16 * c, L * c + L), c == 0, False)
-                mm(S("pE1", 16 * c, 16 * c + 16), whole("uge"), S("eqd", L * c + 16 * c, L * c + 16 * c + 16), False, c == 15)
+                eq(c)
+                eqm(c)
 
         def claims_d():
             tt(whole("dmk"), S("pE1", 0, L), whole("dm"), A.mult)
-            conv(S("pC", 0, 16), "zn", "dmk", 0, 16, 1)
+            mm(S("pC", 0, 16), whole("ih"), whole("plh"), True, False)
+            conv(S("pC", 0, 16), "z65", "dmk", 0, 16, 1, False, True)
 
         def claims_e():
-            ts(whole("win"), S("pC", 0, 16), 0.0, A.is_equal)
-            tt(whole("wt"), whole("win"), S("s6", 80, 96), A.mult)
-            tt(whole("ot"), whole("wt"), whole("cd"), A.add)
-            cp(whole("o16"), whole("ot"))
+            tt(whole("ot"), S("pC", 0, 16), whole("cd"), A.min)
+            ts(whole("o16"), whole("ot"), 2048.0, A.add)
 
         if not last:
-            cp(whole("s16"), S("s6", 0, 64))
-            act(S("pre", 0, 1024, 4), IND(whole("tG"), S("s16", 0, 16)))
+            cp(whole("s16"), whole("s6"))
             claims_a()
-            conv(S("pB", 0, 16), "zB", "pre", 0, 16, 4)
             act(S("pre", 1, 1024, 4), IND(whole("tG"), S("s16", 32, 48)))
             act(S("pre", 2, 1024, 4), IND(whole("lo"), S("s16", 48, 64)))
             act(S("pre", 3, 1024, 4), IND(whole("tG"), S("s16", 16, 32)))
-            claims_b()
-            claims_c(0, 1)
+            if t == 0:
+                consts_scalar3()
             tt(whole("gi"), S("pB", 0, 16), whole("nw"), A.add)
+            eq(0)
             ts(whole("g3"), whole("gi"), 1048576 + 3, A.bitwise_and)
+            eq(15)
             tt(whole("go4"), IND(whole("g3"), S("rep", 0, 4)), S("jq", 0, 64), A.is_equal)
+            eq(14)
+            eqm(0, 15)
             rec("v", lambda: g.vector.tensor_tensor_scan(ap(whole("inc")), ap(whole("msk")), ap(whole("go4")), 0.0, A.mult, A.add),
                 [whole("inc")], [whole("msk"), whole("go4")])
             mm(S("pC", 0, 64), whole("ih"), whole("cst"), True, False)
             mm(S("pC", 0, 64), whole("uge"), whole("go4"), False, False)
             mm(S("pC", 0, 64), whole("ones"), whole("inc"), False, True)
-            claims_c(1, 2)
+            eq(1, 13)
+            eqm(14)
             tt(whole("tt4"), S("pC", 0, 64), whole("go4"), A.mult)
             mm(S("pA", 0, 16), whole("ih"), whole("dmp"), True, False)
             for d in range(4):
                 mm(S("pA", 0, 16), whole("ih"), S("tt4", 16 * d, 16 * d + 16), False, d == 3)
-            claims_c(2, 4)
+            eq(2, 3)
             cp(whole("pos"), S("pA", 0, 16))
+            eq(12)
+            eqm(1, 13, 2, 3, 12)
             cp(IND(whole("idt"), whole("pos")), whole("jb"))
             for k in range(1, N + 1):
                 d = (rank + k) % N
@@ -597,7 +629,7 @@ def rank_program(g, core, T, topo):
                        S("idt", L * d + e, L * d + 64, 4), e == 0, e == 3)
             claims_c(4, 6)
             ts(S("src", 0, 16), S("pB", 0, 16), C(cJ), A.add)
-            claims_c(6, 9)
+            claims_c(6, 10)
             ts(S("src", 16, 64), S("pK0", 16, 64), C(cJ), A.add)
             nxt, snd = "lnd%d" % (t + 1), "snd%d" % t
             for k in range(1, N + 1):
@@ -614,7 +646,8 @@ def rank_program(g, core, T, topo):
                         [], [o], kind="rem", sem=sem, n=ne)
             n_in = sum(len(topo.engines(T.cores[q], core)) for q in range(N) if q != rank)
             rec("g", None, [S(nxt, L * q, L * q + L) for q in range(N) if q != rank], [], kind="land", sem="arr%d" % t, n=n_in)
-            claims_c(9, 16)
+            claims_c(10, 12)
+            claims_b()
             claims_d()
             if t < RO - 2:
                 for d in range(4):
@@ -622,8 +655,9 @@ def rank_program(g, core, T, topo):
             claims_e()
             scatter("tV", lnd, 2)
             scatter("tF", lnd, 0)
+            cp(IND(S("tG", 0, LC), S("o16", 0, 8)), S(lnd, 1, 512, 4))
         else:
-            cp(whole("s16"), S("s6", 0, 64))
+            cp(whole("s16"), whole("s6"))
             claims_a()
             act(whole("yfb"), IND(whole("tG"), S("s16", 0, 16)))
             act(whole("yvb"), IND(whole("lo"), S("s16", 48, 64)))

@@ -5,8 +5,11 @@ TAU = [96, 700, 24, 2496, 300]
 WA = [7, 113, 51, 229, 87, 19, 161, 203, 35, 149, 71, 247, 93, 181, 125, 11]
 WB = [1, 3, 2, 7, 5, 1, 6, 3, 7, 2, 5, 4, 1, 6, 3, 5]
 KP = [3, 18, 45, 71, 102, 125, 150, 187, 208, 233, 260, 291, 318, 345, 382, 407]
-LC, NS, ZG, WGN = 4352, 5376, 5888, 5904
+LC, ZG, WGN = 4352, 5376, 5392
+OFF = 4194304
 LV, ZV, LON = 4096, 5120, 5136
+NC, JW = 4096, 4112
+BIG = 33554432.0
 B16, F16, F32, I32, U16 = "bfloat16", "float16", "float32", "int32", "uint16"
 
 _SB = {
@@ -14,25 +17,30 @@ _SB = {
     "vg": (W, B16), "eqf": (W, B16), "sg": (W, B16), "eqd": (W, B16),
     "lnd0": (1024, B16), "lnd1": (1024, B16), "lnd2": (1024, B16), "lnd3": (1024, B16), "lnd4": (1024, B16),
     "snd0": (768, B16), "snd1": (768, B16), "snd2": (768, B16), "snd3": (768, B16),
-    "pre": (1040, B16), "idt": (1280, B16), "yfb": (L, B16), "yvb": (L, B16), "zb": (384, F32),
+    "pre": (1040, B16), "idt": (1280, B16), "yfb": (L, B16), "yvb": (L, B16), "zb": (384, F32), "zb0": (384, F32),
+    "zts": (384, F32), "vT": (768, B16), "plm": (L, B16),
     "wfs": (L, B16), "wvs": (L, B16), "nms": (L, I32), "nmb": (L, B16), "thf": (L, B16),
-    "pcol": (8, I32), "col": (32, F32), "jf": (L, F32), "jr": (L, F32), "jq": (L, F32), "j4": (144, F32), "lo16": (16, F32),
-    "jb": (L, B16), "ab": (16, F32), "ab2": (16, F32), "ib": (128, B16), "ih": (128, F16), "i3": (128, B16), "i117": (128, B16),
-    "ineg": (128, B16), "ones": (128, B16), "onesh": (128, F16), "uge": (128, B16), "uget": (128, B16), "wn": (128, B16), "shf": (128, B16),
+    "pcol": (16, I32), "col": (32, F32), "jf": (L, F32), "jr": (L, F32), "jq": (L, F32), "j4": (144, F32), "lo16": (16, F32),
+    "jb": (L, B16), "ab": (16, F32), "ab2": (16, F32), "ib": (128, B16), "ih": (128, F16), "i3": (128, B16), "i18": (128, B16),
+    "ineg": (128, B16), "ones": (128, B16), "uge": (128, B16), "uget": (128, B16), "wn": (128, B16), "shf": (128, B16),
     "zA": (144, B16), "zB": (144, B16), "z0": (144, B16), "z15": (144, B16), "zt": (144, B16), "zn": (144, B16),
-    "z65": (144, B16), "z16": (144, B16), "z4": (144, B16), "dk": (2048, F16), "dm": (L, B16), "hc": (L, B16),
-    "c13": (L, B16), "c1": (128, B16), "c2": (L, B16), "crm": (L, F32), "msk": (64, B16), "cst": (64, F16), "dmp": (16, F16),
-    "cd": (16, F32), "c0": (80, F32), "cp": (80, F32), "cq": (80, F32), "rep": (16, U16), "x16": (16, U16),
-    "jw": (6160, F32), "plh": (16, F16),
-    "patf": (8, U16), "patv": (8, U16), "patt": (16, F32), "z1": (144, B16), "zw": (144, B16), "z21": (144, B16),
-    "ui": (16, I32), "u": (16, I32), "zf_": (16, B16), "prod": (16, I32),
-    "cc": (16, I32), "uh": (16, F16), "ch": (16, F16), "hi": (L, I32), "h16": (L, U16), "cmp": (2 * L, B16),
-    "fl": (80, F32), "ta": (16, F32), "tb": (16, F32), "nw": (16, F32), "p6": (80, F32), "q6": (80, F32),
-    "pen": (512, B16), "ka": (128, F32), "k1": (128, F32), "k2": (64, F32), "k3": (32, F32), "best": (16, F32),
-    "ki": (16, I32), "vld": (16, F32), "val": (32, I32), "oh": (L, F16), "vq": (80, F32), "vp": (80, F32), "vp2": (80, F32),
-    "ha": (16, F32), "hb": (16, I32), "t6": (80, F32), "s6": (80, F32), "s16": (80, U16),
+    "z65": (144, B16), "z16": (144, B16), "z4": (144, B16), "dk": (1536, F16), "dm": (L, B16), "hc": (192, B16),
+    "zE": (144, B16), "zS": (144, B16), "iE": (128, B16), "iS": (128, B16), "cE": (128, B16), "ktab": (L, F16), "k32": (64, F32),
+    "c13": (384, B16), "c1": (192, B16), "c2": (L, B16), "msk": (64, B16), "cst": (64, F16), "dmp": (16, F16),
+    "cd": (16, F32), "c0": (80, F32), "own": (80, F32), "rep": (16, U16), "repc": (16, U16), "l15": (4, U16),
+    "iO": (128, B16), "iOn": (128, B16), "i256": (128, B16), "i256n": (128, B16), "iZG": (128, B16), "iZV": (128, B16),
+    "eH": (96, F16), "eB": (96, B16), "eC": (96, B16), "nmw": (6 * L, B16),
+    "jw": (JW, F32), "jm": (JW, B16), "plh": (16, F16), "i32": (128, F32), "esel": (400, B16),
+    "sel0": (8, B16), "blk": (8, B16),
+    "z1": (144, B16), "zw": (144, B16), "z21": (144, B16), "l16": (16, F32),
+    "ui": (16, I32), "u": (16, I32), "zf_": (16, B16), "prod": (16, I32), "uk": (64, F32), "u3": (48, F32),
+    "cc": (16, I32), "uh": (16, F16), "ch": (64, F16), "hi": (L, I32), "h16": (L, U16), "cmp": (2 * L, B16),
+    "ta": (16, F32), "tb": (16, F32), "fin": (16, B16), "nf": (16, B16), "nv": (16, B16), "valb": (16, B16),
+    "pen": (384, B16), "ka": (64, F32), "kb": (64, F32), "kc": (64, F32), "ks": (64, F32), "kt": (64, F32),
+    "k1": (64, F32), "k2": (64, F32), "k3": (32, F32), "step": (L, B16), "ksel": (L, F32),
+    "ki": (16, I32), "val": (16, I32), "ha": (48, F32), "hb": (80, I32), "hm": (80, I32), "s6": (80, F32), "s16": (80, U16),
     "gi": (16, I32), "g3": (16, I32), "go4": (64, B16), "inc": (64, B16), "tt4": (64, F16), "pos": (16, U16), "src": (64, U16),
-    "ex": (L, F16), "plr": (L, F16), "dmk": (L, B16), "win": (16, F32), "wt": (16, F32), "ot": (16, F32), "o16": (16, U16),
+    "plr": (L, F16), "dmk": (L, B16), "ot": (16, F32), "o16": (16, U16),
 }
 _PS = ["pV", "pE0", "pE1", "pK0", "pK1", "pA", "pB", "pC"]
 SCRATCH = {}
@@ -47,9 +55,14 @@ for _k in _SB:
         SCRATCH[_k] = ("sbuf", [128, _SB[_k][0]], _SB[_k][1])
 for _k in _PS:
     SCRATCH[_k] = ("psum", [128, 512], F32)
-NDMA = 24
+NDMA = 26
 SEMAPHORES = ["cv", "ca", "cp_", "cg"] + ["d%d" % i for i in range(NDMA)] + ["arr%d" % i for i in range(4)] + \
              ["out%d" % i for i in range(12)]
+HOP = 0.1
+SLACK, MARGIN = 0.3, 0.2
+PEC, VFIX, AFIX, RISS, RLAT, LOAD = 0.00042, 0.053, 0.065, 0.55, 1.6, 3.5
+SELF, PEHOP, VADD, GAT, SCA = 0.15, 0.1, 0.03, 1.56, 3.8
+CYC = 0.00083
 
 
 def S(name, lo, hi, step=1):
@@ -62,15 +75,72 @@ def IND(win, off):
     return ("ind", win, off)
 
 
+def width(a):
+    return 16 * width(a[2]) if a[0] == "ind" else len(range(a[2], a[3], a[4]))
+
+
 def _mask(a):
     if a[1] in _PS:
         return 1
-    m = 0
     if a[4] == 1:
         return ((1 << (a[3] - a[2])) - 1) << a[2]
+    m = 0
     for i in range(a[2], a[3], a[4]):
         m |= 1 << i
     return m
+
+
+def arrange(ops):
+    n = len(ops)
+    pred = [dict() for _ in ops]
+    acc = {}
+    for i, o in enumerate(ops):
+        for name, m, wr in o["t"]:
+            if name in _PS:
+                j = acc.get(name)
+                if j is not None and j != i:
+                    pred[i][j] = max(pred[i].get(j, 0.0), 0.0 if ops[j]["q"] == o["q"] else PEHOP if ops[j]["q"] == "p" else HOP)
+                acc[name] = i
+                continue
+            for j, mj, wj in acc.get(name, []):
+                if j != i and (m & mj) and (wr or wj):
+                    pred[i][j] = SELF if ops[j]["q"] == o["q"] else HOP
+        for name, m, wr in o["t"]:
+            if name not in _PS:
+                lst = acc.setdefault(name, [])
+                if wr:
+                    lst[:] = [e for e in lst if e[1] & ~m]
+                lst.append((i, m, wr))
+        for j in o.get("after", []):
+            pred[i][j] = max(pred[i].get(j, -99.0), HOP if ops[j]["q"] != o["q"] else -ops[j]["lat"])
+    succ = [dict() for _ in ops]
+    for i in range(n):
+        for j in pred[i]:
+            pred[i][j] += ops[j]["lat"]
+            succ[j][i] = pred[i][j]
+    chain = [0.0] * n
+    for i in range(n - 1, -1, -1):
+        chain[i] = ops[i]["c"] + max([w + chain[k] for k, w in succ[i].items()] + [ops[i]["lat"]])
+    for i in range(n):
+        for j in pred[i]:
+            if ops[j]["q"] != ops[i]["q"] and chain[j] - ops[j]["c"] - pred[i][j] - chain[i] > SLACK:
+                pred[i][j] += MARGIN
+    end = [0.0] * n
+    busy = {}
+    for i in sorted(range(n), key=lambda i: (-chain[i], i)):
+        c = ops[i]["c"]
+        t = max([end[j] + w for j, w in pred[i].items()] + [0.0])
+        starts, ends = busy.setdefault(ops[i]["q"], ([], []))
+        k = len(ends)
+        while k > 0 and ends[k - 1] > t:
+            k -= 1
+        while k < len(starts) and starts[k] < t + c - 1e-9:
+            t = max(t, ends[k])
+            k += 1
+        starts.insert(k, t)
+        ends.insert(k, t + c)
+        end[i] = t + c
+    return [ops[i] for i in sorted(range(n), key=lambda i: (end[i] - ops[i]["c"], i))]
 
 
 def emit(g, T, ops):
@@ -84,25 +154,20 @@ def emit(g, T, ops):
     for i, o in enumerate(ops):
         q = o["q"]
         need = {}
-        touch = [(a, False) for a in o["r"]] + [(a, True) for a in o["w"]]
-        for a, wr in touch:
-            m = _mask(a)
-            ps = a[1] in _PS
-            for j, mj, wj in acc.get(a[1], []):
-                if not (m & mj):
-                    continue
-                qj = ops[j]["q"]
-                if ps:
-                    if qj == q:
-                        continue
-                elif not (wr or wj):
-                    continue
-                s, n, k = tok[j]
-                if known[q].get(s, 0) < n and need.get(s, (0, None))[0] < n:
-                    need[s] = (n, k)
         if o["kind"] != "land":
-            order = sorted(need.items(), key=lambda e: -len(e[1][1]))
-            for s, (n, k) in order:
+            for name, m, wr in o["t"]:
+                for j, mj, wj in acc.get(name, []):
+                    if not (m & mj):
+                        continue
+                    if name in _PS:
+                        if ops[j]["q"] == q:
+                            continue
+                    elif not (wr or wj):
+                        continue
+                    s, n, k = tok[j]
+                    if known[q].get(s, 0) < n and need.get(s, (0, None))[0] < n:
+                        need[s] = (n, k)
+            for s, (n, k) in sorted(need.items(), key=lambda e: -len(e[1][1])):
                 if known[q].get(s, 0) >= n:
                     continue
                 Q[q].wait_ge(T.sem[s], n)
@@ -111,8 +176,9 @@ def emit(g, T, ops):
                     if known[q].get(s2, 0) < k[s2]:
                         known[q][s2] = k[s2]
         if o["kind"] == "c":
-            cnt[q] += 1
-            o["f"]().then_inc(T.sem[CS[q]], 1)
+            for f in o["f"]:
+                cnt[q] += 1
+                f().then_inc(T.sem[CS[q]], 1)
             tok.append((CS[q], cnt[q], dict(known[q])))
             total[CS[q]] = cnt[q]
         elif o["kind"] == "dma":
@@ -126,13 +192,12 @@ def emit(g, T, ops):
         else:
             tok.append((o["sem"], o["n"], {}))
             total[o["sem"]] = o["n"]
-        for a, wr in touch:
-            m = _mask(a)
-            lst = acc.setdefault(a[1], [])
-            if wr and a[1] not in _PS:
-                lst[:] = [e for e in lst if e[1] & ~m]
-            if a[1] in _PS:
+        for name, m, wr in o["t"]:
+            lst = acc.setdefault(name, [])
+            if name in _PS:
                 lst[:] = [e for e in lst if ops[e[0]]["q"] != q]
+            elif wr:
+                lst[:] = [e for e in lst if e[1] & ~m]
             lst.append((i, m, wr))
     for s in total:
         if known["g"].get(s, 0) < total[s]:
@@ -156,41 +221,59 @@ def rank_program(g, core, T, topo):
             return T[a[1]][:, a[2]:a[3]]
         return T[a[1]][:, a[2]:a[3]:a[4]]
 
-    def parts(a):
-        return [a[1], a[2]] if a[0] == "ind" else [a]
+    lines = {}
+    keep = [False]
 
-    def rec(q, f, outs, ins, kind="c", **kw):
+    def rec(q, f, outs, ins, c, kind="c", lat=0.0, **kw):
         r, w = [], []
         for a in ins:
             if isinstance(a, tuple):
-                r += parts(a)
+                r += [a[1], a[2]] if a[0] == "ind" else [a]
         for a in outs:
             if a[0] == "ind":
                 w.append(a[1])
                 r.append(a[2])
             else:
                 w.append(a)
-        d = {"q": q, "f": f, "r": r, "w": w, "kind": kind}
+        d = {"q": q, "f": [f] if kind == "c" and not isinstance(f, list) else f, "kind": kind, "c": c, "lat": lat,
+             "t": [(a[1], _mask(a), False) for a in r] + [(a[1], _mask(a), True) for a in w]}
+        if keep[0]:
+            d["after"] = lines.get(q, [])
+            lines[q] = [len(ops)]
         d.update(kw)
         ops.append(d)
+        return len(ops) - 1
 
     def sc(x):
         return ap(x) if isinstance(x, tuple) else x
 
+    def vc(o, a, b=None):
+        if o[0] == "ind":
+            return 0.05 + SCA * CYC * width(o)
+        if a[0] == "ind":
+            return 0.05 + GAT * CYC * width(o)
+        if b is not None:
+            return max(VFIX, VADD + CYC * width(o) * (1 if a[1] in _PS or b[1] in _PS else 2))
+        two = all(SCRATCH[x[1]][2] in (B16, F16, U16) for x in (o, a))
+        return max(VFIX, VADD + CYC * width(o) * (0.5 if two else 1))
+
     def tt(o, a, b, op):
-        rec("v", lambda: g.vector.tensor_tensor(ap(o), ap(a), ap(b), op), [o], [a, b])
+        rec("v", lambda: g.vector.tensor_tensor(ap(o), ap(a), ap(b), op), [o], [a, b], vc(o, a, b))
 
     def ts(o, a, s1, op0, s2=None, op1=None):
         if op1 is None:
-            rec("v", lambda: g.vector.tensor_scalar(ap(o), ap(a), sc(s1), None, op0), [o], [a, s1])
+            rec("v", lambda: g.vector.tensor_scalar(ap(o), ap(a), sc(s1), None, op0), [o], [a, s1], vc(o, a))
         else:
-            rec("v", lambda: g.vector.tensor_scalar(ap(o), ap(a), sc(s1), sc(s2), op0, op1), [o], [a, s1, s2])
+            rec("v", lambda: g.vector.tensor_scalar(ap(o), ap(a), sc(s1), sc(s2), op0, op1), [o], [a, s1, s2], vc(o, a))
 
     def cp(o, a):
-        rec("v", lambda: g.vector.tensor_copy(ap(o), ap(a)), [o], [a])
+        rec("v", lambda: g.vector.tensor_copy(ap(o), ap(a)), [o], [a], vc(o, a))
 
     def ms(o, c):
-        rec("v", lambda: g.vector.memset(ap(o), c), [o], [])
+        rec("v", lambda: g.vector.memset(ap(o), c), [o], [], vc(o, o))
+
+    def scan(o, a, b, op0, op1):
+        rec("v", lambda: g.vector.tensor_tensor_scan(ap(o), ap(a), ap(b), 0.0, op0, op1), [o], [a, b], vc(o, a))
 
     def act(o, a, func=None, bias=None, scale=None):
         fn = F.Identity if func is None else func
@@ -199,34 +282,36 @@ def rank_program(g, core, T, topo):
             kw["bias"] = sc(bias)
         if scale is not None:
             kw["scale"] = sc(scale)
-        rec("a", lambda: g.scalar.activation(ap(o), ap(a), fn, **kw), [o], [a, bias, scale])
+        c = 0.065 + GAT * CYC * width(o) if a[0] == "ind" else AFIX + CYC * width(o)
+        rec("a", lambda: g.scalar.activation(ap(o), ap(a), fn, **kw), [o], [a, bias, scale], c)
 
-    def fill(name, lo, hi, c):
-        for b in range(lo, hi, L):
-            e = min(hi, b + L)
-            act(S(name, b, e), S("jf", 0, e - b), None, c, 0.0)
+    def mms(calls):
+        rec("p", [lambda e=e: g.tensor.matmul(ap(e[0]), ap(e[1]), ap(e[2]), e[3], e[4]) for e in calls],
+            [e[0] for e in calls], [e[1] for e in calls] + [e[2] for e in calls],
+            sum(PEC * max(min(64, width(e[1])), width(e[2])) for e in calls))
 
     def mm(o, wt, mv, start, stop):
-        rec("p", lambda: g.tensor.matmul(ap(o), ap(wt), ap(mv), start, stop), [o], [wt, mv])
+        mms([(o, wt, mv, start, stop)])
 
-    def iota(o, pat, base, cm, isint=False):
-        if isint:
-            rec("g", lambda: g.iota(ap(o), pat, base, cm), [o], [])
+    def iota(o, pat, base, cm):
+        c = 0.13 + 2 * CYC * width(o)
+        if SCRATCH[o[1]][2] == I32:
+            rec("g", lambda: g.iota(ap(o), pat, base, cm), [o], [], c)
         else:
-            rec("g", lambda: g.iota(ap(o), pat, base, cm, allow_small_or_imprecise_dtypes=True), [o], [])
+            rec("g", lambda: g.iota(ap(o), pat, base, cm, allow_small_or_imprecise_dtypes=True), [o], [], c)
 
-    def dma(q, o, a):
+    def fill(name, lo, hi, c):
+        iota(S(name, lo, hi), [[0, hi - lo]], c, 0)
+
+    def dma(q, o, a, lat=2.5):
         s = "d%d" % nd[0]
         nd[0] += 1
         e = g.sync if q == "s" else g.scalar
-        oo = ap(o) if isinstance(o, tuple) else o
-        aa = ap(a) if isinstance(a, tuple) else a
-        rec(q, lambda: e.dma_start(oo, aa), [o] if isinstance(o, tuple) else [], [a], kind="dma", sem=s)
+        rec(q, lambda: e.dma_start(sc(o), sc(a)), [o] if isinstance(o, tuple) else [], [a], 0.05, kind="dma", lat=lat, sem=s)
 
     def conv(o, z, buf, base, n, stride, first=True, last=True):
-        for r in range(16):
-            mm(o, S(z, 15 - r, 143 - r), S(buf, base + stride * r, base + stride * (r + 16 * n - 16) + 1, stride * 16),
-               first and r == 0, last and r == 15)
+        mms([(o, S(z, 15 - r, 143 - r), S(buf, base + stride * r, base + stride * (r + 16 * n - 16) + 1, stride * 16),
+              first and r == 0, last and r == 15) for r in range(16)])
 
     def C(i):
         return S("col", i, i + 1)
@@ -234,31 +319,39 @@ def rank_program(g, core, T, topo):
     def whole(name):
         return S(name, 0, _SB[name][0])
 
-    dma("s", whole("wfs"), T.wf[:])
-    dma("s", whole("nms"), T.nm[:])
-    dma("s", whole("wvs"), T.wv[:])
-    dma("s", S("tV", 0, W), T.rv[:])
-    dma("s", S("tF", 0, W), T.rf[:])
-    dma("s", S("tG", 0, W), T.rg[:])
+    keep[0] = True
+    for o, a, lat in ((whole("wfs"), T.wf, 2.2), (whole("nms"), T.nm, 2.8), (whole("wvs"), T.wv, 3.1),
+                      (S("tV", 0, W), T.rv, 3 + LOAD), (S("tF", 0, W), T.rf, 3 + 2 * LOAD), (S("tG", 0, W), T.rg, 3 + 3 * LOAD)):
+        dma("s", o, a[:], lat)
+    keep[0] = False
 
-    iota(S("pcol", 0, 1), [[0, 1]], 0, 1, True)
+    iota(S("pcol", 0, 1), [[0, 1]], 0, 1)
     iota(whole("jf"), [[1, L]], 0, 0)
     iota(whole("jr"), [[0, 16], [1, 16]], 0, 0)
     iota(whole("jq"), [[1, 16], [0, 16]], 0, 0)
-    iota(whole("lo16"), [[16, 16]], 0, 1)
+    iota(whole("l16"), [[16, 16]], 0, 1)
     iota(whole("j4"), [[1, 36], [0, 4]], 0, 0)
-    iota(whole("jw"), [[1, 6160]], -2048, 0)
+    iota(whole("jb"), [[1, L]], 0, 0)
+    for b in range(0, JW, 1028):
+        iota(S("jw", b, b + 1028), [[1, 1028]], b - 2048, 0)
+    for b in range(0, W, 1024):
+        iota(S("jm", b, b + 1024), [[0, 8], [1, 128]], 0, 0)
+    fill("jm", W, JW, 200)
     for i in range(16):
         ms(S("ab", i, i + 1), float(WA[i] + 256 * WB[i]))
-    (cP, cR, cG, cJ, cA, cB, c20, cE15, cT, c256, cSH, cKEEP, cFLAG, c4G, c40, cZ, cX, cY, cG16, cW, c21, cU, cAB) = range(23)
+        ms(S("ktab", i, L, 16), float(KP[15 - i]))
+    (cP, cR, cG, cJ, cA, cB, c20, cE15, cT, c256, cSH, cKEEP, cFLAG, c4G, c40, cZ, cX, cY, cG16, cW, c21, cU, cAB,
+     cX2, cAB2, cES, cR0, cL15) = range(28)
     ts(S("pcol", 1, 2), S("pcol", 0, 1), 15, A.bitwise_and)
     ts(S("pcol", 2, 3), S("pcol", 0, 1), 4, A.arith_shift_right)
     ts(S("pcol", 3, 4), S("pcol", 0, 1), 3, A.bitwise_and)
-    ms(whole("hc"), 0.0)
     cp(S("col", 0, 4), S("pcol", 0, 4))
-    for m in range(16):
+    for m in range(4):
+        ms(S("k32", 16 * m, 16 * m + 16), 32.0 * KP[m])
+    ms(whole("hc"), 0.0)
+    for m in range(4, 16):
         if KP[m] % 2 == 0:
-            ms(S("hc", 16 * m, 16 * m + 16), 2048.0)
+            ms(S("hc", 16 * m - 64, 16 * m - 48), 2048.0)
     ts(C(cZ), C(cG), 16.0, A.mult, 15.0, A.add)
     ts(whole("ib"), S("jf", 0, 128), C(cP), A.is_equal)
     ts(C(c20), C(cR), 0.0, A.is_equal, 2.0, A.mult)
@@ -271,161 +364,115 @@ def rank_program(g, core, T, topo):
     tt(whole("ab2"), whole("ab"), S("dm", 0, 16), A.mult)
     ts(C(cU), C(cR), 14.0, A.is_equal)
     ts(C(c256), C(cR), 0.0, A.is_equal, 256.0, A.mult)
-    rec("v", lambda: g.vector.tensor_reduce(ap(C(cAB)), ap(whole("ab2")), AxisListType.X, A.add), [C(cAB)], [whole("ab2")])
+    rec("v", lambda: g.vector.tensor_reduce(ap(C(cAB)), ap(whole("ab2")), AxisListType.X, A.add), [C(cAB)], [whole("ab2")], 0.06)
     tt(C(cW), C(cU), C(cFLAG), A.add)
-    act(whole("z0"), whole("z1"), scale=C(c20))
-    act(S("lnd0", 0, 1024, 4), whole("wfs"))
+    ts(whole("rep"), S("jf", 0, 16), 0.0, A.mult, C(cR), A.add)
+    cp(whole("repc"), S("jf", 0, 16))
+    ts(whole("z0"), whole("z1"), C(c20), A.mult)
     mm(S("pB", 0, L), whole("ones"), whole("wfs"), True, True)
-    mm(S("pC", 0, L), whole("ib"), whole("nmb"), True, False)
-    mm(S("pC", 0, L), S("z0", 0, 128), whole("nmb"), False, False)
-    mm(S("pC", 0, L), S("z0", 1, 129), whole("nmb"), False, True)
+    mms([(S("pC", 0, L), whole("ib"), whole("nmb"), True, False),
+         (S("pC", 0, L), S("z0", 0, 128), whole("nmb"), False, False),
+         (S("pC", 0, L), S("z0", 1, 129), whole("nmb"), False, True)])
     cp(S("pcol", 4, 5), C(cAB))
     ts(whole("thf"), S("pB", 0, L), 0.0, A.is_gt)
     ts(S("pcol", 5, 6), S("pcol", 4, 5), 255, A.bitwise_and)
     ts(S("pcol", 6, 7), S("pcol", 4, 5), 8, A.arith_shift_right)
     tt(S("lnd0", 3, 1024, 4), S("pC", 0, L), whole("thf"), A.mult)
+    for j, a in enumerate(("wfs", "wfs", "wvs")):
+        act(S("lnd0", j, 1024, 4), whole(a))
     cp(S("col", cA, cA + 2), S("pcol", 5, 7))
     ts(C(cX), C(cR), 13.0, A.is_equal, 256.0, A.mult)
     ts(C(cY), C(cR), 1.0, A.is_equal)
     cp(whole("ih"), whole("ib"))
     tt(C(cT), C(cX), C(cY), A.add)
-    act(whole("zw"), whole("z1"), scale=C(cW))
-    act(whole("zA"), whole("z1"), scale=C(cA))
+    ts(whole("zw"), whole("z1"), C(cW), A.mult)
+    ts(whole("zA"), whole("z1"), C(cA), A.mult)
     act(whole("wn"), whole("ones"), scale=C(c256))
-    act(S("lnd0", 2, 1024, 4), whole("wvs"))
     act(whole("zt"), whole("z1"), scale=C(cT))
-    act(S("lnd0", 1, 1024, 4), whole("wfs"))
-    fill("c13", 0, 128, 13.0)
-    fill("c13", 128, L, 2.0)
-    act(whole("i3"), whole("ib"), scale=3.0)
-    act(whole("i117"), whole("ib"), scale=-18.0)
-    fill("c1", 0, 128, -16777216.0)
-    act(whole("c2"), whole("jq"), None, 15.0, -1.0)
-    act(whole("zn"), whole("z1"), scale=-1.0)
-    act(whole("z16"), whole("z1"), scale=16.0)
-    act(whole("ineg"), whole("ib"), scale=-33554432.0)
-
-    def consts_hash(m0, m1):
-        for m in range(m0, m1):
-            ts(S("dk", 128 * m, 128 * m + 128), whole("ib"), float(KP[m]), A.mult)
-
-    def consts_main():
-        ts(C(cE15), C(cR), 15.0, A.is_equal)
-        ts(C(c21), C(cY), 2.0, A.mult)
-        ts(C(cX), C(cU), 256.0, A.mult, C(c256), A.add)
-        tt(C(cAB), C(cP), C(cKEEP), A.subtract)
-        ts(C(cG16), C(cG), 16.0, A.mult)
-        ts(C(c4G), C(cG), 4.0, A.mult, 3.0, A.add)
-        ts(C(c40), C(c20), 2.0, A.mult)
-        tt(C(cSH), C(cAB), C(cX), A.subtract)
-        ts(whole("lo16"), whole("lo16"), C(cG16), A.subtract)
-        ts(whole("z15"), whole("z1"), C(cE15), A.mult)
-        ts(whole("z21"), whole("z1"), C(c21), A.mult)
-        ts(whole("shf"), S("jf", 0, 128), C(cSH), A.is_equal)
-
-    def consts_late():
-        l16 = whole("lo16")
-        rows = ((4, LC, -4, -LC, 1), (4, LC + 3, -3, NS - LC - 3, 0), (4, LC + 1, -4, -LC - 1, 1),
-                (4, LV + 2, -3, 3840 - LV - 2, -256), (0, 6144, 0, -6144, 1))
-        for b, (s0, b0, s1, b1, q) in enumerate(rows):
-            act(S("c0", 16 * b, 16 * b + 16), l16, None, float(b0), float(s0))
-            act(S("cp", 16 * b, 16 * b + 16), l16, None, float(b1), float(s1))
-            act(S("cq", 16 * b, 16 * b + 16), l16, None, float(q), 0.0)
-
-    def consts_lists():
-        ts(whole("rep"), S("jf", 0, 16), 0.0, A.mult, C(cR), A.add)
-        for i, x in enumerate((0, 48, 16, 48, 64, 64)):
-            ms(S("patt", i, i + 1), float(x))
-        ms(S("patt", 8, 11), 0.0)
-        ms(S("patt", 11, 12), 16.0)
-        ms(S("patt", 12, 14), 0.0)
-        ts(S("patf", 0, 6), S("patt", 0, 6), C(cR), A.add)
-        ts(S("patv", 0, 6), S("patt", 8, 14), C(cR), A.add)
-
-    def consts_tail():
-        ts(whole("z4"), whole("j4"), C(c4G), A.is_equal, C(c40), A.mult)
-        ts(whole("uget"), S("jr", 0, 128), C(cR), A.is_le, -1.0, A.mult)
-        ts(whole("msk"), S("jr", 0, 64), 0.0, A.is_gt)
-        tt(whole("uge"), whole("uget"), whole("ones"), A.mult)
-        for d in range(4):
-            ts(S("cst", 16 * d, 16 * d + 16), whole("lo16"), -1.0, A.mult, float(256 * d - 1024), A.add)
-        ts(whole("dmp"), whole("lo16"), 1024.0, A.add)
-        ts(whole("cd"), whole("lo16"), 2048.0, A.add)
-
-    def consts_scalar():
-        act(whole("crm"), whole("jq"), None, 15.0, -1.0)
-        act(whole("zB"), whole("z1"), scale=C(cB))
-        fill("tG", W, LC, 0.0)
-        fill("tG", ZG, WGN, 0.0)
-        fill("lo", ZV, LON, 0.0)
-        fill("pre", 1024, 1040, 0.0)
-
-    def consts_scalar2():
-        act(whole("jb"), whole("jf"))
-        fill("idt", 0, 1280, 256.0)
-
-    def consts_scalar3():
-        act(whole("z65"), whole("z1"), scale=8192.0)
-        fill("tF", W, LC, 0.0)
-        fill("tV", W, LC, 0.0)
-
-    def scatter(tab, lnd, j):
-        cp(IND(S(tab, 0, LC), whole("o16")), S(lnd, j, 1024, 4))
+    fill("c13", 0, 192, 13)
+    fill("c13", 192, 384, 2)
+    act(whole("c1"), S("jf", 0, 192), None, -BIG / 2, 0.0)
+    act(S("cE", 0, 64), S("jf", 0, 64), None, -25 * BIG, 0.0)
+    act(S("cE", 64, 128), S("jf", 0, 64), None, -BIG, 0.0)
+    iota(whole("c2"), [[-1, 16], [0, 16]], 15, 0)
+    for name, of, x in (("i3", "ib", 3.0), ("i18", "ib", -18.0), ("ineg", "ib", -BIG), ("iE", "ib", -6 * BIG), ("iS", "ib", 18 * BIG),
+                        ("zn", "z1", -1.0), ("z16", "z1", 16.0), ("zE", "z1", 2 * BIG), ("zS", "z1", BIG), ("z65", "z1", 8192.0),
+                        ("i32", "ib", 1.0), ("iO", "ib", float(OFF)), ("iOn", "ib", float(-OFF)), ("i256", "ib", 256.0),
+                        ("i256n", "ib", -256.0), ("iZG", "ib", float(ZG)), ("iZV", "ib", float(ZV))):
+        act(whole(name), whole(of), scale=x)
+    for m in range(4, 16):
+        ts(S("dk", 128 * m - 512, 128 * m - 384), whole("ib"), float(KP[m]), A.mult)
+    ts(C(cE15), C(cR), 15.0, A.is_equal)
+    ts(C(cL15), C(cR), 16.0, A.mult, 15.0, A.add)
+    ts(C(c21), C(cY), 2.0, A.mult)
+    ts(C(cX2), C(cU), 256.0, A.mult, C(c256), A.add)
+    tt(C(cAB2), C(cP), C(cKEEP), A.subtract)
+    ts(C(cG16), C(cG), 16.0, A.mult)
+    ts(C(c4G), C(cG), 4.0, A.mult, 3.0, A.add)
+    ts(C(c40), C(c20), 2.0, A.mult)
+    tt(C(cSH), C(cAB2), C(cX2), A.subtract)
+    ts(whole("lo16"), whole("l16"), C(cG16), A.subtract)
+    act(whole("z15"), whole("z1"), scale=C(cE15))
+    act(whole("z21"), whole("z1"), scale=C(c21))
+    act(whole("zB"), whole("z1"), scale=C(cB))
+    ts(whole("shf"), S("jf", 0, 128), C(cSH), A.is_equal)
+    for b, (s0, b0) in enumerate(((4, LC), (4, LC + 1), (0, NC), (4, 2 * L + 3), (4, LV + 2))):
+        act(S("c0", 16 * b, 16 * b + 16), whole("lo16"), None, float(b0), float(s0))
+    act(whole("own"), whole("c0"))
+    ms(S("eH", 0, 48), 0.0)
+    for b, s0, b0 in ((3, 1, 0), (4, 1, 0), (5, 4, 1)):
+        ts(S("eH", 16 * b, 16 * b + 16), whole("lo16"), float(s0), A.mult, float(b0), A.add)
+    for name, lo, hi, x in (("eB", 0, 48, 2048), ("eB", 48, 64, 0), ("eB", 64, 80, 3840), ("eB", 80, 96, LC),
+                            ("eC", 0, 16, 0), ("eC", 16, 48, OFF), ("eC", 48, 80, 0), ("eC", 80, 96, -OFF)):
+        fill(name, lo, hi, x)
+    ts(whole("l15"), S("jf", 0, 4), 0.0, A.mult, C(cL15), A.add)
+    ts(whole("z4"), whole("j4"), C(c4G), A.is_equal, C(c40), A.mult)
+    ts(whole("uget"), S("jr", 0, 128), C(cR), A.is_le, -1.0, A.mult)
+    ts(whole("msk"), S("jr", 0, 64), 0.0, A.is_gt)
+    tt(whole("uge"), whole("uget"), whole("ones"), A.mult)
+    for d in range(4):
+        ts(S("cst", 16 * d, 16 * d + 16), whole("lo16"), -1.0, A.mult, float(256 * d - 1024), A.add)
+    ts(whole("dmp"), whole("lo16"), 1024.0, A.add)
+    ts(whole("cd"), whole("lo16"), 2048.0, A.add)
+    for name, lo, hi in (("tG", W, LC), ("tG", ZG, WGN), ("lo", ZV, LON), ("pre", 1024, 1040), ("tF", W, LC), ("tV", W, LC)):
+        fill(name, lo, hi, 0)
+    fill("idt", 0, 1280, 256)
+    ts(C(cES), C(cP), 3.0, A.mult, -2046.0, A.add)
+    ts(whole("esel"), S("jw", 0, 400), C(cES), A.is_equal)
+    ts(C(cR0), C(cR), 0.0, A.is_equal)
+    ts(whole("sel0"), S("jf", 0, 8), C(cG), A.is_equal, C(cR0), A.mult)
+    ts(whole("blk"), S("jf", 0, 8), C(cG), A.is_equal, 256.0, A.mult)
 
     for t in range(RO):
         lnd = "lnd%d" % t
         last = t == RO - 1
         conv(S("pA", 0, 16), "zA", lnd, 0, 16, 4)
         conv(S("pB", 0, 16), "zw", lnd, 3, 16, 4)
-        mm(S("pK0", 0, L), whole("wn"), S(lnd, 3, 1024, 4), True, True)
-        conv(S("pC", 0, 16), "z0", lnd, 3, 16, 4)
-        dma("s", S("tG", LC, NS), whole(lnd))
-        dma("s", S("lo", LV, ZV), whole(lnd))
-        if t == 0:
-            consts_hash(0, 6)
-        for i, step in enumerate((
-                lambda: cp(whole("ui"), S("pA", 0, 16)),
-                lambda: ts(whole("u"), whole("ui"), 4095, A.bitwise_and),
-                lambda: ts(whole("uh"), whole("u"), -2048.0, A.add),
-                lambda: tt(whole("prod"), S("pB", 0, 16), whole("u"), A.mult),
-                lambda: ts(whole("cc"), whole("prod"), 5, A.arith_shift_right, 4095, A.bitwise_and),
-                lambda: ts(whole("ch"), whole("cc"), -2048.0, A.add))):
-            step()
-            if t == 0 and i < 5:
-                consts_hash(6 + 2 * i, 8 + 2 * i)
-        for bank, m0, m1 in (("pE0", 0, 4), ("pE1", 4, 16)):
-            mm(S(bank, 0, 16 * (m1 - m0)), whole("ib"), S("hc", 16 * m0, 16 * m1), True, False)
-            for m in range(m0, m1):
-                mm(S(bank, 16 * (m - m0), 16 * (m - m0) + 16), S("dk", 128 * m, 128 * m + 128), whole("uh"), False, False)
-            for m in range(m0, m1):
-                mm(S(bank, 16 * (m - m0), 16 * (m - m0) + 16), whole("ih"), whole("ch"), False, m == m1 - 1)
-        mm(S("pV", 0, L), whole("ib"), S(lnd, 2, 1024, 4), True, True)
-        mm(S("pV", L, 2 * L), whole("ib"), S(lnd, 2, 1024, 4), True, True)
-        conv(S("pA", 0, 16), "zt", lnd, 3, 16, 4)
-        tt(S("cmp", 0, L), S(lnd, 0, 1024, 4), S("pK0", 0, L), A.min)
-        act(S("cmp", L, 2 * L), S("cmp", 0, L))
-        cp(S("hi", 0, 64), S("pE0", 0, 64))
-        ts(whole("zf_"), S("pC", 0, 16), 0.0, A.is_equal)
-        ts(S("hi", 0, 64), S("hi", 0, 64), 4095, A.bitwise_and)
-        ts(S("fl", 48, 64), S("pC", 0, 16), 0.0, A.is_gt)
+        mm(S("pK1", 0, L), whole("wn"), S(lnd, 3, 1024, 4), True, True)
+        cp(whole("ui"), S("pA", 0, 16))
+        ts(whole("u"), whole("ui"), 4095, A.bitwise_and)
+        tt(whole("uk"), IND(whole("u"), S("rep", 0, 4)), whole("k32"), A.mult)
+        ts(whole("uh"), whole("u"), -2048.0, A.add)
+        tt(whole("prod"), S("pB", 0, 16), whole("u"), A.mult)
+        tt(S("hi", 0, 64), IND(whole("prod"), S("rep", 0, 4)), whole("uk"), A.add)
+        ts(S("hi", 0, 64), S("hi", 0, 64), 5, A.arith_shift_right, 4095, A.bitwise_and)
         cp(S("h16", 0, 64), S("hi", 0, 64))
-        ts(whole("nw"), S("pC", 0, 16), 0.0, A.is_equal, 1048576.0, A.mult)
-
-        def gf1(m):
-            tt(S("eqf", L * m, L * m + L), IND(S("tF", 0, W), S("h16", 16 * m, 16 * m + 16)), S("cmp", 0, L), A.is_equal)
-
-        def gf2(m):
-            tt(S("eqf", L * m, L * m + 2 * L), IND(S("tF", 0, W), S("h16", 16 * m, 16 * m + 32)), whole("cmp"), A.is_equal)
-
-        if t > 0:
-            gf1(0)
-        cp(S("hi", 64, L), S("pE1", 0, 192))
-        ts(S("hi", 64, L), S("hi", 64, L), 4095, A.bitwise_and)
-        if t > 0:
-            gf1(1)
-        cp(S("h16", 64, L), S("hi", 64, L))
-        if t == 0:
-            consts_main()
+        ts(whole("cc"), whole("prod"), 5, A.arith_shift_right, 4095, A.bitwise_and)
+        ts(whole("ch"), IND(whole("cc"), S("rep", 0, 4)), -2048.0, A.add)
+        tt(S("cmp", 0, L), S(lnd, 0, 1024, 4), S("pK1", 0, L), A.min)
+        mms([(S("pB", 0, 192), whole("ib"), whole("hc"), True, False)] +
+            [(S("pB", 16 * m, 16 * m + 16), S("dk", 128 * m, 128 * m + 128), whole("uh"), False, False) for m in range(12)])
+        mms([(S("pB", 64 * i, 64 * i + 64), whole("ih"), whole("ch"), False, i == 2) for i in range(3)])
+        mms([(S("pV", L * i, L * i + L), whole("ib"), S(lnd, 2, 1024, 4), i == 0, i == 1) for i in range(2)])
+        conv(S("pC", 0, 16), "z0", lnd, 3, 16, 4)
+        conv(S("pA", 0, 16), "zt", lnd, 3, 16, 4)
+        dma("s", S("tG", LC, ZG), whole(lnd), 3.5)
+        dma("s", S("lo", LV, ZV), whole(lnd), 4.5)
+        ts(whole("zf_"), S("pC", 0, 16), 0.0, A.is_equal)
+        if not last:
+            dma("s", S("nmw", 2 * L, 6 * L), whole(lnd), 5.5)
+            ts(whole("tb"), S("pA", 0, 16), 256.0, A.is_equal)
+        ts(whole("ta"), S("pA", 0, 16), 256.0, A.is_ge)
 
         def gv(c):
             act(S("vg", 1024 * c, 1024 * c + 1024), IND(S("tV", 0, W), S("h16", 64 * c, 64 * c + 64)))
@@ -433,249 +480,203 @@ def rank_program(g, core, T, topo):
         def sgn(c):
             act(S("sg", 1024 * c, 1024 * c + 1024), S("lo", 1024 * c, 1024 * c + 1024), F.Sign, -(TAU[t] + 0.5))
 
-        def gf(c):
-            if c == 0 and t > 0:
-                gf2(2)
-            else:
-                gf2(4 * c)
-                gf2(4 * c + 2)
+        def gf(c, m0=0, m1=4, n=2):
+            for m in range(4 * c + m0, 4 * c + m1, n):
+                tt(S("eqf", L * m, L * (m + n)), IND(S("tF", 0, W), S("h16", 16 * m, 16 * (m + n))), S("cmp", 0, L * n), A.is_equal)
 
         def mn(c):
-            for h in range(2):
-                b = 1024 * c + 512 * h
+            for b in (1024 * c, 1024 * c + 512):
                 tt(S("lo", b, b + 512), S("vg", b, b + 512), S("pV", 0, 512), A.min)
 
-        def pe(c, kind, stop=False):
-            h, o = c // 2, 64 * (c % 2)
-            if kind == "E":
-                conv(S("pE%d" % h, o, o + 64), "zn", "eqf", 1024 * c, 64, 1, False, stop)
-            elif kind == "S":
-                conv(S("pE%d" % h, 128 + o, 128 + o + 64), "zn", "sg", 1024 * c, 64, 1, False, stop)
-            else:
-                conv(S("pK%d" % h, o, o + 64), "z16", "lo", 1024 * c, 64, 1, False, False)
+        at = [(("pE0", 64 * c), ("pE0", 192 + 64 * c), ("pK0", 64 * c)) for c in range(3)] + [(("pE1", 0), ("pK1", 64), ("pK1", 0))]
 
-        def init(h):
-            e, k = "pE%d" % h, "pK%d" % h
-            mm(S(e, 0, L), whole("ib"), whole("c13"), True, False)
-            for m in range(8):
-                mm(S(e, 16 * m, 16 * m + 16), whole("i3"), whole("zf_"), False, False)
-            for m in range(8):
-                mm(S(e, 128 + 16 * m, 128 + 16 * m + 16), whole("i117"), whole("zf_"), False, False)
-            mm(S(k, 0, 128), whole("ib"), whole("c1"), True, False)
-            mm(S(k, 0, 128), whole("ib"), S("c2", 128 * h, 128 * h + 128), False, False)
+        def sums(kind, c, stop=False):
+            i = "ESK".index(kind)
+            z = "z16" if i == 2 else "zn" if c < 3 else ("zE", "zS")[i]
+            conv(S(at[c][i][0], at[c][i][1], at[c][i][1] + 64), z, ("eqf", "sg", "lo")[i], 1024 * c, 64, 1, False, stop)
 
-        def relu(h):
-            act(S("pen", L * h, L * h + L), S("pE%d" % h, 0, L), F.Relu)
+        def consts(bank, parts):
+            mms([(S(bank, a, a + width(x)), whole(w), x, i == 0, False) for i, (a, w, x) in enumerate(parts)])
 
-        def pen(h):
-            mm(S("pK%d" % h, 0, 128), whole("ineg"), S("pen", L * h, L * h + 128), False, False)
-            mm(S("pK%d" % h, 0, 128), whole("ineg"), S("pen", L * h + 128, L * h + L), False, True)
+        def bars(bank, a, n, w):
+            mms([(S(bank, b, b + 16), whole(w), whole("zf_"), False, False) for b in range(a, a + n, 16)])
 
+        def rest():
+            cp(S("hi", 64, L), S("pB", 0, 192))
+            ts(S("hi", 64, L), S("hi", 64, L), 4095, A.bitwise_and)
+            cp(S("h16", 64, L), S("hi", 64, L))
+
+        keep[0] = True
         gv(0)
-        init(0)
-        init(1)
+        if t > 0:
+            gf(0, 0, 1, 1)
+        rest()
+        consts("pE0", [(0, "ib", whole("c13"))])
+        consts("pK0", [(0, "ib", whole("c1")), (0, "ib", S("c2", 0, 192))])
+        if t > 0:
+            gf(0, 1, 4, 1); sums("E", 0)
+        gv(1)
+        act(S("cmp", L, 2 * L), S("cmp", 0, L))
+        mn(0); sums("K", 0)
+        sgn(0); sums("S", 0)
+        consts("pK1", [(0, "ib", S("c1", 0, 64)), (0, "ib", S("c2", 192, L)), (64, "ib", S("cE", 64, 128))])
+        consts("pE1", [(0, "ib", S("cE", 0, 64))])
+        for e in (("pE0", 0, 192, "i3"), ("pE0", 192, 192, "i18"), ("pK1", 64, 64, "iS"), ("pE1", 0, 64, "iE")):
+            bars(*e)
+        if t > 0:
+            gf(1); sums("E", 1)
+        gv(2)
+        mn(1); sums("K", 1)
+        sgn(1); sums("S", 1)
+        if t == 0:
+            gf(0); sums("E", 0)
+            gf(1); sums("E", 1)
+        gf(2); sums("E", 2)
+        gv(3)
+        mn(2); sums("K", 2)
+        sgn(2); sums("S", 2, True)
+        mn(3); sums("K", 3)
+        sgn(3)
+        act(whole("pen"), S("pE0", 0, 384), F.Relu)
+        sums("S", 3, True)
+        mms([(S("pK0", 0, 192), whole("ineg"), S("pen", 192 * i, 192 * i + 192), False, i == 1) for i in range(2)])
+        gf(3); sums("E", 3, True)
+        keep[0] = False
+        act(whole("ks"), S("pK1", 64, 128))
         if not last:
             for b, z in ((0, "z21"), (L, "z15")):
-                mm(S("pC", b, b + L), whole("shf"), S(lnd, 3, 1024, 4), True, False)
-                mm(S("pC", b, b + L), S(z, 1, 129), S(lnd, 3, 1024, 4), False, True)
-        if t > 0:
-            gf(0); pe(0, "E")
-            gv(1)
-            mn(0); pe(0, "K")
-            sgn(0); pe(0, "S")
-            gf(1); pe(1, "E")
-            gv(2)
-            mn(1); pe(1, "K")
-            sgn(1); pe(1, "S", True)
+                mms([(S("pC", b, b + L), whole("shf"), S(lnd, 3, 1024, 4), True, False),
+                     (S("pC", b, b + L), S(z, 1, 129), S(lnd, 3, 1024, 4), False, True)])
+            act(S("nmw", 0, 2 * L), S("pC", 0, 2 * L))
         else:
-            gv(1)
-            mn(0); pe(0, "K")
-            sgn(0); pe(0, "S")
-            consts_tail()
-            gv(2)
-            mn(1); pe(1, "K")
-            sgn(1); pe(1, "S")
-            consts_late()
-            gf(0); pe(0, "E")
-            gf(1); pe(1, "E", True)
-        gf(2); pe(2, "E")
-        gv(3)
-        mn(2); pe(2, "K")
-        relu(0); pen(0)
-        sgn(2); pe(2, "S")
-        mn(3); pe(3, "K")
-        sgn(3); pe(3, "S")
-        act(whole("ka"), S("pK0", 0, 128))
-        gf(3); pe(3, "E", True)
-        relu(1); pen(1)
-        ts(whole("tb"), S("pA", 0, 16), 256.0 if not last else -1.0, A.is_equal)
-        ts(whole("ta"), S("pA", 0, 16), 256.0, A.is_ge)
-        tt(S("fl", 16, 32), whole("tb"), S("fl", 48, 64), A.mult)
-        tt(S("fl", 64, 80), whole("ta"), whole("zf_"), A.mult)
-        tt(S("fl", 0, 16), S("fl", 48, 64), S("fl", 16, 32), A.subtract)
-        ts(S("fl", 32, 48), S("fl", 16, 32), 256.0, A.mult)
-        if t > 0:
-            cp(IND(S("tG", 0, LC), S("o16", 8, 16)), S("lnd%d" % (t - 1), 513, 1024, 4))
-        else:
-            consts_lists()
-            consts_scalar()
-        if not last:
-            act(S("tG", NS, ZG), S("pC", 0, 2 * L))
-        if t == 0:
-            consts_scalar2()
-        tt(whole("p6"), IND(whole("fl"), S("patf", 0, 5)), whole("cp"), A.mult)
-        tt(whole("q6"), IND(whole("fl"), S("patf", 0, 5)), whole("cq"), A.mult)
-        tt(S("p6", 0, 32), S("p6", 0, 32), S("fl", 16, 48), A.add)
+            for h in range(2):
+                mms([(S("pC", 0, 384), S(lnd, 512 * h + j, 512 * h + 512, 4), S("esel", 2 - j, 386 - j), j == 0, j == 2)
+                     for j in range(3)])
+                act(S("vT", 384 * h, 384 * h + 384), S("pC", 0, 384))
+            for j, tab in enumerate(("tV", "tF", "tG")):
+                for k in range(0, 32, 4):
+                    mms([(S("pB", 128 * j, 128 * j + 128), whole("ib"), S(tab, 128 * e, 128 * e + 128),
+                          j == 0 and e == 0, j == 2 and e == 31) for e in range(k, k + 4)])
+            act(whole("zb0"), S("pB", 0, 384))
+        def lists(parts, stop=False):
+            mms([(S("pA", 16 * b, 16 * b + 16), whole(w), whole(x), False, stop and i == len(parts) - 1)
+                 for i, (b, w, x) in enumerate(parts)])
 
-        tt(whole("k1"), S("pK1", 0, 128), whole("ka"), A.max)
-        tt(whole("k2"), S("k1", 0, 64), S("k1", 64, 128), A.max)
+        n = 80 if last else 96
+        tt(whole("fin"), whole("ta"), whole("zf_"), A.mult)
+        cp(whole("u3"), IND(whole("u"), S("rep", 0, 3)))
+        consts("pA", [(0, "ih", S("eH", 0, n)), (0, "ib", S("eB", 0, n)), (0, "ib", S("eC", 0, n)), (0, "ih", S("ch", 0, 48))])
+        lists([(0, "iO", "zf_"), (3, "iO", "zf_"), (4, "iO", "zf_"), (2, "iOn", "fin")])
+        if not last:
+            tt(whole("nf"), whole("tb"), whole("zf_"), A.is_gt)
+            lists([(0, "iO", "nf"), (1, "iOn", "nf"), (3, "i256", "nf"), (5, "iO", "nf")])
+        else:
+            lists([(5, "iZG", "zf_"), (6, "iZV", "zf_")])
+
+        cp(whole("ka"), S("pK0", 0, 64))
+        tt(whole("kb"), S("pK0", 64, 128), whole("ka"), A.max)
+        tt(whole("kc"), S("pK0", 128, 192), whole("kb"), A.max)
+        tt(whole("kt"), S("pK1", 0, 64), whole("ks"), A.min)
+        tt(whole("k1"), S("pE1", 0, 64), whole("kt"), A.min)
+        tt(whole("k2"), whole("k1"), whole("kc"), A.max)
         tt(whole("k3"), S("k2", 0, 32), S("k2", 32, 64), A.max)
         tt(whole("ki"), S("k3", 0, 16), S("k3", 16, 32), A.max)
-        ts(S("val", 16, 32), whole("ki"), 15, A.bitwise_and)
-        ts(whole("vld"), whole("ki"), -16777216.0, A.is_ge)
-        tt(whole("oh"), IND(S("val", 16, 32), whole("rep")), whole("crm"), A.is_equal)
-        for m in range(16):
-            mm(S("pA", 0, 16), S("dk", 128 * m, 128 * m + 128), S("oh", 16 * m, 16 * m + 16), m == 0, m == 15)
-        tt(whole("vp2"), IND(whole("vld"), S("rep", 0, 5)), whole("p6"), A.mult)
-        tt(whole("vq"), IND(whole("vld"), S("rep", 0, 5)), whole("q6"), A.mult)
+        ts(whole("val"), whole("ki"), 15, A.bitwise_and)
+        ts(whole("nv"), whole("ki"), -BIG / 2, A.is_lt)
+        tt(whole("step"), IND(whole("val"), whole("repc")), whole("jr"), A.is_lt)
+        scan(whole("ksel"), whole("step"), whole("ktab"), A.mult, A.max)
+        cp(whole("valb"), whole("val"))
+        lists([(b, "iO", "nv") for b in range(5)] + ([] if last else [(5, "iOn", "nv")]) + [(4, "i256n", "valb")], True)
+        tt(S("own", 0, 16), S("pA", 80, 96), S("c0", 0, 16), A.max)
         if last:
-            for b, z in ((0, ZG), (48, ZV)):
-                ts(S("c0", b, b + 16), S("c0", b, b + 16), float(-z), A.add)
-            for b, z in ((0, ZG), (48, ZV)):
-                tt(S("c0", b, b + 16), S("c0", b, b + 16), S("fl", 48, 64), A.mult)
-            for b, z in ((0, ZG), (48, ZV)):
-                ts(S("c0", b, b + 16), S("c0", b, b + 16), float(z), A.add)
-        tt(whole("vp"), whole("vp2"), whole("c0"), A.add)
-        tt(whole("ha"), S("pA", 0, 16), whole("u"), A.mult)
-        tt(whole("hb"), whole("ha"), whole("cc"), A.add)
-        ts(S("val", 0, 16), whole("hb"), 4095, A.bitwise_and)
+            tt(S("own", 64, 80), S("pA", 96, 112), S("c0", 64, 80), A.max)
+        cp(S("hb", 48, 80), S("pA", 48, 80))
+        tt(whole("ha"), IND(whole("ksel"), S("l15", 0, 3)), whole("u3"), A.mult)
+        tt(S("hb", 0, 48), S("pA", 0, 48), whole("ha"), A.add)
+        ts(whole("hm"), whole("hb"), 4095 + 3 * OFF, A.bitwise_and)
+        tt(whole("s6"), whole("hm"), whole("own"), A.min)
+        cp(whole("s16"), whole("s6"))
         if not last:
-            tt(whole("ta"), S("val", 0, 16), S("vq", 0, 16), A.mult)
-            tt(whole("tb"), whole("ta"), S("vp", 0, 16), A.add)
-            cp(whole("x16"), whole("tb"))
-            act(S("pre", 0, 1024, 4), IND(whole("tG"), whole("x16")))
-            conv(S("pB", 0, 16), "zB", "pre", 0, 16, 4)
-        tt(whole("t6"), IND(whole("val"), S("patv", 0, 5)), whole("vq"), A.mult)
-        tt(whole("s6"), whole("t6"), whole("vp"), A.add)
+            act(S("pre", 0, 1024, 4), IND(whole("tG"), S("s16", 0, 16)))
+            mm(S("pB", 0, 16), whole("iO"), whole("zf_"), True, False)
+            conv(S("pB", 0, 16), "zB", "pre", 0, 16, 4, False, True)
 
-        def claims_a():
-            cp(whole("plr"), IND(whole("jw"), S("s16", 64, 80)))
-
-        def claims_b():
-            ts(whole("plh"), S("s6", 64, 80), -2048.0, A.add)
-
-        summed = []
-
-        def eq(*cs):
-            for c in cs:
-                ts(S("eqd", L * c + 16 * c, L * c + L), S("plr", 16 * c, L), 2048.0, A.add, S("s6", 64 + c, 65 + c), A.is_equal)
-
-        def eqm(*cs):
-            for c in cs:
-                summed.append(c)
-                mm(S("pE1", 16 * c, L), whole("ones"), S("eqd", L * c + 16 * c, L * c + L), c == 0, False)
-                mm(S("pE1", 16 * c, 16 * c + 16), whole("uge"), S("eqd", L * c + 16 * c, L * c + 16 * c + 16), False,
-                   len(summed) == 16)
-
-        def claims_c(c0, c1):
-            for c in range(c0, c1):
-                eq(c)
-                eqm(c)
-
-        def claims_d():
+        def claims():
+            cp(whole("plr"), IND(whole("jw"), S("s16", 32, 48)))
+            for c in range(16):
+                ts(S("eqd", L * c + 16 * c, L * c + L), S("plr", 16 * c, L), 2048.0, A.add, S("s6", 32 + c, 33 + c), A.is_equal)
+                mms([(S("pE1", 16 * c, L), whole("ones"), S("eqd", L * c + 16 * c, L * c + L), c == 0, False),
+                     (S("pE1", 16 * c, 16 * c + 16), whole("uge"), S("eqd", L * c + 16 * c, L * c + 16 * c + 16), False, c == 15)])
             tt(whole("dmk"), S("pE1", 0, L), whole("dm"), A.mult)
-            mm(S("pC", 0, 16), whole("ih"), whole("plh"), True, False)
-            conv(S("pC", 0, 16), "z65", "dmk", 0, 16, 1, False, True)
-
-        def claims_e():
-            tt(whole("ot"), S("pC", 0, 16), whole("cd"), A.min)
-            ts(whole("o16"), whole("ot"), 2048.0, A.add)
 
         if not last:
-            cp(whole("s16"), whole("s6"))
-            claims_a()
-            act(S("pre", 1, 1024, 4), IND(whole("tG"), S("s16", 32, 48)))
-            act(S("pre", 2, 1024, 4), IND(whole("lo"), S("s16", 48, 64)))
-            act(S("pre", 3, 1024, 4), IND(whole("tG"), S("s16", 16, 32)))
-            if t == 0:
-                consts_scalar3()
-            tt(whole("gi"), S("pB", 0, 16), whole("nw"), A.add)
-            eq(0)
-            ts(whole("g3"), whole("gi"), 1048576 + 3, A.bitwise_and)
-            eq(15)
+            act(S("pre", 1, 1024, 4), IND(whole("tG"), S("s16", 16, 32)))
+            act(S("pre", 2, 1024, 4), IND(whole("lo"), S("s16", 64, 80)))
+            act(S("pre", 3, 1024, 4), IND(whole("nmw"), S("s16", 48, 64)))
+            cp(whole("gi"), S("pB", 0, 16))
+            ts(whole("g3"), whole("gi"), OFF + 3, A.bitwise_and)
             tt(whole("go4"), IND(whole("g3"), S("rep", 0, 4)), S("jq", 0, 64), A.is_equal)
-            eq(14)
-            eqm(0, 15)
-            rec("v", lambda: g.vector.tensor_tensor_scan(ap(whole("inc")), ap(whole("msk")), ap(whole("go4")), 0.0, A.mult, A.add),
-                [whole("inc")], [whole("msk"), whole("go4")])
-            mm(S("pC", 0, 64), whole("ih"), whole("cst"), True, False)
-            mm(S("pC", 0, 64), whole("uge"), whole("go4"), False, False)
+            scan(whole("inc"), whole("msk"), whole("go4"), A.mult, A.add)
+            mms([(S("pC", 0, 64), whole("ih"), whole("cst"), True, False), (S("pC", 0, 64), whole("uge"), whole("go4"), False, False)])
             mm(S("pC", 0, 64), whole("ones"), whole("inc"), False, True)
-            eq(1, 13)
-            eqm(14)
             tt(whole("tt4"), S("pC", 0, 64), whole("go4"), A.mult)
-            mm(S("pA", 0, 16), whole("ih"), whole("dmp"), True, False)
-            for d in range(4):
-                mm(S("pA", 0, 16), whole("ih"), S("tt4", 16 * d, 16 * d + 16), False, d == 3)
-            eq(2, 3)
-            cp(whole("pos"), S("pA", 0, 16))
-            eq(12)
-            eqm(1, 13, 2, 3, 12)
+            mm(S("pK1", 0, 16), whole("ih"), whole("dmp"), True, False)
+            mms([(S("pK1", 0, 16), whole("ih"), S("tt4", 16 * d, 16 * d + 16), False, d == 3) for d in range(4)])
+            cp(whole("pos"), S("pK1", 0, 16))
             cp(IND(whole("idt"), whole("pos")), whole("jb"))
-            for k in range(1, N + 1):
-                d = (rank + k) % N
-                for e in range(4):
-                    mm(S("pB" if k == 1 else "pK0", 16 * (k - 1), 16 * k), S("z4", 12 - 4 * e, 140 - 4 * e),
-                       S("idt", L * d + e, L * d + 64, 4), e == 0, e == 3)
-            claims_c(4, 6)
-            ts(S("src", 0, 16), S("pB", 0, 16), C(cJ), A.add)
-            claims_c(6, 10)
-            ts(S("src", 16, 64), S("pK0", 16, 64), C(cJ), A.add)
+            for bank, ks in (("pB", (1,)), ("pK0", (2, 3, 4))):
+                mms([(S(bank, 16 * k - 16, 16 * k), S("z4", 12 - 4 * e, 140 - 4 * e),
+                      S("idt", L * ((rank + k) % N) + e, L * ((rank + k) % N) + 64, 4), e == 0, e == 3) for k in ks for e in range(4)])
+                ts(S("src", 16 * ks[0] - 16, 16 * ks[-1]), S(bank, 16 * ks[0] - 16, 16 * ks[-1]), C(cJ), A.add)
             nxt, snd = "lnd%d" % (t + 1), "snd%d" % t
-            for k in range(1, N + 1):
-                d = (rank + k) % N
-                o = S(nxt, L * rank, L * rank + L) if k == N else S(snd, L * (k - 1), L * k)
-                act(o, IND(whole("pre"), S("src", 16 * (k - 1), 16 * k)))
-                if k < N:
-                    dst = T.cores[d]
-                    rid, pid = topo.addr(dst)[0], topo.addr(dst)[1]
-                    msk, ne = topo.mask(core, dst), len(topo.engines(core, dst))
-                    sem = "out%d" % (3 * t + k - 1)
-                    rec("g", lambda o=o, nxt=nxt, sem=sem, t=t, pid=pid, rid=rid, msk=msk: g.remote_dma(
-                        ap(S(nxt, L * rank, L * rank + L)), ap(o), T.sem["arr%d" % t], T.sem[sem], pid, rid, msk),
-                        [], [o], kind="rem", sem=sem, n=ne)
+            here = S(nxt, L * rank, L * rank + L)
+            sent = []
+            for k in range(1, N):
+                o = S(snd, L * (k - 1), L * k)
+                act(o, IND(whole("pre"), S("src", 16 * k - 16, 16 * k)))
+                dst = T.cores[(rank + k) % N]
+                sem = "out%d" % (3 * t + k - 1)
+                sent.append(rec("g", lambda o=o, here=here, sem=sem, t=t, dst=dst: g.remote_dma(
+                    ap(here), ap(o), T.sem["arr%d" % t], T.sem[sem], topo.addr(dst)[1], topo.addr(dst)[0], topo.mask(core, dst)),
+                    [], [o], RISS, kind="rem", lat=RLAT + (3.0 if t == 0 and k == 1 else 0.0), sem=sem,
+                    n=len(topo.engines(core, dst)), after=sent[-1:]))
+            act(here, IND(whole("pre"), S("src", 48, 64)))
             n_in = sum(len(topo.engines(T.cores[q], core)) for q in range(N) if q != rank)
-            rec("g", None, [S(nxt, L * q, L * q + L) for q in range(N) if q != rank], [], kind="land", sem="arr%d" % t, n=n_in)
-            claims_c(10, 12)
-            claims_b()
-            claims_d()
+            rec("x", None, [S(nxt, L * q, L * q + L) for q in range(N) if q != rank], [], 0.0, kind="land", sem="arr%d" % t,
+                n=n_in, after=sent)
             if t < RO - 2:
                 for d in range(4):
-                    fill("idt", L * d, L * d + 64, 256.0)
-            claims_e()
-            scatter("tV", lnd, 2)
-            scatter("tF", lnd, 0)
-            cp(IND(S("tG", 0, LC), S("o16", 0, 8)), S(lnd, 1, 512, 4))
+                    fill("idt", L * d, L * d + 64, 256)
+                    ops[-1]["after"] = sent[-1:]
+            claims()
+            ts(whole("plh"), S("s6", 32, 48), -2048.0, A.add)
+            mm(S("pC", 0, 16), whole("ih"), whole("plh"), True, False)
+            conv(S("pC", 0, 16), "z65", "dmk", 0, 16, 1, False, True)
+            tt(whole("ot"), S("pC", 0, 16), whole("cd"), A.min)
+            ts(whole("o16"), whole("ot"), 2048.0, A.add)
+            for tab, j, n in (("tV", 2, 16), ("tF", 0, 16), ("tG", 1, 4)):
+                for b in range(0, 16, n):
+                    cp(IND(S(tab, 0, LC), S("o16", b, b + n)), S(lnd, 64 * b + j, 64 * (b + n), 4))
         else:
-            cp(whole("s16"), whole("s6"))
-            claims_a()
             act(whole("yfb"), IND(whole("tG"), S("s16", 0, 16)))
-            act(whole("yvb"), IND(whole("lo"), S("s16", 48, 64)))
+            act(whole("yvb"), IND(whole("lo"), S("s16", 64, 80)))
             dma("s", T.yf[:], whole("yfb"))
             dma("s", T.yv[:], whole("yvb"))
-            claims_b()
-            claims_c(0, 16)
-            claims_d()
-            claims_e()
-            for i, (tab, j, bank, out) in enumerate((("tV", 2, "pE0", T.zv), ("tF", 0, "pE1", T.zf), ("tG", 1, "pK0", T.zg))):
-                scatter(tab, lnd, j)
-                if i < 2:
-                    for k in range(32):
-                        mm(S(bank, 0, 128), whole("ib"), S(tab, 128 * k, 128 * k + 128), k == 0, k == 31)
-                else:
-                    tt(whole("dk"), S(tab, 0, W // 2), S(tab, W // 2, W), A.add)
-                    for k in range(16):
-                        mm(S(bank, 0, 128), whole("ih"), S("dk", 128 * k, 128 * k + 128), k == 0, k == 15)
-                act(S("zb", 128 * i, 128 * i + 128), S(bank, 0, 128))
-                dma("s" if i < 2 else "a", out[:], S("zb", 128 * i, 128 * i + 128))
-    emit(g, T, ops)
+            act(whole("plm"), IND(whole("jm"), S("s16", 32, 48)))
+            claims()
+            mms([(S("pC", 8 * h, 8 * h + 8), S("plm", 128 * h, 128 * h + 128), whole("sel0"), h == 0, False) for h in range(2)])
+            mms([(S("pC", 8 * h, 8 * h + 8), S("dmk", 128 * h, 128 * h + 128), whole("blk"), False, h == 1) for h in range(2)])
+            for i in range(16):
+                ts(S("eqf", 128 * i, 128 * i + 128), S("jb", 0, 128), S("pC", i, i + 1), A.is_equal)
+                mm(S("pA", 48 * (i % 8), 48 * (i % 8) + 48), S("eqf", 128 * i, 128 * i + 128), S("vT", 48 * i, 48 * i + 48),
+                   i == 0, i == 15)
+            ends = (("pE0", T.zf, 1), ("pK0", T.zg, 2), ("pK1", T.zv, 0))
+            for j, (bank, out, b) in enumerate(ends):
+                z = S("zts", 128 * j, 128 * j + 128)
+                cp(z, S("pA", j, 384, 3))
+                rec("p", lambda z=z, bank=bank: g.tensor.transpose(ap(S(bank, 0, 128)), ap(z), ap(whole("i32"))),
+                    [S(bank, 0, 128)], [z, whole("i32")], 512 * PEC)
+            for j, (bank, out, b) in enumerate(ends):
+                tt(S("zb", 128 * j, 128 * j + 128), S(bank, 0, 128), S("zb0", 128 * b, 128 * b + 128), A.add)
+                dma("a" if j == 1 else "s", out[:], S("zb", 128 * j, 128 * j + 128))
+    emit(g, T, arrange(ops))

@@ -18,31 +18,34 @@ _SB = {
     "lnd0": (1024, B16), "lnd1": (1024, B16), "lnd2": (1024, B16), "lnd3": (1024, B16), "lnd4": (1024, B16),
     "snd0": (768, B16), "snd1": (768, B16), "snd2": (768, B16), "snd3": (768, B16),
     "pre": (1040, B16), "idt": (1280, B16), "yfb": (L, B16), "yvb": (L, B16), "zb": (384, F32), "zb0": (384, F32),
-    "zts": (384, F32), "vT": (768, B16), "plm": (L, B16),
+    "zts": (384, F32), "vT": (768, B16), "vt": (L, B16), "plm": (L, B16),
     "wfs": (L, B16), "wvs": (L, B16), "nms": (L, I32), "nmb": (L, B16), "thf": (L, B16),
     "pcol": (16, I32), "col": (32, F32), "jf": (L, F32), "jr": (L, F32), "jq": (L, F32), "j4": (144, F32), "lo16": (16, F32),
     "jb": (L, B16), "ab": (16, F32), "ab2": (16, F32), "ib": (128, B16), "ih": (128, F16), "i3": (128, B16), "i18": (128, B16),
     "ineg": (128, B16), "ones": (128, B16), "uge": (128, B16), "uget": (128, B16), "wn": (128, B16), "shf": (128, B16),
-    "zA": (144, B16), "zB": (144, B16), "z0": (144, B16), "z15": (144, B16), "zt": (144, B16), "zn": (144, B16),
-    "z65": (144, B16), "z16": (144, B16), "z4": (144, B16), "dk": (1536, F16), "dm": (L, B16), "hc": (192, B16),
-    "zE": (144, B16), "zS": (144, B16), "iE": (128, B16), "iS": (128, B16), "cE": (128, B16), "ktab": (L, F16), "k32": (64, F32),
+    "zA": (144, B16), "zB": (144, B16), "z0": (144, B16), "zr15": (144, B16), "zX": (144, B16), "zn": (144, B16), "zn2": (144, B16),
+    "zY": (144, B16), "zr13": (144, B16), "wsh": (L, B16), "e16": (16, F32), "nm0": (L, B16),
+    "oH": (80, F16), "oB": (80, B16), "swp": (16, B16), "z65": (144, B16), "z16": (144, B16), "z4": (144, B16), "dk": (1536, F16), "dm": (L, B16), "hc": (192, B16),
+    "zE": (144, B16), "zS": (144, B16), "iE": (128, B16), "iS": (128, B16), "cE": (128, B16), "ktab": (L, F32), "k32": (64, F32),
+    "mk": (L, F32), "lhk": (16, U16), "i4k": (128, B16), "ibn": (128, B16),
     "c13": (384, B16), "c1": (192, B16), "c2": (L, B16), "msk": (64, B16), "cst": (64, F16), "dmp": (16, F16),
-    "cd": (16, F32), "c0": (80, F32), "own": (80, F32), "rep": (16, U16), "repc": (16, U16), "l15": (4, U16),
+    "cd": (16, F32), "c0": (32, F32), "own": (80, F32), "rep": (16, U16), "repc": (16, U16), "l15": (6, U16),
     "iO": (128, B16), "iOn": (128, B16), "i256": (128, B16), "i256n": (128, B16), "iZG": (128, B16), "iZV": (128, B16),
     "eH": (96, F16), "eB": (96, B16), "eC": (96, B16), "nmw": (6 * L, B16),
-    "jw": (JW, F32), "jm": (JW, B16), "plh": (16, F16), "i32": (128, F32), "esel": (400, B16),
+    "jw": (JW, F32), "jm": (JW, B16), "plh": (16, F16), "pq": (16, F32), "pb": (48, B16), "i32": (128, F32),
     "sel0": (8, B16), "blk": (8, B16),
-    "z1": (144, B16), "zw": (144, B16), "z21": (144, B16), "l16": (16, F32),
-    "ui": (16, I32), "u": (16, I32), "zf_": (16, B16), "prod": (16, I32), "uk": (64, F32), "u3": (48, F32),
+    "z1": (144, B16), "zw": (144, B16), "zr1": (144, B16), "l16": (16, F32),
+    "ui": (16, I32), "u": (16, I32), "zf_": (16, B16), "zf4": (64, B16), "hr": (192, I32), "prod": (16, I32), "uk": (64, F32), "hs": (64, I32),
     "cc": (16, I32), "uh": (16, F16), "ch": (64, F16), "hi": (L, I32), "h16": (L, U16), "cmp": (2 * L, B16),
-    "ta": (16, F32), "tb": (16, F32), "fin": (16, B16), "nf": (16, B16), "nv": (16, B16), "valb": (16, B16),
+    "fin": (16, B16), "nf": (16, B16), "nv": (16, B16), "valb": (16, B16),
     "pen": (384, B16), "ka": (64, F32), "kb": (64, F32), "kc": (64, F32), "ks": (64, F32), "kt": (64, F32),
-    "k1": (64, F32), "k2": (64, F32), "k3": (32, F32), "step": (L, B16), "ksel": (L, F32),
-    "ki": (16, I32), "val": (16, I32), "ha": (48, F32), "hb": (80, I32), "hm": (80, I32), "s6": (80, F32), "s16": (80, U16),
+    "k1": (64, F32), "k2": (64, F32), "k3": (32, F32), "step": (L, B16), "ksel": (L + 16, F32),
+    "ki": (16, I32), "val": (16, I32), "hb": (80, F32), "hm": (80, F32), "s6": (80, F32), "s16": (80, U16),
     "gi": (16, I32), "g3": (16, I32), "go4": (64, B16), "inc": (64, B16), "tt4": (64, F16), "pos": (16, U16), "src": (64, U16),
     "plr": (L, F16), "dmk": (L, B16), "ot": (16, F32), "o16": (16, U16),
 }
-_PS = ["pV", "pE0", "pE1", "pK0", "pK1", "pA", "pB", "pC"]
+_PS = ["pV", "pT", "pE0", "pK0", "pK1", "pA", "pB", "pC"]
+WIDE, SP = 1024, 8
 SCRATCH = {}
 _AT = {}
 for _k in _SB:
@@ -54,14 +57,23 @@ for _k in _SB:
     else:
         SCRATCH[_k] = ("sbuf", [128, _SB[_k][0]], _SB[_k][1])
 for _k in _PS:
-    SCRATCH[_k] = ("psum", [128, 512], F32)
+    SCRATCH[_k] = ("psum", [128, 1024], B16) if _k in ("pV", "pT") else ("psum", [128, 512], F32)
 NDMA = 26
 SEMAPHORES = ["cv", "ca", "cp_", "cg"] + ["d%d" % i for i in range(NDMA)] + ["arr%d" % i for i in range(4)] + \
              ["out%d" % i for i in range(12)]
-HOP = 0.1
-SLACK, MARGIN = 0.3, 0.2
-PEC, VFIX, AFIX, RISS, RLAT, LOAD = 0.00042, 0.053, 0.065, 0.55, 1.6, 3.5
-SELF, PEHOP, VADD, GAT, SCA = 0.15, 0.1, 0.03, 1.56, 3.8
+HOP = 0.06
+SLACK, MARGIN, GP, EARLY, MAGIC = 0.3, 0.0, 8, 1, 0
+PEC, VFIX, AFIX, RISS, RLAT, LOAD = 0.00052, 0.053, 0.13, 0.55, 1.3, 3.0
+SELF, PEHOP, VADD, GAT, SCA, F2 = 0.09, 0.07, 0.065, 1.52, 2.2, 1.0
+FROM, TO = {"a": 0.1}, {"a": 0.03, "v": 0.04}
+XV, SV, CV, KV, OV, GC, GF = 0, 0, 0, 0, 0, 2, 1
+BS, EQX, MNX, S3V = 1, 1, 0.6, 1
+ONS, VT = ("i3", "z16", "ibn", "z65"), 0
+SVK = ((), (1,), (1, 3), (1, 2, 3))
+ORDER = ("r0 p0 r1 p1 rest kind m0 kinds b0 a1 m1 b1 a2 m2 b2 s2 m3 a3 b3 tab", "g0 g1 g2 s0 g3 s1 s3 relu ks ka shift",
+         "open K0 E0 names flags K1 S0 E1 K2 E2 S2 K3 S1 S3 pen E3")
+ORDER0 = ("r0 r1 rest m0 kind a0 kinds m1 b0 a1 m2 b1 s2 m3 a2 b2 a3 b3 tab", "g0 g1 g2 s0 g3 s1 s3 relu ks ka shift",
+          "open K0 names flags K1 E0 S0 K2 E1 S2 K3 S1 E2 S3 pen E3")
 CYC = 0.00083
 
 
@@ -117,6 +129,8 @@ def arrange(ops):
     for i in range(n):
         for j in pred[i]:
             pred[i][j] += ops[j]["lat"]
+            if ops[j]["q"] != ops[i]["q"]:
+                pred[i][j] += FROM.get(ops[j]["q"], 0.0) + TO.get(ops[i]["q"], 0.0)
             succ[j][i] = pred[i][j]
     chain = [0.0] * n
     for i in range(n - 1, -1, -1):
@@ -253,9 +267,9 @@ def rank_program(g, core, T, topo):
         if a[0] == "ind":
             return 0.05 + GAT * CYC * width(o)
         if b is not None:
-            return max(VFIX, VADD + CYC * width(o) * (1 if a[1] in _PS or b[1] in _PS else 2))
+            return F2 * max(VFIX, VADD + CYC * width(o) * (1 if a[1] in _PS or b[1] in _PS else 2))
         two = all(SCRATCH[x[1]][2] in (B16, F16, U16) for x in (o, a))
-        return max(VFIX, VADD + CYC * width(o) * (0.5 if two else 1))
+        return F2 * max(VFIX, VADD + CYC * width(o) * (0.5 if two else 1))
 
     def tt(o, a, b, op):
         rec("v", lambda: g.vector.tensor_tensor(ap(o), ap(a), ap(b), op), [o], [a, b], vc(o, a, b))
@@ -282,7 +296,7 @@ def rank_program(g, core, T, topo):
             kw["bias"] = sc(bias)
         if scale is not None:
             kw["scale"] = sc(scale)
-        c = 0.065 + GAT * CYC * width(o) if a[0] == "ind" else AFIX + CYC * width(o)
+        c = 0.065 + GAT * CYC * width(o) if a[0] == "ind" else F2 * (AFIX + CYC * width(o))
         rec("a", lambda: g.scalar.activation(ap(o), ap(a), fn, **kw), [o], [a, bias, scale], c)
 
     def mms(calls):
@@ -290,24 +304,34 @@ def rank_program(g, core, T, topo):
             [e[0] for e in calls], [e[1] for e in calls] + [e[2] for e in calls],
             sum(PEC * max(min(64, width(e[1])), width(e[2])) for e in calls))
 
+    def turn(pairs, ident):
+        rec("p", [lambda e=e: g.tensor.transpose(ap(e[0]), ap(e[1]), ap(whole(ident))) for e in pairs], [e[0] for e in pairs],
+            [e[1] for e in pairs] + [whole(ident)], len(pairs) * 128 * PEC * (4 if ident == "i32" else 1))
+
     def mm(o, wt, mv, start, stop):
         mms([(o, wt, mv, start, stop)])
 
     def iota(o, pat, base, cm):
-        c = 0.13 + 2 * CYC * width(o)
+        c = F2 * (0.13 + 2 * CYC * width(o))
         if SCRATCH[o[1]][2] == I32:
             rec("g", lambda: g.iota(ap(o), pat, base, cm), [o], [], c)
         else:
             rec("g", lambda: g.iota(ap(o), pat, base, cm, allow_small_or_imprecise_dtypes=True), [o], [], c)
 
-    def fill(name, lo, hi, c):
-        iota(S(name, lo, hi), [[0, hi - lo]], c, 0)
+    def fill(name, lo, hi, c, step=1):
+        if GF:
+            iota(S(name, lo, hi, step), [[0, width(S(name, lo, hi, step))]], c, 0)
+        else:
+            ms(S(name, lo, hi, step), float(c))
 
-    def dma(q, o, a, lat=2.5):
+    def gcopy(o, a):
+        rec("g", lambda: g.affine_select(ap(o), ap(a), [[0, width(o)]], A.is_ge, 0.0, 0, 0), [o], [a], 0.17 + 2 * CYC * width(o))
+
+    def dma(q, o, a, lat=2.5, behind=None):
         s = "d%d" % nd[0]
         nd[0] += 1
         e = g.sync if q == "s" else g.scalar
-        rec(q, lambda: e.dma_start(sc(o), sc(a)), [o] if isinstance(o, tuple) else [], [a], 0.05, kind="dma", lat=lat, sem=s)
+        rec(q, lambda: e.dma_start(sc(o), sc(a)), [o] if isinstance(o, tuple) else [], [a, behind], 0.05, kind="dma", lat=lat, sem=s)
 
     def conv(o, z, buf, base, n, stride, first=True, last=True):
         mms([(o, S(z, 15 - r, 143 - r), S(buf, base + stride * r, base + stride * (r + 16 * n - 16) + 1, stride * 16),
@@ -321,7 +345,7 @@ def rank_program(g, core, T, topo):
 
     keep[0] = True
     for o, a, lat in ((whole("wfs"), T.wf, 2.2), (whole("nms"), T.nm, 2.8), (whole("wvs"), T.wv, 3.1),
-                      (S("tV", 0, W), T.rv, 3 + LOAD), (S("tF", 0, W), T.rf, 3 + 2 * LOAD), (S("tG", 0, W), T.rg, 3 + 3 * LOAD)):
+                      (S("tV", 0, W), T.rv, 3 + LOAD)):
         dma("s", o, a[:], lat)
     keep[0] = False
 
@@ -331,101 +355,117 @@ def rank_program(g, core, T, topo):
     iota(whole("jq"), [[1, 16], [0, 16]], 0, 0)
     iota(whole("l16"), [[16, 16]], 0, 1)
     iota(whole("j4"), [[1, 36], [0, 4]], 0, 0)
-    iota(whole("jb"), [[1, L]], 0, 0)
+    act(whole("jb"), whole("jf"))
     for b in range(0, JW, 1028):
         iota(S("jw", b, b + 1028), [[1, 1028]], b - 2048, 0)
-    for b in range(0, W, 1024):
-        iota(S("jm", b, b + 1024), [[0, 8], [1, 128]], 0, 0)
-    fill("jm", W, JW, 200)
     for i in range(16):
         ms(S("ab", i, i + 1), float(WA[i] + 256 * WB[i]))
-        ms(S("ktab", i, L, 16), float(KP[15 - i]))
-    (cP, cR, cG, cJ, cA, cB, c20, cE15, cT, c256, cSH, cKEEP, cFLAG, c4G, c40, cZ, cX, cY, cG16, cW, c21, cU, cAB,
-     cX2, cAB2, cES, cR0, cL15) = range(28)
+    (cP, cR, cG, cJ, cA, cB, cT, cF, cSH, cKEEP, c4G, c40, cZ, cX, cY, cG16, cW, cAB, cX2, cAB2, cES, cL15) = range(22)
     ts(S("pcol", 1, 2), S("pcol", 0, 1), 15, A.bitwise_and)
     ts(S("pcol", 2, 3), S("pcol", 0, 1), 4, A.arith_shift_right)
     ts(S("pcol", 3, 4), S("pcol", 0, 1), 3, A.bitwise_and)
     cp(S("col", 0, 4), S("pcol", 0, 4))
     for m in range(4):
-        ms(S("k32", 16 * m, 16 * m + 16), 32.0 * KP[m])
+        fill("k32", 16 * m, 16 * m + 16, 32 * KP[m])
     ms(whole("hc"), 0.0)
     for m in range(4, 16):
         if KP[m] % 2 == 0:
-            ms(S("hc", 16 * m - 64, 16 * m - 48), 2048.0)
+            fill("hc", 16 * m - 64, 16 * m - 48, 2048)
     ts(C(cZ), C(cG), 16.0, A.mult, 15.0, A.add)
     ts(whole("ib"), S("jf", 0, 128), C(cP), A.is_equal)
-    ts(C(c20), C(cR), 0.0, A.is_equal, 2.0, A.mult)
+    ts(whole("e16"), S("jf", 0, 16), C(cR), A.is_equal)
+
+    def R(i):
+        return S("e16", i, i + 1)
+
     ts(whole("z1"), S("jf", 0, 144), C(cZ), A.is_equal)
-    ts(C(cKEEP), C(cR), 12.0, A.is_le)
-    ts(C(cFLAG), C(cR), 13.0, A.is_equal)
+    ts(C(cKEEP), C(cR), 11.0, A.is_le)
     ts(whole("dm"), whole("jr"), C(cR), A.is_equal)
     ts(whole("ones"), S("jq", 0, 128), C(cG), A.is_equal)
-    ts(whole("nmb"), whole("nms"), C(cKEEP), A.mult, C(cFLAG), A.add)
-    tt(whole("ab2"), whole("ab"), S("dm", 0, 16), A.mult)
-    ts(C(cU), C(cR), 14.0, A.is_equal)
-    ts(C(c256), C(cR), 0.0, A.is_equal, 256.0, A.mult)
-    rec("v", lambda: g.vector.tensor_reduce(ap(C(cAB)), ap(whole("ab2")), AxisListType.X, A.add), [C(cAB)], [whole("ab2")], 0.06)
-    tt(C(cW), C(cU), C(cFLAG), A.add)
+    ts(whole("nmb"), whole("nms"), C(cKEEP), A.mult, R(13), A.add)
+    dma("s", S("tF", 0, W), T.rf[:], 2 + LOAD, S("nmb", 0, 1))
+    dma("s", S("tG", 0, W), T.rg[:], 3 + LOAD, S("tF", 0, 1))
+    act(whole("nm0"), whole("nmb"), F.Relu, 0.5, -1.0)
+    tt(whole("ab2"), whole("ab"), whole("e16"), A.mult)
+    rec("v", lambda: g.vector.tensor_reduce(ap(C(cAB)), ap(whole("ab2")), AxisListType.X, A.add), [C(cAB)], [whole("ab2")], 0.07)
+    tt(C(cW), R(13), R(14), A.add)
     ts(whole("rep"), S("jf", 0, 16), 0.0, A.mult, C(cR), A.add)
     cp(whole("repc"), S("jf", 0, 16))
-    ts(whole("z0"), whole("z1"), C(c20), A.mult)
+    ts(whole("z0"), whole("z1"), R(0), A.mult, 2.0, A.mult)
     mm(S("pB", 0, L), whole("ones"), whole("wfs"), True, True)
     mms([(S("pC", 0, L), whole("ib"), whole("nmb"), True, False),
          (S("pC", 0, L), S("z0", 0, 128), whole("nmb"), False, False),
-         (S("pC", 0, L), S("z0", 1, 129), whole("nmb"), False, True)])
+         (S("pC", 0, L), S("z0", 1, 129), whole("nmb"), False, False),
+         (S("pC", 0, L), S("z0", 3, 131), whole("nm0"), False, True)])
     cp(S("pcol", 4, 5), C(cAB))
-    ts(whole("thf"), S("pB", 0, L), 0.0, A.is_gt)
+    act(whole("thf"), S("pB", 0, L), F.Sign)
     ts(S("pcol", 5, 6), S("pcol", 4, 5), 255, A.bitwise_and)
     ts(S("pcol", 6, 7), S("pcol", 4, 5), 8, A.arith_shift_right)
     tt(S("lnd0", 3, 1024, 4), S("pC", 0, L), whole("thf"), A.mult)
     for j, a in enumerate(("wfs", "wfs", "wvs")):
         act(S("lnd0", j, 1024, 4), whole(a))
     cp(S("col", cA, cA + 2), S("pcol", 5, 7))
-    ts(C(cX), C(cR), 13.0, A.is_equal, 256.0, A.mult)
-    ts(C(cY), C(cR), 1.0, A.is_equal)
     cp(whole("ih"), whole("ib"))
-    tt(C(cT), C(cX), C(cY), A.add)
     ts(whole("zw"), whole("z1"), C(cW), A.mult)
     ts(whole("zA"), whole("z1"), C(cA), A.mult)
-    act(whole("wn"), whole("ones"), scale=C(c256))
-    act(whole("zt"), whole("z1"), scale=C(cT))
+    ts(C(cF), R(12), -256.0, A.mult)
+    tt(C(cY), R(12), R(13), A.add)
+    ts(C(cX), R(13), -256.0, A.mult, R(1), A.add)
+    tt(C(cT), C(cX), C(cF), A.subtract)
+    act(whole("wn"), whole("ones"), scale=C(cF))
+    act(whole("zY"), whole("z1"), scale=C(cY))
+    act(whole("zX"), whole("z1"), scale=C(cT))
     fill("c13", 0, 192, 13)
-    fill("c13", 192, 384, 2)
+    fill("c13", 192, 320, 2)
+    fill("c13", 320, 384, 18)
     act(whole("c1"), S("jf", 0, 192), None, -BIG / 2, 0.0)
     act(S("cE", 0, 64), S("jf", 0, 64), None, -25 * BIG, 0.0)
     act(S("cE", 64, 128), S("jf", 0, 64), None, -BIG, 0.0)
-    iota(whole("c2"), [[-1, 16], [0, 16]], 15, 0)
+    act(whole("c2"), whole("jq"), None, 15.0, -1.0)
     for name, of, x in (("i3", "ib", 3.0), ("i18", "ib", -18.0), ("ineg", "ib", -BIG), ("iE", "ib", -6 * BIG), ("iS", "ib", 18 * BIG),
-                        ("zn", "z1", -1.0), ("z16", "z1", 16.0), ("zE", "z1", 2 * BIG), ("zS", "z1", BIG), ("z65", "z1", 8192.0),
+                        ("zn", "z1", -1.0), ("zn2", "z1", -2.0), ("z16", "z1", 16.0), ("zE", "z1", 2 * BIG), ("zS", "z1", BIG), ("z65", "z1", 8192.0),
                         ("i32", "ib", 1.0), ("iO", "ib", float(OFF)), ("iOn", "ib", float(-OFF)), ("i256", "ib", 256.0),
-                        ("i256n", "ib", -256.0), ("iZG", "ib", float(ZG)), ("iZV", "ib", float(ZV))):
-        act(whole(name), whole(of), scale=x)
+                        ("i256n", "ib", -256.0), ("i4k", "ib", 4096.0), ("ibn", "ib", -1.0), ("iZG", "ib", float(ZG)), ("iZV", "ib", float(ZV))):
+        if name in ("i32", "iZG", "iZV") + ONS:
+            act(whole(name), whole(of), scale=x)
+        else:
+            ts(whole(name), whole(of), x, A.mult)
     for m in range(4, 16):
         ts(S("dk", 128 * m - 512, 128 * m - 384), whole("ib"), float(KP[m]), A.mult)
-    ts(C(cE15), C(cR), 15.0, A.is_equal)
     ts(C(cL15), C(cR), 16.0, A.mult, 15.0, A.add)
-    ts(C(c21), C(cY), 2.0, A.mult)
-    ts(C(cX2), C(cU), 256.0, A.mult, C(c256), A.add)
+    tt(C(cX2), R(0), R(14), A.add)
     tt(C(cAB2), C(cP), C(cKEEP), A.subtract)
     ts(C(cG16), C(cG), 16.0, A.mult)
     ts(C(c4G), C(cG), 4.0, A.mult, 3.0, A.add)
-    ts(C(c40), C(c20), 2.0, A.mult)
-    tt(C(cSH), C(cAB2), C(cX2), A.subtract)
+    ts(C(c40), R(0), 4.0, A.mult)
+    ts(C(cSH), C(cX2), -256.0, A.mult, C(cAB2), A.add)
     ts(whole("lo16"), whole("l16"), C(cG16), A.subtract)
-    act(whole("z15"), whole("z1"), scale=C(cE15))
-    act(whole("z21"), whole("z1"), scale=C(c21))
     act(whole("zB"), whole("z1"), scale=C(cB))
     ts(whole("shf"), S("jf", 0, 128), C(cSH), A.is_equal)
+    for name, i in (("zr1", 1), ("zr15", 15), ("zr13", 13)):
+        act(whole(name), whole("z1"), scale=R(i))
+    mms([(S("pK0", b, b + 128), whole("ib"), x, b == 0 and i == 0, b == 128 and i == 2)
+         for b, xs in ((0, (whole("shf"), S("zr1", 1, 129), S("zr1", 1, 129))), (128, (whole("shf"), S("zr15", 1, 129), S("zr13", 3, 131))))
+         for i, x in enumerate(xs)])
+    act(whole("wsh"), S("pK0", 0, L))
     for b, (s0, b0) in enumerate(((4, LC), (4, LC + 1), (0, NC), (4, 2 * L + 3), (4, LV + 2))):
-        act(S("c0", 16 * b, 16 * b + 16), whole("lo16"), None, float(b0), float(s0))
-    act(whole("own"), whole("c0"))
+        act(S("own", 16 * b, 16 * b + 16), whole("lo16"), None, float(b0), float(s0))
+        ts(S("oH", 16 * b, 16 * b + 16), whole("lo16"), float(s0), A.mult, float(b0 % 256), A.add)
+        fill("oB", 16 * b, 16 * b + 16, b0 - b0 % 256)
+    act(S("c0", 0, 16), S("own", 0, 16))
+    act(S("c0", 16, 32), S("own", 64, 80))
     ms(S("eH", 0, 48), 0.0)
-    for b, s0, b0 in ((3, 1, 0), (4, 1, 0), (5, 4, 1)):
-        ts(S("eH", 16 * b, 16 * b + 16), whole("lo16"), float(s0), A.mult, float(b0), A.add)
-    for name, lo, hi, x in (("eB", 0, 48, 2048), ("eB", 48, 64, 0), ("eB", 64, 80, 3840), ("eB", 80, 96, LC),
+    ms(S("eH", 80, 96), 1.0)
+    for b in (3, 4):
+        cp(S("eH", 16 * b, 16 * b + 16), whole("lo16"))
+    for name, lo, hi, x in (("eB", 0, 48, -61440), ("eB", 48, 64, 0), ("eB", 64, 80, 3840), ("eB", 80, 96, 0),
                             ("eC", 0, 16, 0), ("eC", 16, 48, OFF), ("eC", 48, 80, 0), ("eC", 80, 96, -OFF)):
         fill(name, lo, hi, x)
-    ts(whole("l15"), S("jf", 0, 4), 0.0, A.mult, C(cL15), A.add)
+    ts(S("l15", 0, 3), S("jf", 0, 3), 0.0, A.mult, C(cL15), A.add)
+    ms(S("l15", 3, 6), 256)
+    ts(whole("lhk"), S("jf", 0, 16), C(cL15), A.subtract, 255.0, A.add)
+    act(whole("mk"), whole("jr"), None, 61440.0, -4096.0)
+    fill("ksel", L, L + 16, 0)
     ts(whole("z4"), whole("j4"), C(c4G), A.is_equal, C(c40), A.mult)
     ts(whole("uget"), S("jr", 0, 128), C(cR), A.is_le, -1.0, A.mult)
     ts(whole("msk"), S("jr", 0, 64), 0.0, A.is_gt)
@@ -433,51 +473,76 @@ def rank_program(g, core, T, topo):
     for d in range(4):
         ts(S("cst", 16 * d, 16 * d + 16), whole("lo16"), -1.0, A.mult, float(256 * d - 1024), A.add)
     ts(whole("dmp"), whole("lo16"), 1024.0, A.add)
-    ts(whole("cd"), whole("lo16"), 2048.0, A.add)
-    for name, lo, hi in (("tG", W, LC), ("tG", ZG, WGN), ("lo", ZV, LON), ("pre", 1024, 1040), ("tF", W, LC), ("tV", W, LC)):
+    act(whole("cd"), whole("lo16"), None, 2048.0)
+    for name, lo, hi in (("tG", W, LC), ("tG", ZG, WGN), ("lo", ZV, LON), ("pre", 1024, 1040)):
         fill(name, lo, hi, 0)
-    fill("idt", 0, 1280, 256)
-    ts(C(cES), C(cP), 3.0, A.mult, -2046.0, A.add)
-    ts(whole("esel"), S("jw", 0, 400), C(cES), A.is_equal)
-    ts(C(cR0), C(cR), 0.0, A.is_equal)
-    ts(whole("sel0"), S("jf", 0, 8), C(cG), A.is_equal, C(cR0), A.mult)
+    fill("jm", W, JW, 200)
+    ts(whole("sel0"), S("jf", 0, 8), C(cG), A.is_equal, R(0), A.mult)
     ts(whole("blk"), S("jf", 0, 8), C(cG), A.is_equal, 256.0, A.mult)
 
+    gathered = []
     for t in range(RO):
         lnd = "lnd%d" % t
         last = t == RO - 1
         conv(S("pA", 0, 16), "zA", lnd, 0, 16, 4)
         conv(S("pB", 0, 16), "zw", lnd, 3, 16, 4)
-        mm(S("pK1", 0, L), whole("wn"), S(lnd, 3, 1024, 4), True, True)
+        mms([(S("pK1", 0, L), whole("ib"), S(lnd, 0, 1024, 4), True, False), (S("pK1", 0, L), whole("wn"), S(lnd, 3, 1024, 4), False, True)])
+        if CV:
+            ts(S("cmp", 0, L), S("pK1", 0, L), 0.0, A.max)
+        else:
+            act(S("cmp", 0, L), S("pK1", 0, L), F.Relu)
         cp(whole("ui"), S("pA", 0, 16))
         ts(whole("u"), whole("ui"), 4095, A.bitwise_and)
-        tt(whole("uk"), IND(whole("u"), S("rep", 0, 4)), whole("k32"), A.mult)
+        tt(S("uk", 0, 64), IND(whole("u"), S("rep", 0, 4)), S("k32", 0, 64), A.mult)
         ts(whole("uh"), whole("u"), -2048.0, A.add)
         tt(whole("prod"), S("pB", 0, 16), whole("u"), A.mult)
-        tt(S("hi", 0, 64), IND(whole("prod"), S("rep", 0, 4)), whole("uk"), A.add)
+        tt(S("hi", 0, 64), IND(whole("prod"), S("rep", 0, 4)), S("uk", 0, 64), A.add)
         ts(S("hi", 0, 64), S("hi", 0, 64), 5, A.arith_shift_right, 4095, A.bitwise_and)
         cp(S("h16", 0, 64), S("hi", 0, 64))
         ts(whole("cc"), whole("prod"), 5, A.arith_shift_right, 4095, A.bitwise_and)
         ts(whole("ch"), IND(whole("cc"), S("rep", 0, 4)), -2048.0, A.add)
-        tt(S("cmp", 0, L), S(lnd, 0, 1024, 4), S("pK1", 0, L), A.min)
         mms([(S("pB", 0, 192), whole("ib"), whole("hc"), True, False)] +
             [(S("pB", 16 * m, 16 * m + 16), S("dk", 128 * m, 128 * m + 128), whole("uh"), False, False) for m in range(12)])
         mms([(S("pB", 64 * i, 64 * i + 64), whole("ih"), whole("ch"), False, i == 2) for i in range(3)])
-        mms([(S("pV", L * i, L * i + L), whole("ib"), S(lnd, 2, 1024, 4), i == 0, i == 1) for i in range(2)])
-        conv(S("pC", 0, 16), "z0", lnd, 3, 16, 4)
-        conv(S("pA", 0, 16), "zt", lnd, 3, 16, 4)
-        dma("s", S("tG", LC, ZG), whole(lnd), 3.5)
-        dma("s", S("lo", LV, ZV), whole(lnd), 4.5)
-        ts(whole("zf_"), S("pC", 0, 16), 0.0, A.is_equal)
+        turn([(S("pT", 128 * h, 128 * h + 128), S(lnd, 512 * h + 2, 512 * h + 512, 4)) for h in range(2)], "ib")
+        (cp if VT else act)(whole("vt"), S("pT", 0, L))
+        turn([(S("pV", 128 * i, 128 * i + 128), S("vt", 128 * (i % 2), 128 * (i % 2) + 128)) for i in range(8)], "ib")
+        kind = S("pK1" if last else "pC", 0, 16)
+        conv(kind, "zY", lnd, 3, 16, 4)
+        (gcopy if GC & 2 else cp if GC & 4 else act)(S("cmp", L, 2 * L), S("cmp", 0, L))
+        if t > 0:
+            iota(S("jm", 1024 * t - 1024, 1024 * t), [[0, 8], [1, 128]], 0, 0)
+            ops[-1]["after"] = [len(ops) - 2]
+
+        def kinds():
+            ts(S("zf4", 0, 16), kind, 1.0, A.not_equal)
+            ts(whole("fin"), kind, 2.0, A.is_equal)
+
+        def kinds4():
+            cp(S("zf4", 16, 64), IND(S("zf4", 0, 16), S("rep", 0, 3)))
+
+        def names():
+            if not last:
+                mms([(S("pC", L * i, L * i + L), S("wsh", 128 * i, 128 * i + 128), S(lnd, 3, 1024, 4), i == 0, i == 1) for i in range(2)])
+                conv(S("pA", 0, 16), "zX", lnd, 3, 16, 4)
+
+        def shifted():
+            if not last:
+                act(whole("nf"), S("pA", 0, 16), F.Relu, -255.0, -1.0)
+                act(S("nmw", 0, 2 * L), S("pC", 0, 2 * L))
+
+        behind = S("tF", 0, 1) if t == 0 else None
+        dma("s", S("tG", LC, ZG), whole(lnd), 3.5, behind)
+        dma("s", S("lo", LV, ZV), whole(lnd), 4.5, behind)
         if not last:
-            dma("s", S("nmw", 2 * L, 6 * L), whole(lnd), 5.5)
-            ts(whole("tb"), S("pA", 0, 16), 256.0, A.is_equal)
-        ts(whole("ta"), S("pA", 0, 16), 256.0, A.is_ge)
+            dma("s", S("nmw", 2 * L, 6 * L), whole(lnd), 5.5, behind)
 
         def gv(c):
             act(S("vg", 1024 * c, 1024 * c + 1024), IND(S("tV", 0, W), S("h16", 64 * c, 64 * c + 64)))
 
         def sgn(c):
+            if c == 2:
+                return ts(S("sg", 2048, 3072), S("lo", 2048, 3072), float(TAU[t]), A.is_gt)
             act(S("sg", 1024 * c, 1024 * c + 1024), S("lo", 1024 * c, 1024 * c + 1024), F.Sign, -(TAU[t] + 0.5))
 
         def gf(c, m0=0, m1=4, n=2):
@@ -485,129 +550,133 @@ def rank_program(g, core, T, topo):
                 tt(S("eqf", L * m, L * (m + n)), IND(S("tF", 0, W), S("h16", 16 * m, 16 * (m + n))), S("cmp", 0, L * n), A.is_equal)
 
         def mn(c):
-            for b in (1024 * c, 1024 * c + 512):
-                tt(S("lo", b, b + 512), S("vg", b, b + 512), S("pV", 0, 512), A.min)
+            for b in range(1024 * c, 1024 * c + 1024, WIDE):
+                tt(S("lo", b, b + WIDE), S("vg", b, b + WIDE), S("pV", 0, WIDE), A.min)
+                ops[-1]["c"] *= MNX
 
-        at = [(("pE0", 64 * c), ("pE0", 192 + 64 * c), ("pK0", 64 * c)) for c in range(3)] + [(("pE1", 0), ("pK1", 64), ("pK1", 0))]
+        at = [(("pE0", 64 * c), ("pE0", 192 + 64 * c), ("pK0", 64 * c)) for c in range(3)] + [(("pB", 0), ("pK1", 64), ("pK1", 0))]
 
         def sums(kind, c, stop=False):
             i = "ESK".index(kind)
-            z = "z16" if i == 2 else "zn" if c < 3 else ("zE", "zS")[i]
+            z = "z16" if i == 2 else "zn2" if (i, c) == (1, 2) else "zn" if c < 3 else ("zE", "zS")[i]
             conv(S(at[c][i][0], at[c][i][1], at[c][i][1] + 64), z, ("eqf", "sg", "lo")[i], 1024 * c, 64, 1, False, stop)
 
         def consts(bank, parts):
             mms([(S(bank, a, a + width(x)), whole(w), x, i == 0, False) for i, (a, w, x) in enumerate(parts)])
 
         def bars(bank, a, n, w):
-            mms([(S(bank, b, b + 16), whole(w), whole("zf_"), False, False) for b in range(a, a + n, 16)])
+            mms([(S(bank, b, b + 64), whole(w), whole("zf4"), False, False) for b in range(a, a + n, 64)])
 
-        def rest():
-            cp(S("hi", 64, L), S("pB", 0, 192))
-            ts(S("hi", 64, L), S("hi", 64, L), 4095, A.bitwise_and)
-            cp(S("h16", 64, L), S("hi", 64, L))
+        rest = (lambda: cp(whole("hr"), S("pB", 0, 192)), lambda: ts(S("hi", 64, L), whole("hr"), 4095, A.bitwise_and),
+                lambda: cp(S("h16", 64, L), S("hi", 64, L)))
 
+        def opening():
+            consts("pE0", [(0, "ib", whole("c13"))])
+            consts("pK0", [(0, "ib", whole("c1")), (0, "ib", S("c2", 0, 192))])
+
+        def flags():
+            consts("pK1", [(0, "ib", S("c1", 0, 64)), (0, "ib", S("c2", 192, L)), (64, "ib", S("cE", 64, 128))])
+            consts("pB", [(0, "ib", S("cE", 0, 64))])
+            for e in (("pE0", 0, 192, "i3"), ("pE0", 192, 192, "i18"), ("pK1", 64, 64, "iS"), ("pB", 0, 64, "iE")):
+                bars(*e)
+
+        queues = [o.split() for o in (ORDER0 if t == 0 else ORDER)]
+        ends = ([x for x in queues[2] if x[0] in "ES" and x[1] != "3"][-1], [x for x in queues[2] if x in ("K3", "S3")][-1], "E3")
+        step = {"p0": (lambda: gf(0, 0, 1, 1), []), "p1": (lambda: gf(0, 1, 2, 1), []), "r0": (rest[0], []), "r1": (rest[1], []),
+                "rest": (rest[2], []), "open": (opening, []),
+                "kind": (kinds, []), "kinds": (kinds4, []), "names": (names, ["kinds"]), "shift": (shifted, ["names"]),
+                "ks": (lambda: (cp if KV & 1 else act)(whole("ks"), S("pK1", 64, 128)), [ends[1]]),
+                "ka": (lambda: (cp if KV & 2 else act)(whole("ka"), S("pK0", 0, 64)), ["pen"]),
+                "tab": (lambda: tt(whole("ktab"), IND(whole("hi"), whole("lhk")), whole("mk"), A.add), ["rest"]),
+                "flags": (flags, ["rest", "kinds"]), "relu": (lambda: act(whole("pen"), S("pE0", 0, 384), F.Relu), [ends[0]]),
+                "pen": (lambda: mms([(S("pK0", 0, 192), whole("ineg"), S("pen", 192 * i, 192 * i + 192), False, i == 1)
+                                     for i in range(2)]), ["relu"])}
+        for c in range(4):
+            step["a%d" % c] = (lambda c=c: gf(c, 0, 2), ["rest"])
+            step["b%d" % c] = (lambda c=c: gf(c, 2, 4), ["rest"])
+            step["g%d" % c] = (lambda c=c: gv(c), ["rest"] if c else [])
+            step["m%d" % c] = (lambda c=c: mn(c), ["g%d" % c])
+            step["s%d" % c] = (lambda c=c: sgn(c), ["m%d" % c])
+            for x, y in (("E", "b"), ("K", "m"), ("S", "s")):
+                step["%s%d" % (x, c)] = (lambda c=c, x=x: sums(x, c, "%s%d" % (x, c) in ends), ["%s%d" % (y, c)])
         keep[0] = True
-        gv(0)
-        if t > 0:
-            gf(0, 0, 1, 1)
-        rest()
-        consts("pE0", [(0, "ib", whole("c13"))])
-        consts("pK0", [(0, "ib", whole("c1")), (0, "ib", S("c2", 0, 192))])
-        if t > 0:
-            gf(0, 1, 4, 1); sums("E", 0)
-        gv(1)
-        act(S("cmp", L, 2 * L), S("cmp", 0, L))
-        mn(0); sums("K", 0)
-        sgn(0); sums("S", 0)
-        consts("pK1", [(0, "ib", S("c1", 0, 64)), (0, "ib", S("c2", 192, L)), (64, "ib", S("cE", 64, 128))])
-        consts("pE1", [(0, "ib", S("cE", 0, 64))])
-        for e in (("pE0", 0, 192, "i3"), ("pE0", 192, 192, "i18"), ("pK1", 64, 64, "iS"), ("pE1", 0, 64, "iE")):
-            bars(*e)
-        if t > 0:
-            gf(1); sums("E", 1)
-        gv(2)
-        mn(1); sums("K", 1)
-        sgn(1); sums("S", 1)
-        if t == 0:
-            gf(0); sums("E", 0)
-            gf(1); sums("E", 1)
-        gf(2); sums("E", 2)
-        gv(3)
-        mn(2); sums("K", 2)
-        sgn(2); sums("S", 2, True)
-        mn(3); sums("K", 3)
-        sgn(3)
-        act(whole("pen"), S("pE0", 0, 384), F.Relu)
-        sums("S", 3, True)
-        mms([(S("pK0", 0, 192), whole("ineg"), S("pen", 192 * i, 192 * i + 192), False, i == 1) for i in range(2)])
-        gf(3); sums("E", 3, True)
+        done = []
+        while any(queues):
+            for o in queues:
+                while o and all(x in done for x in step[o[0]][1]):
+                    step[o[0]][0]()
+                    done.append(o.pop(0))
+        if 0 < t < RO - 1:
+            cp(IND(S("tG", 0, LC), S("o16", GP, 16)), S("lnd%d" % (t - 1), 64 * GP + 1, 1024, 4))
         keep[0] = False
-        act(whole("ks"), S("pK1", 64, 128))
-        if not last:
-            for b, z in ((0, "z21"), (L, "z15")):
-                mms([(S("pC", b, b + L), whole("shf"), S(lnd, 3, 1024, 4), True, False),
-                     (S("pC", b, b + L), S(z, 1, 129), S(lnd, 3, 1024, 4), False, True)])
-            act(S("nmw", 0, 2 * L), S("pC", 0, 2 * L))
-        else:
-            for h in range(2):
-                mms([(S("pC", 0, 384), S(lnd, 512 * h + j, 512 * h + 512, 4), S("esel", 2 - j, 386 - j), j == 0, j == 2)
-                     for j in range(3)])
-                act(S("vT", 384 * h, 384 * h + 384), S("pC", 0, 384))
+        if last:
             for j, tab in enumerate(("tV", "tF", "tG")):
-                for k in range(0, 32, 4):
-                    mms([(S("pB", 128 * j, 128 * j + 128), whole("ib"), S(tab, 128 * e, 128 * e + 128),
-                          j == 0 and e == 0, j == 2 and e == 31) for e in range(k, k + 4)])
-            act(whole("zb0"), S("pB", 0, 384))
+                for k in range(0, 32, SP):
+                    mms([(S("pC", 128 * j, 128 * j + 128), whole("ib"), S(tab, 128 * e, 128 * e + 128),
+                          j == 0 and e == 0, j == 2 and e == 31) for e in range(k, k + SP)])
+            act(whole("zb0"), S("pC", 0, 384))
         def lists(parts, stop=False):
-            mms([(S("pA", 16 * b, 16 * b + 16), whole(w), whole(x), False, stop and i == len(parts) - 1)
+            mms([(S("pA", 16 * b, 16 * b + 16), whole(w), S(x, 0, 16), False, stop and i == len(parts) - 1)
                  for i, (b, w, x) in enumerate(parts)])
 
         n = 80 if last else 96
-        tt(whole("fin"), whole("ta"), whole("zf_"), A.mult)
-        cp(whole("u3"), IND(whole("u"), S("rep", 0, 3)))
-        consts("pA", [(0, "ih", S("eH", 0, n)), (0, "ib", S("eB", 0, n)), (0, "ib", S("eC", 0, n)), (0, "ih", S("ch", 0, 48))])
-        lists([(0, "iO", "zf_"), (3, "iO", "zf_"), (4, "iO", "zf_"), (2, "iOn", "fin")])
+        consts("pA", [(0, "ih", S("eH", 0, n)), (0, "ib", S("eB", 0, n)), (0, "ib", S("eC", 0, n))])
+        mm(S("pA", 48, 80), whole("iO"), S("zf4", 0, 32), False, False)
+        lists([(0, "iO", "zf4"), (2, "iOn", "fin")])
         if not last:
-            tt(whole("nf"), whole("tb"), whole("zf_"), A.is_gt)
             lists([(0, "iO", "nf"), (1, "iOn", "nf"), (3, "i256", "nf"), (5, "iO", "nf")])
         else:
-            lists([(5, "iZG", "zf_"), (6, "iZV", "zf_")])
+            lists([(5, "iZG", "zf4"), (6, "iZV", "zf4")])
 
-        cp(whole("ka"), S("pK0", 0, 64))
         tt(whole("kb"), S("pK0", 64, 128), whole("ka"), A.max)
         tt(whole("kc"), S("pK0", 128, 192), whole("kb"), A.max)
         tt(whole("kt"), S("pK1", 0, 64), whole("ks"), A.min)
-        tt(whole("k1"), S("pE1", 0, 64), whole("kt"), A.min)
+        tt(whole("k1"), S("pB", 0, 64), whole("kt"), A.min)
         tt(whole("k2"), whole("k1"), whole("kc"), A.max)
         tt(whole("k3"), S("k2", 0, 32), S("k2", 32, 64), A.max)
         tt(whole("ki"), S("k3", 0, 16), S("k3", 16, 32), A.max)
         ts(whole("val"), whole("ki"), 15, A.bitwise_and)
         ts(whole("nv"), whole("ki"), -BIG / 2, A.is_lt)
-        tt(whole("step"), IND(whole("val"), whole("repc")), whole("jr"), A.is_lt)
-        scan(whole("ksel"), whole("step"), whole("ktab"), A.mult, A.max)
         cp(whole("valb"), whole("val"))
-        lists([(b, "iO", "nv") for b in range(5)] + ([] if last else [(5, "iOn", "nv")]) + [(4, "i256n", "valb")], True)
-        tt(S("own", 0, 16), S("pA", 80, 96), S("c0", 0, 16), A.max)
+        tt(whole("step"), IND(whole("val"), whole("repc")), whole("jr"), A.is_lt)
+        ops[-1]["after"] = [len(ops) - 2]
+        scan(S("ksel", 0, L), whole("step"), whole("ktab"), A.mult, A.max)
+        lists([(b, "iO", "nv") for b in range(5)] + ([] if last else [(5, "iOn", "nv")]))
+        lists([(b, "i4k", "valb") for b in range(3)] + [(4, "i256n", "valb")], True)
+        act(whole("hb"), S("pA", 0, 80))
         if last:
-            tt(S("own", 64, 80), S("pA", 96, 112), S("c0", 64, 80), A.max)
-        cp(S("hb", 48, 80), S("pA", 48, 80))
-        tt(whole("ha"), IND(whole("ksel"), S("l15", 0, 3)), whole("u3"), A.mult)
-        tt(S("hb", 0, 48), S("pA", 0, 48), whole("ha"), A.add)
-        ts(whole("hm"), whole("hb"), 4095 + 3 * OFF, A.bitwise_and)
-        tt(whole("s6"), whole("hm"), whole("own"), A.min)
+            tt(S("own", 0, 16), S("pA", 80, 96), S("c0", 0, 16), A.max)
+            tt(S("own", 64, 80), S("pA", 96, 112), S("c0", 16, 32), A.max)
+        else:
+            if OV:
+                ts(whole("swp"), S("pA", 80, 96), 0.0, A.max)
+            else:
+                act(whole("swp"), S("pA", 80, 96), F.Relu)
+            consts("pK1", [(0, "ih", whole("oH")), (0, "ib", whole("oB"))])
+            mm(S("pK1", 0, 16), whole("ib"), whole("swp"), False, True)
+        tt(whole("hm"), IND(whole("ksel"), S("l15", 0, 5)), whole("hb"), A.add)
+        tt(whole("s6"), whole("hm"), whole("own") if last else S("pK1", 0, 80), A.min)
         cp(whole("s16"), whole("s6"))
         if not last:
-            act(S("pre", 0, 1024, 4), IND(whole("tG"), S("s16", 0, 16)))
-            mm(S("pB", 0, 16), whole("iO"), whole("zf_"), True, False)
+            (cp if XV else act)(S("pre", 0, 1024, 4), IND(whole("tG"), S("s16", 0, 16)))
+            mm(S("pB", 0, 16), whole("iO"), S("zf4", 0, 16), True, False)
             conv(S("pB", 0, 16), "zB", "pre", 0, 16, 4, False, True)
 
         def claims():
             cp(whole("plr"), IND(whole("jw"), S("s16", 32, 48)))
+            if BS:
+                ts(whole("pq"), S("s6", 32, 48), 25165824.0 * 8, A.add, -25165824.0 * 8, A.add)
+                ts(S("pb", 0, 16), whole("pq"), -1.0, A.mult, 2048.0, A.add)
+                tt(S("pb", 16, 32), S("s6", 32, 48), whole("pq"), A.subtract)
             for c in range(16):
-                ts(S("eqd", L * c + 16 * c, L * c + L), S("plr", 16 * c, L), 2048.0, A.add, S("s6", 32 + c, 33 + c), A.is_equal)
-                mms([(S("pE1", 16 * c, L), whole("ones"), S("eqd", L * c + 16 * c, L * c + L), c == 0, False),
-                     (S("pE1", 16 * c, 16 * c + 16), whole("uge"), S("eqd", L * c + 16 * c, L * c + 16 * c + 16), False, c == 15)])
-            tt(whole("dmk"), S("pE1", 0, L), whole("dm"), A.mult)
+                if BS:
+                    ts(S("eqd", L * c + 16 * c, L * c + L), S("plr", 16 * c, L), S("pb", c, c + 1), A.add, S("pb", 16 + c, 17 + c), A.is_equal)
+                else:
+                    ts(S("eqd", L * c + 16 * c, L * c + L), S("plr", 16 * c, L), 2048.0, A.add, S("s6", 32 + c, 33 + c), A.is_equal)
+                    ops[-1]["c"] += (EQX - 1) * 0.5 * CYC * (L - 16 * c)
+                mms([(S("pE0", 16 * c, L), whole("ones"), S("eqd", L * c + 16 * c, L * c + L), c == 0, False),
+                     (S("pE0", 16 * c, 16 * c + 16), whole("uge"), S("eqd", L * c + 16 * c, L * c + 16 * c + 16), False, c == 15)])
+            tt(whole("dmk"), S("pE0", 0, L), whole("dm"), A.mult)
 
         if not last:
             act(S("pre", 1, 1024, 4), IND(whole("tG"), S("s16", 16, 32)))
@@ -623,6 +692,9 @@ def rank_program(g, core, T, topo):
             mm(S("pK1", 0, 16), whole("ih"), whole("dmp"), True, False)
             mms([(S("pK1", 0, 16), whole("ih"), S("tt4", 16 * d, 16 * d + 16), False, d == 3) for d in range(4)])
             cp(whole("pos"), S("pK1", 0, 16))
+            for d in range(4):
+                act(S("idt", L * d, L * d + 64), S("jf", 0, 64), None, 256.0, 0.0)
+                ops[-1]["after"] = list(gathered)
             cp(IND(whole("idt"), whole("pos")), whole("jb"))
             for bank, ks in (("pB", (1,)), ("pK0", (2, 3, 4))):
                 mms([(S(bank, 16 * k - 16, 16 * k), S("z4", 12 - 4 * e, 140 - 4 * e),
@@ -633,7 +705,7 @@ def rank_program(g, core, T, topo):
             sent = []
             for k in range(1, N):
                 o = S(snd, L * (k - 1), L * k)
-                act(o, IND(whole("pre"), S("src", 16 * k - 16, 16 * k)))
+                (cp if k in SVK[SV] else act)(o, IND(whole("pre"), S("src", 16 * k - 16, 16 * k)))
                 dst = T.cores[(rank + k) % N]
                 sem = "out%d" % (3 * t + k - 1)
                 sent.append(rec("g", lambda o=o, here=here, sem=sem, t=t, dst=dst: g.remote_dma(
@@ -641,41 +713,46 @@ def rank_program(g, core, T, topo):
                     [], [o], RISS, kind="rem", lat=RLAT + (3.0 if t == 0 and k == 1 else 0.0), sem=sem,
                     n=len(topo.engines(core, dst)), after=sent[-1:]))
             act(here, IND(whole("pre"), S("src", 48, 64)))
+            gathered[:] = [len(ops) - 1]
             n_in = sum(len(topo.engines(T.cores[q], core)) for q in range(N) if q != rank)
             rec("x", None, [S(nxt, L * q, L * q + L) for q in range(N) if q != rank], [], 0.0, kind="land", sem="arr%d" % t,
                 n=n_in, after=sent)
-            if t < RO - 2:
-                for d in range(4):
-                    fill("idt", L * d, L * d + 64, 256)
-                    ops[-1]["after"] = sent[-1:]
             claims()
-            ts(whole("plh"), S("s6", 32, 48), -2048.0, A.add)
-            mm(S("pC", 0, 16), whole("ih"), whole("plh"), True, False)
+            mms([(S("pC", 0, 16), whole("ib"), S("pb", 16, 32), True, False), (S("pC", 0, 16), whole("ibn"), S("pb", 0, 16), False, False)])
             conv(S("pC", 0, 16), "z65", "dmk", 0, 16, 1, False, True)
             tt(whole("ot"), S("pC", 0, 16), whole("cd"), A.min)
             ts(whole("o16"), whole("ot"), 2048.0, A.add)
-            for tab, j, n in (("tV", 2, 16), ("tF", 0, 16), ("tG", 1, 4)):
-                for b in range(0, 16, n):
-                    cp(IND(S(tab, 0, LC), S("o16", b, b + n)), S(lnd, 64 * b + j, 64 * (b + n), 4))
+            keep[0] = True
+            for tab, j, n in (("tV", 2, 16), ("tF", 0, 16), ("tG", 1, GP if t < RO - 2 else 16)):
+                cp(IND(S(tab, 0, LC), S("o16", 0, n)), S(lnd, j, 64 * n, 4))
+            keep[0] = False
         else:
             act(whole("yfb"), IND(whole("tG"), S("s16", 0, 16)))
             act(whole("yvb"), IND(whole("lo"), S("s16", 64, 80)))
             dma("s", T.yf[:], whole("yfb"))
             dma("s", T.yv[:], whole("yvb"))
             act(whole("plm"), IND(whole("jm"), S("s16", 32, 48)))
+            first = len(ops) - 1
+            for h, bank in enumerate(("pK1", "pK0")):
+                mms([(S(bank, 128 * j, 128 * j + 128), S(lnd, 512 * h + j, 512 * h + 512, 4), whole("ib"), j == 0, j == 2)
+                     for j in range(3)])
+                for j in range(3):
+                    act(S("vT", 384 * h + j, 384 * h + 384, 3), S(bank, 128 * j, 128 * j + 128))
+                    ops[-1]["after"] = [first]
             claims()
-            mms([(S("pC", 8 * h, 8 * h + 8), S("plm", 128 * h, 128 * h + 128), whole("sel0"), h == 0, False) for h in range(2)])
-            mms([(S("pC", 8 * h, 8 * h + 8), S("dmk", 128 * h, 128 * h + 128), whole("blk"), False, h == 1) for h in range(2)])
+            mms([(S("pB", 8 * h, 8 * h + 8), S("plm", 128 * h, 128 * h + 128), whole("sel0"), h == 0, False) for h in range(2)])
+            mms([(S("pB", 8 * h, 8 * h + 8), S("dmk", 128 * h, 128 * h + 128), whole("blk"), False, h == 1) for h in range(2)])
+            if BS:
+                cp(S("pb", 32, 48), S("pB", 0, 16))
             for i in range(16):
-                ts(S("eqf", 128 * i, 128 * i + 128), S("jb", 0, 128), S("pC", i, i + 1), A.is_equal)
+                ts(S("eqf", 128 * i, 128 * i + 128), S("jb", 0, 128), S("pb", 32 + i, 33 + i) if BS else S("pB", i, i + 1), A.is_equal)
                 mm(S("pA", 48 * (i % 8), 48 * (i % 8) + 48), S("eqf", 128 * i, 128 * i + 128), S("vT", 48 * i, 48 * i + 48),
                    i == 0, i == 15)
             ends = (("pE0", T.zf, 1), ("pK0", T.zg, 2), ("pK1", T.zv, 0))
             for j, (bank, out, b) in enumerate(ends):
                 z = S("zts", 128 * j, 128 * j + 128)
                 cp(z, S("pA", j, 384, 3))
-                rec("p", lambda z=z, bank=bank: g.tensor.transpose(ap(S(bank, 0, 128)), ap(z), ap(whole("i32"))),
-                    [S(bank, 0, 128)], [z, whole("i32")], 512 * PEC)
+                turn([(S(bank, 0, 128), z)], "i32")
             for j, (bank, out, b) in enumerate(ends):
                 tt(S("zb", 128 * j, 128 * j + 128), S(bank, 0, 128), S("zb0", 128 * b, 128 * b + 128), A.add)
                 dma("a" if j == 1 else "s", out[:], S("zb", 128 * j, 128 * j + 128))

@@ -7,8 +7,9 @@ WB = [1, 3, 2, 7, 5, 1, 6, 3, 7, 2, 5, 4, 1, 6, 3, 5]
 KP = [3, 18, 45, 71, 102, 125, 150, 187, 208, 233, 260, 291, 318, 345, 382, 407]
 LC, ZG, WGN = 4352, 5376, 5392
 OFF = 4194304
-LV, ZV, LON = 4096, 5120, 5136
+LV, LE, ZV, LON = 4096, 5120, 5184, 5200
 NC, JW = 4096, 4112
+EPS = 2.0 ** -20
 BIG = 33554432.0
 B16, F16, F32, I32, U16 = "bfloat16", "float16", "float32", "int32", "uint16"
 
@@ -16,36 +17,33 @@ _SB = {
     "tF": (4352, B16), "tV": (4352, B16), "tG": (WGN, B16), "lo": (LON, B16),
     "vg": (W, B16), "eqf": (W, B16), "sg": (W, B16), "eqd": (W, B16),
     "lnd0": (1024, B16), "lnd1": (1024, B16), "lnd2": (1024, B16), "lnd3": (1024, B16), "lnd4": (1024, B16),
-    "snd0": (768, B16), "snd1": (768, B16), "snd2": (768, B16), "snd3": (768, B16),
+    "snd0": (1024, B16), "snd1": (1024, B16), "snd2": (1024, B16), "snd3": (1024, B16),
     "pre": (1040, B16), "idt": (1280, B16), "yfb": (L, B16), "yvb": (L, B16), "zb": (384, F32), "zb0": (384, F32),
     "zts": (384, F32), "vT": (768, B16), "vt": (L, B16), "plm": (L, B16),
     "wfs": (L, B16), "wvs": (L, B16), "nms": (L, I32), "nmb": (L, B16), "thf": (L, B16),
-    "pcol": (16, I32), "col": (32, F32), "jf": (L, F32), "jr": (L, F32), "jq": (L, F32), "j4": (144, F32), "lo16": (16, F32),
-    "jb": (L, B16), "ab": (16, F32), "ab2": (16, F32), "ib": (128, B16), "ih": (128, F16), "i3": (128, B16), "i18": (128, B16),
-    "ineg": (128, B16), "ones": (128, B16), "uge": (128, B16), "uget": (128, B16), "wn": (128, B16), "shf": (128, B16),
-    "zA": (144, B16), "zB": (144, B16), "z0": (144, B16), "zr15": (144, B16), "zX": (144, B16), "zn": (144, B16), "zn2": (144, B16),
-    "zY": (144, B16), "zr13": (144, B16), "wsh": (L, B16), "e16": (16, F32), "nm0": (L, B16),
-    "oH": (80, F16), "oB": (80, B16), "swp": (16, B16), "z65": (144, B16), "z16": (144, B16), "z4": (144, B16), "dk": (1536, F16), "dm": (L, B16), "hc": (192, B16),
-    "zE": (144, B16), "zS": (144, B16), "iE": (128, B16), "iS": (128, B16), "cE": (128, B16), "ktab": (L, F32), "k32": (64, F32),
-    "mk": (L, F32), "lhk": (16, U16), "i4k": (128, B16), "ibn": (128, B16),
-    "c13": (384, B16), "c1": (192, B16), "c2": (L, B16), "msk": (64, B16), "cst": (64, F16), "dmp": (16, F16),
+    "pcol": (16, I32), "col": (32, F32), "jf": (144, F32), "jr": (L, F32), "jq": (128, F32), "j4": (144, F32), "lo16": (16, F32),
+    "jb": (L, B16), "ab": (16, F32), "ab2": (16, F32), "ib": (128, B16), "ih": (128, F16), "nil": (128, B16),
+    "ones": (128, B16), "uge": (128, B16), "uget": (128, B16), "wn": (128, B16), "onB": (128, B16), "shf": (128, B16),
+    "zA": (144, B16), "zB": (144, B16), "z0": (144, B16), "z0n": (144, B16), "zX": (144, B16), "z1": (144, B16),
+    "zr1": (144, B16), "zr13": (144, B16), "z16": (144, B16), "z4": (144, B16), "zE": (144, B16),
+    "wsh": (L, B16), "e16": (16, F32), "nm0": (L, B16), "l16": (16, F32),
+    "oH": (80, F16), "oB": (80, B16), "dk": (1536, F16), "dm": (L, B16), "hc": (192, B16),
+    "iE": (128, B16), "iS": (128, B16), "i16": (128, B16), "ibn": (128, B16), "i32": (128, F32),
+    "iO": (128, B16), "iOn": (128, B16), "i256": (128, B16), "iZG": (128, B16), "iZV": (128, B16),
+    "cE": (64, B16), "ktab": (L, F32), "k32": (80, F32), "repn": (16, U16), "mk": (L, F32), "lhk": (16, U16),
+    "c13": (576, B16), "c1": (320, B16), "c2": (384, B16), "msk": (64, B16), "cst": (64, F16), "dmp": (16, F16),
     "cd": (16, F32), "c0": (32, F32), "own": (80, F32), "rep": (16, U16), "repc": (16, U16), "l15": (6, U16),
-    "iO": (128, B16), "iOn": (128, B16), "i256": (128, B16), "i256n": (128, B16), "iZG": (128, B16), "iZV": (128, B16),
-    "eH": (96, F16), "eB": (96, B16), "eC": (96, B16), "nmw": (6 * L, B16),
-    "jw": (JW, F32), "jm": (JW, B16), "plh": (16, F16), "pq": (16, F32), "pb": (48, B16), "i32": (128, F32),
-    "sel0": (8, B16), "blk": (8, B16),
-    "z1": (144, B16), "zw": (144, B16), "zr1": (144, B16), "l16": (16, F32),
-    "ui": (16, I32), "u": (16, I32), "zf_": (16, B16), "zf4": (64, B16), "hr": (192, I32), "prod": (16, I32), "uk": (64, F32), "hs": (64, I32),
-    "cc": (16, I32), "uh": (16, F16), "ch": (64, F16), "hi": (L, I32), "h16": (L, U16), "cmp": (2 * L, B16),
+    "eH": (80, F16), "eB": (80, B16), "eC": (80, B16), "nmw": (6 * L, B16),
+    "jw": (JW, F32), "jm": (JW, B16), "pq": (16, F32), "pb": (48, B16), "sel0": (8, B16),
+    "ui": (32, I32), "u": (16, I32), "zf4": (64, B16), "hr": (192, I32), "uk": (80, F32),
+    "uh": (16, F16), "ch": (64, F16), "hi": (L + 16, I32), "h16": (L, U16), "cmp": (2 * L, B16),
     "fin": (16, B16), "nf": (16, B16), "nv": (16, B16), "valb": (16, B16),
-    "pen": (384, B16), "ka": (64, F32), "kb": (64, F32), "kc": (64, F32), "ks": (64, F32), "kt": (64, F32),
-    "k1": (64, F32), "k2": (64, F32), "k3": (32, F32), "step": (L, B16), "ksel": (L + 16, F32),
+    "pen": (384, B16), "ks": (64, F32), "kt": (320, F32), "k2": (320, F32), "k3": (32, F32), "step": (L, B16), "ksel": (L + 16, F32),
     "ki": (16, I32), "val": (16, I32), "hb": (80, F32), "hm": (80, F32), "s6": (80, F32), "s16": (80, U16),
     "gi": (16, I32), "g3": (16, I32), "go4": (64, B16), "inc": (64, B16), "tt4": (64, F16), "pos": (16, U16), "src": (64, U16),
     "plr": (L, F16), "dmk": (L, B16), "ot": (16, F32), "o16": (16, U16),
 }
 _PS = ["pV", "pT", "pE0", "pK0", "pK1", "pA", "pB", "pC"]
-WIDE, SP = 1024, 8
 SCRATCH = {}
 _AT = {}
 for _k in _SB:
@@ -56,25 +54,40 @@ for _k in _SB:
         SCRATCH[_a] = ("sbuf", [128, _n + (_SB[_k][0] + 15) // 16 * 16], _SB[_k][1])
     else:
         SCRATCH[_k] = ("sbuf", [128, _SB[_k][0]], _SB[_k][1])
+DIMS = {"lnd%d" % _k: (L, 4) for _k in range(RO)}
+for _k in DIMS:
+    SCRATCH[_k] = ("sbuf", [128] + list(DIMS[_k]), _SB[_k][1])
 for _k in _PS:
     SCRATCH[_k] = ("psum", [128, 1024], B16) if _k in ("pV", "pT") else ("psum", [128, 512], F32)
 NDMA = 26
 SEMAPHORES = ["cv", "ca", "cp_", "cg"] + ["d%d" % i for i in range(NDMA)] + ["arr%d" % i for i in range(4)] + \
              ["out%d" % i for i in range(12)]
-HOP = 0.06
-SLACK, MARGIN, GP, EARLY, MAGIC = 0.3, 0.0, 8, 1, 0
-PEC, VFIX, AFIX, RISS, RLAT, LOAD = 0.00052, 0.053, 0.13, 0.55, 1.3, 3.0
-SELF, PEHOP, VADD, GAT, SCA, F2 = 0.09, 0.07, 0.065, 1.52, 2.2, 1.0
+CYC, PEC, VFIX, AFIX, RISS, RLAT, LOAD = 0.00083, 0.00052, 0.053, 0.13, 0.55, 1.3, 3.0
+HOP, SELF, PEHOP, VADD, GAT, SCA, MNX = 0.06, 0.09, 0.07, 0.065, 1.52, 2.2, 0.6
 FROM, TO = {"a": 0.1}, {"a": 0.03, "v": 0.04}
-XV, SV, CV, KV, OV, GC, GF = 0, 0, 0, 0, 0, 2, 1
-BS, EQX, MNX, S3V = 1, 1, 0.6, 1
-ONS, VT = ("i3", "z16", "ibn", "z65"), 0
-SVK = ((), (1,), (1, 3), (1, 2, 3))
-ORDER = ("r0 p0 r1 p1 rest kind m0 kinds b0 a1 m1 b1 a2 m2 b2 s2 m3 a3 b3 tab", "g0 g1 g2 s0 g3 s1 s3 relu ks ka shift",
-         "open K0 E0 names flags K1 S0 E1 K2 E2 S2 K3 S1 S3 pen E3")
-ORDER0 = ("r0 r1 rest m0 kind a0 kinds m1 b0 a1 m2 b1 s2 m3 a2 b2 a3 b3 tab", "g0 g1 g2 s0 g3 s1 s3 relu ks ka shift",
-          "open K0 names flags K1 E0 S0 K2 E1 S2 K3 S1 E2 S3 pen E3")
-CYC = 0.00083
+GP, SP = 8, 2
+CLAIMS = [0, 1, 2, 13, 14, 15] + list(range(3, 13))
+ONV = ((), (2,))
+ORDER = ("ui u w t uh sh h0 ch p0 r0 kind r1 kinds rest p1 m0 b0 a1 m1 b1 a2 m2 b2 s2 m3 a3 b3 tab",
+         "cmp vt g0 nf g1 s0 g2 g3 s1 s3 relu ks shift",
+         "open H C T X dk V8 names flags K0 parts E0 S0 K1 E1 K2 E2 S2 S1 K3 S3 E3 pen", "cmp2 jm")
+ORDER0 = ("ab ab ab pc pc pc ab pc ab cZ cY keep ab ab e16 ab z1 ab* A cW A z0 A repn A A rep A zA nmb ones z0n cF dk dk dk dk "
+          "ui dk u w dk t uh sh ih h0 ch aux dk* cX cX cX r0 yv r1 yv rest m0 kind a0 kinds "
+          "m1 b0 a1 m2 b1 a2 m3 b2 a3 b3 cL kt lhk kt repc tab l15* lo16 eH*",
+          "z16 zE x0 nm0 thf vt wn cmp g0 zX g1 g2 s0 g3 s1 s2 s3 nf zr13 relu ks zB wsh shift",
+          "H there T init C dk V8 X open K0 flags K1 E0 S0 K2 E1 S1 K3 E2 S2 S3 E3 pen parts wshp names",
+          "pcol jf nil ib jq k32* hc l16 iOn ibn c13* c1* cmp2 c2* cE* i256 iS iE jw jr mk iO i16 jb e* jw zero* jw jw")
+
+
+def boxed(dims, cols):
+    out = []
+    for d in range(len(dims)):
+        below = 1
+        for e in dims[d + 1:]:
+            below *= e
+        x = sorted(set(c // below % dims[d] for c in cols))
+        out.append(x[0] if len(x) == 1 else slice(x[0], x[-1] + 1, x[1] - x[0]))
+    return (slice(0, 128),) + tuple(out)
 
 
 def S(name, lo, hi, step=1):
@@ -83,12 +96,20 @@ def S(name, lo, hi, step=1):
     return ("ap", name, lo, hi, step)
 
 
+def BOX(name, cols):
+    return ("ap", name, 0, 0, 0, cols)
+
+
 def IND(win, off):
     return ("ind", win, off)
 
 
+def columns(a):
+    return a[5] if len(a) > 5 else range(a[2], a[3], a[4])
+
+
 def width(a):
-    return 16 * width(a[2]) if a[0] == "ind" else len(range(a[2], a[3], a[4]))
+    return 16 * width(a[2]) if a[0] == "ind" else len(columns(a))
 
 
 def _mask(a):
@@ -97,7 +118,7 @@ def _mask(a):
     if a[4] == 1:
         return ((1 << (a[3] - a[2])) - 1) << a[2]
     m = 0
-    for i in range(a[2], a[3], a[4]):
+    for i in columns(a):
         m |= 1 << i
     return m
 
@@ -132,16 +153,21 @@ def arrange(ops):
             if ops[j]["q"] != ops[i]["q"]:
                 pred[i][j] += FROM.get(ops[j]["q"], 0.0) + TO.get(ops[i]["q"], 0.0)
             succ[j][i] = pred[i][j]
+    left = [len(s) for s in succ]
+    todo = [i for i in range(n) if not left[i]]
     chain = [0.0] * n
-    for i in range(n - 1, -1, -1):
+    depth = [0] * n
+    for i in todo:
         chain[i] = ops[i]["c"] + max([w + chain[k] for k, w in succ[i].items()] + [ops[i]["lat"]])
-    for i in range(n):
+        depth[i] = 1 + max([depth[k] for k in succ[i]] + [0])
         for j in pred[i]:
-            if ops[j]["q"] != ops[i]["q"] and chain[j] - ops[j]["c"] - pred[i][j] - chain[i] > SLACK:
-                pred[i][j] += MARGIN
+            left[j] -= 1
+            if not left[j]:
+                todo.append(j)
+    assert len(todo) == n, [ops[i].get("nm") for i in range(n) if left[i]][-9:]
     end = [0.0] * n
     busy = {}
-    for i in sorted(range(n), key=lambda i: (-chain[i], i)):
+    for i in sorted(range(n), key=lambda i: (-round(chain[i], 6), -depth[i], i)):
         c = ops[i]["c"]
         t = max([end[j] + w for j, w in pred[i].items()] + [0.0])
         starts, ends = busy.setdefault(ops[i]["q"], ([], []))
@@ -154,7 +180,7 @@ def arrange(ops):
         starts.insert(k, t)
         ends.insert(k, t + c)
         end[i] = t + c
-    return [ops[i] for i in sorted(range(n), key=lambda i: (end[i] - ops[i]["c"], i))]
+    return [ops[i] for i in sorted(range(n), key=lambda i: (round(end[i] - ops[i]["c"], 6), -depth[i], i))]
 
 
 def emit(g, T, ops):
@@ -231,12 +257,19 @@ def rank_program(g, core, T, topo):
     def ap(a):
         if a[0] == "ind":
             return ap(a[1]).indirect(ap(a[2]))
+        if a[1] in DIMS:
+            return T[a[1]][boxed(DIMS[a[1]], list(columns(a)))]
         if a[4] == 1:
             return T[a[1]][:, a[2]:a[3]]
         return T[a[1]][:, a[2]:a[3]:a[4]]
 
     lines = {}
     keep = [False]
+    named = {}
+
+    def line(i):
+        ops[i]["after"] = lines.get(ops[i]["q"], [])
+        lines[ops[i]["q"]] = [i]
 
     def rec(q, f, outs, ins, c, kind="c", lat=0.0, **kw):
         r, w = [], []
@@ -249,14 +282,16 @@ def rank_program(g, core, T, topo):
                 r.append(a[2])
             else:
                 w.append(a)
-        d = {"q": q, "f": [f] if kind == "c" and not isinstance(f, list) else f, "kind": kind, "c": c, "lat": lat,
-             "t": [(a[1], _mask(a), False) for a in r] + [(a[1], _mask(a), True) for a in w]}
+        ops.append({"q": q, "f": [f] if kind == "c" and not isinstance(f, list) else f, "kind": kind, "c": c, "lat": lat,
+                    "t": [(a[1], _mask(a), False) for a in r] + [(a[1], _mask(a), True) for a in w]})
         if keep[0]:
-            d["after"] = lines.get(q, [])
-            lines[q] = [len(ops)]
-        d.update(kw)
-        ops.append(d)
+            line(len(ops) - 1)
+        ops[-1].update(kw)
         return len(ops) - 1
+
+    def name(x, i):
+        named.setdefault(x, []).append(i)
+        ops[i]["nm"] = x
 
     def sc(x):
         return ap(x) if isinstance(x, tuple) else x
@@ -267,27 +302,26 @@ def rank_program(g, core, T, topo):
         if a[0] == "ind":
             return 0.05 + GAT * CYC * width(o)
         if b is not None:
-            return F2 * max(VFIX, VADD + CYC * width(o) * (1 if a[1] in _PS or b[1] in _PS else 2))
+            return max(VFIX, VADD + CYC * width(o) * (1 if a[1] in _PS or b[1] in _PS else 2))
         two = all(SCRATCH[x[1]][2] in (B16, F16, U16) for x in (o, a))
-        return F2 * max(VFIX, VADD + CYC * width(o) * (0.5 if two else 1))
+        return max(VFIX, VADD + CYC * width(o) * (0.5 if two else 1))
 
     def tt(o, a, b, op):
-        rec("v", lambda: g.vector.tensor_tensor(ap(o), ap(a), ap(b), op), [o], [a, b], vc(o, a, b))
+        return rec("v", lambda: g.vector.tensor_tensor(ap(o), ap(a), ap(b), op), [o], [a, b], vc(o, a, b))
 
     def ts(o, a, s1, op0, s2=None, op1=None):
         if op1 is None:
-            rec("v", lambda: g.vector.tensor_scalar(ap(o), ap(a), sc(s1), None, op0), [o], [a, s1], vc(o, a))
-        else:
-            rec("v", lambda: g.vector.tensor_scalar(ap(o), ap(a), sc(s1), sc(s2), op0, op1), [o], [a, s1, s2], vc(o, a))
+            return rec("v", lambda: g.vector.tensor_scalar(ap(o), ap(a), sc(s1), None, op0), [o], [a, s1], vc(o, a))
+        return rec("v", lambda: g.vector.tensor_scalar(ap(o), ap(a), sc(s1), sc(s2), op0, op1), [o], [a, s1, s2], vc(o, a))
 
     def cp(o, a):
-        rec("v", lambda: g.vector.tensor_copy(ap(o), ap(a)), [o], [a], vc(o, a))
+        return rec("v", lambda: g.vector.tensor_copy(ap(o), ap(a)), [o], [a], vc(o, a))
 
     def ms(o, c):
-        rec("v", lambda: g.vector.memset(ap(o), c), [o], [], vc(o, o))
+        return rec("v", lambda: g.vector.memset(ap(o), c), [o], [], vc(o, o))
 
     def scan(o, a, b, op0, op1):
-        rec("v", lambda: g.vector.tensor_tensor_scan(ap(o), ap(a), ap(b), 0.0, op0, op1), [o], [a, b], vc(o, a))
+        return rec("v", lambda: g.vector.tensor_tensor_scan(ap(o), ap(a), ap(b), 0.0, op0, op1), [o], [a, b], vc(o, a))
 
     def act(o, a, func=None, bias=None, scale=None):
         fn = F.Identity if func is None else func
@@ -296,36 +330,36 @@ def rank_program(g, core, T, topo):
             kw["bias"] = sc(bias)
         if scale is not None:
             kw["scale"] = sc(scale)
-        c = 0.065 + GAT * CYC * width(o) if a[0] == "ind" else F2 * (AFIX + CYC * width(o))
-        rec("a", lambda: g.scalar.activation(ap(o), ap(a), fn, **kw), [o], [a, bias, scale], c)
+        c = 0.065 + GAT * CYC * width(o) if a[0] == "ind" else AFIX + CYC * width(o)
+        return rec("a", lambda: g.scalar.activation(ap(o), ap(a), fn, **kw), [o], [a, bias, scale], c)
 
     def mms(calls):
-        rec("p", [lambda e=e: g.tensor.matmul(ap(e[0]), ap(e[1]), ap(e[2]), e[3], e[4]) for e in calls],
-            [e[0] for e in calls], [e[1] for e in calls] + [e[2] for e in calls],
-            sum(PEC * max(min(64, width(e[1])), width(e[2])) for e in calls))
+        return rec("p", [lambda e=e: g.tensor.matmul(ap(e[0]), ap(e[1]), ap(e[2]), e[3], e[4]) for e in calls],
+                   [e[0] for e in calls], [e[1] for e in calls] + [e[2] for e in calls],
+                   sum(PEC * max(min(64, width(e[1])), width(e[2])) for e in calls))
 
     def turn(pairs, ident):
-        rec("p", [lambda e=e: g.tensor.transpose(ap(e[0]), ap(e[1]), ap(whole(ident))) for e in pairs], [e[0] for e in pairs],
-            [e[1] for e in pairs] + [whole(ident)], len(pairs) * 128 * PEC * (4 if ident == "i32" else 1))
+        return rec("p", [lambda e=e: g.tensor.transpose(ap(e[0]), ap(e[1]), ap(whole(ident))) for e in pairs], [e[0] for e in pairs],
+                   [e[1] for e in pairs] + [whole(ident)], len(pairs) * 128 * PEC * (4 if ident == "i32" else 1))
 
     def mm(o, wt, mv, start, stop):
-        mms([(o, wt, mv, start, stop)])
+        return mms([(o, wt, mv, start, stop)])
 
     def iota(o, pat, base, cm):
-        c = F2 * (0.13 + 2 * CYC * width(o))
+        c = 0.13 + 2 * CYC * width(o)
         if SCRATCH[o[1]][2] == I32:
-            rec("g", lambda: g.iota(ap(o), pat, base, cm), [o], [], c)
-        else:
-            rec("g", lambda: g.iota(ap(o), pat, base, cm, allow_small_or_imprecise_dtypes=True), [o], [], c)
+            return rec("g", lambda: g.iota(ap(o), pat, base, cm), [o], [], c)
+        return rec("g", lambda: g.iota(ap(o), pat, base, cm, allow_small_or_imprecise_dtypes=True), [o], [], c)
 
-    def fill(name, lo, hi, c, step=1):
-        if GF:
-            iota(S(name, lo, hi, step), [[0, width(S(name, lo, hi, step))]], c, 0)
-        else:
-            ms(S(name, lo, hi, step), float(c))
+    def fill(buf, lo, hi, c):
+        return iota(S(buf, lo, hi), [[0, hi - lo]], c, 0)
 
     def gcopy(o, a):
-        rec("g", lambda: g.affine_select(ap(o), ap(a), [[0, width(o)]], A.is_ge, 0.0, 0, 0), [o], [a], 0.17 + 2 * CYC * width(o))
+        return rec("g", lambda: g.affine_select(ap(o), ap(a), [[0, width(o)]], A.is_ge, 0.0, 0, 0), [o], [a], 0.17 + 2 * CYC * width(o))
+
+    def diag(buf, x):
+        o, a = whole(buf), whole("nil")
+        name(buf, rec("g", lambda: g.affine_select(ap(o), ap(a), [[-1, 128]], A.not_equal, float(x), 0, 1), [o], [a], 0.17 + 256 * CYC))
 
     def dma(q, o, a, lat=2.5, behind=None):
         s = "d%d" % nd[0]
@@ -334,138 +368,141 @@ def rank_program(g, core, T, topo):
         rec(q, lambda: e.dma_start(sc(o), sc(a)), [o] if isinstance(o, tuple) else [], [a, behind], 0.05, kind="dma", lat=lat, sem=s)
 
     def conv(o, z, buf, base, n, stride, first=True, last=True):
-        mms([(o, S(z, 15 - r, 143 - r), S(buf, base + stride * r, base + stride * (r + 16 * n - 16) + 1, stride * 16),
-              first and r == 0, last and r == 15) for r in range(16)])
+        return mms([(o, S(z, 15 - r, 143 - r), S(buf, base + stride * r, base + stride * (r + 16 * n - 16) + 1, stride * 16),
+                     first and r == 0, last and r == 15) for r in range(16)])
+
+    def lanes_of(a, b):
+        return topo.engines(a, b)
 
     def C(i):
         return S("col", i, i + 1)
 
-    def whole(name):
-        return S(name, 0, _SB[name][0])
-
-    keep[0] = True
-    for o, a, lat in ((whole("wfs"), T.wf, 2.2), (whole("nms"), T.nm, 2.8), (whole("wvs"), T.wv, 3.1),
-                      (S("tV", 0, W), T.rv, 3 + LOAD)):
-        dma("s", o, a[:], lat)
-    keep[0] = False
-
-    iota(S("pcol", 0, 1), [[0, 1]], 0, 1)
-    iota(whole("jf"), [[1, L]], 0, 0)
-    iota(whole("jr"), [[0, 16], [1, 16]], 0, 0)
-    iota(whole("jq"), [[1, 16], [0, 16]], 0, 0)
-    iota(whole("l16"), [[16, 16]], 0, 1)
-    iota(whole("j4"), [[1, 36], [0, 4]], 0, 0)
-    act(whole("jb"), whole("jf"))
-    for b in range(0, JW, 1028):
-        iota(S("jw", b, b + 1028), [[1, 1028]], b - 2048, 0)
-    for i in range(16):
-        ms(S("ab", i, i + 1), float(WA[i] + 256 * WB[i]))
-    (cP, cR, cG, cJ, cA, cB, cT, cF, cSH, cKEEP, c4G, c40, cZ, cX, cY, cG16, cW, cAB, cX2, cAB2, cES, cL15) = range(22)
-    ts(S("pcol", 1, 2), S("pcol", 0, 1), 15, A.bitwise_and)
-    ts(S("pcol", 2, 3), S("pcol", 0, 1), 4, A.arith_shift_right)
-    ts(S("pcol", 3, 4), S("pcol", 0, 1), 3, A.bitwise_and)
-    cp(S("col", 0, 4), S("pcol", 0, 4))
-    for m in range(4):
-        fill("k32", 16 * m, 16 * m + 16, 32 * KP[m])
-    ms(whole("hc"), 0.0)
-    for m in range(4, 16):
-        if KP[m] % 2 == 0:
-            fill("hc", 16 * m - 64, 16 * m - 48, 2048)
-    ts(C(cZ), C(cG), 16.0, A.mult, 15.0, A.add)
-    ts(whole("ib"), S("jf", 0, 128), C(cP), A.is_equal)
-    ts(whole("e16"), S("jf", 0, 16), C(cR), A.is_equal)
-
     def R(i):
         return S("e16", i, i + 1)
 
-    ts(whole("z1"), S("jf", 0, 144), C(cZ), A.is_equal)
-    ts(C(cKEEP), C(cR), 11.0, A.is_le)
+    def whole(buf):
+        return S(buf, 0, _SB[buf][0])
+
+    keep[0] = True
+    for o, a, lat in ((whole("wfs"), T.wf, 2.2), (whole("nms"), T.nm, 2.6), (whole("wvs"), T.wv, 2.8),
+                      (S("tV", 0, W), T.rv, 2.6 + LOAD)):
+        dma("s", o, a[:], lat)
+    keep[0] = False
+
+    name("pcol", iota(S("pcol", 0, 1), [[0, 1]], 0, 1))
+    name("jf", iota(whole("jf"), [[1, 144]], 0, 0))
+    name("jr", iota(whole("jr"), [[0, 16], [1, 16]], 0, 0))
+    name("jq", iota(whole("jq"), [[1, 8], [0, 16]], 0, 0))
+    name("l16", iota(whole("l16"), [[16, 16]], 0, 1))
+    name("zero", iota(whole("j4"), [[1, 36], [0, 4]], 0, 0))
+    name("jb", iota(whole("jb"), [[1, L]], 0, 0))
+    name("mk", iota(whole("mk"), [[0, 16], [-4096, 16]], 61440, 0))
+    name("nil", fill("nil", 0, 128, 0))
+    for b in range(0, JW, 1028):
+        name("jw", iota(S("jw", b, b + 1028), [[1, 1028]], b - 2048, 0))
+    for buf, x in (("ib", 1), ("ibn", -1), ("iE", -2 * BIG), ("iS", 16 * BIG), ("iO", OFF), ("iOn", -OFF), ("i256", 256), ("i16", 16)):
+        diag(buf, x)
+    for i in range(16):
+        name("ab", ms(S("ab", i, i + 1), float(WA[i] + 256 * WB[i])))
+    (cP, cR, cG, cJ, cA, cB, cT, cF, cSH, cKEEP, c4G, c40, cZ, cX, cY, cG16, cW, cAB, cX2, cAB2, cES, cL15, cD, cD2) = range(24)
+    name("pc", ts(S("pcol", 1, 2), S("pcol", 0, 1), 15, A.bitwise_and))
+    name("pc", ts(S("pcol", 2, 3), S("pcol", 0, 1), 4, A.arith_shift_right))
+    name("pc", ts(S("pcol", 3, 4), S("pcol", 0, 1), 3, A.bitwise_and))
+    name("pc", cp(S("col", 0, 4), S("pcol", 0, 4)))
+    for m in range(5):
+        name("k32", fill("k32", 16 * m, 16 * m + 16, 1 + 32 * ([0] + KP)[m]))
+    assert all(KP[m] % 2 == m % 2 for m in range(4, 16))
+    name("hc", iota(whole("hc"), [[0, 6], [-2048, 2], [0, 16]], 2048, 0))
+    name("cZ", ts(C(cZ), C(cG), 16.0, A.mult, 15.0, A.add))
+    name("cY", ts(C(cY), C(cR), 2.0, A.mult, 1.0, A.add))
+    name("e16", ts(whole("e16"), S("jf", 0, 16), C(cR), A.is_equal))
+    name("z1", ts(whole("z1"), whole("jf"), C(cZ), A.is_equal))
+    name("keep", ts(C(cKEEP), C(cR), 4.0, A.is_le, EPS, A.mult))
+    name("cW", ts(C(cW), R(13), EPS, A.mult))
     ts(whole("dm"), whole("jr"), C(cR), A.is_equal)
-    ts(whole("ones"), S("jq", 0, 128), C(cG), A.is_equal)
-    ts(whole("nmb"), whole("nms"), C(cKEEP), A.mult, R(13), A.add)
-    dma("s", S("tF", 0, W), T.rf[:], 2 + LOAD, S("nmb", 0, 1))
-    dma("s", S("tG", 0, W), T.rg[:], 3 + LOAD, S("tF", 0, 1))
-    act(whole("nm0"), whole("nmb"), F.Relu, 0.5, -1.0)
-    tt(whole("ab2"), whole("ab"), whole("e16"), A.mult)
-    rec("v", lambda: g.vector.tensor_reduce(ap(C(cAB)), ap(whole("ab2")), AxisListType.X, A.add), [C(cAB)], [whole("ab2")], 0.07)
-    tt(C(cW), R(13), R(14), A.add)
-    ts(whole("rep"), S("jf", 0, 16), 0.0, A.mult, C(cR), A.add)
-    cp(whole("repc"), S("jf", 0, 16))
-    ts(whole("z0"), whole("z1"), R(0), A.mult, 2.0, A.mult)
-    mm(S("pB", 0, L), whole("ones"), whole("wfs"), True, True)
-    mms([(S("pC", 0, L), whole("ib"), whole("nmb"), True, False),
-         (S("pC", 0, L), S("z0", 0, 128), whole("nmb"), False, False),
-         (S("pC", 0, L), S("z0", 1, 129), whole("nmb"), False, False),
-         (S("pC", 0, L), S("z0", 3, 131), whole("nm0"), False, True)])
-    cp(S("pcol", 4, 5), C(cAB))
-    act(whole("thf"), S("pB", 0, L), F.Sign)
-    ts(S("pcol", 5, 6), S("pcol", 4, 5), 255, A.bitwise_and)
-    ts(S("pcol", 6, 7), S("pcol", 4, 5), 8, A.arith_shift_right)
-    tt(S("lnd0", 3, 1024, 4), S("pC", 0, L), whole("thf"), A.mult)
-    for j, a in enumerate(("wfs", "wfs", "wvs")):
-        act(S("lnd0", j, 1024, 4), whole(a))
-    cp(S("col", cA, cA + 2), S("pcol", 5, 7))
-    cp(whole("ih"), whole("ib"))
-    ts(whole("zw"), whole("z1"), C(cW), A.mult)
-    ts(whole("zA"), whole("z1"), C(cA), A.mult)
-    ts(C(cF), R(12), -256.0, A.mult)
-    tt(C(cY), R(12), R(13), A.add)
-    ts(C(cX), R(13), -256.0, A.mult, R(1), A.add)
-    tt(C(cT), C(cX), C(cF), A.subtract)
-    act(whole("wn"), whole("ones"), scale=C(cF))
-    act(whole("zY"), whole("z1"), scale=C(cY))
-    act(whole("zX"), whole("z1"), scale=C(cT))
-    fill("c13", 0, 192, 13)
-    fill("c13", 192, 320, 2)
-    fill("c13", 320, 384, 18)
-    act(whole("c1"), S("jf", 0, 192), None, -BIG / 2, 0.0)
-    act(S("cE", 0, 64), S("jf", 0, 64), None, -25 * BIG, 0.0)
-    act(S("cE", 64, 128), S("jf", 0, 64), None, -BIG, 0.0)
-    act(whole("c2"), whole("jq"), None, 15.0, -1.0)
-    for name, of, x in (("i3", "ib", 3.0), ("i18", "ib", -18.0), ("ineg", "ib", -BIG), ("iE", "ib", -6 * BIG), ("iS", "ib", 18 * BIG),
-                        ("zn", "z1", -1.0), ("zn2", "z1", -2.0), ("z16", "z1", 16.0), ("zE", "z1", 2 * BIG), ("zS", "z1", BIG), ("z65", "z1", 8192.0),
-                        ("i32", "ib", 1.0), ("iO", "ib", float(OFF)), ("iOn", "ib", float(-OFF)), ("i256", "ib", 256.0),
-                        ("i256n", "ib", -256.0), ("i4k", "ib", 4096.0), ("ibn", "ib", -1.0), ("iZG", "ib", float(ZG)), ("iZV", "ib", float(ZV))):
-        if name in ("i32", "iZG", "iZV") + ONS:
-            act(whole(name), whole(of), scale=x)
-        else:
-            ts(whole(name), whole(of), x, A.mult)
+    name("ones", ts(whole("ones"), whole("jq"), C(cG), A.is_equal))
+    name("nmb", ts(whole("nmb"), whole("nms"), C(cKEEP), A.mult, C(cW), A.add))
+    dma("s", S("tF", 0, W), T.rf[:], 2.4 + LOAD, S("nmb", 0, 1))
+    dma("s", S("tG", 0, W), T.rg[:], 2 + LOAD, S("tF", 0, 1))
+    name("nm0", act(whole("nm0"), whole("nmb"), F.Relu, EPS * EPS / 2, -1.0))
+    name("A", tt(whole("ab2"), whole("ab"), whole("e16"), A.mult))
+    name("A", rec("v", lambda: g.vector.tensor_reduce(ap(C(cAB)), ap(whole("ab2")), AxisListType.X, A.add), [C(cAB)],
+                  [whole("ab2")], 0.07))
+    name("A", cp(S("pcol", 4, 5), C(cAB)))
+    name("A", ts(S("pcol", 5, 6), S("pcol", 4, 5), 255, A.bitwise_and))
+    name("A", ts(S("pcol", 6, 7), S("pcol", 4, 5), 8, A.arith_shift_right))
+    name("A", cp(S("col", cA, cA + 2), S("pcol", 5, 7)))
+    name("repn", ts(whole("repn"), S("jf", 0, 16), 0.0, A.mult, C(cY), A.add))
+    name("rep", ts(whole("rep"), S("jf", 0, 16), 0.0, A.mult, C(cR), A.add))
+    name("repc", cp(whole("repc"), S("jf", 0, 16)))
+    name("z0", ts(whole("z0"), whole("z1"), R(0), A.mult, 2 / EPS, A.mult))
+    name("z0n", ts(whole("z0n"), whole("z1"), R(0), A.mult, -4 / EPS, A.mult))
+    name("there", mm(S("pE0", 0, L), whole("ones"), whole("wfs"), True, True))
+    name("init", mms([(S("pC", 0, L), whole("ib"), whole("nmb"), True, False),
+                      (S("pC", 0, L), S("z0", 5, 133), whole("nmb"), False, False),
+                      (S("pC", 0, L), S("z0n", 7, 135), whole("nmb"), False, False),
+                      (S("pC", 0, L), S("z0", 1, 129), whole("nm0"), False, True)]))
+    name("thf", act(whole("thf"), S("pE0", 0, L), F.Sign))
+    name("aux", tt(S("lnd0", 3, 1024, 4), S("pC", 0, L), whole("thf"), A.mult))
+    name("x0", act(S("lnd0", 0, 1024, 4), whole("wfs")))
+    name("yv", cp(S("lnd0", 1, 1024, 4), whole("wfs")))
+    name("yv", cp(S("lnd0", 2, 1024, 4), whole("wvs")))
+    name("ih", cp(whole("ih"), whole("ib")))
+    name("zA", ts(whole("zA"), whole("z1"), C(cA), A.mult))
+    name("cF", ts(C(cF), R(14), -256.0 / EPS, A.mult))
+    name("cX", ts(C(cX), R(13), -256.0, A.mult, R(1), A.add))
+    name("cX", ts(C(cES), R(14), 512.0, A.mult, C(cX), A.add))
+    name("cX", ts(C(cT), C(cES), 1 / EPS, A.mult))
+    name("wn", act(whole("wn"), whole("ones"), scale=C(cF)))
+    name("zX", act(whole("zX"), whole("z1"), scale=C(cT)))
+    name("c13", fill("c13", 0, 192, -13))
+    name("c13", fill("c13", 192, 576, -2))
+    for k in range(2):
+        for c in ONV[k]:
+            name("c13", fill("c13", 192 + 192 * k + 64 * c, 256 + 192 * k + 64 * c, -18))
+    name("c1", fill("c1", 0, 320, 4))
+    name("c1", iota(S("c1", 1, 320, 5), [[0, 64]], 200, 0))
+    name("cE", fill("cE", 0, 64, 16))
+    name("c2", iota(S("c2", 0, 320), [[-1, 4], [0, 16], [-4, 5]], 23, 0))
+    name("c2", iota(S("c2", 320, 384), [[-1, 4], [0, 16]], 3, 0))
+    name("kt", ms(whole("kt"), 1e29))
+    name("kt", ms(S("kt", 0, 320, 5), -1e29))
+    name("z16", act(whole("z16"), whole("z1"), scale=16.0))
+    name("zE", act(whole("zE"), whole("z1"), scale=2 * BIG))
     for m in range(4, 16):
-        ts(S("dk", 128 * m - 512, 128 * m - 384), whole("ib"), float(KP[m]), A.mult)
-    ts(C(cL15), C(cR), 16.0, A.mult, 15.0, A.add)
-    tt(C(cX2), R(0), R(14), A.add)
-    tt(C(cAB2), C(cP), C(cKEEP), A.subtract)
-    ts(C(cG16), C(cG), 16.0, A.mult)
+        name("dk", ts(S("dk", 128 * m - 512, 128 * m - 384), whole("ib"), float(KP[m]), A.mult))
+    name("cL", ts(C(cL15), C(cR), 16.0, A.mult, 15.0, A.add))
+    ts(C(cX2), C(cR), 2.0, A.is_ge, C(cKEEP), A.mult)
+    ts(C(cAB2), C(cX2), -257.0 / EPS, A.mult, C(cP), A.add)
+    tt(C(cD), R(0), R(13), A.add)
+    name("lo16", ts(C(cG16), C(cG), 16.0, A.mult))
     ts(C(c4G), C(cG), 4.0, A.mult, 3.0, A.add)
     ts(C(c40), R(0), 4.0, A.mult)
-    ts(C(cSH), C(cX2), -256.0, A.mult, C(cAB2), A.add)
-    ts(whole("lo16"), whole("l16"), C(cG16), A.subtract)
-    act(whole("zB"), whole("z1"), scale=C(cB))
+    ts(C(cD2), C(cD), -256.0, A.mult, 256.0, A.add)
+    tt(C(cSH), C(cD2), C(cAB2), A.add)
+    name("eH", ts(whole("lo16"), whole("l16"), C(cG16), A.subtract))
+    name("zB", act(whole("zB"), whole("z1"), scale=C(cB)))
     ts(whole("shf"), S("jf", 0, 128), C(cSH), A.is_equal)
-    for name, i in (("zr1", 1), ("zr15", 15), ("zr13", 13)):
-        act(whole(name), whole("z1"), scale=R(i))
-    mms([(S("pK0", b, b + 128), whole("ib"), x, b == 0 and i == 0, b == 128 and i == 2)
-         for b, xs in ((0, (whole("shf"), S("zr1", 1, 129), S("zr1", 1, 129))), (128, (whole("shf"), S("zr15", 1, 129), S("zr13", 3, 131))))
-         for i, x in enumerate(xs)])
-    act(whole("wsh"), S("pK0", 0, L))
-    for b, (s0, b0) in enumerate(((4, LC), (4, LC + 1), (0, NC), (4, 2 * L + 3), (4, LV + 2))):
-        act(S("own", 16 * b, 16 * b + 16), whole("lo16"), None, float(b0), float(s0))
-        ts(S("oH", 16 * b, 16 * b + 16), whole("lo16"), float(s0), A.mult, float(b0 % 256), A.add)
-        fill("oB", 16 * b, 16 * b + 16, b0 - b0 % 256)
-    act(S("c0", 0, 16), S("own", 0, 16))
-    act(S("c0", 16, 32), S("own", 64, 80))
-    ms(S("eH", 0, 48), 0.0)
-    ms(S("eH", 80, 96), 1.0)
+    ts(whole("zr1"), whole("z1"), R(1), A.mult, 2 / EPS, A.mult)
+    name("zr13", act(whole("zr13"), whole("z1"), scale=R(13)))
+    name("wshp", mms([(S("pC", b, b + 128), whole(w), x, b == 0 and i == 0, b == 128 and i == 3)
+                      for b, xs in ((0, (("ib", whole("shf")), ("ib", S("zr1", 5, 133)), ("ibn", S("zr1", 7, 135)), ("ibn", S("zr1", 7, 135)))),
+                                    (128, (("ib", whole("shf")), ("ib", S("z0", 5, 133)), ("ib", S("z0n", 7, 135)), ("ib", S("zr13", 1, 129)))))
+                      for i, (w, x) in enumerate(xs)]))
+    name("wsh", act(whole("wsh"), S("pC", 0, L)))
+    mine = ((4, LC), (4, LC + 1), (0, NC), (4, 2 * L + 3), (4, LV + 2))
+    for b, (s0, b0) in enumerate(mine):
+        ts(S("oH", 16 * b, 16 * b + 16), whole("lo16"), float(s0), A.mult, float(b0 % 256 + (b == 0)), A.add)
+        name("e", fill("oB", 16 * b, 16 * b + 16, b0 - b0 % 256))
+    name("eH", ms(S("eH", 0, 48), 0.0))
     for b in (3, 4):
-        cp(S("eH", 16 * b, 16 * b + 16), whole("lo16"))
-    for name, lo, hi, x in (("eB", 0, 48, -61440), ("eB", 48, 64, 0), ("eB", 64, 80, 3840), ("eB", 80, 96, 0),
-                            ("eC", 0, 16, 0), ("eC", 16, 48, OFF), ("eC", 48, 80, 0), ("eC", 80, 96, -OFF)):
-        fill(name, lo, hi, x)
-    ts(S("l15", 0, 3), S("jf", 0, 3), 0.0, A.mult, C(cL15), A.add)
-    ms(S("l15", 3, 6), 256)
-    ts(whole("lhk"), S("jf", 0, 16), C(cL15), A.subtract, 255.0, A.add)
-    act(whole("mk"), whole("jr"), None, 61440.0, -4096.0)
-    fill("ksel", L, L + 16, 0)
+        name("eH", cp(S("eH", 16 * b, 16 * b + 16), whole("lo16")))
+    for buf, lo, hi, x in (("eB", 0, 48, -61440), ("eB", 48, 64, 0), ("eB", 64, 80, 3840),
+                           ("eC", 0, 16, 0), ("eC", 16, 48, OFF), ("eC", 48, 80, 0), ("ksel", L, L + 16, 0)):
+        name("e", fill(buf, lo, hi, x))
+    name("l15", ts(S("l15", 0, 3), S("jf", 0, 3), 0.0, A.mult, C(cL15), A.add))
+    name("l15", ms(S("l15", 3, 6), 256))
+    name("lhk", ts(whole("lhk"), S("jf", 0, 16), C(cL15), A.subtract, 255.0, A.add))
     ts(whole("z4"), whole("j4"), C(c4G), A.is_equal, C(c40), A.mult)
     ts(whole("uget"), S("jr", 0, 128), C(cR), A.is_le, -1.0, A.mult)
     ts(whole("msk"), S("jr", 0, 64), 0.0, A.is_gt)
@@ -474,66 +511,43 @@ def rank_program(g, core, T, topo):
         ts(S("cst", 16 * d, 16 * d + 16), whole("lo16"), -1.0, A.mult, float(256 * d - 1024), A.add)
     ts(whole("dmp"), whole("lo16"), 1024.0, A.add)
     act(whole("cd"), whole("lo16"), None, 2048.0)
-    for name, lo, hi in (("tG", W, LC), ("tG", ZG, WGN), ("lo", ZV, LON), ("pre", 1024, 1040)):
-        fill(name, lo, hi, 0)
-    fill("jm", W, JW, 200)
+    for buf, lo, hi in (("tG", W, LC), ("tG", ZG, WGN), ("lo", LE, LON), ("pre", 1024, 1040)):
+        name("zero", fill(buf, lo, hi, 0))
+    name("zero", fill("jm", W, JW, 200))
     ts(whole("sel0"), S("jf", 0, 8), C(cG), A.is_equal, R(0), A.mult)
-    ts(whole("blk"), S("jf", 0, 8), C(cG), A.is_equal, 256.0, A.mult)
 
     gathered = []
     for t in range(RO):
         lnd = "lnd%d" % t
         last = t == RO - 1
-        conv(S("pA", 0, 16), "zA", lnd, 0, 16, 4)
-        conv(S("pB", 0, 16), "zw", lnd, 3, 16, 4)
-        mms([(S("pK1", 0, L), whole("ib"), S(lnd, 0, 1024, 4), True, False), (S("pK1", 0, L), whole("wn"), S(lnd, 3, 1024, 4), False, True)])
-        if CV:
-            ts(S("cmp", 0, L), S("pK1", 0, L), 0.0, A.max)
-        else:
-            act(S("cmp", 0, L), S("pK1", 0, L), F.Relu)
-        cp(whole("ui"), S("pA", 0, 16))
-        ts(whole("u"), whole("ui"), 4095, A.bitwise_and)
-        tt(S("uk", 0, 64), IND(whole("u"), S("rep", 0, 4)), S("k32", 0, 64), A.mult)
-        ts(whole("uh"), whole("u"), -2048.0, A.add)
-        tt(whole("prod"), S("pB", 0, 16), whole("u"), A.mult)
-        tt(S("hi", 0, 64), IND(whole("prod"), S("rep", 0, 4)), S("uk", 0, 64), A.add)
-        ts(S("hi", 0, 64), S("hi", 0, 64), 5, A.arith_shift_right, 4095, A.bitwise_and)
-        cp(S("h16", 0, 64), S("hi", 0, 64))
-        ts(whole("cc"), whole("prod"), 5, A.arith_shift_right, 4095, A.bitwise_and)
-        ts(whole("ch"), IND(whole("cc"), S("rep", 0, 4)), -2048.0, A.add)
-        mms([(S("pB", 0, 192), whole("ib"), whole("hc"), True, False)] +
-            [(S("pB", 16 * m, 16 * m + 16), S("dk", 128 * m, 128 * m + 128), whole("uh"), False, False) for m in range(12)])
-        mms([(S("pB", 64 * i, 64 * i + 64), whole("ih"), whole("ch"), False, i == 2) for i in range(3)])
-        turn([(S("pT", 128 * h, 128 * h + 128), S(lnd, 512 * h + 2, 512 * h + 512, 4)) for h in range(2)], "ib")
-        (cp if VT else act)(whole("vt"), S("pT", 0, L))
-        turn([(S("pV", 128 * i, 128 * i + 128), S("vt", 128 * (i % 2), 128 * (i % 2) + 128)) for i in range(8)], "ib")
-        kind = S("pK1" if last else "pC", 0, 16)
-        conv(kind, "zY", lnd, 3, 16, 4)
-        (gcopy if GC & 2 else cp if GC & 4 else act)(S("cmp", L, 2 * L), S("cmp", 0, L))
-        if t > 0:
-            iota(S("jm", 1024 * t - 1024, 1024 * t), [[0, 8], [1, 128]], 0, 0)
-            ops[-1]["after"] = [len(ops) - 2]
+        onv = ONV[min(t, 1)]
+
+        def hashes():
+            if t == 0:
+                conv(S("pA", 0, 32, 2), "zA", "wfs", 0, 16, 1, True, False)
+                conv(S("pA", 1, 32, 2), "z0", "nmb", 0, 16, 1, False, True)
+            else:
+                mms([(S("pA", 0, 32), S("zA", 15 - r, 143 - r), BOX(lnd, [64 * c + 4 * r + j for c in range(16) for j in (0, 3)]),
+                      r == 0, r == 15) for r in range(16)])
+
+        def later():
+            mms([(S("pB", 0, 192), whole("ib"), whole("hc"), True, False)] +
+                [(S("pB", 16 * m, 16 * m + 16), S("dk", 128 * m, 128 * m + 128), whole("uh"), False, False) for m in range(12)])
+            mms([(S("pB", 64 * i, 64 * i + 64), whole("ih"), whole("ch"), False, i == 2) for i in range(3)])
+
+        kind = S("pA", 32, 48)
 
         def kinds():
-            ts(S("zf4", 0, 16), kind, 1.0, A.not_equal)
-            ts(whole("fin"), kind, 2.0, A.is_equal)
-
-        def kinds4():
-            cp(S("zf4", 16, 64), IND(S("zf4", 0, 16), S("rep", 0, 3)))
+            ts(S("zf4", 0, 16), kind, 0.0, A.is_ge, 3.0, A.mult)
+            ts(whole("fin"), kind, 256.0, A.is_ge)
 
         def names():
             if not last:
                 mms([(S("pC", L * i, L * i + L), S("wsh", 128 * i, 128 * i + 128), S(lnd, 3, 1024, 4), i == 0, i == 1) for i in range(2)])
-                conv(S("pA", 0, 16), "zX", lnd, 3, 16, 4)
-
-        def shifted():
-            if not last:
-                act(whole("nf"), S("pA", 0, 16), F.Relu, -255.0, -1.0)
-                act(S("nmw", 0, 2 * L), S("pC", 0, 2 * L))
 
         behind = S("tF", 0, 1) if t == 0 else None
         dma("s", S("tG", LC, ZG), whole(lnd), 3.5, behind)
-        dma("s", S("lo", LV, ZV), whole(lnd), 4.5, behind)
+        dma("s", S("lo", LV, LE), whole(lnd), 4.5, behind)
         if not last:
             dma("s", S("nmw", 2 * L, 6 * L), whole(lnd), 5.5, behind)
 
@@ -541,25 +555,28 @@ def rank_program(g, core, T, topo):
             act(S("vg", 1024 * c, 1024 * c + 1024), IND(S("tV", 0, W), S("h16", 64 * c, 64 * c + 64)))
 
         def sgn(c):
-            if c == 2:
-                return ts(S("sg", 2048, 3072), S("lo", 2048, 3072), float(TAU[t]), A.is_gt)
-            act(S("sg", 1024 * c, 1024 * c + 1024), S("lo", 1024 * c, 1024 * c + 1024), F.Sign, -(TAU[t] + 0.5))
+            o, a = S("sg", 1024 * c, 1024 * c + 1024), S("lo", 1024 * c, 1024 * c + 1024)
+            if c in onv:
+                ts(o, a, float(TAU[t]), A.is_gt, 2.0, A.mult)
+            else:
+                act(o, a, F.Sign, -(TAU[t] + 0.5))
 
-        def gf(c, m0=0, m1=4, n=2):
-            for m in range(4 * c + m0, 4 * c + m1, n):
-                tt(S("eqf", L * m, L * (m + n)), IND(S("tF", 0, W), S("h16", 16 * m, 16 * (m + n))), S("cmp", 0, L * n), A.is_equal)
+        def gf(c, m, n):
+            m += 4 * c
+            tt(S("eqf", L * m, L * (m + n)), IND(S("tF", 0, W), S("h16", 16 * m, 16 * (m + n))), S("cmp", 0, L * n), A.is_equal)
 
         def mn(c):
-            for b in range(1024 * c, 1024 * c + 1024, WIDE):
-                tt(S("lo", b, b + WIDE), S("vg", b, b + WIDE), S("pV", 0, WIDE), A.min)
-                ops[-1]["c"] *= MNX
+            b = 1024 * c
+            ops[tt(S("lo", b, b + 1024), S("vg", b, b + 1024), S("pV", 0, 1024), A.min)]["c"] *= MNX
 
-        at = [(("pE0", 64 * c), ("pE0", 192 + 64 * c), ("pK0", 64 * c)) for c in range(3)] + [(("pB", 0), ("pK1", 64), ("pK1", 0))]
+        five = [S("pK0", j, 320, 5) for j in range(5)]
+        at = [(S("pE0", 64 * c, 64 * c + 64), S("pE0", 192 + 64 * c, 256 + 64 * c), five[2 + c]) for c in range(3)]
+        at.append((five[1], S("pK1", 64, 128), S("pK1", 0, 64)))
 
-        def sums(kind, c, stop=False):
-            i = "ESK".index(kind)
-            z = "z16" if i == 2 else "zn2" if (i, c) == (1, 2) else "zn" if c < 3 else ("zE", "zS")[i]
-            conv(S(at[c][i][0], at[c][i][1], at[c][i][1] + 64), z, ("eqf", "sg", "lo")[i], 1024 * c, 64, 1, False, stop)
+        def sums(what, c, stop=False):
+            i = "ESK".index(what)
+            z = "z16" if i == 2 else "z1" if c < 3 else "zE"
+            conv(at[c][i], z, ("eqf", "sg", "lo")[i], 1024 * c, 64, 1, False, stop)
 
         def consts(bank, parts):
             mms([(S(bank, a, a + width(x)), whole(w), x, i == 0, False) for i, (a, w, x) in enumerate(parts)])
@@ -567,45 +584,88 @@ def rank_program(g, core, T, topo):
         def bars(bank, a, n, w):
             mms([(S(bank, b, b + 64), whole(w), whole("zf4"), False, False) for b in range(a, a + n, 64)])
 
-        rest = (lambda: cp(whole("hr"), S("pB", 0, 192)), lambda: ts(S("hi", 64, L), whole("hr"), 4095, A.bitwise_and),
-                lambda: cp(S("h16", 64, L), S("hi", 64, L)))
-
         def opening():
-            consts("pE0", [(0, "ib", whole("c13"))])
-            consts("pK0", [(0, "ib", whole("c1")), (0, "ib", S("c2", 0, 192))])
+            b = 192 + 192 * min(t, 1)
+            consts("pE0", [(0, "ib", S("c13", 0, 192)), (192, "ib", S("c13", b, b + 192))])
+            consts("pK0", [(0, "iOn", whole("c1")), (0, "ib", S("c2", 0, 320))])
 
         def flags():
-            consts("pK1", [(0, "ib", S("c1", 0, 64)), (0, "ib", S("c2", 192, L)), (64, "ib", S("cE", 64, 128))])
-            consts("pB", [(0, "ib", S("cE", 0, 64))])
-            for e in (("pE0", 0, 192, "i3"), ("pE0", 192, 192, "i18"), ("pK1", 64, 64, "iS"), ("pB", 0, 64, "iE")):
+            consts("pK1", [(0, "iOn", S("c1", 0, 320, 5)), (0, "ib", S("c2", 320, 384)), (64, "iOn", whole("cE"))])
+            for e in (("pE0", 0, 192, "ibn"), ("pE0", 192, 192, "i256"), ("pK1", 64, 64, "iS")):
                 bars(*e)
+            mm(five[1], whole("iE"), whole("zf4"), False, False)
+
+        def lists(some, stop=False):
+            mms([(S("pA", 16 * b, 16 * b + 16), whole(w), S(x, 0, 16), False, stop and i == len(some) - 1)
+                 for i, (b, w, x) in enumerate(some)])
+
+        def parts():
+            consts("pA", [(0, "ih", whole("eH")), (0, "ib", whole("eB")), (0, "ib", whole("eC"))])
+            mm(S("pA", 48, 80), whole("iO"), S("zf4", 0, 32), False, False)
+            lists([(0, "iO", "zf4"), (2, "iOn", "fin")] + ([] if last else [(0, "iO", "nf"), (1, "iOn", "nf"), (3, "i256", "nf")]))
 
         queues = [o.split() for o in (ORDER0 if t == 0 else ORDER)]
-        ends = ([x for x in queues[2] if x[0] in "ES" and x[1] != "3"][-1], [x for x in queues[2] if x in ("K3", "S3")][-1], "E3")
-        step = {"p0": (lambda: gf(0, 0, 1, 1), []), "p1": (lambda: gf(0, 1, 2, 1), []), "r0": (rest[0], []), "r1": (rest[1], []),
-                "rest": (rest[2], []), "open": (opening, []),
-                "kind": (kinds, []), "kinds": (kinds4, []), "names": (names, ["kinds"]), "shift": (shifted, ["names"]),
-                "ks": (lambda: (cp if KV & 1 else act)(whole("ks"), S("pK1", 64, 128)), [ends[1]]),
-                "ka": (lambda: (cp if KV & 2 else act)(whole("ka"), S("pK0", 0, 64)), ["pen"]),
-                "tab": (lambda: tt(whole("ktab"), IND(whole("hi"), whole("lhk")), whole("mk"), A.add), ["rest"]),
-                "flags": (flags, ["rest", "kinds"]), "relu": (lambda: act(whole("pen"), S("pE0", 0, 384), F.Relu), [ends[0]]),
-                "pen": (lambda: mms([(S("pK0", 0, 192), whole("ineg"), S("pen", 192 * i, 192 * i + 192), False, i == 1)
-                                     for i in range(2)]), ["relu"])}
+        sm = [x for x in queues[2] if len(x) == 2 and x[1].isdigit()]
+        ends = ([x for x in sm if x[0] in "ES" and x[1] != "3"][-1], [x for x in sm if x in ("K3", "S3")][-1],
+                [x for x in queues[2] if x in ("pen", "E3")][-1])
+        step = {
+            "H": (hashes, []), "ui": (lambda: cp(whole("ui"), S("pA", 0, 32)), ["H"]),
+            "u": (lambda: ts(whole("u"), S("ui", 0, 32, 2), 4095, A.bitwise_and), []),
+            "w": (lambda: tt(whole("uk"), IND(whole("ui"), S("repn", 0, 5)), whole("k32"), A.add), []),
+            "t": (lambda: tt(S("hi", 0, 80), IND(whole("u"), S("rep", 0, 5)), whole("uk"), A.mult), []),
+            "uh": (lambda: ts(whole("uh"), whole("u"), -2048.0, A.add), []),
+            "sh": (lambda: ts(S("hi", 0, 80), S("hi", 0, 80), 5, A.arith_shift_right, 4095, A.bitwise_and), []),
+            "h0": (lambda: cp(S("h16", 0, 64), S("hi", 16, 80)), []),
+            "ch": (lambda: ts(whole("ch"), IND(S("hi", 0, 16), S("rep", 0, 4)), -2048.0, A.add), []),
+            "dk": (later, ["ch"]), "r0": (lambda: cp(whole("hr"), S("pB", 0, 192)), ["dk"]),
+            "r1": (lambda: ts(S("hi", 80, L + 16), whole("hr"), 4095, A.bitwise_and), []),
+            "rest": (lambda: cp(S("h16", 64, L), S("hi", 80, L + 16)), []),
+            "C": (lambda: mms([(S("pK1", 0, L), whole("ib"), S(lnd, 0, 1024, 4), True, False),
+                               (S("pK1", 0, L), whole("wn"), S(lnd, 3, 1024, 4), False, True)]), []),
+            "cmp": (lambda: act(S("cmp", 0, L), S("pK1", 0, L), F.Relu), ["C"]),
+            "cmp2": (lambda: gcopy(S("cmp", L, 2 * L), S("cmp", 0, L)), ["cmp"]),
+            "jm": (lambda: iota(S("jm", 1024 * t - 1024, 1024 * t), [[0, 8], [1, 128]], 0, 0), []),
+            "T": (lambda: turn([(S("pT", 128 * h, 128 * h + 128), S("wvs", 128 * h, 128 * h + 128) if t == 0 else
+                                 S(lnd, 512 * h + 2, 512 * h + 512, 4)) for h in range(2)], "ib"), []),
+            "vt": (lambda: act(whole("vt"), S("pT", 0, L)), ["T"]),
+            "V8": (lambda: turn([(S("pV", 128 * i, 128 * i + 128), S("vt", 128 * (i % 2), 128 * (i % 2) + 128))
+                                 for i in range(8)], "ib"), ["vt"]),
+            "X": (lambda: conv(kind, "zX", lnd, 3, 16, 4), ["ui"]), "kind": (kinds, ["X"]),
+            "kinds": (lambda: cp(S("zf4", 16, 64), IND(S("zf4", 0, 16), S("rep", 0, 3))), []),
+            "open": (opening, []), "flags": (flags, ["kinds", "cmp2", "open"]), "names": (names, []),
+            "shift": (lambda: last or act(S("nmw", 0, 2 * L), S("pC", 0, 2 * L)), ["names"]),
+            "nf": (lambda: last or act(whole("nf"), kind, F.Relu, -255.0, -1.0), ["X"]),
+            "p0": (lambda: gf(0, 0, 1), ["cmp"]), "p1": (lambda: gf(0, 1, 1), []),
+            "relu": (lambda: act(whole("pen"), S("pE0", 0, 384), F.Relu, None, -BIG), [ends[0]]),
+            "pen": (lambda: mms([(five[2 + i % 3], whole("ibn"), S("pen", 64 * i, 64 * i + 64), False, ends[2] == "pen" and i == 5)
+                                 for i in range(6)]), ["relu"]),
+            "parts": (parts, ["kinds", "nf"]),
+            "ks": (lambda: act(whole("ks"), S("pK1", 64, 128)), [ends[1]]),
+            "tab": (lambda: tt(whole("ktab"), IND(S("hi", 16, L + 16), whole("lhk")), whole("mk"), A.add), ["rest"])}
         for c in range(4):
-            step["a%d" % c] = (lambda c=c: gf(c, 0, 2), ["rest"])
-            step["b%d" % c] = (lambda c=c: gf(c, 2, 4), ["rest"])
-            step["g%d" % c] = (lambda c=c: gv(c), ["rest"] if c else [])
-            step["m%d" % c] = (lambda c=c: mn(c), ["g%d" % c])
+            step["a%d" % c] = (lambda c=c: gf(c, 0, 2), ["rest", "cmp2"])
+            step["b%d" % c] = (lambda c=c: gf(c, 2, 2), ["rest", "cmp2"])
+            step["g%d" % c] = (lambda c=c: gv(c), ["rest"] if c else ["h0"])
+            step["m%d" % c] = (lambda c=c: mn(c), ["g%d" % c, "V8"])
             step["s%d" % c] = (lambda c=c: sgn(c), ["m%d" % c])
-            for x, y in (("E", "b"), ("K", "m"), ("S", "s")):
-                step["%s%d" % (x, c)] = (lambda c=c, x=x: sums(x, c, "%s%d" % (x, c) in ends), ["%s%d" % (y, c)])
+            for x, y in (("E", "ab"), ("K", "m"), ("S", "s")):
+                step["%s%d" % (x, c)] = (lambda c=c, x=x: sums(x, c, "%s%d" % (x, c) in ends),
+                                         [e for e in ("%s%d" % (z, c) for z in y) if e in queues[0] + queues[1]])
         keep[0] = True
         done = []
         while any(queues):
-            for o in queues:
-                while o and all(x in done for x in step[o[0]][1]):
-                    step[o[0]][0]()
-                    done.append(o.pop(0))
+            for k, o in enumerate(queues):
+                while o:
+                    x = o[0].rstrip("*")
+                    if named.get(x) and ops[named[x][0]]["q"] == "vapg"[k]:
+                        for i in range(len(named[x]) if x != o[0] else 1):
+                            line(named[x].pop(0))
+                    elif all(y in done for y in step[x][1]):
+                        step[x][0]()
+                        done.append(x)
+                    else:
+                        break
+                    o.pop(0)
         if 0 < t < RO - 1:
             cp(IND(S("tG", 0, LC), S("o16", GP, 16)), S("lnd%d" % (t - 1), 64 * GP + 1, 1024, 4))
         keep[0] = False
@@ -615,70 +675,45 @@ def rank_program(g, core, T, topo):
                     mms([(S("pC", 128 * j, 128 * j + 128), whole("ib"), S(tab, 128 * e, 128 * e + 128),
                           j == 0 and e == 0, j == 2 and e == 31) for e in range(k, k + SP)])
             act(whole("zb0"), S("pC", 0, 384))
-        def lists(parts, stop=False):
-            mms([(S("pA", 16 * b, 16 * b + 16), whole(w), S(x, 0, 16), False, stop and i == len(parts) - 1)
-                 for i, (b, w, x) in enumerate(parts)])
 
-        n = 80 if last else 96
-        consts("pA", [(0, "ih", S("eH", 0, n)), (0, "ib", S("eB", 0, n)), (0, "ib", S("eC", 0, n))])
-        mm(S("pA", 48, 80), whole("iO"), S("zf4", 0, 32), False, False)
-        lists([(0, "iO", "zf4"), (2, "iOn", "fin")])
-        if not last:
-            lists([(0, "iO", "nf"), (1, "iOn", "nf"), (3, "i256", "nf"), (5, "iO", "nf")])
-        else:
-            lists([(5, "iZG", "zf4"), (6, "iZV", "zf4")])
+            mms([(S("pB", 16 * i, 16 * i + 16), whole(w), S("zf4", 0, 16), i == 0, i == 1) for i, w in enumerate(("iZG", "iZV"))])
+            tt(S("own", 0, 16), S("pB", 0, 16), S("c0", 0, 16), A.max)
+            tt(S("own", 64, 80), S("pB", 16, 32), S("c0", 16, 32), A.max)
 
-        tt(whole("kb"), S("pK0", 64, 128), whole("ka"), A.max)
-        tt(whole("kc"), S("pK0", 128, 192), whole("kb"), A.max)
-        tt(whole("kt"), S("pK1", 0, 64), whole("ks"), A.min)
-        tt(whole("k1"), S("pB", 0, 64), whole("kt"), A.min)
-        tt(whole("k2"), whole("k1"), whole("kc"), A.max)
-        tt(whole("k3"), S("k2", 0, 32), S("k2", 32, 64), A.max)
+        tt(S("kt", 1, 320, 5), S("pK1", 0, 64), whole("ks"), A.min)
+        scan(whole("k2"), S("pK0", 0, 320), whole("kt"), A.max, A.min)
+        tt(whole("k3"), S("k2", 4, 160, 5), S("k2", 164, 320, 5), A.max)
         tt(whole("ki"), S("k3", 0, 16), S("k3", 16, 32), A.max)
         ts(whole("val"), whole("ki"), 15, A.bitwise_and)
         ts(whole("nv"), whole("ki"), -BIG / 2, A.is_lt)
-        cp(whole("valb"), whole("val"))
+        ts(whole("valb"), whole("val"), 256.0, A.mult)
         tt(whole("step"), IND(whole("val"), whole("repc")), whole("jr"), A.is_lt)
         ops[-1]["after"] = [len(ops) - 2]
         scan(S("ksel", 0, L), whole("step"), whole("ktab"), A.mult, A.max)
-        lists([(b, "iO", "nv") for b in range(5)] + ([] if last else [(5, "iOn", "nv")]))
-        lists([(b, "i4k", "valb") for b in range(3)] + [(4, "i256n", "valb")], True)
+        lists([(b, "iO", "nv") for b in range(5)])
+        lists([(b, "i16", "valb") for b in range(3)] + [(4, "ibn", "valb")], True)
         act(whole("hb"), S("pA", 0, 80))
-        if last:
-            tt(S("own", 0, 16), S("pA", 80, 96), S("c0", 0, 16), A.max)
-            tt(S("own", 64, 80), S("pA", 96, 112), S("c0", 16, 32), A.max)
-        else:
-            if OV:
-                ts(whole("swp"), S("pA", 80, 96), 0.0, A.max)
-            else:
-                act(whole("swp"), S("pA", 80, 96), F.Relu)
+        if not last:
             consts("pK1", [(0, "ih", whole("oH")), (0, "ib", whole("oB"))])
-            mm(S("pK1", 0, 16), whole("ib"), whole("swp"), False, True)
+            mm(S("pK1", 0, 16), whole("ibn"), whole("nv"), False, True)
         tt(whole("hm"), IND(whole("ksel"), S("l15", 0, 5)), whole("hb"), A.add)
         tt(whole("s6"), whole("hm"), whole("own") if last else S("pK1", 0, 80), A.min)
         cp(whole("s16"), whole("s6"))
-        if not last:
-            (cp if XV else act)(S("pre", 0, 1024, 4), IND(whole("tG"), S("s16", 0, 16)))
-            mm(S("pB", 0, 16), whole("iO"), S("zf4", 0, 16), True, False)
-            conv(S("pB", 0, 16), "zB", "pre", 0, 16, 4, False, True)
 
         def claims():
-            cp(whole("plr"), IND(whole("jw"), S("s16", 32, 48)))
-            if BS:
-                ts(whole("pq"), S("s6", 32, 48), 25165824.0 * 8, A.add, -25165824.0 * 8, A.add)
-                ts(S("pb", 0, 16), whole("pq"), -1.0, A.mult, 2048.0, A.add)
-                tt(S("pb", 16, 32), S("s6", 32, 48), whole("pq"), A.subtract)
-            for c in range(16):
-                if BS:
-                    ts(S("eqd", L * c + 16 * c, L * c + L), S("plr", 16 * c, L), S("pb", c, c + 1), A.add, S("pb", 16 + c, 17 + c), A.is_equal)
-                else:
-                    ts(S("eqd", L * c + 16 * c, L * c + L), S("plr", 16 * c, L), 2048.0, A.add, S("s6", 32 + c, 33 + c), A.is_equal)
-                    ops[-1]["c"] += (EQX - 1) * 0.5 * CYC * (L - 16 * c)
+            (cp if last else act)(whole("plr"), IND(whole("jw"), S("s16", 32, 48)))
+            ts(whole("pq"), S("s6", 32, 48), 25165824.0 * 8, A.add, -25165824.0 * 8, A.add)
+            ts(S("pb", 0, 16), whole("pq"), -1.0, A.mult, 2048.0, A.add)
+            tt(S("pb", 16, 32), S("s6", 32, 48), whole("pq"), A.subtract)
+            for c in CLAIMS:
+                ts(S("eqd", L * c + 16 * c, L * c + L), S("plr", 16 * c, L), S("pb", c, c + 1), A.add, S("pb", 16 + c, 17 + c), A.is_equal)
                 mms([(S("pE0", 16 * c, L), whole("ones"), S("eqd", L * c + 16 * c, L * c + L), c == 0, False),
-                     (S("pE0", 16 * c, 16 * c + 16), whole("uge"), S("eqd", L * c + 16 * c, L * c + 16 * c + 16), False, c == 15)])
-            tt(whole("dmk"), S("pE0", 0, L), whole("dm"), A.mult)
+                     (S("pE0", 16 * c, 16 * c + 16), whole("uge"), S("eqd", L * c + 16 * c, L * c + 16 * c + 16), False, c == CLAIMS[-1])])
 
         if not last:
+            cp(S("pre", 0, 1024, 4), IND(whole("tG"), S("s16", 0, 16)))
+            mm(S("pB", 0, 16), whole("iO"), S("zf4", 0, 16), True, False)
+            conv(S("pB", 0, 16), "zB", "pre", 0, 16, 4, False, True)
             act(S("pre", 1, 1024, 4), IND(whole("tG"), S("s16", 16, 32)))
             act(S("pre", 2, 1024, 4), IND(whole("lo"), S("s16", 64, 80)))
             act(S("pre", 3, 1024, 4), IND(whole("nmw"), S("s16", 48, 64)))
@@ -694,7 +729,7 @@ def rank_program(g, core, T, topo):
             cp(whole("pos"), S("pK1", 0, 16))
             for d in range(4):
                 act(S("idt", L * d, L * d + 64), S("jf", 0, 64), None, 256.0, 0.0)
-                ops[-1]["after"] = list(gathered)
+                ops[-1]["after"] = list(gathered) if t else list(lines["a"])
             cp(IND(whole("idt"), whole("pos")), whole("jb"))
             for bank, ks in (("pB", (1,)), ("pK0", (2, 3, 4))):
                 mms([(S(bank, 16 * k - 16, 16 * k), S("z4", 12 - 4 * e, 140 - 4 * e),
@@ -705,21 +740,34 @@ def rank_program(g, core, T, topo):
             sent = []
             for k in range(1, N):
                 o = S(snd, L * (k - 1), L * k)
-                (cp if k in SVK[SV] else act)(o, IND(whole("pre"), S("src", 16 * k - 16, 16 * k)))
+                act(o, IND(whole("pre"), S("src", 16 * k - 16, 16 * k)))
                 dst = T.cores[(rank + k) % N]
                 sem = "out%d" % (3 * t + k - 1)
                 sent.append(rec("g", lambda o=o, here=here, sem=sem, t=t, dst=dst: g.remote_dma(
-                    ap(here), ap(o), T.sem["arr%d" % t], T.sem[sem], topo.addr(dst)[1], topo.addr(dst)[0], topo.mask(core, dst)),
+                    ap(here), ap(o), T.sem["arr%d" % t], T.sem[sem], topo.addr(dst)[1], topo.addr(dst)[0],
+                    sum(1 << e for e in lanes_of(core, dst))),
                     [], [o], RISS, kind="rem", lat=RLAT + (3.0 if t == 0 and k == 1 else 0.0), sem=sem,
-                    n=len(topo.engines(core, dst)), after=sent[-1:]))
-            act(here, IND(whole("pre"), S("src", 48, 64)))
-            gathered[:] = [len(ops) - 1]
-            n_in = sum(len(topo.engines(T.cores[q], core)) for q in range(N) if q != rank)
+                    n=len(lanes_of(core, dst)), after=sent[-1:] or lines["g"]))
+            act(S(snd, 768, 1024), IND(whole("pre"), S("src", 48, 64)))
+            gathered[:] = [act(here, S(snd, 768, 1024))]
+            n_in = sum(len(lanes_of(T.cores[q], core)) for q in range(N) if q != rank)
             rec("x", None, [S(nxt, L * q, L * q + L) for q in range(N) if q != rank], [], 0.0, kind="land", sem="arr%d" % t,
                 n=n_in, after=sent)
+            lines["g"] = sent[-1:]
+            if t in (1, 2):
+                first = len(ops)
+                if t == 1:
+                    for buf, of, x in (("i32", "ib", 1.0), ("iZG", "ib", ZG / 3), ("iZV", "ib", ZV / 3), ("onB", "ones", -BIG)):
+                        act(whole(buf), whole(of), scale=x)
+                else:
+                    for o, b in [(S("own", 16 * b, 16 * b + 16), b) for b in range(5)] + [(S("c0", 0, 16), 0), (S("c0", 16, 32), 4)]:
+                        act(o, whole("lo16"), None, float(mine[b][1]), float(mine[b][0]))
+                for i in range(first, len(ops)):
+                    ops[i]["after"] = list(gathered)
             claims()
+            tt(whole("dmk"), S("pE0", 0, L), whole("dm"), A.mult)
             mms([(S("pC", 0, 16), whole("ib"), S("pb", 16, 32), True, False), (S("pC", 0, 16), whole("ibn"), S("pb", 0, 16), False, False)])
-            conv(S("pC", 0, 16), "z65", "dmk", 0, 16, 1, False, True)
+            conv(S("pC", 0, 16), "zE", "dmk", 0, 16, 1, False, True)
             tt(whole("ot"), S("pC", 0, 16), whole("cd"), A.min)
             ts(whole("o16"), whole("ot"), 2048.0, A.add)
             keep[0] = True
@@ -727,32 +775,42 @@ def rank_program(g, core, T, topo):
                 cp(IND(S(tab, 0, LC), S("o16", 0, n)), S(lnd, j, 64 * n, 4))
             keep[0] = False
         else:
+            keep[0] = True
+            act(whole("plm"), IND(whole("jm"), S("s16", 32, 48)))
             act(whole("yfb"), IND(whole("tG"), S("s16", 0, 16)))
             act(whole("yvb"), IND(whole("lo"), S("s16", 64, 80)))
+            keep[0] = False
             dma("s", T.yf[:], whole("yfb"))
             dma("s", T.yv[:], whole("yvb"))
-            act(whole("plm"), IND(whole("jm"), S("s16", 32, 48)))
-            first = len(ops) - 1
-            for h, bank in enumerate(("pK1", "pK0")):
-                mms([(S(bank, 128 * j, 128 * j + 128), S(lnd, 512 * h + j, 512 * h + 512, 4), whole("ib"), j == 0, j == 2)
+            banks = ("pK1", "pK0")
+            for h in range(2):
+                mms([(S(banks[h], j, 384, 3), S(lnd, 512 * h + j, 512 * h + 512, 4), whole("ib"), j == 0, False)
                      for j in range(3)])
-                for j in range(3):
-                    act(S("vT", 384 * h + j, 384 * h + 384, 3), S(bank, 128 * j, 128 * j + 128))
-                    ops[-1]["after"] = [first]
+            mms([(S("pB", 8 * h, 8 * h + 8), S("plm", 128 * h, 128 * h + 128), whole("sel0"), h == 0, h == 1) for h in range(2)])
             claims()
-            mms([(S("pB", 8 * h, 8 * h + 8), S("plm", 128 * h, 128 * h + 128), whole("sel0"), h == 0, False) for h in range(2)])
-            mms([(S("pB", 8 * h, 8 * h + 8), S("dmk", 128 * h, 128 * h + 128), whole("blk"), False, h == 1) for h in range(2)])
-            if BS:
-                cp(S("pb", 32, 48), S("pB", 0, 16))
+            lines["v"] = [len(ops) - 2]
+            keep[0] = True
+            cp(S("pb", 32, 48), S("pB", 0, 16))
             for i in range(16):
-                ts(S("eqf", 128 * i, 128 * i + 128), S("jb", 0, 128), S("pb", 32 + i, 33 + i) if BS else S("pB", i, i + 1), A.is_equal)
-                mm(S("pA", 48 * (i % 8), 48 * (i % 8) + 48), S("eqf", 128 * i, 128 * i + 128), S("vT", 48 * i, 48 * i + 48),
-                   i == 0, i == 15)
+                if i == 1:
+                    tt(whole("dmk"), S("pE0", 0, L), whole("dm"), A.mult)
+                ts(S("eqf", 128 * i, 128 * i + 128), S("jb", 0, 128), S("pb", 32 + i, 33 + i), A.is_equal)
+            keep[0] = False
+            for h in range(2):
+                mms([(S(banks[h], j, 384, 3), S("dmk", 128 * h, 128 * h + 128), whole("onB"), False, j == 2)
+                     for j in range(3)])
+                act(S("vT", 384 * h, 384 * h + 384), S(banks[h], 0, 384), F.Relu)
+            for h in range(2):
+                for b, bank in enumerate(("pA", "pB")):
+                    for e in range(4):
+                        i = 8 * h + 4 * b + e
+                        mm(S(bank, 48 * e, 48 * e + 48), S("eqf", 128 * i, 128 * i + 128), S("vT", 48 * i, 48 * i + 48),
+                           h == 0 and e == 0, h == 1 and e == 3)
+            act(S("zts", 0, 192), S("pA", 0, 192))
+            cp(S("zts", 192, 384), S("pB", 0, 192))
             ends = (("pE0", T.zf, 1), ("pK0", T.zg, 2), ("pK1", T.zv, 0))
             for j, (bank, out, b) in enumerate(ends):
-                z = S("zts", 128 * j, 128 * j + 128)
-                cp(z, S("pA", j, 384, 3))
-                turn([(S(bank, 0, 128), z)], "i32")
+                turn([(S(bank, 0, 128), S("zts", j, 384, 3))], "i32")
             for j, (bank, out, b) in enumerate(ends):
                 tt(S("zb", 128 * j, 128 * j + 128), S(bank, 0, 128), S("zb0", 128 * b, 128 * b + 128), A.add)
                 dma("a" if j == 1 else "s", out[:], S("zb", 128 * j, 128 * j + 128))

@@ -23,25 +23,27 @@ _SB = {
     "wfs": (L, B16), "wvs": (L, B16), "nms": (L, I32), "nmb": (L, B16), "thf": (L, B16),
     "pcol": (16, I32), "col": (32, F32), "jf": (144, F32), "jr": (L, F32), "jq": (128, F32), "j4": (144, F32), "lo16": (16, F32),
     "jb": (L, B16), "ab": (16, F32), "ab2": (16, F32), "ib": (128, B16), "ih": (128, F16), "nil": (128, B16),
-    "ones": (128, B16), "uge": (128, B16), "uget": (128, B16), "wn": (128, B16), "onB": (128, B16), "shf": (128, B16),
+    "ones": (128, B16), "uge": (128, B16), "uget": (128, B16), "wn": (128, B16), "shf": (128, B16),
     "zA": (144, B16), "zB": (144, B16), "z0": (144, B16), "z0n": (144, B16), "zX": (144, B16), "z1": (144, B16),
     "zr1": (144, B16), "zr13": (144, B16), "z16": (144, B16), "z4": (144, B16), "zE": (144, B16),
     "wsh": (L, B16), "e16": (16, F32), "nm0": (L, B16), "l16": (16, F32),
-    "oH": (80, F16), "oB": (80, B16), "dk": (1536, F16), "dm": (L, B16), "hc": (192, B16),
+    "oH": (48, F16), "dk": (1536, F16), "dm": (L, B16), "hc": (192, B16),
     "iE": (128, B16), "iS": (128, B16), "i16": (128, B16), "ibn": (128, B16), "i32": (128, F32),
     "iO": (128, B16), "iOn": (128, B16), "i256": (128, B16), "iZG": (128, B16), "iZV": (128, B16),
-    "cE": (64, B16), "ktab": (L, F32), "k32": (80, F32), "repn": (16, U16), "mk": (L, F32), "lhk": (16, U16),
-    "c13": (576, B16), "c1": (320, B16), "c2": (384, B16), "msk": (64, B16), "cst": (64, F16), "dmp": (16, F16),
-    "cd": (16, F32), "c0": (32, F32), "own": (80, F32), "rep": (16, U16), "repc": (16, U16), "l15": (6, U16),
-    "eH": (80, F16), "eB": (80, B16), "eC": (80, B16), "nmw": (6 * L, B16),
+    "cE": (64, B16), "ktab": (L, F32), "k32": (96, F32), "repn": (16, U16), "mk": (L, F32), "lhk": (16, U16),
+    "c13": (192, B16), "c1": (320, B16), "c2": (384, B16), "msk": (L, B16), "onS": (128, B16), "ugS": (128, B16), "pz": (L, B16), "cst": (64, B16), "dm4": (64, F16), "tt2": (32, F16), "oS": (32, F32),
+    "cd": (16, F32), "c0": (32, F32), "own": (32, F32), "rep": (16, U16), "repc": (16, U16), "l15": (6, U16),
+    "eH": (32, F16), "nmw": (6 * L, B16),
     "jw": (JW, F32), "jm": (JW, B16), "pq": (16, F32), "pb": (48, B16), "sel0": (8, B16),
-    "ui": (32, I32), "u": (16, I32), "zf4": (64, B16), "hr": (192, I32), "uk": (80, F32),
+    "ui": (32, I32), "u": (16, I32), "zf4": (64, B16), "hr": (192, I32), "hq": (192, F16), "iq": (128, B16), "uk": (80, F32),
     "uh": (16, F16), "ch": (64, F16), "hi": (L + 16, I32), "h16": (L, U16), "cmp": (2 * L, B16),
-    "fin": (16, B16), "nf": (16, B16), "nv": (16, B16), "valb": (16, B16),
-    "pen": (384, B16), "ks": (64, F32), "kt": (320, F32), "k2": (320, F32), "k3": (32, F32), "step": (L, B16), "ksel": (L + 16, F32),
-    "ki": (16, I32), "val": (16, I32), "hb": (80, F32), "hm": (80, F32), "s6": (80, F32), "s16": (80, U16),
+    "nfin": (16, B16), "nf": (16, B16), "nv": (16, B16), "valb": (16, B16),
+    "ck": (L, F32), "cs": (L, F32), "rst": (L, B16), "nfb": (16, F32), "ci": (16, I32), "cm": (16, I32), "cl": (16, U16),
+    "cF": (64, B16), "sel8": (8, B16), "dgl": (16, U16), "ugw": (L, B16),
+    "pen": (448, B16), "ks": (64, F32), "kt": (320, F32), "k2": (320, F32), "k3": (32, F32), "step": (L, B16), "ksel": (L + 16, F32),
+    "ki": (16, I32), "val": (16, I32), "hb": (80, F32), "hm": (80, F32), "s16": (80, U16),
     "gi": (16, I32), "g3": (16, I32), "go4": (64, B16), "inc": (64, B16), "tt4": (64, F16), "pos": (16, U16), "src": (64, U16),
-    "plr": (L, F16), "dmk": (L, B16), "ot": (16, F32), "o16": (16, U16),
+    "plr": (L, F16), "plh": (L, F16), "oneh": (128, F16), "dmk": (L, B16), "o16": (16, U16),
 }
 _PS = ["pV", "pT", "pE0", "pK0", "pK1", "pA", "pB", "pC"]
 SCRATCH = {}
@@ -59,24 +61,35 @@ for _k in DIMS:
     SCRATCH[_k] = ("sbuf", [128] + list(DIMS[_k]), _SB[_k][1])
 for _k in _PS:
     SCRATCH[_k] = ("psum", [128, 1024], B16) if _k in ("pV", "pT") else ("psum", [128, 512], F32)
-NDMA = 26
+NDMA = 27
 SEMAPHORES = ["cv", "ca", "cp_", "cg"] + ["d%d" % i for i in range(NDMA)] + ["arr%d" % i for i in range(4)] + \
              ["out%d" % i for i in range(12)]
-CYC, PEC, VFIX, AFIX, RISS, RLAT, LOAD = 0.00083, 0.00052, 0.053, 0.13, 0.55, 1.3, 3.0
-HOP, SELF, PEHOP, VADD, GAT, SCA, MNX = 0.06, 0.09, 0.07, 0.065, 1.52, 2.2, 0.6
+CYC, PEC, VFIX, AFIX, RISS, RLAT, LOAD = 0.00083, 0.00052, 0.053, 0.14, 0.55, 1.3, 3.0
+HOP, SELF, PEHOP, VADD, GAT, SCA, MNX = 0.07, 0.085, 0.07, 0.065, 1.52, 2.2, 0.6
+LAG = 0.0
 FROM, TO = {"a": 0.1}, {"a": 0.03, "v": 0.04}
-GP, SP = 8, 2
-CLAIMS = [0, 1, 2, 13, 14, 15] + list(range(3, 13))
-ONV = ((), (2,))
-ORDER = ("ui u w t uh sh h0 ch p0 r0 kind r1 kinds rest p1 m0 b0 a1 m1 b1 a2 m2 b2 s2 m3 a3 b3 tab",
-         "cmp vt g0 nf g1 s0 g2 g3 s1 s3 relu ks shift",
-         "open H C T X dk V8 names flags K0 parts E0 S0 K1 E1 K2 E2 S2 S1 K3 S3 E3 pen", "cmp2 jm")
-ORDER0 = ("ab ab ab pc pc pc ab pc ab cZ cY keep ab ab e16 ab z1 ab* A cW A z0 A repn A A rep A zA nmb ones z0n cF dk dk dk dk "
-          "ui dk u w dk t uh sh ih h0 ch aux dk* cX cX cX r0 yv r1 yv rest m0 kind a0 kinds "
-          "m1 b0 a1 m2 b1 a2 m3 b2 a3 b3 cL kt lhk kt repc tab l15* lo16 eH*",
-          "z16 zE x0 nm0 thf vt wn cmp g0 zX g1 g2 s0 g3 s1 s2 s3 nf zr13 relu ks zB wsh shift",
-          "H there T init C dk V8 X open K0 flags K1 E0 S0 K2 E1 S1 K3 E2 S2 S3 E3 pen parts wshp names",
-          "pcol jf nil ib jq k32* hc l16 iOn ibn c13* c1* cmp2 c2* cE* i256 iS iE jw jr mk iO i16 jb e* jw zero* jw jw")
+GP, SP = 8, 1
+CLAIMS = [0, 13, 14, 15, 1, 9] + list(range(2, 9)) + [10, 11, 12]
+NAB, NDK = 6, 4
+EARLY = 14
+SENDV = ()
+FUSE = (2,)
+ONA = (13, 15)
+ONV = ((2,), (2,), ())
+ORDER = ("ui u w t uh sh h0 ch p0 r0 kind r1 kinds rest p1 m0 b0 a1 m1 b1 a2 m2 b2 s2 m3 a3 b3 tab tG cut",
+         "cmp vt g0 g1 s0 g2 g3 s1 s3 relu ks nf nfin shift",
+         "open H C T X dk V8 names flags K0 E0 S0 K1 E1 K2 E2 S2 S1 K3 S3 E3 pen parts", "cmp2 jw* jm zero")
+ORDER4 = ("ui u w t uh sh h0 ch p0 r0 kind r1 kinds rest p1 b0 own a1 b1 m0 a2 b2 a3 b3 tab m1 m2 ck cs ci cm cl* m3 eq* dmk "
+          "best pm best one best one best* one one one sv one* step ksel hm s16 z*",
+          "cmp vt g0 g1 g2 g3 s0 vT relu s1 s2 plr plm relus s3 ks hot* yv zts* zb0 yf",
+          "open H C T X dk V8 om opens flags parts E0 E1 K0 TT E2 S0 E3 K1 pen K2 pen3 S1 S2 K3 pens S3", "cmp2 jm vT2")
+ORDER0 = ("ab ab ab pc pc pc ab pc ab cZ cY keep ab ab e16 ab z1 ab* A cW A z0 A repn rep zA cX cX cX cF nmb ones z0n dk* "
+          "ui lo16 u w ih t uh sh lo16 h0 ch aux cL r0 lhk r1 B rest "
+          "m2 m0 kind kinds s2 m1 a0 b0 a1 m3 b1 e2 a3 b3 tab shf* repc cut z4",
+          "da da da x0 da da nm0 da* thf vt wn zX z16 zE g0 cmp g1 s0 g3 ct f2 s1 s3 relu zr13 ks eH* nf nfin oH* wsh zB "
+          "shift oneh onS* pz cd",
+          "H there T init dk V8 C X open K2 T2 K0 S2 K1 S0 flags E0 C8 K3 E1 E2 S1 S3 E3 pen wshp parts names",
+          "pcol jf nil ib jq k32* hc l16 iOn c13* c1* c2* cE* ibn i256 iS iE iO cmp2 yv* jr mk kt* i16 zero dm* zero zero zero iq uge msk* jb zero*")
 
 
 def boxed(dims, cols):
@@ -158,7 +171,7 @@ def arrange(ops):
     chain = [0.0] * n
     depth = [0] * n
     for i in todo:
-        chain[i] = ops[i]["c"] + max([w + chain[k] for k, w in succ[i].items()] + [ops[i]["lat"]])
+        chain[i] = (1e-3 if ops[i].get("idle") else ops[i]["c"]) + max([w + chain[k] for k, w in succ[i].items()] + [ops[i]["lat"]])
         depth[i] = 1 + max([depth[k] for k in succ[i]] + [0])
         for j in pred[i]:
             left[j] -= 1
@@ -383,9 +396,12 @@ def rank_program(g, core, T, topo):
     def whole(buf):
         return S(buf, 0, _SB[buf][0])
 
+    def lin(x, o, a, scale=1.0, bias=0.0):
+        name(x, act(o, a, None, bias, scale) if x in ORDER0[1].replace("*", "").split() else ts(o, a, scale, A.mult, bias, A.add))
+
     keep[0] = True
     for o, a, lat in ((whole("wfs"), T.wf, 2.2), (whole("nms"), T.nm, 2.6), (whole("wvs"), T.wv, 2.8),
-                      (S("tV", 0, W), T.rv, 2.6 + LOAD)):
+                      (S("tV", 0, W), T.rv, 2.6 + LOAD + LAG)):
         dma("s", o, a[:], lat)
     keep[0] = False
 
@@ -400,17 +416,22 @@ def rank_program(g, core, T, topo):
     name("nil", fill("nil", 0, 128, 0))
     for b in range(0, JW, 1028):
         name("jw", iota(S("jw", b, b + 1028), [[1, 1028]], b - 2048, 0))
-    for buf, x in (("ib", 1), ("ibn", -1), ("iE", -2 * BIG), ("iS", 16 * BIG), ("iO", OFF), ("iOn", -OFF), ("i256", 256), ("i16", 16)):
+    for buf, x in (("ib", 1), ("ibn", -1), ("iE", -2 * BIG), ("iS", 16 * BIG), ("iO", OFF), ("iOn", -OFF), ("i256", 256), ("i16", 16),
+                   ("iq", -W)):
         diag(buf, x)
-    for i in range(16):
-        name("ab", ms(S("ab", i, i + 1), float(WA[i] + 256 * WB[i])))
-    (cP, cR, cG, cJ, cA, cB, cT, cF, cSH, cKEEP, c4G, c40, cZ, cX, cY, cG16, cW, cAB, cX2, cAB2, cES, cL15, cD, cD2) = range(24)
+    both = [WA[i] + WB[i] / 16 for i in range(16)]
+    for i in range(NAB):
+        name("ab", ms(S("ab", i, i + 1), both[i]))
+    for i in range(NAB, 16, 2):
+        name("ab", ts(S("ab", i, i + 2), S("jf", 0, 2), both[i + 1] - both[i], A.mult, both[i], A.add))
+    (cP, cR, cG, cJ, cA, cB, cT, cF, cSH, cKEEP, c4G, c40, cZ, cX, cY, cG16, cW, cAB, cX2, cAB2, cES, cL15, cD, cD2, c16R) = range(25)
     name("pc", ts(S("pcol", 1, 2), S("pcol", 0, 1), 15, A.bitwise_and))
     name("pc", ts(S("pcol", 2, 3), S("pcol", 0, 1), 4, A.arith_shift_right))
     name("pc", ts(S("pcol", 3, 4), S("pcol", 0, 1), 3, A.bitwise_and))
     name("pc", cp(S("col", 0, 4), S("pcol", 0, 4)))
-    for m in range(5):
-        name("k32", fill("k32", 16 * m, 16 * m + 16, 1 + 32 * ([0] + KP)[m]))
+    for m in range(0, 6, 2):
+        k0, k1 = ([0] + KP)[m:m + 2]
+        name("k32", iota(S("k32", 16 * m, 16 * m + 32), [[32 * (k1 - k0), 2], [0, 16]], 1 + 32 * k0, 0))
     assert all(KP[m] % 2 == m % 2 for m in range(4, 16))
     name("hc", iota(whole("hc"), [[0, 6], [-2048, 2], [0, 16]], 2048, 0))
     name("cZ", ts(C(cZ), C(cG), 16.0, A.mult, 15.0, A.add))
@@ -419,19 +440,19 @@ def rank_program(g, core, T, topo):
     name("z1", ts(whole("z1"), whole("jf"), C(cZ), A.is_equal))
     name("keep", ts(C(cKEEP), C(cR), 4.0, A.is_le, EPS, A.mult))
     name("cW", ts(C(cW), R(13), EPS, A.mult))
-    ts(whole("dm"), whole("jr"), C(cR), A.is_equal)
+    name("dm", gcopy(S("dm", 0, 16), whole("e16")))
+    for n in (16, 32, 64, 128):
+        name("dm", gcopy(S("dm", n, 2 * n), S("dm", 0, n)))
     name("ones", ts(whole("ones"), whole("jq"), C(cG), A.is_equal))
     name("nmb", ts(whole("nmb"), whole("nms"), C(cKEEP), A.mult, C(cW), A.add))
-    dma("s", S("tF", 0, W), T.rf[:], 2.4 + LOAD, S("nmb", 0, 1))
+    dma("s", S("tF", 0, W), T.rf[:], 2 * LOAD - 0.6 + LAG, S("nmb", 0, 1))
     dma("s", S("tG", 0, W), T.rg[:], 2 + LOAD, S("tF", 0, 1))
     name("nm0", act(whole("nm0"), whole("nmb"), F.Relu, EPS * EPS / 2, -1.0))
     name("A", tt(whole("ab2"), whole("ab"), whole("e16"), A.mult))
     name("A", rec("v", lambda: g.vector.tensor_reduce(ap(C(cAB)), ap(whole("ab2")), AxisListType.X, A.add), [C(cAB)],
                   [whole("ab2")], 0.07))
-    name("A", cp(S("pcol", 4, 5), C(cAB)))
-    name("A", ts(S("pcol", 5, 6), S("pcol", 4, 5), 255, A.bitwise_and))
-    name("A", ts(S("pcol", 6, 7), S("pcol", 4, 5), 8, A.arith_shift_right))
-    name("A", cp(S("col", cA, cA + 2), S("pcol", 5, 7)))
+    name("A", ts(C(cA), C(cAB), 3.0 * OFF, A.add, -3.0 * OFF, A.add))
+    name("B", ts(C(cB), C(cAB), C(cA), A.subtract, 16.0, A.mult))
     name("repn", ts(whole("repn"), S("jf", 0, 16), 0.0, A.mult, C(cY), A.add))
     name("rep", ts(whole("rep"), S("jf", 0, 16), 0.0, A.mult, C(cR), A.add))
     name("repc", cp(whole("repc"), S("jf", 0, 16)))
@@ -445,32 +466,34 @@ def rank_program(g, core, T, topo):
     name("thf", act(whole("thf"), S("pE0", 0, L), F.Sign))
     name("aux", tt(S("lnd0", 3, 1024, 4), S("pC", 0, L), whole("thf"), A.mult))
     name("x0", act(S("lnd0", 0, 1024, 4), whole("wfs")))
-    name("yv", cp(S("lnd0", 1, 1024, 4), whole("wfs")))
-    name("yv", cp(S("lnd0", 2, 1024, 4), whole("wvs")))
+    name("yv", gcopy(S("lnd0", 1, 1024, 4), whole("wfs")))
+    name("yv", gcopy(S("lnd0", 2, 1024, 4), whole("wvs")))
+    lin("oneh", whole("oneh"), whole("ones"))
     name("ih", cp(whole("ih"), whole("ib")))
     name("zA", ts(whole("zA"), whole("z1"), C(cA), A.mult))
     name("cF", ts(C(cF), R(14), -256.0 / EPS, A.mult))
     name("cX", ts(C(cX), R(13), -256.0, A.mult, R(1), A.add))
     name("cX", ts(C(cES), R(14), 512.0, A.mult, C(cX), A.add))
     name("cX", ts(C(cT), C(cES), 1 / EPS, A.mult))
-    name("wn", act(whole("wn"), whole("ones"), scale=C(cF)))
-    name("zX", act(whole("zX"), whole("z1"), scale=C(cT)))
-    name("c13", fill("c13", 0, 192, -13))
-    name("c13", fill("c13", 192, 576, -2))
-    for k in range(2):
-        for c in ONV[k]:
-            name("c13", fill("c13", 192 + 192 * k + 64 * c, 256 + 192 * k + 64 * c, -18))
+    lin("wn", whole("wn"), whole("ones"), C(cF))
+    lin("zX", whole("zX"), whole("z1"), C(cT))
+    name("c13", fill("c13", 0, 64, -13))
+    name("c13", iota(S("c13", 64, 192), [[-16, 2], [0, 64]], -2, 0))
     name("c1", fill("c1", 0, 320, 4))
     name("c1", iota(S("c1", 1, 320, 5), [[0, 64]], 200, 0))
     name("cE", fill("cE", 0, 64, 16))
     name("c2", iota(S("c2", 0, 320), [[-1, 4], [0, 16], [-4, 5]], 23, 0))
     name("c2", iota(S("c2", 320, 384), [[-1, 4], [0, 16]], 3, 0))
-    name("kt", ms(whole("kt"), 1e29))
-    name("kt", ms(S("kt", 0, 320, 5), -1e29))
-    name("z16", act(whole("z16"), whole("z1"), scale=16.0))
-    name("zE", act(whole("zE"), whole("z1"), scale=2 * BIG))
+    name("kt", fill("kt", 0, 320, 2 ** 24 - 1))
+    name("kt", rec("g", lambda: g.affine_select(ap(S("kt", 0, 320, 5)), ap(S("jf", 0, 64)), [[0, 64]], A.is_gt, -1e29, 0, 0),
+                   [S("kt", 0, 320, 5)], [S("jf", 0, 64)], 0.17 + 128 * CYC))
+    lin("z16", whole("z16"), whole("z1"), 16.0)
+    lin("zE", whole("zE"), whole("z1"), 2 * BIG)
     for m in range(4, 16):
-        name("dk", ts(S("dk", 128 * m - 512, 128 * m - 384), whole("ib"), float(KP[m]), A.mult))
+        if m < 4 + NDK:
+            name("dk", ts(S("dk", 128 * m - 512, 128 * m - 384), whole("ib"), float(KP[m]), A.mult))
+        else:
+            name("da", act(S("dk", 128 * m - 512, 128 * m - 384), whole("ib"), scale=float(KP[m])))
     name("cL", ts(C(cL15), C(cR), 16.0, A.mult, 15.0, A.add))
     ts(C(cX2), C(cR), 2.0, A.is_ge, C(cKEEP), A.mult)
     ts(C(cAB2), C(cX2), -257.0 / EPS, A.mult, C(cP), A.add)
@@ -480,11 +503,11 @@ def rank_program(g, core, T, topo):
     ts(C(c40), R(0), 4.0, A.mult)
     ts(C(cD2), C(cD), -256.0, A.mult, 256.0, A.add)
     tt(C(cSH), C(cD2), C(cAB2), A.add)
-    name("eH", ts(whole("lo16"), whole("l16"), C(cG16), A.subtract))
-    name("zB", act(whole("zB"), whole("z1"), scale=C(cB)))
-    ts(whole("shf"), S("jf", 0, 128), C(cSH), A.is_equal)
-    ts(whole("zr1"), whole("z1"), R(1), A.mult, 2 / EPS, A.mult)
-    name("zr13", act(whole("zr13"), whole("z1"), scale=R(13)))
+    name("lo16", ts(whole("lo16"), whole("l16"), C(cG16), A.subtract))
+    lin("zB", whole("zB"), whole("z1"), C(cB))
+    name("shf", ts(whole("shf"), S("jf", 0, 128), C(cSH), A.is_equal))
+    name("shf", ts(whole("zr1"), whole("z1"), R(1), A.mult, 2 / EPS, A.mult))
+    lin("zr13", whole("zr13"), whole("z1"), R(13))
     name("wshp", mms([(S("pC", b, b + 128), whole(w), x, b == 0 and i == 0, b == 128 and i == 3)
                       for b, xs in ((0, (("ib", whole("shf")), ("ib", S("zr1", 5, 133)), ("ibn", S("zr1", 7, 135)), ("ibn", S("zr1", 7, 135)))),
                                     (128, (("ib", whole("shf")), ("ib", S("z0", 5, 133)), ("ib", S("z0n", 7, 135)), ("ib", S("zr13", 1, 129)))))
@@ -492,35 +515,40 @@ def rank_program(g, core, T, topo):
     name("wsh", act(whole("wsh"), S("pC", 0, L)))
     mine = ((4, LC), (4, LC + 1), (0, NC), (4, 2 * L + 3), (4, LV + 2))
     for b, (s0, b0) in enumerate(mine):
-        ts(S("oH", 16 * b, 16 * b + 16), whole("lo16"), float(s0), A.mult, float(b0 % 256 + (b == 0)), A.add)
-        name("e", fill("oB", 16 * b, 16 * b + 16, b0 - b0 % 256))
-    name("eH", ms(S("eH", 0, 48), 0.0))
-    for b in (3, 4):
-        name("eH", cp(S("eH", 16 * b, 16 * b + 16), whole("lo16")))
-    for buf, lo, hi, x in (("eB", 0, 48, -61440), ("eB", 48, 64, 0), ("eB", 64, 80, 3840),
-                           ("eC", 0, 16, 0), ("eC", 16, 48, OFF), ("eC", 48, 80, 0), ("ksel", L, L + 16, 0)):
-        name("e", fill(buf, lo, hi, x))
-    name("l15", ts(S("l15", 0, 3), S("jf", 0, 3), 0.0, A.mult, C(cL15), A.add))
-    name("l15", ms(S("l15", 3, 6), 256))
+        if b < 3:
+            lin("oH", S("oH", 16 * b, 16 * b + 16), whole("lo16"), float(s0), float(b0 % W + (b == 0)))
+        else:
+            lin("oH", S("oS", 16 * b - 48, 16 * b - 32), whole("lo16"), float(s0), float(b0))
+    for b in range(2):
+        lin("eH", S("eH", 16 * b, 16 * b + 16), whole("lo16"))
     name("lhk", ts(whole("lhk"), S("jf", 0, 16), C(cL15), A.subtract, 255.0, A.add))
-    ts(whole("z4"), whole("j4"), C(c4G), A.is_equal, C(c40), A.mult)
-    ts(whole("uget"), S("jr", 0, 128), C(cR), A.is_le, -1.0, A.mult)
-    ts(whole("msk"), S("jr", 0, 64), 0.0, A.is_gt)
-    tt(whole("uge"), whole("uget"), whole("ones"), A.mult)
-    for d in range(4):
-        ts(S("cst", 16 * d, 16 * d + 16), whole("lo16"), -1.0, A.mult, float(256 * d - 1024), A.add)
-    ts(whole("dmp"), whole("lo16"), 1024.0, A.add)
-    act(whole("cd"), whole("lo16"), None, 2048.0)
-    for buf, lo, hi in (("tG", W, LC), ("tG", ZG, WGN), ("lo", LE, LON), ("pre", 1024, 1040)):
+    name("z4", ts(whole("z4"), whole("j4"), C(c4G), A.is_equal, C(c40), A.mult))
+    lin("uget", whole("uget"), whole("ones"), -1.0)
+    name("uge", rec("g", lambda: g.affine_select(ap(whole("uge")), ap(whole("uget")), [[-1, 128]], A.is_ge, 0.0, 0, 1),
+                    [whole("uge")], [whole("uget")], 0.17 + 256 * CYC))
+    name("msk", fill("msk", 0, L, 1))
+    name("msk", iota(S("msk", 0, L, 16), [[0, 16]], 0, 0))
+    lin("onS", whole("onS"), whole("ones"), 8192.0)
+    lin("onS", whole("ugS"), whole("uge"), 8192.0)
+    lin("pz", whole("pz"), whole("dm"), OFF + 2048.0, -1.0 * OFF)
+    name("zero", iota(whole("cst"), [[256, 4], [0, 16]], W, 0))
+    ts(whole("dm4"), IND(whole("lo16"), S("rep", 0, 4)), 1024.0, A.add)
+    lin("cd", whole("cd"), whole("lo16"), 1.0, 4096.0)
+    dma("s", S("tG", W, LC), whole("wfs"), 2.5, S("tF", 0, 1))
+    for buf, lo, hi in (("tG", ZG, WGN), ("lo", LE, LON), ("pre", 1024, 1040)):
         name("zero", fill(buf, lo, hi, 0))
-    name("zero", fill("jm", W, JW, 200))
+    for d in range(4):
+        name("zero", fill("idt", L * d, L * d + 64, 256))
     ts(whole("sel0"), S("jf", 0, 8), C(cG), A.is_equal, R(0), A.mult)
+    ts(C(c16R), C(cR), 16.0, A.mult)
+    ts(whole("dgl"), whole("lo16"), 17.0, A.mult, C(c16R), A.subtract)
 
     gathered = []
     for t in range(RO):
         lnd = "lnd%d" % t
         last = t == RO - 1
-        onv = ONV[min(t, 1)]
+        var = 2 if last else min(t, 1)
+        onv = ONV[var]
 
         def hashes():
             if t == 0:
@@ -530,16 +558,17 @@ def rank_program(g, core, T, topo):
                 mms([(S("pA", 0, 32), S("zA", 15 - r, 143 - r), BOX(lnd, [64 * c + 4 * r + j for c in range(16) for j in (0, 3)]),
                       r == 0, r == 15) for r in range(16)])
 
-        def later():
-            mms([(S("pB", 0, 192), whole("ib"), whole("hc"), True, False)] +
-                [(S("pB", 16 * m, 16 * m + 16), S("dk", 128 * m, 128 * m + 128), whole("uh"), False, False) for m in range(12)])
-            mms([(S("pB", 64 * i, 64 * i + 64), whole("ih"), whole("ch"), False, i == 2) for i in range(3)])
+        def later(bank, stop):
+            mms([(S(bank, 0, 192), whole("ib"), whole("hc"), True, False)] +
+                [(S(bank, 16 * m, 16 * m + 16), S("dk", 128 * m, 128 * m + 128), whole("uh"), False, False) for m in range(12)])
+            mms([(S(bank, 64 * i, 64 * i + 64), whole("ih"), whole("ch"), False, stop and i == 2) for i in range(3)])
 
         kind = S("pA", 32, 48)
 
         def kinds():
             ts(S("zf4", 0, 16), kind, 0.0, A.is_ge, 3.0, A.mult)
-            ts(whole("fin"), kind, 256.0, A.is_ge)
+            if last:
+                ts(whole("nfb"), kind, 256.0, A.is_lt, BIG, A.mult)
 
         def names():
             if not last:
@@ -572,10 +601,12 @@ def rank_program(g, core, T, topo):
         five = [S("pK0", j, 320, 5) for j in range(5)]
         at = [(S("pE0", 64 * c, 64 * c + 64), S("pE0", 192 + 64 * c, 256 + 64 * c), five[2 + c]) for c in range(3)]
         at.append((five[1], S("pK1", 64, 128), S("pK1", 0, 64)))
+        if last:
+            at = [(S("pE0", 64 * c, 64 * c + 64), S("pB", 64 * c, 64 * c + 64) if c < 3 else five[1], at[c][2]) for c in range(4)]
 
         def sums(what, c, stop=False):
             i = "ESK".index(what)
-            z = "z16" if i == 2 else "z1" if c < 3 else "zE"
+            z = "z16" if i == 2 else "z1" if c < 3 or (last and i == 0) else "zE"
             conv(at[c][i], z, ("eqf", "sg", "lo")[i], 1024 * c, 64, 1, False, stop)
 
         def consts(bank, parts):
@@ -584,12 +615,19 @@ def rank_program(g, core, T, topo):
         def bars(bank, a, n, w):
             mms([(S(bank, b, b + 64), whole(w), whole("zf4"), False, False) for b in range(a, a + n, 64)])
 
+        def over(a):
+            return [(a + 64 * c, "ib", S("c13", 128, 192) if c in onv else S("c13", 64, 128)) for c in range(3)]
+
         def opening():
-            b = 192 + 192 * min(t, 1)
-            consts("pE0", [(0, "ib", S("c13", 0, 192)), (192, "ib", S("c13", b, b + 192))])
+            consts("pE0", [(64 * c, "ib", S("c13", 0, 64)) for c in range(4 if last else 3)] + ([] if last else over(192)))
             consts("pK0", [(0, "iOn", whole("c1")), (0, "ib", S("c2", 0, 320))])
+            if last:
+                mm(five[1], whole("iO"), whole("cF"), False, False)
 
         def flags():
+            if last:
+                consts("pK1", [(0, "iOn", S("c1", 0, 320, 5)), (0, "ib", S("c2", 320, 384))])
+                return bars("pE0", 0, L, "ibn")
             consts("pK1", [(0, "iOn", S("c1", 0, 320, 5)), (0, "ib", S("c2", 320, 384)), (64, "iOn", whole("cE"))])
             for e in (("pE0", 0, 192, "ibn"), ("pE0", 192, 192, "i256"), ("pK1", 64, 64, "iS")):
                 bars(*e)
@@ -600,58 +638,94 @@ def rank_program(g, core, T, topo):
                  for i, (b, w, x) in enumerate(some)])
 
         def parts():
-            consts("pA", [(0, "ih", whole("eH")), (0, "ib", whole("eB")), (0, "ib", whole("eC"))])
-            mm(S("pA", 48, 80), whole("iO"), S("zf4", 0, 32), False, False)
-            lists([(0, "iO", "zf4"), (2, "iOn", "fin")] + ([] if last else [(0, "iO", "nf"), (1, "iOn", "nf"), (3, "i256", "nf")]))
+            if last:
+                return consts("pA", [(0, "iO", S("zf4", 0, 32)), (16, "ih", S("eH", 0, 16))])
+            consts("pA", [(48, "ih", whole("eH")), (48, "iO", S("zf4", 0, 32))])
+            lists([(0, "iO", "zf4"), (2, "iO", "nfin"), (0, "iO", "nf"), (1, "iO", "cE"), (1, "iOn", "nf"), (3, "i16", "nf")])
 
-        queues = [o.split() for o in (ORDER0 if t == 0 else ORDER)]
-        sm = [x for x in queues[2] if len(x) == 2 and x[1].isdigit()]
-        ends = ([x for x in sm if x[0] in "ES" and x[1] != "3"][-1], [x for x in sm if x in ("K3", "S3")][-1],
-                [x for x in queues[2] if x in ("pen", "E3")][-1])
+        def lacks(outs, a, stop):
+            mms([(o, whole("ibn"), S("pen", a + 64 * i, a + 64 * i + 64), False, stop and i == len(outs) - 1) for i, o in enumerate(outs)])
+
+        queues = [o.split() for o in (ORDER0 if t == 0 else ORDER4 if last else ORDER)]
+        banks = ("E0 E1 E2 E3", "K3 pen3", "K0 K1 K2 pen pens S3", "S0 S1 S2") if last else \
+                ("E0 E1 E2 S0 S1 S2", "K3 S3", "K0 K1 K2 pen E3")
+        ends = [[x for x in queues[2] if x in b.split()][-1] for b in banks]
         step = {
             "H": (hashes, []), "ui": (lambda: cp(whole("ui"), S("pA", 0, 32)), ["H"]),
             "u": (lambda: ts(whole("u"), S("ui", 0, 32, 2), 4095, A.bitwise_and), []),
-            "w": (lambda: tt(whole("uk"), IND(whole("ui"), S("repn", 0, 5)), whole("k32"), A.add), []),
+            "w": (lambda: tt(whole("uk"), IND(whole("ui"), S("repn", 0, 5)), S("k32", 0, 80), A.add), []),
             "t": (lambda: tt(S("hi", 0, 80), IND(whole("u"), S("rep", 0, 5)), whole("uk"), A.mult), []),
             "uh": (lambda: ts(whole("uh"), whole("u"), -2048.0, A.add), []),
             "sh": (lambda: ts(S("hi", 0, 80), S("hi", 0, 80), 5, A.arith_shift_right, 4095, A.bitwise_and), []),
             "h0": (lambda: cp(S("h16", 0, 64), S("hi", 16, 80)), []),
             "ch": (lambda: ts(whole("ch"), IND(S("hi", 0, 16), S("rep", 0, 4)), -2048.0, A.add), []),
-            "dk": (later, ["ch"]), "r0": (lambda: cp(whole("hr"), S("pB", 0, 192)), ["dk"]),
-            "r1": (lambda: ts(S("hi", 80, L + 16), whole("hr"), 4095, A.bitwise_and), []),
-            "rest": (lambda: cp(S("h16", 64, L), S("hi", 80, L + 16)), []),
-            "C": (lambda: mms([(S("pK1", 0, L), whole("ib"), S(lnd, 0, 1024, 4), True, False),
+            "dk": (lambda: later("pK1", True), ["ch", "cmp"]), "dk2": (lambda: later("pB", False), ["ch"]),
+            "r0": (lambda: ts(whole("hq"), S("pK1", 0, 192), 1.0 / W, A.mult, 1535.5 + 0.5 / W, A.add), ["dk"]),
+            "mod": (lambda: mm(S("pB", 0, 192), whole("iq"), whole("hq"), False, True), ["r0", "dk2"]),
+            "rest": (lambda: ts(S("h16", 64, L), S("pB", 0, 192), 1536.0 * W, A.add), ["mod"]),
+            "r1": (lambda: ts(S("hi", 80, L + 16), S("pB", 0, 192), 1536.0 * W, A.add), ["mod"]),
+            "C": (lambda: mms([(S("pK1", 0, L), whole("ib"), S(lnd, 0, 1024, 4) if t else whole("wfs"), True, False),
                                (S("pK1", 0, L), whole("wn"), S(lnd, 3, 1024, 4), False, True)]), []),
             "cmp": (lambda: act(S("cmp", 0, L), S("pK1", 0, L), F.Relu), ["C"]),
             "cmp2": (lambda: gcopy(S("cmp", L, 2 * L), S("cmp", 0, L)), ["cmp"]),
             "jm": (lambda: iota(S("jm", 1024 * t - 1024, 1024 * t), [[0, 8], [1, 128]], 0, 0), []),
+            "zero": (lambda: t < 2 or fill("eqd", 2048 * t - W, 2048 * t - 2048, 0), []),
             "T": (lambda: turn([(S("pT", 128 * h, 128 * h + 128), S("wvs", 128 * h, 128 * h + 128) if t == 0 else
                                  S(lnd, 512 * h + 2, 512 * h + 512, 4)) for h in range(2)], "ib"), []),
             "vt": (lambda: act(whole("vt"), S("pT", 0, L)), ["T"]),
             "V8": (lambda: turn([(S("pV", 128 * i, 128 * i + 128), S("vt", 128 * (i % 2), 128 * (i % 2) + 128))
                                  for i in range(8)], "ib"), ["vt"]),
+            "T2": (lambda: turn([(S("pT", 128 * h, 128 * h + 128), S("cmp", 128 * h, 128 * h + 128)) for h in range(2)], "ib"), ["cmp", "vt"]),
+            "ct": (lambda: act(whole("thf"), S("pT", 0, L)), ["T2"]),
+            "C8": (lambda: turn([(S("pT", 128 * i, 128 * i + 128), S("thf", 128 * (i % 2), 128 * (i % 2) + 128))
+                                 for i in range(8)], "ib"), ["ct"]),
             "X": (lambda: conv(kind, "zX", lnd, 3, 16, 4), ["ui"]), "kind": (kinds, ["X"]),
-            "kinds": (lambda: cp(S("zf4", 16, 64), IND(S("zf4", 0, 16), S("rep", 0, 3))), []),
-            "open": (opening, []), "flags": (flags, ["kinds", "cmp2", "open"]), "names": (names, []),
+            "kinds": (lambda: [gcopy(S("zf4", n, 2 * n), S("zf4", 0, n)) for n in (16, 32)] if "kinds" in ORDER[3] else
+                      cp(S("zf4", 16, 64), IND(S("zf4", 0, 16), S("rep", 0, 3))), ["kind"]),
+            "nfin": (lambda: act(whole("nfin"), kind, F.Relu, 256.0, -1.0), ["X"]),
+            "open": (opening, []), "flags": (flags, ["kinds", "cmp2", "open", "r0"]), "names": (names, []),
             "shift": (lambda: last or act(S("nmw", 0, 2 * L), S("pC", 0, 2 * L)), ["names"]),
-            "nf": (lambda: last or act(whole("nf"), kind, F.Relu, -255.0, -1.0), ["X"]),
+            "nf": (lambda: last or act(whole("nf"), kind, F.Relu, -4080.0, -16.0), ["X"]),
             "p0": (lambda: gf(0, 0, 1), ["cmp"]), "p1": (lambda: gf(0, 1, 1), []),
-            "relu": (lambda: act(whole("pen"), S("pE0", 0, 384), F.Relu, None, -BIG), [ends[0]]),
-            "pen": (lambda: mms([(five[2 + i % 3], whole("ibn"), S("pen", 64 * i, 64 * i + 64), False, ends[2] == "pen" and i == 5)
-                                 for i in range(6)]), ["relu"]),
-            "parts": (parts, ["kinds", "nf"]),
-            "ks": (lambda: act(whole("ks"), S("pK1", 64, 128)), [ends[1]]),
-            "tab": (lambda: tt(whole("ktab"), IND(S("hi", 16, L + 16), whole("lhk")), whole("mk"), A.add), ["rest"])}
+            "relu": (lambda: act(S("pen", 0, L if last else 384), S("pE0", 0, L if last else 384), F.Relu, None, -BIG), [ends[0]]),
+            "pen": (lambda: lacks(five[2:] * (1 if last else 2), 0, "pen" in ends), ["relu"]),
+            "parts": (parts, ["kinds"] if last else ["kinds", "nf", "nfin"]),
+            "ks": (lambda: act(S("kt", 1, 320, 5), S("pK1", 0, 64)) if last else act(whole("ks"), S("pK1", 64, 128)), [ends[1]]),
+            "cut": (lambda: tt(S("kt", 1, 320, 5), S("pK1", 0, 64), whole("ks"), A.min), ["ks"]),
+            "tG": (lambda: cp(IND(S("tG", 0, LC), S("o16", GP, 16)), S("lnd%d" % (t - 1), 64 * GP + 1, 1024, 4)), []),
+            "pen3": (lambda: lacks([S("pK1", 0, 64)], 192, "pen3" in ends), ["relu"]),
+            "relus": (lambda: act(S("pen", L, 448), S("pB", 0, 192), F.Relu, None, -BIG), [ends[-1]]),
+            "pens": (lambda: lacks(five[2:], L, "pens" in ends), ["relus"]),
+            "om": (lambda: mms([(S("pB", 16 * i, 16 * i + 16), whole(w), S("zf4", 0, 16), i == 0, i == 1)
+                                for i, w in enumerate(("iZG", "iZV"))]), ["kind", "r1", "rest"]),
+            "own": (lambda: tt(whole("own"), S("pB", 0, 32), whole("c0"), A.max), ["om"]),
+            "opens": (lambda: consts("pB", over(0)), ["own"]),
+            "TT": (lambda: turn([(S("pT", L * j + 128 * h, L * j + 128 * h + 128), S(lnd, 512 * h + j, 512 * h + 512, 4))
+                                 for h in range(2) for j in range(2)], "ib"), ["vt"]),
+            "vT": (lambda: [act(S("vT", j, 768, 3), S("pT", L * j, L * j + L)) for j in range(2)], ["TT"]),
+            "vT2": (lambda: gcopy(S("vT", 2, 768, 3), whole("vt")), ["vt"]),
+            "tab": (lambda: tt(whole("ktab"), IND(S("hi", 16, L + 16), whole("lhk")), whole("mk"), A.add), ["r1"])}
+        if t in (0, RO - 1) or "mod" not in ORDER[2]:
+            step.update({"dk": (lambda: later("pB", True), ["ch"]), "r0": (lambda: cp(whole("hr"), S("pB", 0, 192)), ["dk"]),
+                         "r1": (lambda: ts(S("hi", 80, L + 16), whole("hr"), 4095, A.bitwise_and), ["r0"]),
+                         "rest": (lambda: cp(S("h16", 64, L), S("hi", 80, L + 16)), ["r1"])})
         for c in range(4):
             step["a%d" % c] = (lambda c=c: gf(c, 0, 2), ["rest", "cmp2"])
             step["b%d" % c] = (lambda c=c: gf(c, 2, 2), ["rest", "cmp2"])
             step["g%d" % c] = (lambda c=c: gv(c), ["rest"] if c else ["h0"])
             step["m%d" % c] = (lambda c=c: mn(c), ["g%d" % c, "V8"])
+            if t == 0 and c in FUSE:
+                step["m%d" % c] = (lambda c=c: [tt(S("lo", L * m, L * m + L), IND(S("tV", 0, W), S("h16", 16 * m, 16 * m + 16)), whole("wvs"), A.min)
+                                                for m in range(4 * c, 4 * c + 4)], ["rest"])
             step["s%d" % c] = (lambda c=c: sgn(c), ["m%d" % c])
-            for x, y in (("E", "ab"), ("K", "m"), ("S", "s")):
+            step["f%d" % c] = (lambda c=c: act(S("eqd", 1024 * c, 1024 * c + 1024), IND(S("tF", 0, W), S("h16", 64 * c, 64 * c + 64))), ["rest"])
+            step["e%d" % c] = (lambda c=c: ops[tt(S("eqf", 1024 * c, 1024 * c + 1024), S("eqd", 1024 * c, 1024 * c + 1024), S("pT", 0, 1024),
+                                                  A.is_equal)].update(c=MNX * vc(S("eqf", 0, 1024), S("pT", 0, 1024), S("pT", 0, 1024))),
+                               ["f%d" % c, "C8"])
+            for x, y in (("E", "abe"), ("K", "m"), ("S", "s")):
                 step["%s%d" % (x, c)] = (lambda c=c, x=x: sums(x, c, "%s%d" % (x, c) in ends),
                                          [e for e in ("%s%d" % (z, c) for z in y) if e in queues[0] + queues[1]])
-        keep[0] = True
+        keep[0] = not last
         done = []
         while any(queues):
             for k, o in enumerate(queues):
@@ -660,76 +734,108 @@ def rank_program(g, core, T, topo):
                     if named.get(x) and ops[named[x][0]]["q"] == "vapg"[k]:
                         for i in range(len(named[x]) if x != o[0] else 1):
                             line(named[x].pop(0))
+                    elif x not in step:
+                        pass
                     elif all(y in done for y in step[x][1]):
+                        first = len(ops)
                         step[x][0]()
+                        for i in range(first, len(ops) if last else first):
+                            name(x, i)
                         done.append(x)
                     else:
                         break
                     o.pop(0)
-        if 0 < t < RO - 1:
-            cp(IND(S("tG", 0, LC), S("o16", GP, 16)), S("lnd%d" % (t - 1), 64 * GP + 1, 1024, 4))
         keep[0] = False
         if last:
             for j, tab in enumerate(("tV", "tF", "tG")):
                 for k in range(0, 32, SP):
                     mms([(S("pC", 128 * j, 128 * j + 128), whole("ib"), S(tab, 128 * e, 128 * e + 128),
                           j == 0 and e == 0, j == 2 and e == 31) for e in range(k, k + SP)])
-            act(whole("zb0"), S("pC", 0, 384))
+                    ops[-1]["idle"] = True
+                    if j == 0 and k == EARLY:
+                        ops[-1]["after"] = named["H"][-1:]
+            name("zb0", act(whole("zb0"), S("pC", 0, 384)))
 
-            mms([(S("pB", 16 * i, 16 * i + 16), whole(w), S("zf4", 0, 16), i == 0, i == 1) for i, w in enumerate(("iZG", "iZV"))])
-            tt(S("own", 0, 16), S("pB", 0, 16), S("c0", 0, 16), A.max)
-            tt(S("own", 64, 80), S("pB", 16, 32), S("c0", 16, 32), A.max)
+        def call(x, i):
+            if last:
+                name(x, i)
 
-        tt(S("kt", 1, 320, 5), S("pK1", 0, 64), whole("ks"), A.min)
-        scan(whole("k2"), S("pK0", 0, 320), whole("kt"), A.max, A.min)
-        tt(whole("k3"), S("k2", 4, 160, 5), S("k2", 164, 320, 5), A.max)
-        tt(whole("ki"), S("k3", 0, 16), S("k3", 16, 32), A.max)
-        ts(whole("val"), whole("ki"), 15, A.bitwise_and)
-        ts(whole("nv"), whole("ki"), -BIG / 2, A.is_lt)
-        ts(whole("valb"), whole("val"), 256.0, A.mult)
-        tt(whole("step"), IND(whole("val"), whole("repc")), whole("jr"), A.is_lt)
+        call("best", scan(whole("k2"), S("pK0", 0, 320), whole("kt"), A.max, A.min))
+        call("best", tt(whole("k3"), S("k2", 4, 160, 5), S("k2", 164, 320, 5), A.max))
+        call("best", tt(whole("ki"), S("k3", 0, 16), S("k3", 16, 32), A.max))
+        call("best", ts(whole("val"), whole("ki"), 15, A.bitwise_and))
+        call("best", ts(whole("nv"), whole("ki"), -BIG / 2, A.is_lt))
+        call("best", ts(whole("valb"), whole("val"), 256.0, A.mult, -3840.0, A.add))
+        call("step", tt(whole("step"), IND(whole("val"), whole("repc")), whole("jr"), A.is_lt))
         ops[-1]["after"] = [len(ops) - 2]
-        scan(S("ksel", 0, L), whole("step"), whole("ktab"), A.mult, A.max)
-        lists([(b, "iO", "nv") for b in range(5)])
-        lists([(b, "i16", "valb") for b in range(3)] + [(4, "ibn", "valb")], True)
-        act(whole("hb"), S("pA", 0, 80))
-        if not last:
-            consts("pK1", [(0, "ih", whole("oH")), (0, "ib", whole("oB"))])
+        call("ksel", scan(S("ksel", 0, L), whole("step"), whole("ktab"), A.mult, A.max))
+        n = 2 if last else 5
+        picked = []
+        lists([(b, "iO", "nv") for b in range(n)])
+        lists([(b, "i16", "valb") for b in range(1 if last else 3)] + [(n - 1, "ibn", "valb")], True)
+        if last:
+            call("sv", tt(S("s16", 16, 32), S("pA", 16, 32), S("own", 16, 32), A.min))
+            call("hm", tt(S("hm", 0, 16), S("ksel", 15, L, 16), S("pA", 0, 16), A.add))
+            call("s16", tt(S("s16", 0, 16), S("hm", 0, 16), S("own", 0, 16), A.min))
+        else:
+            consts("pK1", [(0, "ih", whole("oH")), (0, "i256", S("cE", 0, 48))])
             mm(S("pK1", 0, 16), whole("ibn"), whole("nv"), False, True)
-        tt(whole("hm"), IND(whole("ksel"), S("l15", 0, 5)), whole("hb"), A.add)
-        tt(whole("s6"), whole("hm"), whole("own") if last else S("pK1", 0, 80), A.min)
-        cp(whole("s16"), whole("s6"))
+            tt(S("s16", 48, 80), S("pA", 48, 80), whole("oS"), A.min)
+            for bs in ((0,), (2, 1)):
+                for b in bs:
+                    yadd = tt(S("hm", 16 * b, 16 * b + 16), S("ksel", 15, L, 16), S("pA", 16 * b, 16 * b + 16), A.add)
+                for b in bs:
+                    tt(S("s16", 16 * b, 16 * b + 16), S("hm", 16 * b, 16 * b + 16), S("pK1", 16 * b, 16 * b + 16), A.min)
+                picked.append(len(ops) - 1)
 
-        def claims():
-            (cp if last else act)(whole("plr"), IND(whole("jw"), S("s16", 32, 48)))
-            ts(whole("pq"), S("s6", 32, 48), 25165824.0 * 8, A.add, -25165824.0 * 8, A.add)
-            ts(S("pb", 0, 16), whole("pq"), -1.0, A.mult, 2048.0, A.add)
-            tt(S("pb", 16, 32), S("s6", 32, 48), whole("pq"), A.subtract)
+        def claims(cl, of, *cut):
+            if t:
+                call("plr", act(whole("plr"), IND(whole("jw"), cl)))
+                for i in picked:
+                    ops[i]["after"] = [len(ops) - 1]
+            for o in (S("pb", 0, 16), whole("pq")):
+                call("cl", ts(o, of, *cut, -2048.0, A.add))
+            if 0 < t < RO - 1:
+                ops[yadd]["after"] = [len(ops) - 1]
+            if not t:
+                tt(whole("plh"), IND(whole("pq"), whole("repc")), whole("dm"), A.mult)
+                mm(S("pE0", L, 2 * L), whole("oneh"), whole("plh"), True, True)
+                act(whole("plr"), S("pE0", L, 2 * L))
+            call("cl", tt(S("pb", 16, 32), whole("pq"), S("pb", 0, 16), A.subtract))
             for c in CLAIMS:
-                ts(S("eqd", L * c + 16 * c, L * c + L), S("plr", 16 * c, L), S("pb", c, c + 1), A.add, S("pb", 16 + c, 17 + c), A.is_equal)
-                mms([(S("pE0", 16 * c, L), whole("ones"), S("eqd", L * c + 16 * c, L * c + L), c == 0, False),
-                     (S("pE0", 16 * c, 16 * c + 16), whole("uge"), S("eqd", L * c + 16 * c, L * c + 16 * c + 16), False, c == CLAIMS[-1])])
+                call("eq", ts(S("eqd", L * c + 16 * c, L * c + L), S("plr", 16 * c, L), S("pb", c, c + 1), A.subtract,
+                              S("pb", 16 + c, 17 + c), A.is_equal))
+                if last:
+                    mms([(S("pE0", 8 * h, 8 * h + 8), S("eqd", L * c + 128 * h, L * c + 128 * h + 128), whole("sel8"),
+                          c == CLAIMS[0] and h == c // 8, False) for h in range(c // 8, 2)])
+                    continue
+                if c == CLAIMS[0]:
+                    mms([(S("pE0", 0, L), whole("ib"), whole("pz"), True, False), (S("pE0", 0, L), whole("ih"), whole("plr"), False, False)])
+                    ops[-1]["after"] = ranked
+                mms([(S("pE0", 16 * c, L), whole("onS"), S("eqd", L * c + 16 * c, L * c + L), False, False),
+                     (S("pE0", 16 * c, 16 * c + 16), whole("ugS"), S("eqd", L * c + 16 * c, L * c + 16 * c + 16), False, c == CLAIMS[-1])])
 
         if not last:
-            cp(S("pre", 0, 1024, 4), IND(whole("tG"), S("s16", 0, 16)))
+            ops[cp(S("pre", 0, 1024, 4), IND(whole("tG"), S("s16", 0, 16)))]["after"] = picked[:1]
             mm(S("pB", 0, 16), whole("iO"), S("zf4", 0, 16), True, False)
             conv(S("pB", 0, 16), "zB", "pre", 0, 16, 4, False, True)
-            act(S("pre", 1, 1024, 4), IND(whole("tG"), S("s16", 16, 32)))
+            picked[:] = [act(S("pre", 1, 1024, 4), IND(whole("tG"), S("s16", 16, 32))),
+                         act(S("pre", 3, 1024, 4), IND(whole("nmw"), S("s16", 48, 64)))]
             act(S("pre", 2, 1024, 4), IND(whole("lo"), S("s16", 64, 80)))
-            act(S("pre", 3, 1024, 4), IND(whole("nmw"), S("s16", 48, 64)))
             cp(whole("gi"), S("pB", 0, 16))
             ts(whole("g3"), whole("gi"), OFF + 3, A.bitwise_and)
             tt(whole("go4"), IND(whole("g3"), S("rep", 0, 4)), S("jq", 0, 64), A.is_equal)
-            scan(whole("inc"), whole("msk"), whole("go4"), A.mult, A.add)
-            mms([(S("pC", 0, 64), whole("ih"), whole("cst"), True, False), (S("pC", 0, 64), whole("uge"), whole("go4"), False, False)])
-            mm(S("pC", 0, 64), whole("ones"), whole("inc"), False, True)
-            tt(whole("tt4"), S("pC", 0, 64), whole("go4"), A.mult)
-            mm(S("pK1", 0, 16), whole("ih"), whole("dmp"), True, False)
-            mms([(S("pK1", 0, 16), whole("ih"), S("tt4", 16 * d, 16 * d + 16), False, d == 3) for d in range(4)])
-            cp(whole("pos"), S("pK1", 0, 16))
+            scan(whole("inc"), S("msk", 0, 64), whole("go4"), A.mult, A.add)
+            mm(S("pC", 0, 64), whole("ib"), whole("cst"), True, False)
+            mms([(S("pC", 0, 64), whole(w), whole("go4"), False, False) for w in ("uge", "iq")])
+            ranked = [mm(S("pC", 0, 64), whole("ones"), whole("inc"), False, True)]
+            tt(whole("tt4"), S("pC", 0, 64), whole("dm4"), A.min)
+            tt(whole("tt2"), S("tt4", 0, 32), S("tt4", 32, 64), A.min)
+            tt(whole("pos"), S("tt2", 0, 16), S("tt2", 16, 32), A.min)
             for d in range(4):
-                act(S("idt", L * d, L * d + 64), S("jf", 0, 64), None, 256.0, 0.0)
-                ops[-1]["after"] = list(gathered) if t else list(lines["a"])
+                if t:
+                    act(S("idt", L * d, L * d + 64), S("jf", 0, 64), None, 256.0, 0.0)
+                    ops[-1]["after"] = list(gathered)
             cp(IND(whole("idt"), whole("pos")), whole("jb"))
             for bank, ks in (("pB", (1,)), ("pK0", (2, 3, 4))):
                 mms([(S(bank, 16 * k - 16, 16 * k), S("z4", 12 - 4 * e, 140 - 4 * e),
@@ -740,7 +846,7 @@ def rank_program(g, core, T, topo):
             sent = []
             for k in range(1, N):
                 o = S(snd, L * (k - 1), L * k)
-                act(o, IND(whole("pre"), S("src", 16 * k - 16, 16 * k)))
+                (cp if k in SENDV else act)(o, IND(whole("pre"), S("src", 16 * k - 16, 16 * k)))
                 dst = T.cores[(rank + k) % N]
                 sem = "out%d" % (3 * t + k - 1)
                 sent.append(rec("g", lambda o=o, here=here, sem=sem, t=t, dst=dst: g.remote_dma(
@@ -751,67 +857,77 @@ def rank_program(g, core, T, topo):
             act(S(snd, 768, 1024), IND(whole("pre"), S("src", 48, 64)))
             gathered[:] = [act(here, S(snd, 768, 1024))]
             n_in = sum(len(lanes_of(T.cores[q], core)) for q in range(N) if q != rank)
-            rec("x", None, [S(nxt, L * q, L * q + L) for q in range(N) if q != rank], [], 0.0, kind="land", sem="arr%d" % t,
-                n=n_in, after=sent)
+            landed = rec("x", None, [S(nxt, L * q, L * q + L) for q in range(N) if q != rank], [], 0.0, kind="land",
+                         sem="arr%d" % t, n=n_in, after=sent)
             lines["g"] = sent[-1:]
-            if t in (1, 2):
+            if t < 3:
                 first = len(ops)
-                if t == 1:
-                    for buf, of, x in (("i32", "ib", 1.0), ("iZG", "ib", ZG / 3), ("iZV", "ib", ZV / 3), ("onB", "ones", -BIG)):
+                if t == 0:
+                    for buf, of, x in (("i32", "ib", 1.0), ("iZG", "ib", ZG / 3), ("iZV", "ib", ZV / 3)):
                         act(whole(buf), whole(of), scale=x)
+                    act(whole("sel8"), S("ones", 0, 128, 16), scale=256.0)
+                elif t == 1:
+                    act(whole("rst"), whole("jr"), F.Sign, C(cY), -2.0)
+                    act(whole("ugw"), whole("rst"), None, -0.5, -0.5)
                 else:
-                    for o, b in [(S("own", 16 * b, 16 * b + 16), b) for b in range(5)] + [(S("c0", 0, 16), 0), (S("c0", 16, 32), 4)]:
+                    for o, b in ((S("c0", 0, 16), 0), (S("c0", 16, 32), 4)):
                         act(o, whole("lo16"), None, float(mine[b][1]), float(mine[b][0]))
+                    act(whole("rst"), whole("jr"), F.Relu, 1e29, -1e29)
                 for i in range(first, len(ops)):
                     ops[i]["after"] = list(gathered)
-            claims()
-            tt(whole("dmk"), S("pE0", 0, L), whole("dm"), A.mult)
-            mms([(S("pC", 0, 16), whole("ib"), S("pb", 16, 32), True, False), (S("pC", 0, 16), whole("ibn"), S("pb", 0, 16), False, False)])
-            conv(S("pC", 0, 16), "zE", "dmk", 0, 16, 1, False, True)
-            tt(whole("ot"), S("pC", 0, 16), whole("cd"), A.min)
-            ts(whole("o16"), whole("ot"), 2048.0, A.add)
+                first = len(ops)
+                if t == 1:
+                    fill("jm", W, JW, 200)
+                    fill("cF", 0, 64, -72 if 3 in ONV[2] else 184)
+                for i in range(first, len(ops)):
+                    ops[i]["after"] = list(sent[-1:])
+
+            claims(S("s16", 32, 48), S("s16", 32, 48))
+            scan(whole("cs"), whole("msk"), S("pE0", 0, L), A.mult, A.max)
+            tt(whole("o16"), S("cs", 15, L, 16), whole("cd"), A.min)
             keep[0] = True
             for tab, j, n in (("tV", 2, 16), ("tF", 0, 16), ("tG", 1, GP if t < RO - 2 else 16)):
                 cp(IND(S(tab, 0, LC), S("o16", 0, n)), S(lnd, j, 64 * n, 4))
             keep[0] = False
         else:
-            keep[0] = True
-            act(whole("plm"), IND(whole("jm"), S("s16", 32, 48)))
-            act(whole("yfb"), IND(whole("tG"), S("s16", 0, 16)))
-            act(whole("yvb"), IND(whole("lo"), S("s16", 64, 80)))
-            keep[0] = False
+            call("yf", act(whole("yfb"), IND(whole("tG"), S("s16", 0, 16))))
+            call("yv", act(whole("yvb"), IND(whole("lo"), S("s16", 16, 32))))
             dma("s", T.yf[:], whole("yfb"))
             dma("s", T.yv[:], whole("yvb"))
-            banks = ("pK1", "pK0")
-            for h in range(2):
-                mms([(S(banks[h], j, 384, 3), S(lnd, 512 * h + j, 512 * h + 512, 4), whole("ib"), j == 0, False)
-                     for j in range(3)])
-            mms([(S("pB", 8 * h, 8 * h + 8), S("plm", 128 * h, 128 * h + 128), whole("sel0"), h == 0, h == 1) for h in range(2)])
-            claims()
-            lines["v"] = [len(ops) - 2]
-            keep[0] = True
-            cp(S("pb", 32, 48), S("pB", 0, 16))
-            for i in range(16):
-                if i == 1:
-                    tt(whole("dmk"), S("pE0", 0, L), whole("dm"), A.mult)
-                ts(S("eqf", 128 * i, 128 * i + 128), S("jb", 0, 128), S("pb", 32 + i, 33 + i), A.is_equal)
-            keep[0] = False
-            for h in range(2):
-                mms([(S(banks[h], j, 384, 3), S("dmk", 128 * h, 128 * h + 128), whole("onB"), False, j == 2)
-                     for j in range(3)])
-                act(S("vT", 384 * h, 384 * h + 384), S(banks[h], 0, 384), F.Relu)
-            for h in range(2):
-                for b, bank in enumerate(("pA", "pB")):
+            call("ck", tt(whole("ck"), IND(S("pen", 0, L), whole("lhk")), whole("ktab"), A.add))
+            call("cs", scan(whole("cs"), whole("rst"), whole("ck"), A.add, A.min))
+            call("ci", tt(whole("ci"), S("cs", 15, L, 16), whole("nfb"), A.add))
+            call("cm", ts(whole("cm"), whole("ci"), 4095 + 63 * 2 ** 25, A.bitwise_and))
+            call("cl", ts(whole("cl"), whole("cm"), float(NC), A.min))
+            claims(whole("cl"), whole("cm"), float(NC), A.min)
+            call("plm", act(whole("plm"), IND(whole("jm"), whole("cl"))))
+            call("dmk", tt(whole("dmk"), IND(whole("eqd"), whole("dgl")), whole("ugw"), A.mult))
+            mms([(S("pE0", 8 * h, 8 * h + 8), S(x, 128 * h, 128 * h + 128), whole(w), False, h == 1 and x == "dmk")
+                 for x, w in (("plm", "sel0"), ("dmk", "sel8")) for h in range(2)])
+            call("pm", cp(S("pb", 32, 48), S("pE0", 0, 16)))
+            for b, bank in enumerate(("pK1", "pB")):
+                for h in range(2):
                     for e in range(4):
                         i = 8 * h + 4 * b + e
+                        o = S("eqf", 128 * i, 128 * i + 128)
+                        if i in ONA:
+                            call("hot", act(S("sg", 128 * i, 128 * i + 128), S("jb", 0, 128), F.Abs, S("pb", 32 + i, 33 + i), -1.0))
+                            call("hot", act(o, S("sg", 128 * i, 128 * i + 128), F.Relu, 1.0, -1.0))
+                        else:
+                            call("one", ts(o, S("jb", 0, 128), S("pb", 32 + i, 33 + i), A.is_equal))
                         mm(S(bank, 48 * e, 48 * e + 48), S("eqf", 128 * i, 128 * i + 128), S("vT", 48 * i, 48 * i + 48),
                            h == 0 and e == 0, h == 1 and e == 3)
-            act(S("zts", 0, 192), S("pA", 0, 192))
-            cp(S("zts", 192, 384), S("pB", 0, 192))
+            call("zts", act(S("zts", 0, 192), S("pK1", 0, 192)))
+            call("zts", act(S("zts", 192, 384), S("pB", 0, 192)))
             ends = (("pE0", T.zf, 1), ("pK0", T.zg, 2), ("pK1", T.zv, 0))
             for j, (bank, out, b) in enumerate(ends):
                 turn([(S(bank, 0, 128), S("zts", j, 384, 3))], "i32")
             for j, (bank, out, b) in enumerate(ends):
-                tt(S("zb", 128 * j, 128 * j + 128), S(bank, 0, 128), S("zb0", 128 * b, 128 * b + 128), A.add)
+                call("z", tt(S("zb", 128 * j, 128 * j + 128), S(bank, 0, 128), S("zb0", 128 * b, 128 * b + 128), A.add))
                 dma("a" if j == 1 else "s", out[:], S("zb", 128 * j, 128 * j + 128))
+            for o in ORDER4:
+                for x in o.split():
+                    some = named[x.rstrip("*")]
+                    for i in range(len(some) if x[-1] == "*" or x in step else 1):
+                        line(some.pop(0))
     emit(g, T, arrange(ops))

from concourse.mybir import AluOpType, AxisListType, ActivationFunctionType

W, L, RO = 4096, 256, 5
TAU = [96, 700, 24, 2496, 300]
WA = [7, 113, 51, 229, 87, 19, 161, 203, 35, 149, 71, 247, 93, 181, 125, 11]
WB = [1, 3, 2, 7, 5, 1, 6, 3, 7, 2, 5, 4, 1, 6, 3, 5]
KP = [3, 18, 45, 71, 102, 125, 150, 187, 208, 233, 260, 291, 318, 345, 382, 407]
LC, ZG, WGN = 4352, 5376, 5392
OFF = 4194304
LV, LE, ZV, LON = 4096, 5120, 5184, 5200
NC, JW = 4096, 4112
EPS = 2.0 ** -20
BIG = 33554432.0
B16, F16, F32, I32, U16 = "bfloat16", "float16", "float32", "int32", "uint16"

_SB = {
    "tF": (4352, B16), "tV": (4352, B16), "tG": (WGN, B16), "lo": (LON, B16),
    "vg": (W, B16), "eqf": (W, B16), "sg": (W, B16), "eqd": (W, B16),
    "lnd0": (1024, B16), "lnd1": (1024, B16), "lnd2": (1024, B16), "lnd3": (1024, B16), "lnd4": (1024, B16),
    "snd0": (1024, B16), "snd1": (1024, B16), "snd2": (1024, B16), "snd3": (1024, B16),
    "pre": (1040, B16), "idt": (1280, B16), "yfb": (L, B16), "yvb": (L, B16), "zb": (384, F32), "zb0": (384, F32),
    "zts": (384, F32), "vT": (768, B16), "vt": (L, B16), "plm": (L, B16),
    "wfs": (L, B16), "wvs": (L, B16), "nms": (L, I32), "nmb": (L, B16), "thf": (L, B16),
    "pcol": (16, I32), "col": (32, F32), "jf": (144, F32), "jr": (L, F32), "jq": (128, F32), "j4": (144, F32), "lo16": (16, F32),
    "jb": (L, B16), "ab": (16, F32), "ab2": (16, F32), "ib": (128, B16), "ih": (128, F16), "nil": (128, B16),
    "ones": (128, B16), "uge": (128, B16), "uget": (128, B16), "wn": (128, B16), "shf": (128, B16),
    "zA": (144, B16), "zB": (144, B16), "z0": (144, B16), "z0n": (144, B16), "zX": (144, B16), "z1": (144, B16),
    "zr1": (144, B16), "zr13": (144, B16), "z16": (144, B16), "z4": (144, B16), "zE": (144, B16),
    "wsh": (L, B16), "e16": (16, F32), "nm0": (L, B16), "l16": (16, F32),
    "oH": (48, F16), "dk": (1536, F16), "dm": (L, B16), "hc": (192, B16),
    "iE": (128, B16), "iS": (128, B16), "i16": (128, B16), "ibn": (128, B16), "i32": (128, F32),
    "iO": (128, B16), "iOn": (128, B16), "i256": (128, B16), "iZG": (128, B16), "iZV": (128, B16),
    "cE": (64, B16), "ktab": (L, F32), "k32": (96, F32), "repn": (16, U16), "mk": (L, F32), "lhk": (16, U16),
    "c13": (192, B16), "c1": (320, B16), "c2": (384, B16), "msk": (L, B16), "onS": (128, B16), "ugS": (128, B16), "pz": (L, B16), "cst": (64, B16), "dm4": (64, F16), "tt2": (32, F16), "oS": (32, F32),
    "cd": (16, F32), "c0": (32, F32), "own": (32, F32), "rep": (16, U16), "repc": (16, U16), "l15": (6, U16),
    "eH": (32, F16), "nmw": (6 * L, B16),
    "jw": (JW, F32), "jm": (JW, B16), "pq": (16, F32), "pb": (48, B16), "sel0": (8, B16),
    "ui": (32, I32), "u": (16, I32), "zf4": (64, B16), "hr": (192, I32), "hq": (192, F16), "iq": (128, B16), "uk": (80, F32),
    "uh": (16, F16), "ch": (64, F16), "hi": (L + 16, I32), "h16": (L, U16), "cmp": (2 * L, B16),
    "nfin": (16, B16), "nf": (16, B16), "nv": (16, B16), "valb": (16, B16),
    "ck": (L, F32), "cs": (L, F32), "rst": (L, B16), "nfb": (16, F32), "ci": (16, I32), "cm": (16, I32), "cl": (16, U16),
    "cF": (64, B16), "sel8": (8, B16), "dgl": (16, U16), "ugw": (L, B16),
    "pen": (448, B16), "ks": (64, F32), "kt": (320, F32), "k2": (320, F32), "k3": (32, F32), "step": (L, B16), "ksel": (L + 16, F32),
    "ki": (16, I32), "val": (16, I32), "hb": (80, F32), "hm": (80, F32), "s16": (80, U16),
    "gi": (16, I32), "g3": (16, I32), "go4": (64, B16), "inc": (64, B16), "tt4": (64, F16), "pos": (16, U16), "src": (64, U16),
    "plr": (L, F16), "plh": (L, F16), "oneh": (128, F16), "dmk": (L, B16), "o16": (16, U16),
}
_PS = ["pV", "pT", "pE0", "pK0", "pK1", "pA", "pB", "pC"]
SCRATCH = {}
_AT = {}
for _k in _SB:
    if _SB[_k][0] <= 96:
        _a = "small_" + _SB[_k][1]
        _n = SCRATCH[_a][1][1] if _a in SCRATCH else 0
        _AT[_k] = (_a, _n)
        SCRATCH[_a] = ("sbuf", [128, _n + (_SB[_k][0] + 15) // 16 * 16], _SB[_k][1])
    else:
        SCRATCH[_k] = ("sbuf", [128, _SB[_k][0]], _SB[_k][1])
DIMS = {"lnd%d" % _k: (L, 4) for _k in range(RO)}
for _k in DIMS:
    SCRATCH[_k] = ("sbuf", [128] + list(DIMS[_k]), _SB[_k][1])
for _k in _PS:
    SCRATCH[_k] = ("psum", [128, 1024], B16) if _k in ("pV", "pT") else ("psum", [128, 512], F32)
NDMA = 27
SEMAPHORES = ["cv", "ca", "cp_", "cg"] + ["d%d" % i for i in range(NDMA)] + ["arr%d" % i for i in range(4)] + \
             ["out%d" % i for i in range(12)]
CYC, PEC, VFIX, AFIX, RISS, RLAT, LOAD = 0.00083, 0.00052, 0.053, 0.14, 0.55, 1.3, 3.0
HOP, SELF, PEHOP, VADD, GAT, SCA, MNX = 0.07, 0.085, 0.07, 0.065, 1.52, 2.2, 0.6
LAG = 0.0
FROM, TO = {"a": 0.1}, {"a": 0.03, "v": 0.04}
GP, SP = 8, 1
CLAIMS = [0, 13, 14, 15, 1, 9] + list(range(2, 9)) + [10, 11, 12]
NAB, NDK = 6, 4
EARLY = 14
SENDV = ()
FUSE = (2,)
ONA = (13, 15)
ONV = ((2,), (2,), ())
ORDER = ("ui u w t uh sh h0 ch p0 r0 kind r1 kinds rest p1 m0 b0 a1 m1 b1 a2 m2 b2 s2 m3 a3 b3 tab tG cut",
         "cmp vt g0 g1 s0 g2 g3 s1 s3 relu ks nf nfin shift",
         "open H C T X dk V8 names flags K0 E0 S0 K1 E1 K2 E2 S2 S1 K3 S3 E3 pen parts", "cmp2 jw* jm zero")
ORDER4 = ("ui u w t uh sh h0 ch p0 r0 kind r1 kinds rest p1 b0 own a1 b1 m0 a2 b2 a3 b3 tab m1 m2 ck cs ci cm cl* m3 eq* dmk "
          "best pm best one best one best* one one one sv one* step ksel hm s16 z*",
          "cmp vt g0 g1 g2 g3 s0 vT relu s1 s2 plr plm relus s3 ks hot* yv zts* zb0 yf",
          "open H C T X dk V8 om opens flags parts E0 E1 K0 TT E2 S0 E3 K1 pen K2 pen3 S1 S2 K3 pens S3", "cmp2 jm vT2")
ORDER0 = ("ab ab ab pc pc pc ab pc ab cZ cY keep ab ab e16 ab z1 ab* A cW A z0 A repn rep zA cX cX cX cF nmb ones z0n dk* "
          "ui lo16 u w ih t uh sh lo16 h0 ch aux cL r0 lhk r1 B rest "
          "m2 m0 kind kinds s2 m1 a0 b0 a1 m3 b1 e2 a3 b3 tab shf* repc cut z4",
          "da da da x0 da da nm0 da* thf vt wn zX z16 zE g0 cmp g1 s0 g3 ct f2 s1 s3 relu zr13 ks eH* nf nfin oH* wsh zB "
          "shift oneh onS* pz cd",
          "H there T init dk V8 C X open K2 T2 K0 S2 K1 S0 flags E0 C8 K3 E1 E2 S1 S3 E3 pen wshp parts names",
          "pcol jf nil ib jq k32* hc l16 iOn c13* c1* c2* cE* ibn i256 iS iE iO cmp2 yv* jr mk kt* i16 zero dm* zero zero zero iq uge msk* jb zero*")


def boxed(dims, cols):
    out = []
    for d in range(len(dims)):
        below = 1
        for e in dims[d + 1:]:
            below *= e
        x = sorted(set(c // below % dims[d] for c in cols))
        out.append(x[0] if len(x) == 1 else slice(x[0], x[-1] + 1, x[1] - x[0]))
    return (slice(0, 128),) + tuple(out)


def S(name, lo, hi, step=1):
    if name in _AT:
        return ("ap", _AT[name][0], _AT[name][1] + lo, _AT[name][1] + hi, step)
    return ("ap", name, lo, hi, step)


def BOX(name, cols):
    return ("ap", name, 0, 0, 0, cols)


def IND(win, off):
    return ("ind", win, off)


def columns(a):
    return a[5] if len(a) > 5 else range(a[2], a[3], a[4])


def width(a):
    return 16 * width(a[2]) if a[0] == "ind" else len(columns(a))


def _mask(a):
    if a[1] in _PS:
        return 1
    if a[4] == 1:
        return ((1 << (a[3] - a[2])) - 1) << a[2]
    m = 0
    for i in columns(a):
        m |= 1 << i
    return m


def arrange(ops):
    n = len(ops)
    pred = [dict() for _ in ops]
    acc = {}
    for i, o in enumerate(ops):
        for name, m, wr in o["t"]:
            if name in _PS:
                j = acc.get(name)
                if j is not None and j != i:
                    pred[i][j] = max(pred[i].get(j, 0.0), 0.0 if ops[j]["q"] == o["q"] else PEHOP if ops[j]["q"] == "p" else HOP)
                acc[name] = i
                continue
            for j, mj, wj in acc.get(name, []):
                if j != i and (m & mj) and (wr or wj):
                    pred[i][j] = SELF if ops[j]["q"] == o["q"] else HOP
        for name, m, wr in o["t"]:
            if name not in _PS:
                lst = acc.setdefault(name, [])
                if wr:
                    lst[:] = [e for e in lst if e[1] & ~m]
                lst.append((i, m, wr))
        for j in o.get("after", []):
            pred[i][j] = max(pred[i].get(j, -99.0), HOP if ops[j]["q"] != o["q"] else -ops[j]["lat"])
    succ = [dict() for _ in ops]
    for i in range(n):
        for j in pred[i]:
            pred[i][j] += ops[j]["lat"]
            if ops[j]["q"] != ops[i]["q"]:
                pred[i][j] += FROM.get(ops[j]["q"], 0.0) + TO.get(ops[i]["q"], 0.0)
            succ[j][i] = pred[i][j]
    left = [len(s) for s in succ]
    todo = [i for i in range(n) if not left[i]]
    chain = [0.0] * n
    depth = [0] * n
    for i in todo:
        chain[i] = (1e-3 if ops[i].get("idle") else ops[i]["c"]) + max([w + chain[k] for k, w in succ[i].items()] + [ops[i]["lat"]])
        depth[i] = 1 + max([depth[k] for k in succ[i]] + [0])
        for j in pred[i]:
            left[j] -= 1
            if not left[j]:
                todo.append(j)
    assert len(todo) == n, [ops[i].get("nm") for i in range(n) if left[i]][-9:]
    end = [0.0] * n
    busy = {}
    for i in sorted(range(n), key=lambda i: (-round(chain[i], 6), -depth[i], i)):
        c = ops[i]["c"]
        t = max([end[j] + w for j, w in pred[i].items()] + [0.0])
        starts, ends = busy.setdefault(ops[i]["q"], ([], []))
        k = len(ends)
        while k > 0 and ends[k - 1] > t:
            k -= 1
        while k < len(starts) and starts[k] < t + c - 1e-9:
            t = max(t, ends[k])
            k += 1
        starts.insert(k, t)
        ends.insert(k, t + c)
        end[i] = t + c
    return [ops[i] for i in sorted(range(n), key=lambda i: (round(end[i] - ops[i]["c"], 6), -depth[i], i))]


def emit(g, T, ops):
    Q = {"v": g.vector, "a": g.scalar, "p": g.tensor, "s": g.sync, "g": g}
    CS = {"v": "cv", "a": "ca", "p": "cp_", "g": "cg"}
    cnt = {"v": 0, "a": 0, "p": 0, "g": 0}
    known = {q: {} for q in Q}
    acc = {}
    total = {}
    tok = []
    for i, o in enumerate(ops):
        q = o["q"]
        need = {}
        if o["kind"] != "land":
            for name, m, wr in o["t"]:
                for j, mj, wj in acc.get(name, []):
                    if not (m & mj):
                        continue
                    if name in _PS:
                        if ops[j]["q"] == q:
                            continue
                    elif not (wr or wj):
                        continue
                    s, n, k = tok[j]
                    if known[q].get(s, 0) < n and need.get(s, (0, None))[0] < n:
                        need[s] = (n, k)
            for s, (n, k) in sorted(need.items(), key=lambda e: -len(e[1][1])):
                if known[q].get(s, 0) >= n:
                    continue
                Q[q].wait_ge(T.sem[s], n)
                known[q][s] = n
                for s2 in k:
                    if known[q].get(s2, 0) < k[s2]:
                        known[q][s2] = k[s2]
        if o["kind"] == "c":
            for f in o["f"]:
                cnt[q] += 1
                f().then_inc(T.sem[CS[q]], 1)
            tok.append((CS[q], cnt[q], dict(known[q])))
            total[CS[q]] = cnt[q]
        elif o["kind"] == "dma":
            o["f"]().then_inc(T.sem[o["sem"]], 16)
            tok.append((o["sem"], 16, dict(known[q])))
            total[o["sem"]] = 16
        elif o["kind"] == "rem":
            o["f"]()
            tok.append((o["sem"], o["n"], dict(known[q])))
            total[o["sem"]] = o["n"]
        else:
            tok.append((o["sem"], o["n"], {}))
            total[o["sem"]] = o["n"]
        for name, m, wr in o["t"]:
            lst = acc.setdefault(name, [])
            if name in _PS:
                lst[:] = [e for e in lst if ops[e[0]]["q"] != q]
            elif wr:
                lst[:] = [e for e in lst if e[1] & ~m]
            lst.append((i, m, wr))
    for s in total:
        if known["g"].get(s, 0) < total[s]:
            g.wait_ge(T.sem[s], total[s])


def rank_program(g, core, T, topo):
    rank = T.rank_of(core)
    if rank is None:
        return
    N = len(T.cores)
    A = AluOpType
    F = ActivationFunctionType
    ops = []
    nd = [0]

    def ap(a):
        if a[0] == "ind":
            return ap(a[1]).indirect(ap(a[2]))
        if a[1] in DIMS:
            return T[a[1]][boxed(DIMS[a[1]], list(columns(a)))]
        if a[4] == 1:
            return T[a[1]][:, a[2]:a[3]]
        return T[a[1]][:, a[2]:a[3]:a[4]]

    lines = {}
    keep = [False]
    named = {}

    def line(i):
        ops[i]["after"] = lines.get(ops[i]["q"], [])
        lines[ops[i]["q"]] = [i]

    def rec(q, f, outs, ins, c, kind="c", lat=0.0, **kw):
        r, w = [], []
        for a in ins:
            if isinstance(a, tuple):
                r += [a[1], a[2]] if a[0] == "ind" else [a]
        for a in outs:
            if a[0] == "ind":
                w.append(a[1])
                r.append(a[2])
            else:
                w.append(a)
        ops.append({"q": q, "f": [f] if kind == "c" and not isinstance(f, list) else f, "kind": kind, "c": c, "lat": lat,
                    "t": [(a[1], _mask(a), False) for a in r] + [(a[1], _mask(a), True) for a in w]})
        if keep[0]:
            line(len(ops) - 1)
        ops[-1].update(kw)
        return len(ops) - 1

    def name(x, i):
        named.setdefault(x, []).append(i)
        ops[i]["nm"] = x

    def sc(x):
        return ap(x) if isinstance(x, tuple) else x

    def vc(o, a, b=None):
        if o[0] == "ind":
            return 0.05 + SCA * CYC * width(o)
        if a[0] == "ind":
            return 0.05 + GAT * CYC * width(o)
        if b is not None:
            return max(VFIX, VADD + CYC * width(o) * (1 if a[1] in _PS or b[1] in _PS else 2))
        two = all(SCRATCH[x[1]][2] in (B16, F16, U16) for x in (o, a))
        return max(VFIX, VADD + CYC * width(o) * (0.5 if two else 1))

    def tt(o, a, b, op):
        return rec("v", lambda: g.vector.tensor_tensor(ap(o), ap(a), ap(b), op), [o], [a, b], vc(o, a, b))

    def ts(o, a, s1, op0, s2=None, op1=None):
        if op1 is None:
            return rec("v", lambda: g.vector.tensor_scalar(ap(o), ap(a), sc(s1), None, op0), [o], [a, s1], vc(o, a))
        return rec("v", lambda: g.vector.tensor_scalar(ap(o), ap(a), sc(s1), sc(s2), op0, op1), [o], [a, s1, s2], vc(o, a))

    def cp(o, a):
        return rec("v", lambda: g.vector.tensor_copy(ap(o), ap(a)), [o], [a], vc(o, a))

    def ms(o, c):
        return rec("v", lambda: g.vector.memset(ap(o), c), [o], [], vc(o, o))

    def scan(o, a, b, op0, op1):
        return rec("v", lambda: g.vector.tensor_tensor_scan(ap(o), ap(a), ap(b), 0.0, op0, op1), [o], [a, b], vc(o, a))

    def act(o, a, func=None, bias=None, scale=None):
        fn = F.Identity if func is None else func
        kw = {}
        if bias is not None:
            kw["bias"] = sc(bias)
        if scale is not None:
            kw["scale"] = sc(scale)
        c = 0.065 + GAT * CYC * width(o) if a[0] == "ind" else AFIX + CYC * width(o)
        return rec("a", lambda: g.scalar.activation(ap(o), ap(a), fn, **kw), [o], [a, bias, scale], c)

    def mms(calls):
        return rec("p", [lambda e=e: g.tensor.matmul(ap(e[0]), ap(e[1]), ap(e[2]), e[3], e[4]) for e in calls],
                   [e[0] for e in calls], [e[1] for e in calls] + [e[2] for e in calls],
                   sum(PEC * max(min(64, width(e[1])), width(e[2])) for e in calls))

    def turn(pairs, ident):
        return rec("p", [lambda e=e: g.tensor.transpose(ap(e[0]), ap(e[1]), ap(whole(ident))) for e in pairs], [e[0] for e in pairs],
                   [e[1] for e in pairs] + [whole(ident)], len(pairs) * 128 * PEC * (4 if ident == "i32" else 1))

    def mm(o, wt, mv, start, stop):
        return mms([(o, wt, mv, start, stop)])

    def iota(o, pat, base, cm):
        c = 0.13 + 2 * CYC * width(o)
        if SCRATCH[o[1]][2] == I32:
            return rec("g", lambda: g.iota(ap(o), pat, base, cm), [o], [], c)
        return rec("g", lambda: g.iota(ap(o), pat, base, cm, allow_small_or_imprecise_dtypes=True), [o], [], c)

    def fill(buf, lo, hi, c):
        return iota(S(buf, lo, hi), [[0, hi - lo]], c, 0)

    def gcopy(o, a):
        return rec("g", lambda: g.affine_select(ap(o), ap(a), [[0, width(o)]], A.is_ge, 0.0, 0, 0), [o], [a], 0.17 + 2 * CYC * width(o))

    def diag(buf, x):
        o, a = whole(buf), whole("nil")
        name(buf, rec("g", lambda: g.affine_select(ap(o), ap(a), [[-1, 128]], A.not_equal, float(x), 0, 1), [o], [a], 0.17 + 256 * CYC))

    def dma(q, o, a, lat=2.5, behind=None):
        s = "d%d" % nd[0]
        nd[0] += 1
        e = g.sync if q == "s" else g.scalar
        rec(q, lambda: e.dma_start(sc(o), sc(a)), [o] if isinstance(o, tuple) else [], [a, behind], 0.05, kind="dma", lat=lat, sem=s)

    def conv(o, z, buf, base, n, stride, first=True, last=True):
        return mms([(o, S(z, 15 - r, 143 - r), S(buf, base + stride * r, base + stride * (r + 16 * n - 16) + 1, stride * 16),
                     first and r == 0, last and r == 15) for r in range(16)])

    def lanes_of(a, b):
        return topo.engines(a, b)

    def C(i):
        return S("col", i, i + 1)

    def R(i):
        return S("e16", i, i + 1)

    def whole(buf):
        return S(buf, 0, _SB[buf][0])

    def lin(x, o, a, scale=1.0, bias=0.0):
        name(x, act(o, a, None, bias, scale) if x in ORDER0[1].replace("*", "").split() else ts(o, a, scale, A.mult, bias, A.add))

    keep[0] = True
    for o, a, lat in ((whole("wfs"), T.wf, 2.2), (whole("nms"), T.nm, 2.6), (whole("wvs"), T.wv, 2.8),
                      (S("tV", 0, W), T.rv, 2.6 + LOAD + LAG)):
        dma("s", o, a[:], lat)
    keep[0] = False

    name("pcol", iota(S("pcol", 0, 1), [[0, 1]], 0, 1))
    name("jf", iota(whole("jf"), [[1, 144]], 0, 0))
    name("jr", iota(whole("jr"), [[0, 16], [1, 16]], 0, 0))
    name("jq", iota(whole("jq"), [[1, 8], [0, 16]], 0, 0))
    name("l16", iota(whole("l16"), [[16, 16]], 0, 1))
    name("zero", iota(whole("j4"), [[1, 36], [0, 4]], 0, 0))
    name("jb", iota(whole("jb"), [[1, L]], 0, 0))
    name("mk", iota(whole("mk"), [[0, 16], [-4096, 16]], 61440, 0))
    name("nil", fill("nil", 0, 128, 0))
    for b in range(0, JW, 1028):
        name("jw", iota(S("jw", b, b + 1028), [[1, 1028]], b - 2048, 0))
    for buf, x in (("ib", 1), ("ibn", -1), ("iE", -2 * BIG), ("iS", 16 * BIG), ("iO", OFF), ("iOn", -OFF), ("i256", 256), ("i16", 16),
                   ("iq", -W)):
        diag(buf, x)
    both = [WA[i] + WB[i] / 16 for i in range(16)]
    for i in range(NAB):
        name("ab", ms(S("ab", i, i + 1), both[i]))
    for i in range(NAB, 16, 2):
        name("ab", ts(S("ab", i, i + 2), S("jf", 0, 2), both[i + 1] - both[i], A.mult, both[i], A.add))
    (cP, cR, cG, cJ, cA, cB, cT, cF, cSH, cKEEP, c4G, c40, cZ, cX, cY, cG16, cW, cAB, cX2, cAB2, cES, cL15, cD, cD2, c16R) = range(25)
    name("pc", ts(S("pcol", 1, 2), S("pcol", 0, 1), 15, A.bitwise_and))
    name("pc", ts(S("pcol", 2, 3), S("pcol", 0, 1), 4, A.arith_shift_right))
    name("pc", ts(S("pcol", 3, 4), S("pcol", 0, 1), 3, A.bitwise_and))
    name("pc", cp(S("col", 0, 4), S("pcol", 0, 4)))
    for m in range(0, 6, 2):
        k0, k1 = ([0] + KP)[m:m + 2]
        name("k32", iota(S("k32", 16 * m, 16 * m + 32), [[32 * (k1 - k0), 2], [0, 16]], 1 + 32 * k0, 0))
    assert all(KP[m] % 2 == m % 2 for m in range(4, 16))
    name("hc", iota(whole("hc"), [[0, 6], [-2048, 2], [0, 16]], 2048, 0))
    name("cZ", ts(C(cZ), C(cG), 16.0, A.mult, 15.0, A.add))
    name("cY", ts(C(cY), C(cR), 2.0, A.mult, 1.0, A.add))
    name("e16", ts(whole("e16"), S("jf", 0, 16), C(cR), A.is_equal))
    name("z1", ts(whole("z1"), whole("jf"), C(cZ), A.is_equal))
    name("keep", ts(C(cKEEP), C(cR), 4.0, A.is_le, EPS, A.mult))
    name("cW", ts(C(cW), R(13), EPS, A.mult))
    name("dm", gcopy(S("dm", 0, 16), whole("e16")))
    for n in (16, 32, 64, 128):
        name("dm", gcopy(S("dm", n, 2 * n), S("dm", 0, n)))
    name("ones", ts(whole("ones"), whole("jq"), C(cG), A.is_equal))
    name("nmb", ts(whole("nmb"), whole("nms"), C(cKEEP), A.mult, C(cW), A.add))
    dma("s", S("tF", 0, W), T.rf[:], 2 * LOAD - 0.6 + LAG, S("nmb", 0, 1))
    dma("s", S("tG", 0, W), T.rg[:], 2 + LOAD, S("tF", 0, 1))
    name("nm0", act(whole("nm0"), whole("nmb"), F.Relu, EPS * EPS / 2, -1.0))
    name("A", tt(whole("ab2"), whole("ab"), whole("e16"), A.mult))
    name("A", rec("v", lambda: g.vector.tensor_reduce(ap(C(cAB)), ap(whole("ab2")), AxisListType.X, A.add), [C(cAB)],
                  [whole("ab2")], 0.07))
    name("A", ts(C(cA), C(cAB), 3.0 * OFF, A.add, -3.0 * OFF, A.add))
    name("B", ts(C(cB), C(cAB), C(cA), A.subtract, 16.0, A.mult))
    name("repn", ts(whole("repn"), S("jf", 0, 16), 0.0, A.mult, C(cY), A.add))
    name("rep", ts(whole("rep"), S("jf", 0, 16), 0.0, A.mult, C(cR), A.add))
    name("repc", cp(whole("repc"), S("jf", 0, 16)))
    name("z0", ts(whole("z0"), whole("z1"), R(0), A.mult, 2 / EPS, A.mult))
    name("z0n", ts(whole("z0n"), whole("z1"), R(0), A.mult, -4 / EPS, A.mult))
    name("there", mm(S("pE0", 0, L), whole("ones"), whole("wfs"), True, True))
    name("init", mms([(S("pC", 0, L), whole("ib"), whole("nmb"), True, False),
                      (S("pC", 0, L), S("z0", 5, 133), whole("nmb"), False, False),
                      (S("pC", 0, L), S("z0n", 7, 135), whole("nmb"), False, False),
                      (S("pC", 0, L), S("z0", 1, 129), whole("nm0"), False, True)]))
    name("thf", act(whole("thf"), S("pE0", 0, L), F.Sign))
    name("aux", tt(S("lnd0", 3, 1024, 4), S("pC", 0, L), whole("thf"), A.mult))
    name("x0", act(S("lnd0", 0, 1024, 4), whole("wfs")))
    name("yv", gcopy(S("lnd0", 1, 1024, 4), whole("wfs")))
    name("yv", gcopy(S("lnd0", 2, 1024, 4), whole("wvs")))
    lin("oneh", whole("oneh"), whole("ones"))
    name("ih", cp(whole("ih"), whole("ib")))
    name("zA", ts(whole("zA"), whole("z1"), C(cA), A.mult))
    name("cF", ts(C(cF), R(14), -256.0 / EPS, A.mult))
    name("cX", ts(C(cX), R(13), -256.0, A.mult, R(1), A.add))
    name("cX", ts(C(cES), R(14), 512.0, A.mult, C(cX), A.add))
    name("cX", ts(C(cT), C(cES), 1 / EPS, A.mult))
    lin("wn", whole("wn"), whole("ones"), C(cF))
    lin("zX", whole("zX"), whole("z1"), C(cT))
    name("c13", fill("c13", 0, 64, -13))
    name("c13", iota(S("c13", 64, 192), [[-16, 2], [0, 64]], -2, 0))
    name("c1", fill("c1", 0, 320, 4))
    name("c1", iota(S("c1", 1, 320, 5), [[0, 64]], 200, 0))
    name("cE", fill("cE", 0, 64, 16))
    name("c2", iota(S("c2", 0, 320), [[-1, 4], [0, 16], [-4, 5]], 23, 0))
    name("c2", iota(S("c2", 320, 384), [[-1, 4], [0, 16]], 3, 0))
    name("kt", fill("kt", 0, 320, 2 ** 24 - 1))
    name("kt", rec("g", lambda: g.affine_select(ap(S("kt", 0, 320, 5)), ap(S("jf", 0, 64)), [[0, 64]], A.is_gt, -1e29, 0, 0),
                   [S("kt", 0, 320, 5)], [S("jf", 0, 64)], 0.17 + 128 * CYC))
    lin("z16", whole("z16"), whole("z1"), 16.0)
    lin("zE", whole("zE"), whole("z1"), 2 * BIG)
    for m in range(4, 16):
        if m < 4 + NDK:
            name("dk", ts(S("dk", 128 * m - 512, 128 * m - 384), whole("ib"), float(KP[m]), A.mult))
        else:
            name("da", act(S("dk", 128 * m - 512, 128 * m - 384), whole("ib"), scale=float(KP[m])))
    name("cL", ts(C(cL15), C(cR), 16.0, A.mult, 15.0, A.add))
    ts(C(cX2), C(cR), 2.0, A.is_ge, C(cKEEP), A.mult)
    ts(C(cAB2), C(cX2), -257.0 / EPS, A.mult, C(cP), A.add)
    tt(C(cD), R(0), R(13), A.add)
    name("lo16", ts(C(cG16), C(cG), 16.0, A.mult))
    ts(C(c4G), C(cG), 4.0, A.mult, 3.0, A.add)
    ts(C(c40), R(0), 4.0, A.mult)
    ts(C(cD2), C(cD), -256.0, A.mult, 256.0, A.add)
    tt(C(cSH), C(cD2), C(cAB2), A.add)
    name("lo16", ts(whole("lo16"), whole("l16"), C(cG16), A.subtract))
    lin("zB", whole("zB"), whole("z1"), C(cB))
    name("shf", ts(whole("shf"), S("jf", 0, 128), C(cSH), A.is_equal))
    name("shf", ts(whole("zr1"), whole("z1"), R(1), A.mult, 2 / EPS, A.mult))
    lin("zr13", whole("zr13"), whole("z1"), R(13))
    name("wshp", mms([(S("pC", b, b + 128), whole(w), x, b == 0 and i == 0, b == 128 and i == 3)
                      for b, xs in ((0, (("ib", whole("shf")), ("ib", S("zr1", 5, 133)), ("ibn", S("zr1", 7, 135)), ("ibn", S("zr1", 7, 135)))),
                                    (128, (("ib", whole("shf")), ("ib", S("z0", 5, 133)), ("ib", S("z0n", 7, 135)), ("ib", S("zr13", 1, 129)))))
                      for i, (w, x) in enumerate(xs)]))
    name("wsh", act(whole("wsh"), S("pC", 0, L)))
    mine = ((4, LC), (4, LC + 1), (0, NC), (4, 2 * L + 3), (4, LV + 2))
    for b, (s0, b0) in enumerate(mine):
        if b < 3:
            lin("oH", S("oH", 16 * b, 16 * b + 16), whole("lo16"), float(s0), float(b0 % W + (b == 0)))
        else:
            lin("oH", S("oS", 16 * b - 48, 16 * b - 32), whole("lo16"), float(s0), float(b0))
    for b in range(2):
        lin("eH", S("eH", 16 * b, 16 * b + 16), whole("lo16"))
    name("lhk", ts(whole("lhk"), S("jf", 0, 16), C(cL15), A.subtract, 255.0, A.add))
    name("z4", ts(whole("z4"), whole("j4"), C(c4G), A.is_equal, C(c40), A.mult))
    lin("uget", whole("uget"), whole("ones"), -1.0)
    name("uge", rec("g", lambda: g.affine_select(ap(whole("uge")), ap(whole("uget")), [[-1, 128]], A.is_ge, 0.0, 0, 1),
                    [whole("uge")], [whole("uget")], 0.17 + 256 * CYC))
    name("msk", fill("msk", 0, L, 1))
    name("msk", iota(S("msk", 0, L, 16), [[0, 16]], 0, 0))
    lin("onS", whole("onS"), whole("ones"), 8192.0)
    lin("onS", whole("ugS"), whole("uge"), 8192.0)
    lin("pz", whole("pz"), whole("dm"), OFF + 2048.0, -1.0 * OFF)
    name("zero", iota(whole("cst"), [[256, 4], [0, 16]], W, 0))
    ts(whole("dm4"), IND(whole("lo16"), S("rep", 0, 4)), 1024.0, A.add)
    lin("cd", whole("cd"), whole("lo16"), 1.0, 4096.0)
    dma("s", S("tG", W, LC), whole("wfs"), 2.5, S("tF", 0, 1))
    for buf, lo, hi in (("tG", ZG, WGN), ("lo", LE, LON), ("pre", 1024, 1040)):
        name("zero", fill(buf, lo, hi, 0))
    for d in range(4):
        name("zero", fill("idt", L * d, L * d + 64, 256))
    ts(whole("sel0"), S("jf", 0, 8), C(cG), A.is_equal, R(0), A.mult)
    ts(C(c16R), C(cR), 16.0, A.mult)
    ts(whole("dgl"), whole("lo16"), 17.0, A.mult, C(c16R), A.subtract)

    gathered = []
    for t in range(RO):
        lnd = "lnd%d" % t
        last = t == RO - 1
        var = 2 if last else min(t, 1)
        onv = ONV[var]

        def hashes():
            if t == 0:
                conv(S("pA", 0, 32, 2), "zA", "wfs", 0, 16, 1, True, False)
                conv(S("pA", 1, 32, 2), "z0", "nmb", 0, 16, 1, False, True)
            else:
                mms([(S("pA", 0, 32), S("zA", 15 - r, 143 - r), BOX(lnd, [64 * c + 4 * r + j for c in range(16) for j in (0, 3)]),
                      r == 0, r == 15) for r in range(16)])

        def later(bank, stop):
            mms([(S(bank, 0, 192), whole("ib"), whole("hc"), True, False)] +
                [(S(bank, 16 * m, 16 * m + 16), S("dk", 128 * m, 128 * m + 128), whole("uh"), False, False) for m in range(12)])
            mms([(S(bank, 64 * i, 64 * i + 64), whole("ih"), whole("ch"), False, stop and i == 2) for i in range(3)])

        kind = S("pA", 32, 48)

        def kinds():
            ts(S("zf4", 0, 16), kind, 0.0, A.is_ge, 3.0, A.mult)
            if last:
                ts(whole("nfb"), kind, 256.0, A.is_lt, BIG, A.mult)

        def names():
            if not last:
                mms([(S("pC", L * i, L * i + L), S("wsh", 128 * i, 128 * i + 128), S(lnd, 3, 1024, 4), i == 0, i == 1) for i in range(2)])

        behind = S("tF", 0, 1) if t == 0 else None
        dma("s", S("tG", LC, ZG), whole(lnd), 3.5, behind)
        dma("s", S("lo", LV, LE), whole(lnd), 4.5, behind)
        if not last:
            dma("s", S("nmw", 2 * L, 6 * L), whole(lnd), 5.5, behind)

        def gv(c):
            act(S("vg", 1024 * c, 1024 * c + 1024), IND(S("tV", 0, W), S("h16", 64 * c, 64 * c + 64)))

        def sgn(c):
            o, a = S("sg", 1024 * c, 1024 * c + 1024), S("lo", 1024 * c, 1024 * c + 1024)
            if c in onv:
                ts(o, a, float(TAU[t]), A.is_gt, 2.0, A.mult)
            else:
                act(o, a, F.Sign, -(TAU[t] + 0.5))

        def gf(c, m, n):
            m += 4 * c
            tt(S("eqf", L * m, L * (m + n)), IND(S("tF", 0, W), S("h16", 16 * m, 16 * (m + n))), S("cmp", 0, L * n), A.is_equal)

        def mn(c):
            b = 1024 * c
            ops[tt(S("lo", b, b + 1024), S("vg", b, b + 1024), S("pV", 0, 1024), A.min)]["c"] *= MNX

        five = [S("pK0", j, 320, 5) for j in range(5)]
        at = [(S("pE0", 64 * c, 64 * c + 64), S("pE0", 192 + 64 * c, 256 + 64 * c), five[2 + c]) for c in range(3)]
        at.append((five[1], S("pK1", 64, 128), S("pK1", 0, 64)))
        if last:
            at = [(S("pE0", 64 * c, 64 * c + 64), S("pB", 64 * c, 64 * c + 64) if c < 3 else five[1], at[c][2]) for c in range(4)]

        def sums(what, c, stop=False):
            i = "ESK".index(what)
            z = "z16" if i == 2 else "z1" if c < 3 or (last and i == 0) else "zE"
            conv(at[c][i], z, ("eqf", "sg", "lo")[i], 1024 * c, 64, 1, False, stop)

        def consts(bank, parts):
            mms([(S(bank, a, a + width(x)), whole(w), x, i == 0, False) for i, (a, w, x) in enumerate(parts)])

        def bars(bank, a, n, w):
            mms([(S(bank, b, b + 64), whole(w), whole("zf4"), False, False) for b in range(a, a + n, 64)])

        def over(a):
            return [(a + 64 * c, "ib", S("c13", 128, 192) if c in onv else S("c13", 64, 128)) for c in range(3)]

        def opening():
            consts("pE0", [(64 * c, "ib", S("c13", 0, 64)) for c in range(4 if last else 3)] + ([] if last else over(192)))
            consts("pK0", [(0, "iOn", whole("c1")), (0, "ib", S("c2", 0, 320))])
            if last:
                mm(five[1], whole("iO"), whole("cF"), False, False)

        def flags():
            if last:
                consts("pK1", [(0, "iOn", S("c1", 0, 320, 5)), (0, "ib", S("c2", 320, 384))])
                return bars("pE0", 0, L, "ibn")
            consts("pK1", [(0, "iOn", S("c1", 0, 320, 5)), (0, "ib", S("c2", 320, 384)), (64, "iOn", whole("cE"))])
            for e in (("pE0", 0, 192, "ibn"), ("pE0", 192, 192, "i256"), ("pK1", 64, 64, "iS")):
                bars(*e)
            mm(five[1], whole("iE"), whole("zf4"), False, False)

        def lists(some, stop=False):
            mms([(S("pA", 16 * b, 16 * b + 16), whole(w), S(x, 0, 16), False, stop and i == len(some) - 1)
                 for i, (b, w, x) in enumerate(some)])

        def parts():
            if last:
                return consts("pA", [(0, "iO", S("zf4", 0, 32)), (16, "ih", S("eH", 0, 16))])
            consts("pA", [(48, "ih", whole("eH")), (48, "iO", S("zf4", 0, 32))])
            lists([(0, "iO", "zf4"), (2, "iO", "nfin"), (0, "iO", "nf"), (1, "iO", "cE"), (1, "iOn", "nf"), (3, "i16", "nf")])

        def lacks(outs, a, stop):
            mms([(o, whole("ibn"), S("pen", a + 64 * i, a + 64 * i + 64), False, stop and i == len(outs) - 1) for i, o in enumerate(outs)])

        queues = [o.split() for o in (ORDER0 if t == 0 else ORDER4 if last else ORDER)]
        banks = ("E0 E1 E2 E3", "K3 pen3", "K0 K1 K2 pen pens S3", "S0 S1 S2") if last else \
                ("E0 E1 E2 S0 S1 S2", "K3 S3", "K0 K1 K2 pen E3")
        ends = [[x for x in queues[2] if x in b.split()][-1] for b in banks]
        step = {
            "H": (hashes, []), "ui": (lambda: cp(whole("ui"), S("pA", 0, 32)), ["H"]),
            "u": (lambda: ts(whole("u"), S("ui", 0, 32, 2), 4095, A.bitwise_and), []),
            "w": (lambda: tt(whole("uk"), IND(whole("ui"), S("repn", 0, 5)), S("k32", 0, 80), A.add), []),
            "t": (lambda: tt(S("hi", 0, 80), IND(whole("u"), S("rep", 0, 5)), whole("uk"), A.mult), []),
            "uh": (lambda: ts(whole("uh"), whole("u"), -2048.0, A.add), []),
            "sh": (lambda: ts(S("hi", 0, 80), S("hi", 0, 80), 5, A.arith_shift_right, 4095, A.bitwise_and), []),
            "h0": (lambda: cp(S("h16", 0, 64), S("hi", 16, 80)), []),
            "ch": (lambda: ts(whole("ch"), IND(S("hi", 0, 16), S("rep", 0, 4)), -2048.0, A.add), []),
            "dk": (lambda: later("pK1", True), ["ch", "cmp"]), "dk2": (lambda: later("pB", False), ["ch"]),
            "r0": (lambda: ts(whole("hq"), S("pK1", 0, 192), 1.0 / W, A.mult, 1535.5 + 0.5 / W, A.add), ["dk"]),
            "mod": (lambda: mm(S("pB", 0, 192), whole("iq"), whole("hq"), False, True), ["r0", "dk2"]),
            "rest": (lambda: ts(S("h16", 64, L), S("pB", 0, 192), 1536.0 * W, A.add), ["mod"]),
            "r1": (lambda: ts(S("hi", 80, L + 16), S("pB", 0, 192), 1536.0 * W, A.add), ["mod"]),
            "C": (lambda: mms([(S("pK1", 0, L), whole("ib"), S(lnd, 0, 1024, 4) if t else whole("wfs"), True, False),
                               (S("pK1", 0, L), whole("wn"), S(lnd, 3, 1024, 4), False, True)]), []),
            "cmp": (lambda: act(S("cmp", 0, L), S("pK1", 0, L), F.Relu), ["C"]),
            "cmp2": (lambda: gcopy(S("cmp", L, 2 * L), S("cmp", 0, L)), ["cmp"]),
            "jm": (lambda: iota(S("jm", 1024 * t - 1024, 1024 * t), [[0, 8], [1, 128]], 0, 0), []),
            "zero": (lambda: t < 2 or fill("eqd", 2048 * t - W, 2048 * t - 2048, 0), []),
            "T": (lambda: turn([(S("pT", 128 * h, 128 * h + 128), S("wvs", 128 * h, 128 * h + 128) if t == 0 else
                                 S(lnd, 512 * h + 2, 512 * h + 512, 4)) for h in range(2)], "ib"), []),
            "vt": (lambda: act(whole("vt"), S("pT", 0, L)), ["T"]),
            "V8": (lambda: turn([(S("pV", 128 * i, 128 * i + 128), S("vt", 128 * (i % 2), 128 * (i % 2) + 128))
                                 for i in range(8)], "ib"), ["vt"]),
            "T2": (lambda: turn([(S("pT", 128 * h, 128 * h + 128), S("cmp", 128 * h, 128 * h + 128)) for h in range(2)], "ib"), ["cmp", "vt"]),
            "ct": (lambda: act(whole("thf"), S("pT", 0, L)), ["T2"]),
            "C8": (lambda: turn([(S("pT", 128 * i, 128 * i + 128), S("thf", 128 * (i % 2), 128 * (i % 2) + 128))
                                 for i in range(8)], "ib"), ["ct"]),
            "X": (lambda: conv(kind, "zX", lnd, 3, 16, 4), ["ui"]), "kind": (kinds, ["X"]),
            "kinds": (lambda: [gcopy(S("zf4", n, 2 * n), S("zf4", 0, n)) for n in (16, 32)] if "kinds" in ORDER[3] else
                      cp(S("zf4", 16, 64), IND(S("zf4", 0, 16), S("rep", 0, 3))), ["kind"]),
            "nfin": (lambda: act(whole("nfin"), kind, F.Relu, 256.0, -1.0), ["X"]),
            "open": (opening, []), "flags": (flags, ["kinds", "cmp2", "open", "r0"]), "names": (names, []),
            "shift": (lambda: last or act(S("nmw", 0, 2 * L), S("pC", 0, 2 * L)), ["names"]),
            "nf": (lambda: last or act(whole("nf"), kind, F.Relu, -4080.0, -16.0), ["X"]),
            "p0": (lambda: gf(0, 0, 1), ["cmp"]), "p1": (lambda: gf(0, 1, 1), []),
            "relu": (lambda: act(S("pen", 0, L if last else 384), S("pE0", 0, L if last else 384), F.Relu, None, -BIG), [ends[0]]),
            "pen": (lambda: lacks(five[2:] * (1 if last else 2), 0, "pen" in ends), ["relu"]),
            "parts": (parts, ["kinds"] if last else ["kinds", "nf", "nfin"]),
            "ks": (lambda: act(S("kt", 1, 320, 5), S("pK1", 0, 64)) if last else act(whole("ks"), S("pK1", 64, 128)), [ends[1]]),
            "cut": (lambda: tt(S("kt", 1, 320, 5), S("pK1", 0, 64), whole("ks"), A.min), ["ks"]),
            "tG": (lambda: cp(IND(S("tG", 0, LC), S("o16", GP, 16)), S("lnd%d" % (t - 1), 64 * GP + 1, 1024, 4)), []),
            "pen3": (lambda: lacks([S("pK1", 0, 64)], 192, "pen3" in ends), ["relu"]),
            "relus": (lambda: act(S("pen", L, 448), S("pB", 0, 192), F.Relu, None, -BIG), [ends[-1]]),
            "pens": (lambda: lacks(five[2:], L, "pens" in ends), ["relus"]),
            "om": (lambda: mms([(S("pB", 16 * i, 16 * i + 16), whole(w), S("zf4", 0, 16), i == 0, i == 1)
                                for i, w in enumerate(("iZG", "iZV"))]), ["kind", "r1", "rest"]),
            "own": (lambda: tt(whole("own"), S("pB", 0, 32), whole("c0"), A.max), ["om"]),
            "opens": (lambda: consts("pB", over(0)), ["own"]),
            "TT": (lambda: turn([(S("pT", L * j + 128 * h, L * j + 128 * h + 128), S(lnd, 512 * h + j, 512 * h + 512, 4))
                                 for h in range(2) for j in range(2)], "ib"), ["vt"]),
            "vT": (lambda: [act(S("vT", j, 768, 3), S("pT", L * j, L * j + L)) for j in range(2)], ["TT"]),
            "vT2": (lambda: gcopy(S("vT", 2, 768, 3), whole("vt")), ["vt"]),
            "tab": (lambda: tt(whole("ktab"), IND(S("hi", 16, L + 16), whole("lhk")), whole("mk"), A.add), ["r1"])}
        if t in (0, RO - 1) or "mod" not in ORDER[2]:
            step.update({"dk": (lambda: later("pB", True), ["ch"]), "r0": (lambda: cp(whole("hr"), S("pB", 0, 192)), ["dk"]),
                         "r1": (lambda: ts(S("hi", 80, L + 16), whole("hr"), 4095, A.bitwise_and), ["r0"]),
                         "rest": (lambda: cp(S("h16", 64, L), S("hi", 80, L + 16)), ["r1"])})
        for c in range(4):
            step["a%d" % c] = (lambda c=c: gf(c, 0, 2), ["rest", "cmp2"])
            step["b%d" % c] = (lambda c=c: gf(c, 2, 2), ["rest", "cmp2"])
            step["g%d" % c] = (lambda c=c: gv(c), ["rest"] if c else ["h0"])
            step["m%d" % c] = (lambda c=c: mn(c), ["g%d" % c, "V8"])
            if t == 0 and c in FUSE:
                step["m%d" % c] = (lambda c=c: [tt(S("lo", L * m, L * m + L), IND(S("tV", 0, W), S("h16", 16 * m, 16 * m + 16)), whole("wvs"), A.min)
                                                for m in range(4 * c, 4 * c + 4)], ["rest"])
            step["s%d" % c] = (lambda c=c: sgn(c), ["m%d" % c])
            step["f%d" % c] = (lambda c=c: act(S("eqd", 1024 * c, 1024 * c + 1024), IND(S("tF", 0, W), S("h16", 64 * c, 64 * c + 64))), ["rest"])
            step["e%d" % c] = (lambda c=c: ops[tt(S("eqf", 1024 * c, 1024 * c + 1024), S("eqd", 1024 * c, 1024 * c + 1024), S("pT", 0, 1024),
                                                  A.is_equal)].update(c=MNX * vc(S("eqf", 0, 1024), S("pT", 0, 1024), S("pT", 0, 1024))),
                               ["f%d" % c, "C8"])
            for x, y in (("E", "abe"), ("K", "m"), ("S", "s")):
                step["%s%d" % (x, c)] = (lambda c=c, x=x: sums(x, c, "%s%d" % (x, c) in ends),
                                         [e for e in ("%s%d" % (z, c) for z in y) if e in queues[0] + queues[1]])
        keep[0] = not last
        done = []
        while any(queues):
            for k, o in enumerate(queues):
                while o:
                    x = o[0].rstrip("*")
                    if named.get(x) and ops[named[x][0]]["q"] == "vapg"[k]:
                        for i in range(len(named[x]) if x != o[0] else 1):
                            line(named[x].pop(0))
                    elif x not in step:
                        pass
                    elif all(y in done for y in step[x][1]):
                        first = len(ops)
                        step[x][0]()
                        for i in range(first, len(ops) if last else first):
                            name(x, i)
                        done.append(x)
                    else:
                        break
                    o.pop(0)
        keep[0] = False
        if last:
            for j, tab in enumerate(("tV", "tF", "tG")):
                for k in range(0, 32, SP):
                    mms([(S("pC", 128 * j, 128 * j + 128), whole("ib"), S(tab, 128 * e, 128 * e + 128),
                          j == 0 and e == 0, j == 2 and e == 31) for e in range(k, k + SP)])
                    ops[-1]["idle"] = True
                    if j == 0 and k == EARLY:
                        ops[-1]["after"] = named["H"][-1:]
            name("zb0", act(whole("zb0"), S("pC", 0, 384)))

        def call(x, i):
            if last:
                name(x, i)

        call("best", scan(whole("k2"), S("pK0", 0, 320), whole("kt"), A.max, A.min))
        call("best", tt(whole("k3"), S("k2", 4, 160, 5), S("k2", 164, 320, 5), A.max))
        call("best", tt(whole("ki"), S("k3", 0, 16), S("k3", 16, 32), A.max))
        call("best", ts(whole("val"), whole("ki"), 15, A.bitwise_and))
        call("best", ts(whole("nv"), whole("ki"), -BIG / 2, A.is_lt))
        call("best", ts(whole("valb"), whole("val"), 256.0, A.mult, -3840.0, A.add))
        call("step", tt(whole("step"), IND(whole("val"), whole("repc")), whole("jr"), A.is_lt))
        ops[-1]["after"] = [len(ops) - 2]
        call("ksel", scan(S("ksel", 0, L), whole("step"), whole("ktab"), A.mult, A.max))
        n = 2 if last else 5
        picked = []
        lists([(b, "iO", "nv") for b in range(n)])
        lists([(b, "i16", "valb") for b in range(1 if last else 3)] + [(n - 1, "ibn", "valb")], True)
        if last:
            call("sv", tt(S("s16", 16, 32), S("pA", 16, 32), S("own", 16, 32), A.min))
            call("hm", tt(S("hm", 0, 16), S("ksel", 15, L, 16), S("pA", 0, 16), A.add))
            call("s16", tt(S("s16", 0, 16), S("hm", 0, 16), S("own", 0, 16), A.min))
        else:
            consts("pK1", [(0, "ih", whole("oH")), (0, "i256", S("cE", 0, 48))])
            mm(S("pK1", 0, 16), whole("ibn"), whole("nv"), False, True)
            tt(S("s16", 48, 80), S("pA", 48, 80), whole("oS"), A.min)
            for bs in ((0,), (2, 1)):
                for b in bs:
                    yadd = tt(S("hm", 16 * b, 16 * b + 16), S("ksel", 15, L, 16), S("pA", 16 * b, 16 * b + 16), A.add)
                for b in bs:
                    tt(S("s16", 16 * b, 16 * b + 16), S("hm", 16 * b, 16 * b + 16), S("pK1", 16 * b, 16 * b + 16), A.min)
                picked.append(len(ops) - 1)

        def claims(cl, of, *cut):
            if t:
                call("plr", act(whole("plr"), IND(whole("jw"), cl)))
                for i in picked:
                    ops[i]["after"] = [len(ops) - 1]
            for o in (S("pb", 0, 16), whole("pq")):
                call("cl", ts(o, of, *cut, -2048.0, A.add))
            if 0 < t < RO - 1:
                ops[yadd]["after"] = [len(ops) - 1]
            if not t:
                tt(whole("plh"), IND(whole("pq"), whole("repc")), whole("dm"), A.mult)
                mm(S("pE0", L, 2 * L), whole("oneh"), whole("plh"), True, True)
                act(whole("plr"), S("pE0", L, 2 * L))
            call("cl", tt(S("pb", 16, 32), whole("pq"), S("pb", 0, 16), A.subtract))
            for c in CLAIMS:
                call("eq", ts(S("eqd", L * c + 16 * c, L * c + L), S("plr", 16 * c, L), S("pb", c, c + 1), A.subtract,
                              S("pb", 16 + c, 17 + c), A.is_equal))
                if last:
                    mms([(S("pE0", 8 * h, 8 * h + 8), S("eqd", L * c + 128 * h, L * c + 128 * h + 128), whole("sel8"),
                          c == CLAIMS[0] and h == c // 8, False) for h in range(c // 8, 2)])
                    continue
                if c == CLAIMS[0]:
                    mms([(S("pE0", 0, L), whole("ib"), whole("pz"), True, False), (S("pE0", 0, L), whole("ih"), whole("plr"), False, False)])
                    ops[-1]["after"] = ranked
                mms([(S("pE0", 16 * c, L), whole("onS"), S("eqd", L * c + 16 * c, L * c + L), False, False),
                     (S("pE0", 16 * c, 16 * c + 16), whole("ugS"), S("eqd", L * c + 16 * c, L * c + 16 * c + 16), False, c == CLAIMS[-1])])

        if not last:
            ops[cp(S("pre", 0, 1024, 4), IND(whole("tG"), S("s16", 0, 16)))]["after"] = picked[:1]
            mm(S("pB", 0, 16), whole("iO"), S("zf4", 0, 16), True, False)
            conv(S("pB", 0, 16), "zB", "pre", 0, 16, 4, False, True)
            picked[:] = [act(S("pre", 1, 1024, 4), IND(whole("tG"), S("s16", 16, 32))),
                         act(S("pre", 3, 1024, 4), IND(whole("nmw"), S("s16", 48, 64)))]
            act(S("pre", 2, 1024, 4), IND(whole("lo"), S("s16", 64, 80)))
            cp(whole("gi"), S("pB", 0, 16))
            ts(whole("g3"), whole("gi"), OFF + 3, A.bitwise_and)
            tt(whole("go4"), IND(whole("g3"), S("rep", 0, 4)), S("jq", 0, 64), A.is_equal)
            scan(whole("inc"), S("msk", 0, 64), whole("go4"), A.mult, A.add)
            mm(S("pC", 0, 64), whole("ib"), whole("cst"), True, False)
            mms([(S("pC", 0, 64), whole(w), whole("go4"), False, False) for w in ("uge", "iq")])
            ranked = [mm(S("pC", 0, 64), whole("ones"), whole("inc"), False, True)]
            tt(whole("tt4"), S("pC", 0, 64), whole("dm4"), A.min)
            tt(whole("tt2"), S("tt4", 0, 32), S("tt4", 32, 64), A.min)
            tt(whole("pos"), S("tt2", 0, 16), S("tt2", 16, 32), A.min)
            for d in range(4):
                if t:
                    act(S("idt", L * d, L * d + 64), S("jf", 0, 64), None, 256.0, 0.0)
                    ops[-1]["after"] = list(gathered)
            cp(IND(whole("idt"), whole("pos")), whole("jb"))
            for bank, ks in (("pB", (1,)), ("pK0", (2, 3, 4))):
                mms([(S(bank, 16 * k - 16, 16 * k), S("z4", 12 - 4 * e, 140 - 4 * e),
                      S("idt", L * ((rank + k) % N) + e, L * ((rank + k) % N) + 64, 4), e == 0, e == 3) for k in ks for e in range(4)])
                ts(S("src", 16 * ks[0] - 16, 16 * ks[-1]), S(bank, 16 * ks[0] - 16, 16 * ks[-1]), C(cJ), A.add)
            nxt, snd = "lnd%d" % (t + 1), "snd%d" % t
            here = S(nxt, L * rank, L * rank + L)
            sent = []
            for k in range(1, N):
                o = S(snd, L * (k - 1), L * k)
                (cp if k in SENDV else act)(o, IND(whole("pre"), S("src", 16 * k - 16, 16 * k)))
                dst = T.cores[(rank + k) % N]
                sem = "out%d" % (3 * t + k - 1)
                sent.append(rec("g", lambda o=o, here=here, sem=sem, t=t, dst=dst: g.remote_dma(
                    ap(here), ap(o), T.sem["arr%d" % t], T.sem[sem], topo.addr(dst)[1], topo.addr(dst)[0],
                    sum(1 << e for e in lanes_of(core, dst))),
                    [], [o], RISS, kind="rem", lat=RLAT + (3.0 if t == 0 and k == 1 else 0.0), sem=sem,
                    n=len(lanes_of(core, dst)), after=sent[-1:] or lines["g"]))
            act(S(snd, 768, 1024), IND(whole("pre"), S("src", 48, 64)))
            gathered[:] = [act(here, S(snd, 768, 1024))]
            n_in = sum(len(lanes_of(T.cores[q], core)) for q in range(N) if q != rank)
            landed = rec("x", None, [S(nxt, L * q, L * q + L) for q in range(N) if q != rank], [], 0.0, kind="land",
                         sem="arr%d" % t, n=n_in, after=sent)
            lines["g"] = sent[-1:]
            if t < 3:
                first = len(ops)
                if t == 0:
                    for buf, of, x in (("i32", "ib", 1.0), ("iZG", "ib", ZG / 3), ("iZV", "ib", ZV / 3)):
                        act(whole(buf), whole(of), scale=x)
                    act(whole("sel8"), S("ones", 0, 128, 16), scale=256.0)
                elif t == 1:
                    act(whole("rst"), whole("jr"), F.Sign, C(cY), -2.0)
                    act(whole("ugw"), whole("rst"), None, -0.5, -0.5)
                else:
                    for o, b in ((S("c0", 0, 16), 0), (S("c0", 16, 32), 4)):
                        act(o, whole("lo16"), None, float(mine[b][1]), float(mine[b][0]))
                    act(whole("rst"), whole("jr"), F.Relu, 1e29, -1e29)
                for i in range(first, len(ops)):
                    ops[i]["after"] = list(gathered)
                first = len(ops)
                if t == 1:
                    fill("jm", W, JW, 200)
                    fill("cF", 0, 64, -72 if 3 in ONV[2] else 184)
                for i in range(first, len(ops)):
                    ops[i]["after"] = list(sent[-1:])

            claims(S("s16", 32, 48), S("s16", 32, 48))
            scan(whole("cs"), whole("msk"), S("pE0", 0, L), A.mult, A.max)
            tt(whole("o16"), S("cs", 15, L, 16), whole("cd"), A.min)
            keep[0] = True
            for tab, j, n in (("tV", 2, 16), ("tF", 0, 16), ("tG", 1, GP if t < RO - 2 else 16)):
                cp(IND(S(tab, 0, LC), S("o16", 0, n)), S(lnd, j, 64 * n, 4))
            keep[0] = False
        else:
            call("yf", act(whole("yfb"), IND(whole("tG"), S("s16", 0, 16))))
            call("yv", act(whole("yvb"), IND(whole("lo"), S("s16", 16, 32))))
            dma("s", T.yf[:], whole("yfb"))
            dma("s", T.yv[:], whole("yvb"))
            call("ck", tt(whole("ck"), IND(S("pen", 0, L), whole("lhk")), whole("ktab"), A.add))
            call("cs", scan(whole("cs"), whole("rst"), whole("ck"), A.add, A.min))
            call("ci", tt(whole("ci"), S("cs", 15, L, 16), whole("nfb"), A.add))
            call("cm", ts(whole("cm"), whole("ci"), 4095 + 63 * 2 ** 25, A.bitwise_and))
            call("cl", ts(whole("cl"), whole("cm"), float(NC), A.min))
            claims(whole("cl"), whole("cm"), float(NC), A.min)
            call("plm", act(whole("plm"), IND(whole("jm"), whole("cl"))))
            call("dmk", tt(whole("dmk"), IND(whole("eqd"), whole("dgl")), whole("ugw"), A.mult))
            mms([(S("pE0", 8 * h, 8 * h + 8), S(x, 128 * h, 128 * h + 128), whole(w), False, h == 1 and x == "dmk")
                 for x, w in (("plm", "sel0"), ("dmk", "sel8")) for h in range(2)])
            call("pm", cp(S("pb", 32, 48), S("pE0", 0, 16)))
            for b, bank in enumerate(("pK1", "pB")):
                for h in range(2):
                    for e in range(4):
                        i = 8 * h + 4 * b + e
                        o = S("eqf", 128 * i, 128 * i + 128)
                        if i in ONA:
                            call("hot", act(S("sg", 128 * i, 128 * i + 128), S("jb", 0, 128), F.Abs, S("pb", 32 + i, 33 + i), -1.0))
                            call("hot", act(o, S("sg", 128 * i, 128 * i + 128), F.Relu, 1.0, -1.0))
                        else:
                            call("one", ts(o, S("jb", 0, 128), S("pb", 32 + i, 33 + i), A.is_equal))
                        mm(S(bank, 48 * e, 48 * e + 48), S("eqf", 128 * i, 128 * i + 128), S("vT", 48 * i, 48 * i + 48),
                           h == 0 and e == 0, h == 1 and e == 3)
            call("zts", act(S("zts", 0, 192), S("pK1", 0, 192)))
            call("zts", act(S("zts", 192, 384), S("pB", 0, 192)))
            ends = (("pE0", T.zf, 1), ("pK0", T.zg, 2), ("pK1", T.zv, 0))
            for j, (bank, out, b) in enumerate(ends):
                turn([(S(bank, 0, 128), S("zts", j, 384, 3))], "i32")
            for j, (bank, out, b) in enumerate(ends):
                call("z", tt(S("zb", 128 * j, 128 * j + 128), S(bank, 0, 128), S("zb0", 128 * b, 128 * b + 128), A.add))
                dma("a" if j == 1 else "s", out[:], S("zb", 128 * j, 128 * j + 128))
            for o in ORDER4:
                for x in o.split():
                    some = named[x.rstrip("*")]
                    for i in range(len(some) if x[-1] == "*" or x in step else 1):
                        line(some.pop(0))
    emit(g, T, arrange(ops))
